import numpy as np
import ml_dtypes


def mxq(x, axis, fmt="e4m3"):
    dtype, down = {"e4m3": (ml_dtypes.float8_e4m3fn, 7), "e5m2": (ml_dtypes.float8_e5m2, 14)}[fmt]
    v = np.moveaxis(np.asarray(x, np.float32).astype(ml_dtypes.bfloat16).astype(np.float64), axis, -1)
    blocks = v.reshape(v.shape[:-1] + (-1, 32))
    amax = np.abs(blocks).max(-1, keepdims=True)
    byte = np.maximum(np.where(amax > 0, np.frexp(amax)[1] - 1 + 127, 0) - down, 1)
    scale = np.exp2(byte - 127.0)
    codes = (blocks / scale).astype(np.float32).astype(dtype).astype(np.float64)
    return np.moveaxis((codes * scale).reshape(v.shape), -1, axis)


WIDE = False


def mx_kscale(k):
    if not WIDE:
        return np.ones(k)
    levels = np.array([10, -10, 5, -5, 0])
    if k % 512:
        return np.exp2(np.random.permutation(np.resize(levels, k // 32))).repeat(32)
    a = np.empty((k // 512, 16))
    for p in range(k // 512):
        a[p, :8] = np.random.permutation(np.resize(levels, 8))
        for g in range(8):
            far = levels[np.abs(levels - a[p, g]) >= 10]
            a[p, g + 8] = far[np.random.randint(len(far))]
    return np.exp2(a.ravel()).repeat(32)


BF16 = ml_dtypes.bfloat16


def bf(x):
    return np.asarray(x, np.float32).astype(BF16)


def f64(x):
    return np.asarray(x).astype(np.float64)


E2M1 = np.array([0.0, 0.5, 1.0, 1.5, 2.0, 3.0, 4.0, 6.0, -0.0, -0.5, -1.0, -1.5, -2.0, -3.0, -4.0, -6.0])


def pack_weight(w, fmt):
    k, n = w.shape
    w = f64(bf(w)).reshape(k // 32, 32, n)
    amax = np.abs(w).max(1)
    if fmt == "e4m3":
        byte = np.frexp(amax)[1] - 1 + 127 - 7
    else:
        mant, ex = np.frexp(amax / 6.0)
        byte = np.where(mant > 0.5, ex, ex - 1) + 127
    byte = np.clip(np.where(amax > 0, byte, 1), 1, 254)
    scaled = (w * np.exp2(127.0 - byte)[:, None, :]).reshape(k, n).astype(np.float32)
    by_word = np.ascontiguousarray(scaled.reshape(k // 512, 128, 4, n).transpose(0, 1, 3, 2))
    if fmt == "e4m3":
        words = by_word.astype(ml_dtypes.float8_e4m3fn).view(np.uint8)
    else:
        c = by_word.astype(ml_dtypes.float4_e2m1fn).view(np.uint8) & 0xF
        words = c[..., 0::2] | (c[..., 1::2] << 4)
    return np.ascontiguousarray(words), np.ascontiguousarray(byte.astype(np.uint8).reshape(k // 512, 16, n))


def unpack_weight(words, scales, fmt):
    g, p, n, _ = words.shape
    if fmt == "e4m3":
        vals = np.ascontiguousarray(words).view(ml_dtypes.float8_e4m3fn).astype(np.float64)
    else:
        nib = np.empty((g, p, n, 4), np.uint8)
        nib[..., 0::2] = words & 0xF
        nib[..., 1::2] = words >> 4
        vals = E2M1[nib]
    vals = vals * np.repeat(np.exp2(scales.astype(np.float64) - 127.0), 8, axis=1)[..., None]
    return vals.transpose(0, 1, 3, 2).reshape(g * 512, n)
def pack4(w):
    words, scales = pack_weight(w, "e2m1")
    return words.reshape(words.shape[0], 128, -1), scales


def unpack4(words, scales):
    return unpack_weight(words.reshape(words.shape[0], 128, -1, 2), scales, "e2m1")


M, KA, KB, N, C = 2048, 512, 1024, 1024, 512


def draw0():
    s = mx_kscale(KA)
    u = mx_kscale(KB)
    r = mx_kscale(M)
    wb = np.random.standard_normal((KB, N)) / np.sqrt(2 * KB) / u[:, None]
    z = np.random.standard_normal((M, C)) / np.sqrt(M) / r[:, None]
    wb_words, wb_scales = pack4(wb)
    z_words, z_scales = pack4(z)
    return {"xa": bf(np.random.standard_normal((M, KA)) * s),
            "wa": bf(np.random.standard_normal((KA, N)) / np.sqrt(2 * KA) / s[:, None]),
            "xb": bf(np.random.standard_normal((M, KB)) * u),
            "wb_words": wb_words, "wb_scales": wb_scales,
            "omega": bf(np.random.uniform(0.5, 1.5, M) * r),
            "z_words": z_words, "z_scales": z_scales,
            "target": bf(0.5 * np.random.standard_normal((C, N))),
            "prec": bf(1 + 0.1 * np.random.standard_normal(N))}


def core(xa, wa, xb, wb_words, wb_scales, omega, z_words, z_scales, target, prec):
    wb = unpack4(wb_words, wb_scales)
    z = unpack4(z_words, z_scales)
    h = (mxq(f64(xa), 1, "e4m3") @ mxq(f64(wa), 0, "e4m3")) + (mxq(f64(xb), 1, "e4m3") @ wb)
    v = h * h * f64(omega)[:, None]
    m = z.T @ mxq(v, 0, "e4m3")
    return (m - f64(target)) * f64(prec)


def e4m3fn_bytes(y):
    return np.clip(np.asarray(y, np.float64), -448.0, 448.0).astype(np.float32).astype(ml_dtypes.float8_e4m3fn).view(np.uint8)


def e4m3fn_values(b):
    return np.asarray(b, np.uint8).view(ml_dtypes.float8_e4m3fn).astype(np.float64)


def setup_inputs():
    d = draw0()
    x0 = np.asarray(d['xb']).astype(np.float64)
    s = (np.max(np.abs(x0), axis=(0,), keepdims=True) / 448.0).astype(np.float32)
    out = {}
    for k, v in d.items():
        if k == 'xb':
            out['xb_bytes'] = e4m3fn_bytes(x0 / s.astype(np.float64))
            out['xb_scale'] = s
        else:
            out[k] = v
    return out


def reference(xa, wa, xb_bytes, xb_scale, wb_words, wb_scales, omega, z_words, z_scales, target, prec):
    return core(xa, wa, e4m3fn_values(xb_bytes) * xb_scale.astype(np.float64), wb_words, wb_scales, omega, z_words, z_scales, target, prec)

@@ -1,0 +1,349 @@
+from contextlib import ExitStack
+
+import concourse.mybir as mybir
+from concourse.masks import make_identity
+
+F32 = mybir.dt.float32
+BF16 = mybir.dt.bfloat16
+U32 = mybir.dt.uint32
+I32 = mybir.dt.int32
+U8 = mybir.dt.uint8
+FP8 = mybir.dt.float8_e4m3fn
+FP8X4 = mybir.dt.float8_e4m3fn_x4
+FP4X4 = mybir.dt.float4_e2m1fn_x4
+MULT = mybir.AluOpType.mult
+SUBTRACT = mybir.AluOpType.subtract
+SQUARE = mybir.ActivationFunctionType.Square
+
+M, KA, KB, N, C = 2048, 512, 1024, 1024, 512
+P = 128
+PACK = 4
+K_PASS = P * PACK
+GROUPS = M // K_PASS
+B_PASSES = KB // K_PASS
+HALF = 512
+C_TILES = C // P
+
+BANKS = {"flip": 3, "prod": 5}
+MOMENT_BANK = {
+    (0, 0): "prod", (0, 1): "prod", (0, 2): "flip", (0, 3): "flip",
+    (1, 0): "prod", (1, 1): "prod", (1, 2): "flip", (1, 3): "prod",
+}
+
+FLOPS = 2 * M * N * (KA + KB) + 2 * C * N * M
+
+
+def tile_projection_moment_gap_s3_kernel(
+    tc, xa, wa, xb_bytes, xb_scale, wb_words, wb_scales, omega, z_words, z_scales, target, prec, out
+):
+    nc = tc.nc
+    with ExitStack() as ctx:
+        ctx.enter_context(tc.manual_schedule())
+        keep = ctx.enter_context(tc.tile_pool(name="keep", bufs=1))
+        work = ctx.enter_context(tc.tile_pool(name="work", bufs=2))
+        psum = ctx.enter_context(tc.psum_pool(name="psum", bufs=2))
+
+        xa_rows = [keep.tile([P, PACK, KA], BF16, name="xa_rows%d" % g) for g in range(GROUPS)]
+        xb_codes_in = [keep.tile([P, PACK, KB], U8, name="xb_codes_in%d" % g) for g in range(GROUPS)]
+        scale_col = keep.tile([P, 2, PACK], F32, name="scale_col")
+        scale_rows = keep.tile([P, KB], F32, name="scale_rows")
+        wa_rows = [keep.tile([P, PACK, HALF], BF16, name="wa_rows%d" % i) for i in range(2)]
+        wa_codes = keep.tile([P, N], U32, name="wa_codes", align_bytes=64)
+        wa_bytes = keep.tile([P, N], U8, name="wa_bytes", align_bytes=64)
+        wb_tile = keep.tile([P, B_PASSES, 2 * N], U8, name="wb_tile", align_bytes=64)
+        wb_bytes = keep.tile([P, B_PASSES, N], U8, name="wb_bytes", align_bytes=64)
+        z_tile = keep.tile([P, GROUPS, 2 * C], U8, name="z_tile", align_bytes=64)
+        z_bytes = keep.tile([P, GROUPS, C], U8, name="z_bytes", align_bytes=64)
+        omega_bf16 = keep.tile([P, GROUPS, PACK], BF16, name="omega_bf16")
+        omega_f32 = keep.tile([P, GROUPS, PACK], F32, name="omega_f32")
+        prec_rows = keep.tile([P, N], BF16, name="prec_rows")
+        target_rows = keep.tile([P, C_TILES, N], BF16, name="target_rows")
+        ident = keep.tile([P, P], F32, name="ident")
+        zeros = keep.tile([P, HALF], BF16, name="zeros")
+
+        nc.sync.dma_start(out=scale_col[:], in_=xb_scale.rearrange("o (h p j) -> p (o h) j", h=2, j=PACK))
+        nc.vector.memset(wb_bytes[:].rearrange("p g n -> p (g n)").bitcast(I32), 0)
+        nc.vector.memset(z_bytes[:].rearrange("p g n -> p (g n)").bitcast(I32), 0)
+        nc.gpsimd.memset(zeros[:], 0.0)
+        make_identity(nc, ident[:])
+
+        def load_xa(g):
+            rows = xa[K_PASS * g : K_PASS * (g + 1), :]
+            nc.sync.dma_start(out=xa_rows[g][:], in_=rows.rearrange("(p t) k -> p t k", t=PACK))
+
+        def load_xb(g, t0, t1):
+            rows = xb_bytes[K_PASS * g : K_PASS * (g + 1), :].rearrange("(p t) k -> p t k", t=PACK)
+            nc.sync.dma_start(out=xb_codes_in[g][:, t0:t1, :], in_=rows[:, t0:t1, :])
+
+        def load_wa(half):
+            rows = wa.rearrange("(p j) n -> p j n", j=PACK)
+            nc.sync.dma_start(out=wa_rows[half][:], in_=rows[:, :, HALF * half : HALF * (half + 1)])
+
+        def load_scale_bytes(plane, scale_bytes):
+            rows = scale_bytes.rearrange("g (q r) n -> r q g n", r=4)
+            for r in range(4):
+                nc.sync.dma_start(out=plane[r:P:32].bitcast(I32), in_=rows[r].bitcast(I32))
+
+        nc.sync.dma_start(out=omega_bf16[:], in_=omega.rearrange("(g p t) -> p g t", p=P, t=PACK))
+        load_wa(0)
+        load_xb(0, 0, 2)
+        load_xa(0)
+        load_xb(0, 2, 4)
+        load_wa(1)
+        load_scale_bytes(wb_bytes, wb_scales)
+        nc.sync.dma_start(out=wb_tile[:], in_=wb_words.rearrange("g p n -> p g n"))
+        load_xb(1, 0, 4)
+        load_xa(1)
+        load_xa(2)
+        load_xb(2, 0, 4)
+        load_xa(3)
+        load_xb(3, 0, 4)
+        load_scale_bytes(z_bytes, z_scales)
+        nc.sync.dma_start(out=z_tile[:], in_=z_words.rearrange("g p n -> p g n"))
+        nc.sync.dma_start(out=prec_rows[:], in_=prec.partition_broadcast(P))
+        nc.sync.dma_start(out=target_rows[:], in_=target.rearrange("(ct c) n -> c ct n", c=P))
+
+        idle_bank = psum.tile([P, HALF], F32, name="prod", bufs=BANKS["prod"])
+
+        def keep_tensor_busy(count):
+            for i in range(count):
+                nc.tensor.matmul(out=idle_bank[:], lhsT=zeros[:, :P], rhs=zeros[:], start=True, stop=True)
+
+        def spread_xb_scale():
+            for half, copy in ((0, nc.vector.tensor_copy), (1, nc.scalar.copy)):
+                bank = psum.tile([P, PACK, P], F32, name="flip", bufs=BANKS["flip"])
+                for j in range(PACK):
+                    nc.tensor.transpose(bank[:, j, :], scale_col[:, half, j : j + 1].to_broadcast([P, P]), ident[:])
+                copy(
+                    out=scale_rows[:, HALF * half : HALF * (half + 1)].rearrange("p (n j) -> p n j", j=PACK),
+                    in_=bank[:].rearrange("p j n -> p n j"),
+                )
+
+        grouped = {}
+        codes = {}
+
+        def quantize(name, part=0, parts=1):
+            if part == 0:
+                codes[name] = (
+                    keep.tile([P, K_PASS], U32, name="codes_%s%d%d" % name, align_bytes=64),
+                    keep.tile([P, K_PASS], U8, name="bytes_%s%d%d" % name, align_bytes=64),
+                )
+            words, scale_bytes = codes[name]
+            width = K_PASS // parts
+            cols = slice(width * part, width * (part + 1))
+            nc.vector.quantize_mx(
+                out=words[:, cols].bitcast(FP8X4),
+                scales=scale_bytes[:, cols],
+                in_=grouped[name][:, PACK * width * part : PACK * width * (part + 1)],
+            )
+
+        def group_wa(half):
+            tile = work.tile([P, PACK * HALF], BF16, name="wa_grouped", align_bytes=64)
+            nc.scalar.copy(
+                out=tile[:].rearrange("p (n j) -> p n j", j=PACK), in_=wa_rows[half][:].rearrange("p j n -> p n j")
+            )
+            grouped["wa", half] = tile
+
+        def quantize_wa(half):
+            cols = slice(HALF * half, HALF * (half + 1))
+            nc.vector.quantize_mx(
+                out=wa_codes[:, cols].bitcast(FP8X4), scales=wa_bytes[:, cols], in_=grouped["wa", half][:]
+            )
+
+        xb_rows = {}
+
+        def scale_xb(g, t, parts=1):
+            tile = work.tile([P, KB], BF16, name="xb_scaled", bufs=6)
+            width = KB // parts
+            for i in range(parts):
+                ks = slice(width * i, width * (i + 1))
+                nc.vector.tensor_tensor(
+                    out=tile[:, ks], in0=xb_codes_in[g][:, t, ks].bitcast(FP8), in1=scale_rows[:, ks], op=MULT
+                )
+            xb_rows[g, t] = tile
+
+        def turn(rows, dst, pair):
+            bank = psum.tile([P, 2, 2, P], F32, name="flip", bufs=BANKS["flip"])
+            for i in range(2):
+                for u in range(2):
+                    nc.tensor.transpose(bank[:, i, u, :], rows[i][:, u::2], ident[:])
+            width = 2 * P * PACK
+            nc.scalar.copy(
+                out=dst[:, width * pair : width * (pair + 1)].bitcast(F32).rearrange("p (t r u) -> p t r u", t=2, u=2),
+                in_=bank[:].rearrange("p t u r -> p t r u"),
+            )
+
+        def turn_xa(g):
+            dst = work.tile([P, PACK * K_PASS], BF16, name="x_grouped", bufs=6, align_bytes=64)
+            for pair in range(2):
+                turn([xa_rows[g][:, 2 * pair + i, :].bitcast(F32) for i in range(2)], dst, pair)
+            grouped["a", g, 0] = dst
+
+        def turn_xb(g, pair):
+            for b in range(B_PASSES):
+                if pair == 0:
+                    dst = work.tile([P, PACK * K_PASS], BF16, name="x_grouped", bufs=6, align_bytes=64)
+                    grouped["b", g, b] = dst
+                ks = slice(K_PASS * b, K_PASS * (b + 1))
+                turn([xb_rows[g, 2 * pair + i][:, ks].bitcast(F32) for i in range(2)], grouped["b", g, b], pair)
+
+        def quantize_xb(g, part=0, parts=1):
+            for b in range(B_PASSES):
+                quantize(("b", g, b), part, parts)
+
+        squares = {}
+        pairs = {}
+
+        def project(g, half, t):
+            bank = psum.tile([P, HALF], F32, name="prod", bufs=BANKS["prod"])
+            samples = slice(P * t, P * (t + 1))
+            cols = slice(HALF * half, HALF * (half + 1))
+            words, scale_bytes = codes["a", g, 0]
+            nc.tensor.matmul_mx(
+                out=bank[:],
+                lhsT=words[:, samples].bitcast(FP8X4),
+                lhsT_scale=scale_bytes[:, samples],
+                rhs=wa_codes[:, cols].bitcast(FP8X4),
+                rhs_scale=wa_bytes[:, cols],
+                start=True,
+                stop=False,
+            )
+            for b in range(B_PASSES):
+                words, scale_bytes = codes["b", g, b]
+                nc.tensor.matmul_mx(
+                    out=bank[:],
+                    lhsT=words[:, samples].bitcast(FP8X4),
+                    lhsT_scale=scale_bytes[:, samples],
+                    rhs=wb_tile[:, b, 2 * HALF * half : 2 * HALF * (half + 1)].bitcast(FP4X4),
+                    rhs_scale=wb_bytes[:, b, cols],
+                    start=False,
+                    stop=(b == B_PASSES - 1),
+                )
+            tile = work.tile([P, HALF], F32, name="square", bufs=9)
+            nc.scalar.activation(out=tile[:], in_=bank[:], func=SQUARE)
+            squares[g, half, t] = tile
+
+        def weigh(g, half, t):
+            if t == 0:
+                pairs[g, half] = work.tile([P, PACK * HALF], BF16, name="v_pairs", bufs=4)
+            slots = pairs[g, half][:].rearrange("p (a n e) -> p a n e", a=2, e=2)
+            nc.vector.tensor_scalar(
+                out=slots[:, t // 2, :, t % 2],
+                in0=squares[g, half, t][:],
+                scalar1=omega_f32[:, g, t : t + 1],
+                scalar2=None,
+                op0=MULT,
+            )
+            if t == PACK - 1:
+                tile = work.tile([P, PACK * HALF], BF16, name="v_grouped", bufs=4, align_bytes=64)
+                nc.scalar.copy(
+                    out=tile[:].bitcast(F32).rearrange("p (n a) -> p n a", a=2),
+                    in_=pairs[g, half][:].bitcast(F32).rearrange("p (a n) -> p n a", a=2),
+                )
+                grouped["v", g, half] = tile
+
+        sums = {}
+        gaps = {}
+
+        def moment(half, ct):
+            tag = MOMENT_BANK[half, ct]
+            sums[half, ct] = psum.tile([P, HALF], F32, name=tag, bufs=BANKS[tag])
+            for g in range(GROUPS):
+                words, scale_bytes = codes["v", g, half]
+                nc.tensor.matmul_mx(
+                    out=sums[half, ct][:],
+                    lhsT=z_tile[:, g, 2 * P * ct : 2 * P * (ct + 1)].bitcast(FP4X4),
+                    lhsT_scale=z_bytes[:, g, P * ct : P * (ct + 1)],
+                    rhs=words[:].bitcast(FP8X4),
+                    rhs_scale=scale_bytes[:],
+                    start=(g == 0),
+                    stop=(g == GROUPS - 1),
+                )
+
+        def subtract_target(half, ct):
+            tile = work.tile([P, HALF], F32, name="gap", bufs=4)
+            cols = slice(HALF * half, HALF * (half + 1))
+            nc.vector.tensor_tensor(out=tile[:], in0=sums[half, ct][:], in1=target_rows[:, ct, cols], op=SUBTRACT)
+            gaps[half, ct] = tile
+
+        def scale_and_store(half, ct, engine):
+            tile = work.tile([P, HALF], F32, name="result", bufs=4)
+            cols = slice(HALF * half, HALF * (half + 1))
+            engine.tensor_tensor(out=tile[:], in0=gaps[half, ct][:], in1=prec_rows[:, cols], op=MULT)
+            nc.sync.dma_start(out=out[P * ct : P * (ct + 1), cols], in_=tile[:])
+
+        keep_tensor_busy(3)
+        spread_xb_scale()
+        keep_tensor_busy(3)
+        group_wa(0)
+        turn_xa(0)
+        keep_tensor_busy(2)
+        scale_xb(0, 0, parts=2)
+        scale_xb(0, 1)
+        turn_xb(0, 0)
+        keep_tensor_busy(2)
+        scale_xb(0, 2)
+        scale_xb(0, 3)
+        quantize(("a", 0, 0))
+        quantize_wa(0)
+        quantize_xb(0, 0, 2)
+        group_wa(1)
+        turn_xb(0, 1)
+        nc.vector.tensor_copy(out=omega_f32[:], in_=omega_bf16[:])
+
+        order = [(g, half, t) for g in range(GROUPS) for half in range(2) for t in range(PACK)]
+        scale_xb(1, 0)
+        project(*order[0])
+        project(*order[1])
+        scale_xb(1, 1)
+        quantize_xb(0, 1, 2)
+        quantize_wa(1)
+        scale_xb(1, 2)
+        scale_xb(1, 3)
+        turn_xa(1)
+
+        weighed = 0
+        for step in range(17):
+            g, phase = divmod(step + 3, 4)
+            if phase in (0, 1) and g < GROUPS:
+                turn_xb(g, phase)
+            if phase == 2 and 1 <= g < GROUPS - 1:
+                turn_xa(g + 1)
+
+            until = 2 * step + (1 if step < 12 else 0)
+            while weighed < until:
+                weigh(*order[weighed])
+                weighed += 1
+            for bank in order[2 * step + 2 : 2 * step + 4]:
+                project(*bank)
+
+            if step == 0:
+                quantize(("a", 1, 0))
+            if phase == 3 and 2 <= g + 1 < GROUPS:
+                quantize(("a", g + 1, 0))
+            if phase == 1 and g < GROUPS:
+                quantize_xb(g)
+            if 1 <= step <= 8:
+                scale_xb(*divmod(step + 7, PACK))
+            if step >= 4 and step % 2 == 0 and step < 16:
+                quantize(("v",) + divmod(step // 2 - 2, 2))
+            if step == 15:
+                quantize(("v", 3, 0))
+
+        for ct in range(C_TILES):
+            moment(0, ct)
+        subtract_target(0, 0)
+        scale_and_store(0, 0, nc.gpsimd)
+        subtract_target(0, 1)
+        quantize(("v", 3, 1))
+        subtract_target(0, 2)
+        scale_and_store(0, 1, nc.vector)
+        subtract_target(0, 3)
+        scale_and_store(0, 2, nc.vector)
+        previous = (0, 3)
+        for ct in range(C_TILES):
+            moment(1, ct)
+            subtract_target(1, ct)
+            scale_and_store(*previous, nc.vector)
+            previous = (1, ct)
+        scale_and_store(*previous, nc.vector)

@@ -12,23 +12,31 @@ FP8 = mybir.dt.float8_e4m3fn
 FP8X4 = mybir.dt.float8_e4m3fn_x4
 FP4X4 = mybir.dt.float4_e2m1fn_x4
 MULT = mybir.AluOpType.mult
+ADD = mybir.AluOpType.add
+MAX = mybir.AluOpType.max
+IS_GE = mybir.AluOpType.is_ge
 SUBTRACT = mybir.AluOpType.subtract
 SQUARE = mybir.ActivationFunctionType.Square
+SQRT = mybir.ActivationFunctionType.Sqrt
+ABS = mybir.ActivationFunctionType.Abs
+SIGN = mybir.ActivationFunctionType.Sign
 
 M, KA, KB, N, C = 2048, 512, 1024, 1024, 512
 P = 128
 PACK = 4
 K_PASS = P * PACK
 GROUPS = M // K_PASS
-B_PASSES = KB // K_PASS
+ROWS = GROUPS * PACK
+PASSES = (KA + KB) // K_PASS
 HALF = 512
+QUARTER = 256
 C_TILES = C // P
 
-BANKS = {"flip": 3, "prod": 5}
-MOMENT_BANK = {
-    (0, 0): "prod", (0, 1): "prod", (0, 2): "flip", (0, 3): "flip",
-    (1, 0): "prod", (1, 1): "prod", (1, 2): "flip", (1, 3): "prod",
-}
+XB_BUFS = 6
+XG_BUFS = 4
+VP_BUFS = 5
+SORT_BUFS = 4
+SORT_A = 2
 
 FLOPS = 2 * M * N * (KA + KB) + 2 * C * N * M
 
@@ -41,309 +49,501 @@ def tile_projection_moment_gap_s3_kernel(
         ctx.enter_context(tc.manual_schedule())
         keep = ctx.enter_context(tc.tile_pool(name="keep", bufs=1))
         work = ctx.enter_context(tc.tile_pool(name="work", bufs=2))
-        psum = ctx.enter_context(tc.psum_pool(name="psum", bufs=2))
+        psum = ctx.enter_context(tc.psum_pool(name="psum", bufs=1))
 
-        xa_rows = [keep.tile([P, PACK, KA], BF16, name="xa_rows%d" % g) for g in range(GROUPS)]
-        xb_codes_in = [keep.tile([P, PACK, KB], U8, name="xb_codes_in%d" % g) for g in range(GROUPS)]
+        def bank(i):
+            return psum.tile([P, HALF], F32, name="bank%d" % i)
+
+        def small(name, dtype=F32):
+            return keep.tile([P, ROWS], dtype, name=name)
+
         scale_col = keep.tile([P, 2, PACK], F32, name="scale_col")
         scale_rows = keep.tile([P, KB], F32, name="scale_rows")
         wa_rows = [keep.tile([P, PACK, HALF], BF16, name="wa_rows%d" % i) for i in range(2)]
         wa_codes = keep.tile([P, N], U32, name="wa_codes", align_bytes=64)
         wa_bytes = keep.tile([P, N], U8, name="wa_bytes", align_bytes=64)
-        wb_tile = keep.tile([P, B_PASSES, 2 * N], U8, name="wb_tile", align_bytes=64)
-        wb_bytes = keep.tile([P, B_PASSES, N], U8, name="wb_bytes", align_bytes=64)
+        wb_tiles = [keep.tile([P, 2, 2 * HALF], U8, name="wb_tile%d" % i, align_bytes=64) for i in range(2)]
+        wb_bytes = keep.tile([P, 2, N], U8, name="wb_bytes", align_bytes=64)
         z_tile = keep.tile([P, GROUPS, 2 * C], U8, name="z_tile", align_bytes=64)
         z_bytes = keep.tile([P, GROUPS, C], U8, name="z_bytes", align_bytes=64)
         omega_bf16 = keep.tile([P, GROUPS, PACK], BF16, name="omega_bf16")
-        omega_f32 = keep.tile([P, GROUPS, PACK], F32, name="omega_f32")
         prec_rows = keep.tile([P, N], BF16, name="prec_rows")
         target_rows = keep.tile([P, C_TILES, N], BF16, name="target_rows")
         ident = keep.tile([P, P], F32, name="ident")
-        zeros = keep.tile([P, HALF], BF16, name="zeros")
+        ident_bf16 = keep.tile([P, P], BF16, name="ident_bf16")
 
-        nc.sync.dma_start(out=scale_col[:], in_=xb_scale.rearrange("o (h p j) -> p (o h) j", h=2, j=PACK))
-        nc.vector.memset(wb_bytes[:].rearrange("p g n -> p (g n)").bitcast(I32), 0)
-        nc.vector.memset(z_bytes[:].rearrange("p g n -> p (g n)").bitcast(I32), 0)
-        nc.gpsimd.memset(zeros[:], 0.0)
-        make_identity(nc, ident[:])
+        xa_rows = {}
+        xa_tiles = {}
+        xb_in = {}
 
-        def load_xa(g):
-            rows = xa[K_PASS * g : K_PASS * (g + 1), :]
-            nc.sync.dma_start(out=xa_rows[g][:], in_=rows.rearrange("(p t) k -> p t k", t=PACK))
+        def load_x(store, src, dtype, width, name, r0, count):
+            g, t0 = divmod(r0, PACK)
+            tile = keep.tile([P, count, width], dtype, name="%s%d" % (name, r0))
+            rows = src[K_PASS * g : K_PASS * (g + 1), :].rearrange("(p t) k -> p t k", t=PACK)
+            nc.sync.dma_start(out=tile[:], in_=rows[:, t0 : t0 + count, :])
+            for i in range(count):
+                store[r0 + i] = tile[:, i, :]
+            return tile
 
-        def load_xb(g, t0, t1):
-            rows = xb_bytes[K_PASS * g : K_PASS * (g + 1), :].rearrange("(p t) k -> p t k", t=PACK)
-            nc.sync.dma_start(out=xb_codes_in[g][:, t0:t1, :], in_=rows[:, t0:t1, :])
+        def load_xa(r0, count):
+            xa_tiles[r0] = load_x(xa_rows, xa, BF16, KA, "xa_rows", r0, count)
+
+        def load_xb(r0, count):
+            load_x(xb_in, xb_bytes, U8, KB, "xb_in", r0, count)
 
         def load_wa(half):
             rows = wa.rearrange("(p j) n -> p j n", j=PACK)
             nc.sync.dma_start(out=wa_rows[half][:], in_=rows[:, :, HALF * half : HALF * (half + 1)])
+
+        def load_wb(half):
+            words = wb_words.rearrange("g p n -> p g n")
+            nc.sync.dma_start(out=wb_tiles[half][:], in_=words[:, :, 2 * HALF * half : 2 * HALF * (half + 1)])
 
         def load_scale_bytes(plane, scale_bytes):
             rows = scale_bytes.rearrange("g (q r) n -> r q g n", r=4)
             for r in range(4):
                 nc.sync.dma_start(out=plane[r:P:32].bitcast(I32), in_=rows[r].bitcast(I32))
 
-        nc.sync.dma_start(out=omega_bf16[:], in_=omega.rearrange("(g p t) -> p g t", p=P, t=PACK))
-        load_wa(0)
-        load_xb(0, 0, 2)
-        load_xa(0)
-        load_xb(0, 2, 4)
-        load_wa(1)
-        load_scale_bytes(wb_bytes, wb_scales)
-        nc.sync.dma_start(out=wb_tile[:], in_=wb_words.rearrange("g p n -> p g n"))
-        load_xb(1, 0, 4)
-        load_xa(1)
-        load_xa(2)
-        load_xb(2, 0, 4)
-        load_xa(3)
-        load_xb(3, 0, 4)
-        load_scale_bytes(z_bytes, z_scales)
-        nc.sync.dma_start(out=z_tile[:], in_=z_words.rearrange("g p n -> p g n"))
-        nc.sync.dma_start(out=prec_rows[:], in_=prec.partition_broadcast(P))
-        nc.sync.dma_start(out=target_rows[:], in_=target.rearrange("(ct c) n -> c ct n", c=P))
+        def load_scale_col():
+            nc.sync.dma_start(out=scale_col[:], in_=xb_scale.rearrange("o (h p j) -> p (o h) j", h=2, j=PACK))
 
-        idle_bank = psum.tile([P, HALF], F32, name="prod", bufs=BANKS["prod"])
+        def load_omega():
+            nc.sync.dma_start(out=omega_bf16[:], in_=omega.rearrange("(g p t) -> p g t", p=P, t=PACK))
 
-        def keep_tensor_busy(count):
-            for i in range(count):
-                nc.tensor.matmul(out=idle_bank[:], lhsT=zeros[:, :P], rhs=zeros[:], start=True, stop=True)
+        def load_rest():
+            load_scale_bytes(z_bytes, z_scales)
+            nc.sync.dma_start(out=z_tile[:], in_=z_words.rearrange("g p n -> p g n"))
+            nc.sync.dma_start(out=target_rows[:], in_=target.rearrange("(ct c) n -> c ct n", c=P))
+            nc.sync.dma_start(out=prec_rows[:], in_=prec.partition_broadcast(P))
 
-        def spread_xb_scale():
-            for half, copy in ((0, nc.vector.tensor_copy), (1, nc.scalar.copy)):
-                bank = psum.tile([P, PACK, P], F32, name="flip", bufs=BANKS["flip"])
-                for j in range(PACK):
-                    nc.tensor.transpose(bank[:, j, :], scale_col[:, half, j : j + 1].to_broadcast([P, P]), ident[:])
-                copy(
-                    out=scale_rows[:, HALF * half : HALF * (half + 1)].rearrange("p (n j) -> p n j", j=PACK),
-                    in_=bank[:].rearrange("p j n -> p n j"),
+        omega_flat = omega_bf16[:].rearrange("p g t -> p (g t)")
+        size, sign, power, inv_power = small("size"), small("sign"), small("power"), small("inv_power")
+        radicand, guess, half_guess, inv_guess = small("radicand"), small("guess"), small("half_guess"), small("inv_guess")
+        quotient, root, factor = small("quotient"), small("root"), small("factor", BF16)
+        root_steps = [
+            lambda: nc.scalar.activation(out=size[:], in_=omega_flat, func=ABS),
+            lambda: nc.scalar.activation(out=sign[:], in_=omega_flat, func=SIGN),
+            lambda: nc.vector.tensor_scalar(
+                out=power[:], in0=size[:], scalar1=2.0**-64, scalar2=2.0**-64, op0=IS_GE, op1=MAX
+            ),
+            lambda: nc.vector.reciprocal(out=inv_power[:], in_=power[:]),
+            lambda: nc.vector.tensor_tensor(out=radicand[:], in0=size[:], in1=inv_power[:], op=MULT),
+            lambda: nc.scalar.activation(out=guess[:], in_=radicand[:], func=SQRT, scale=2.0**-10),
+            lambda: nc.vector.tensor_tensor(out=factor[:], in0=sign[:], in1=power[:], op=MULT),
+            lambda: nc.vector.tensor_scalar(
+                out=half_guess[:], in0=guess[:], scalar1=2.0**-60, scalar2=16.0, op0=MAX, op1=MULT
+            ),
+            lambda: nc.vector.reciprocal(out=inv_guess[:], in_=half_guess[:]),
+            lambda: nc.vector.tensor_tensor(out=quotient[:], in0=radicand[:], in1=inv_guess[:], op=MULT),
+            lambda: nc.vector.scalar_tensor_tensor(
+                out=root[:], in0=quotient[:], scalar=0.25, in1=half_guess[:], op0=MULT, op1=ADD
+            ),
+        ]
+
+        def root_step(first, last):
+            for step in root_steps[first:last]:
+                step()
+
+        def spread_scale(half, where, copy):
+            tile = bank(where)
+            for j in range(PACK):
+                nc.tensor.transpose(
+                    tile[:, P * j : P * (j + 1)], scale_col[:, half, j : j + 1].to_broadcast([P, P]), ident[:]
                 )
-
-        grouped = {}
-        codes = {}
-
-        def quantize(name, part=0, parts=1):
-            if part == 0:
-                codes[name] = (
-                    keep.tile([P, K_PASS], U32, name="codes_%s%d%d" % name, align_bytes=64),
-                    keep.tile([P, K_PASS], U8, name="bytes_%s%d%d" % name, align_bytes=64),
-                )
-            words, scale_bytes = codes[name]
-            width = K_PASS // parts
-            cols = slice(width * part, width * (part + 1))
-            nc.vector.quantize_mx(
-                out=words[:, cols].bitcast(FP8X4),
-                scales=scale_bytes[:, cols],
-                in_=grouped[name][:, PACK * width * part : PACK * width * (part + 1)],
+            copy(
+                out=scale_rows[:, HALF * half : HALF * (half + 1)].rearrange("p (n j) -> p n j", j=PACK),
+                in_=tile[:].rearrange("p (j n) -> p n j", j=PACK),
             )
 
-        def group_wa(half):
-            tile = work.tile([P, PACK * HALF], BF16, name="wa_grouped", align_bytes=64)
-            nc.scalar.copy(
-                out=tile[:].rearrange("p (n j) -> p n j", j=PACK), in_=wa_rows[half][:].rearrange("p j n -> p n j")
+        spread_banks = {}
+
+        def spread_turn(half, where):
+            spread_banks[half] = bank(where)
+            for j in range(PACK):
+                nc.tensor.transpose(
+                    spread_banks[half][:, P * j : P * (j + 1)], scale_col[:, half, j : j + 1].to_broadcast([P, P]), ident[:]
+                )
+
+        def spread_copy(half, copy):
+            copy(
+                out=scale_rows[:, HALF * half : HALF * (half + 1)].rearrange("p (n j) -> p n j", j=PACK),
+                in_=spread_banks[half][:].rearrange("p (j n) -> p n j", j=PACK),
             )
-            grouped["wa", half] = tile
+
+        wa_grouped = {}
+
+        def group_wa(half, banks, copy):
+            wa_grouped[half] = work.tile([P, PACK * HALF], BF16, name="wa_grouped", align_bytes=64)
+            for i, where in enumerate(banks):
+                tile = psum.tile([P, 2 * HALF], BF16, name="bank%d" % where)
+                for j in range(2):
+                    c0 = P * (2 * i + j)
+                    nc.tensor.matmul(
+                        out=tile[:, HALF * j : HALF * (j + 1)],
+                        lhsT=ident_bf16[:],
+                        rhs=wa_rows[half][:, :, c0 : c0 + P].rearrange("p j n -> p n j"),
+                        start=True,
+                        stop=True,
+                    )
+                copy(out=wa_grouped[half][:, 2 * HALF * i : 2 * HALF * (i + 1)], in_=tile[:])
+
+        def group_wa_vector(half):
+            wa_grouped[half] = work.tile([P, PACK * HALF], BF16, name="wa_grouped", align_bytes=64)
+            nc.vector.tensor_copy(
+                out=wa_grouped[half][:].rearrange("p (c i j) -> p c j i", i=4, j=PACK),
+                in_=wa_rows[half][:].rearrange("p j (c i) -> p c j i", i=4),
+            )
 
         def quantize_wa(half):
             cols = slice(HALF * half, HALF * (half + 1))
-            nc.vector.quantize_mx(
-                out=wa_codes[:, cols].bitcast(FP8X4), scales=wa_bytes[:, cols], in_=grouped["wa", half][:]
-            )
+            nc.vector.quantize_mx(out=wa_codes[:, cols].bitcast(FP8X4), scales=wa_bytes[:, cols], in_=wa_grouped[half][:])
 
         xb_rows = {}
 
-        def scale_xb(g, t, parts=1):
-            tile = work.tile([P, KB], BF16, name="xb_scaled", bufs=6)
-            width = KB // parts
-            for i in range(parts):
-                ks = slice(width * i, width * (i + 1))
-                nc.vector.tensor_tensor(
-                    out=tile[:, ks], in0=xb_codes_in[g][:, t, ks].bitcast(FP8), in1=scale_rows[:, ks], op=MULT
-                )
-            xb_rows[g, t] = tile
+        def scale_xb(r, part=0, parts=1):
+            if part == 0:
+                xb_rows[r] = work.tile([P, KB], BF16, name="xb_scaled", bufs=XB_BUFS)
+            ks = slice(KB // parts * part, KB // parts * (part + 1))
+            nc.vector.tensor_tensor(out=xb_rows[r][:, ks], in0=xb_in[r][:, ks].bitcast(FP8), in1=scale_rows[:, ks], op=MULT)
 
-        def turn(rows, dst, pair):
-            bank = psum.tile([P, 2, 2, P], F32, name="flip", bufs=BANKS["flip"])
-            for i in range(2):
+        x_grouped = {}
+        x_codes = {}
+
+        sorted_words = {}
+
+        def sort_words(r, count, first, last):
+            n = count * (last - first)
+            tile = work.tile([P, n, 2, P], F32, name="sorted", bufs=SORT_BUFS)
+            if first == 0:
+                src = xa_tiles[r][:].rearrange("p t k -> p (t k)").bitcast(F32)
+            else:
+                src = xb_rows[r][:].bitcast(F32)
+            nc.vector.tensor_copy(out=tile[:], in_=src.rearrange("p (s m u) -> p s u m", m=P, u=2))
+            for i in range(count):
+                for s in range(first, last):
+                    sorted_words[r + i, s] = tile[:, (last - first) * i + s - first]
+
+        def piece(r, s, u):
+            if (r, s) in sorted_words:
+                return sorted_words[r, s][:, u, :]
+            if s == 0:
+                return xa_rows[r].bitcast(F32)[:, u::2]
+            return xb_rows[r][:, K_PASS * (s - 1) : K_PASS * s].bitcast(F32)[:, u::2]
+
+        def turn(pieces, where, copy=nc.scalar.copy):
+            tile = bank(where)
+            for i, (r, s) in enumerate(pieces):
                 for u in range(2):
-                    nc.tensor.transpose(bank[:, i, u, :], rows[i][:, u::2], ident[:])
-            width = 2 * P * PACK
-            nc.scalar.copy(
-                out=dst[:, width * pair : width * (pair + 1)].bitcast(F32).rearrange("p (t r u) -> p t r u", t=2, u=2),
-                in_=bank[:].rearrange("p t u r -> p t r u"),
+                    nc.tensor.transpose(tile[:, P * (2 * i + u) : P * (2 * i + u + 1)], piece(r, s, u), ident[:])
+            pair = pieces[0][0] // 2
+            if pair not in x_grouped:
+                x_grouped[pair] = work.tile([P, 2 * PASSES, K_PASS], BF16, name="x_grouped", bufs=XG_BUFS, align_bytes=64)
+            slots = [PASSES * (r % 2) + s for r, s in pieces]
+            dst = x_grouped[pair][:, slots[0] : slots[1] + 1 : slots[1] - slots[0], :]
+            copy(
+                out=dst.bitcast(F32).rearrange("p i (m u) -> p i m u", u=2),
+                in_=tile[:].rearrange("p (i u m) -> p i m u", i=2, u=2),
             )
 
-        def turn_xa(g):
-            dst = work.tile([P, PACK * K_PASS], BF16, name="x_grouped", bufs=6, align_bytes=64)
-            for pair in range(2):
-                turn([xa_rows[g][:, 2 * pair + i, :].bitcast(F32) for i in range(2)], dst, pair)
-            grouped["a", g, 0] = dst
+        def quantize_x(r, first=0, last=PASSES):
+            if r not in x_codes:
+                x_codes[r] = (
+                    keep.tile([P, PASSES * P], U32, name="x_codes%d" % r, align_bytes=64),
+                    keep.tile([P, PASSES * P], U8, name="x_bytes%d" % r, align_bytes=64),
+                )
+            words, scale_bytes = x_codes[r]
+            cols = slice(P * first, P * last)
+            base = PASSES * (r % 2)
+            nc.vector.quantize_mx(
+                out=words[:, cols].bitcast(FP8X4),
+                scales=scale_bytes[:, cols],
+                in_=x_grouped[r // 2][:, base + first : base + last, :].rearrange("p s k -> p (s k)"),
+            )
 
-        def turn_xb(g, pair):
-            for b in range(B_PASSES):
-                if pair == 0:
-                    dst = work.tile([P, PACK * K_PASS], BF16, name="x_grouped", bufs=6, align_bytes=64)
-                    grouped["b", g, b] = dst
-                ks = slice(K_PASS * b, K_PASS * (b + 1))
-                turn([xb_rows[g, 2 * pair + i][:, ks].bitcast(F32) for i in range(2)], grouped["b", g, b], pair)
-
-        def quantize_xb(g, part=0, parts=1):
-            for b in range(B_PASSES):
-                quantize(("b", g, b), part, parts)
-
-        squares = {}
         pairs = {}
+        v_codes = {}
 
-        def project(g, half, t):
-            bank = psum.tile([P, HALF], F32, name="prod", bufs=BANKS["prod"])
-            samples = slice(P * t, P * (t + 1))
-            cols = slice(HALF * half, HALF * (half + 1))
-            words, scale_bytes = codes["a", g, 0]
-            nc.tensor.matmul_mx(
-                out=bank[:],
-                lhsT=words[:, samples].bitcast(FP8X4),
-                lhsT_scale=scale_bytes[:, samples],
-                rhs=wa_codes[:, cols].bitcast(FP8X4),
-                rhs_scale=wa_bytes[:, cols],
-                start=True,
-                stop=False,
-            )
-            for b in range(B_PASSES):
-                words, scale_bytes = codes["b", g, b]
+        def project(r, c0, width, where):
+            g, t = divmod(r, PACK)
+            tile = bank(where)
+            cols = slice(c0, c0 + width)
+            half, off = divmod(c0, HALF)
+            words, scale_bytes = x_codes[r]
+            for s in range(PASSES):
+                if s == 0:
+                    rhs, rhs_scale = wa_codes[:, cols].bitcast(FP8X4), wa_bytes[:, cols]
+                else:
+                    rhs = wb_tiles[half][:, s - 1, 2 * off : 2 * (off + width)].bitcast(FP4X4)
+                    rhs_scale = wb_bytes[:, s - 1, cols]
                 nc.tensor.matmul_mx(
-                    out=bank[:],
-                    lhsT=words[:, samples].bitcast(FP8X4),
-                    lhsT_scale=scale_bytes[:, samples],
-                    rhs=wb_tile[:, b, 2 * HALF * half : 2 * HALF * (half + 1)].bitcast(FP4X4),
-                    rhs_scale=wb_bytes[:, b, cols],
-                    start=False,
-                    stop=(b == B_PASSES - 1),
+                    out=tile[:, :width],
+                    lhsT=words[:, P * s : P * (s + 1)].bitcast(FP8X4),
+                    lhsT_scale=scale_bytes[:, P * s : P * (s + 1)],
+                    rhs=rhs,
+                    rhs_scale=rhs_scale,
+                    start=(s == 0),
+                    stop=(s == PASSES - 1),
                 )
-            tile = work.tile([P, HALF], F32, name="square", bufs=9)
-            nc.scalar.activation(out=tile[:], in_=bank[:], func=SQUARE)
-            squares[g, half, t] = tile
+            if (g, c0) not in pairs:
+                pairs[g, c0] = work.tile([P, PACK * width], BF16, name="v_pairs", bufs=VP_BUFS)
+            slots = pairs[g, c0][:].rearrange("p (a n e) -> p a n e", a=2, e=2)
+            nc.scalar.activation(out=slots[:, t // 2, :, t % 2], in_=tile[:, :width], func=SQUARE, scale=root[:, r : r + 1])
 
-        def weigh(g, half, t):
-            if t == 0:
-                pairs[g, half] = work.tile([P, PACK * HALF], BF16, name="v_pairs", bufs=4)
-            slots = pairs[g, half][:].rearrange("p (a n e) -> p a n e", a=2, e=2)
-            nc.vector.tensor_scalar(
-                out=slots[:, t // 2, :, t % 2],
-                in0=squares[g, half, t][:],
-                scalar1=omega_f32[:, g, t : t + 1],
-                scalar2=None,
-                op0=MULT,
+        v_grouped = {}
+
+        def sign_v(g, c0, width):
+            tile = work.tile([P, PACK * width], BF16, name="v_grouped", bufs=3, align_bytes=64)
+            factors = factor[:, PACK * g : PACK * (g + 1)].rearrange("p (a e) -> p a e", a=2)
+            nc.vector.tensor_tensor(
+                out=tile[:].rearrange("p (n a e) -> p n a e", a=2, e=2),
+                in0=pairs[g, c0][:].rearrange("p (a n e) -> p n a e", a=2, e=2),
+                in1=factors.unsqueeze(1).to_broadcast([P, width, 2, 2]),
+                op=MULT,
             )
-            if t == PACK - 1:
-                tile = work.tile([P, PACK * HALF], BF16, name="v_grouped", bufs=4, align_bytes=64)
-                nc.scalar.copy(
-                    out=tile[:].bitcast(F32).rearrange("p (n a) -> p n a", a=2),
-                    in_=pairs[g, half][:].bitcast(F32).rearrange("p (a n) -> p n a", a=2),
-                )
-                grouped["v", g, half] = tile
+            v_grouped[g, c0] = tile
+
+        def quantize_v(g, c0, width):
+            words = keep.tile([P, width], U32, name="v_codes%d_%d" % (g, c0), align_bytes=64)
+            scale_bytes = keep.tile([P, width], U8, name="v_bytes%d_%d" % (g, c0), align_bytes=64)
+            nc.vector.quantize_mx(out=words[:].bitcast(FP8X4), scales=scale_bytes[:], in_=v_grouped[g, c0][:])
+            for q in range(width // QUARTER):
+                v_codes[g, c0 + QUARTER * q] = (words[:, QUARTER * q :], scale_bytes[:, QUARTER * q :])
 
         sums = {}
+
+        def moment(c0, width, cts, groups, where=None):
+            if where is not None:
+                sums[c0, cts] = bank(where)
+            for g in groups:
+                words, scale_bytes = v_codes[g, c0]
+                for i, ct in enumerate(cts):
+                    nc.tensor.matmul_mx(
+                        out=sums[c0, cts][:, width * i : width * (i + 1)],
+                        lhsT=z_tile[:, g, 2 * P * ct : 2 * P * (ct + 1)].bitcast(FP4X4),
+                        lhsT_scale=z_bytes[:, g, P * ct : P * (ct + 1)],
+                        rhs=words[:, :width].bitcast(FP8X4),
+                        rhs_scale=scale_bytes[:, :width],
+                        start=(g == 0 and i == 0),
+                        stop=(g == GROUPS - 1 and i == len(cts) - 1),
+                    )
+
         gaps = {}
 
-        def moment(half, ct):
-            tag = MOMENT_BANK[half, ct]
-            sums[half, ct] = psum.tile([P, HALF], F32, name=tag, bufs=BANKS[tag])
-            for g in range(GROUPS):
-                words, scale_bytes = codes["v", g, half]
-                nc.tensor.matmul_mx(
-                    out=sums[half, ct][:],
-                    lhsT=z_tile[:, g, 2 * P * ct : 2 * P * (ct + 1)].bitcast(FP4X4),
-                    lhsT_scale=z_bytes[:, g, P * ct : P * (ct + 1)],
-                    rhs=words[:].bitcast(FP8X4),
-                    rhs_scale=scale_bytes[:],
-                    start=(g == 0),
-                    stop=(g == GROUPS - 1),
-                )
+        def subtract_target(c0, width, cts):
+            tile = work.tile([P, len(cts), width], F32, name="gap", bufs=4)
+            nc.vector.tensor_tensor(
+                out=tile[:],
+                in0=sums[c0, cts][:].rearrange("p (i n) -> p i n", i=len(cts)),
+                in1=target_rows[:, cts[0] : cts[-1] + 1, c0 : c0 + width],
+                op=SUBTRACT,
+            )
+            gaps[c0, cts] = tile
 
-        def subtract_target(half, ct):
-            tile = work.tile([P, HALF], F32, name="gap", bufs=4)
-            cols = slice(HALF * half, HALF * (half + 1))
-            nc.vector.tensor_tensor(out=tile[:], in0=sums[half, ct][:], in1=target_rows[:, ct, cols], op=SUBTRACT)
-            gaps[half, ct] = tile
+        def scale_and_store(c0, width, cts, engine=nc.vector):
+            tile = work.tile([P, len(cts), width], F32, name="result", bufs=4)
+            engine.tensor_tensor(
+                out=tile[:],
+                in0=gaps[c0, cts][:],
+                in1=prec_rows[:, c0 : c0 + width].unsqueeze(1).to_broadcast([P, len(cts), width]),
+                op=MULT,
+            )
+            rows = out.rearrange("(ct c) n -> c ct n", c=P)
+            nc.sync.dma_start(out=rows[:, cts[0] : cts[-1] + 1, c0 : c0 + width], in_=tile[:])
 
-        def scale_and_store(half, ct, engine):
-            tile = work.tile([P, HALF], F32, name="result", bufs=4)
-            cols = slice(HALF * half, HALF * (half + 1))
-            engine.tensor_tensor(out=tile[:], in0=gaps[half, ct][:], in1=prec_rows[:, cols], op=MULT)
-            nc.sync.dma_start(out=out[P * ct : P * (ct + 1), cols], in_=tile[:])
+        load_scale_col()
+        make_identity(nc, ident[:])
+        nc.vector.memset(wb_bytes[:].rearrange("p g n -> p (g n)").bitcast(I32), 0)
+        nc.gpsimd.memset(z_bytes[:].rearrange("p g n -> p (g n)").bitcast(I32), 0)
+        load_omega()
+        load_xb(0, 2)
+        load_wa(0)
+        load_xa(0, 2)
+        load_xb(2, 2)
+        load_xa(2, 2)
+        load_scale_bytes(wb_bytes, wb_scales)
+        load_wb(0)
+        load_wa(1)
+        load_xb(4, 2)
+        load_xa(4, 2)
+        load_xa(6, 2)
+        load_wb(1)
+        load_xb(6, 2)
+        load_xb(8, 4)
+        load_xa(8, 2)
+        load_xa(10, 2)
+        load_xb(12, 4)
+        load_xa(12, 2)
+        load_xa(14, 2)
+        load_rest()
 
-        keep_tensor_busy(3)
-        spread_xb_scale()
-        keep_tensor_busy(3)
-        group_wa(0)
-        turn_xa(0)
-        keep_tensor_busy(2)
-        scale_xb(0, 0, parts=2)
-        scale_xb(0, 1)
-        turn_xb(0, 0)
-        keep_tensor_busy(2)
-        scale_xb(0, 2)
-        scale_xb(0, 3)
-        quantize(("a", 0, 0))
-        quantize_wa(0)
-        quantize_xb(0, 0, 2)
-        group_wa(1)
-        turn_xb(0, 1)
-        nc.vector.tensor_copy(out=omega_f32[:], in_=omega_bf16[:])
+        zeros = keep.tile([P, HALF], BF16, name="zeros")
+        nc.vector.memset(zeros[:].bitcast(I32), 0)
 
-        order = [(g, half, t) for g in range(GROUPS) for half in range(2) for t in range(PACK)]
-        scale_xb(1, 0)
-        project(*order[0])
-        project(*order[1])
-        scale_xb(1, 1)
-        quantize_xb(0, 1, 2)
-        quantize_wa(1)
-        scale_xb(1, 2)
-        scale_xb(1, 3)
-        turn_xa(1)
+        def warm_up(count, where):
+            tile = bank(where)
+            for i in range(count):
+                nc.tensor.matmul(out=tile[:], lhsT=zeros[:, :P], rhs=zeros[:], start=True, stop=True)
 
-        weighed = 0
-        for step in range(17):
-            g, phase = divmod(step + 3, 4)
-            if phase in (0, 1) and g < GROUPS:
-                turn_xb(g, phase)
-            if phase == 2 and 1 <= g < GROUPS - 1:
-                turn_xa(g + 1)
+        S, V = nc.scalar.copy, nc.vector.tensor_copy
+        flips = [0]
+        count = [0]
 
-            until = 2 * step + (1 if step < 12 else 0)
-            while weighed < until:
-                weigh(*order[weighed])
-                weighed += 1
-            for bank in order[2 * step + 2 : 2 * step + 4]:
-                project(*bank)
+        def ta(r):
+            flips[0] += 1
+            return ("turn", [(r, 0), (r + 1, 0)], (flips[0] - 1) % 3)
 
-            if step == 0:
-                quantize(("a", 1, 0))
-            if phase == 3 and 2 <= g + 1 < GROUPS:
-                quantize(("a", g + 1, 0))
-            if phase == 1 and g < GROUPS:
-                quantize_xb(g)
-            if 1 <= step <= 8:
-                scale_xb(*divmod(step + 7, PACK))
-            if step >= 4 and step % 2 == 0 and step < 16:
-                quantize(("v",) + divmod(step // 2 - 2, 2))
-            if step == 15:
-                quantize(("v", 3, 0))
+        def tb(r):
+            flips[0] += 1
+            return ("turn", [(r, 1), (r, 2)], (flips[0] - 1) % 3)
 
-        for ct in range(C_TILES):
-            moment(0, ct)
-        subtract_target(0, 0)
-        scale_and_store(0, 0, nc.gpsimd)
-        subtract_target(0, 1)
-        quantize(("v", 3, 1))
-        subtract_target(0, 2)
-        scale_and_store(0, 1, nc.vector)
-        subtract_target(0, 3)
-        scale_and_store(0, 2, nc.vector)
-        previous = (0, 3)
-        for ct in range(C_TILES):
-            moment(1, ct)
-            subtract_target(1, ct)
-            scale_and_store(*previous, nc.vector)
-            previous = (1, ct)
-        scale_and_store(*previous, nc.vector)
+        def pr(r, c0, width=HALF, banks=(3, 4, 5, 6, 7)):
+            count[0] += 1
+            return ("proj", r, c0, width, banks[(count[0] - 1) % len(banks)])
+
+        def sc(r):
+            return ("scale", r)
+
+        def qx(r):
+            return ("qx", r)
+
+        def sv(g, c0, width=HALF):
+            return ("sign", g, c0, width)
+
+        def qv(g, c0, width=HALF):
+            return ("qv", g, c0, width)
+
+        def mo(c0, width, cts, where, groups=range(GROUPS)):
+            return ("mom", c0, width, cts, groups, where)
+
+        def su(c0, width, cts):
+            return ("sub", c0, width, cts)
+
+        def mu(c0, width, cts, engine=nc.vector):
+            return ("mul", c0, width, cts, engine)
+
+        def so(r, is_b):
+            return ("sort", r, is_b)
+
+        def ro(i):
+            return ("root", i)
+
+        H, Q, Q2, Q3, G = HALF, QUARTER, HALF, HALF + QUARTER, nc.gpsimd
+
+        tensor_order = [ro(0), ro(1), ("warm", 2, 7), ("spread", 0, 3, S), ("spread_t", 1, 4), ("warm", 2, 7), ro(5),
+            ("gwa", 0, (5, 6), S), tb(0), ta(0), ("warm", 2, 7), tb(1), ta(2), tb(2), ("warm", 1, 7), pr(0, 0), pr(1, 0), tb(3), ta(4), pr(2, 0), ta(6), pr(3, 0), pr(0, H), pr(1, H)]
+        tensor_order += [tb(4), tb(5), pr(2, H), pr(3, H), tb(6), tb(7), pr(4, 0), pr(5, 0), pr(4, H)]
+        tensor_order += [ta(8), ta(10), pr(6, 0), pr(7, 0), tb(8), tb(9), pr(5, H), pr(6, H), pr(7, H), tb(10), tb(11), pr(8, 0), pr(9, 0)]
+        tensor_order += [ta(12), ta(14), pr(10, 0), pr(11, 0), tb(12), tb(13), pr(8, H), pr(9, H), tb(14), tb(15), pr(12, 0), pr(13, 0), pr(10, H), pr(14, 0), pr(15, 0), pr(11, H)]
+        count[0] = 0
+        last = (0, 1, 2, 6)
+        tensor_order += [pr(12 + t, Q2, QUARTER, last) for t in range(PACK)]
+        count[0] = 0
+        tensor_order += [pr(12 + t, Q3, QUARTER, (7, 3, 4, 5)) for t in range(PACK)]
+        tensor_order += [mo(0, H, (ct,), ct) for ct in (0, 1, 2)] + [mo(0, H, (3,), 6)]
+        tensor_order += [mo(Q2, Q, (0, 1), 7), mo(Q2, Q, (2, 3), 3), mo(Q3, Q, (0, 1), 4), mo(Q3, Q, (2, 3), 5)]
+
+        vector_order = [("ident",), ro(2), ro(3), ("spread_c", 1, V), ro(4), sc(0), ro(6), sc(1), ro(7), sc(2), ro(8), ("qwa", 0), ro(9), qx(0), ro(10), qx(1),
+            sc(3), qx(2), ("gwav", 1), sc(4), qx(3), ("qwa", 1), sc(5), sc(6), sc(7), qx(4), qx(5), sv(0, 0), sc(8), qv(0, 0), qx(6), qx(7), sc(9),
+            sc(10), sv(0, H), sc(11), qv(0, H), qx(8), qx(9), sc(12), sv(1, 0), sc(13), qx(10), qx(11), qv(1, 0), sc(14), sc(15), sv(1, H), qx(12), qx(13), qv(1, H),
+            sv(2, 0), qx(14), qx(15), qv(2, 0), sv(3, 0), sv(2, H), qv(3, 0), qv(2, H), sv(3, Q2, Q), su(0, H, (0,)), qv(3, Q2, Q),
+            sv(3, Q3, Q), mu(0, H, (0,)), su(0, H, (1,)), qv(3, Q3, Q), mu(0, H, (1,)), su(0, H, (2,)), su(0, H, (3,)), mu(0, H, (2,)),
+            mu(0, H, (3,)), su(Q2, Q, (0, 1)), su(Q2, Q, (2, 3)), mu(Q2, Q, (0, 1)), su(Q3, Q, (0, 1)), mu(Q2, Q, (2, 3)),
+            su(Q3, Q, (2, 3)), mu(Q3, Q, (0, 1)), mu(Q3, Q, (2, 3))]
+
+        def run(item):
+            kind, args = item[0], item[1:]
+            calls[kind](*args)
+
+        ROOT_NEEDS = [(), (), (0,), (2,), (3,), (4,), (1, 2), (5,), (7,), (8,), (9,)]
+
+        def needs(item):
+            kind, a = item[0], item[1:]
+            if kind == "turn":
+                out_ = []
+                for r, s in a[0]:
+                    if s > 0:
+                        out_.append(("scale", r))
+                    key = ("sort", r - r % SORT_A if s == 0 else r, s > 0)
+                    if key in planned:
+                        out_.append(key)
+                    if r // 2 >= XG_BUFS:
+                        out_ += [("qx", 2 * (r // 2 - XG_BUFS)), ("qx", 2 * (r // 2 - XG_BUFS) + 1)]
+                return out_
+            if kind == "scale":
+                return [("spread", 0), ("spread", 1)] + ([("turned", a[0] - XB_BUFS, 1), ("turned", a[0] - XB_BUFS, 2)] if a[0] >= XB_BUFS else [])
+            if kind == "sort":
+                return [("scale", a[0])] if a[1] else []
+            if kind == "spread_c":
+                return [("spread_t", a[0])]
+            if kind == "gwa":
+                return [("ident",)]
+            if kind == "qx":
+                return [("turned", a[0], s) for s in range(PASSES)]
+            if kind == "qwa":
+                return [("gwa", a[0])]
+            if kind == "proj":
+                return [("qx", a[0]), ("qwa", a[1] // HALF), ("root", 10)]
+            if kind == "sign":
+                return [("proj", PACK * a[0] + t, a[1]) for t in range(PACK)]
+            if kind == "qv":
+                return [("sign", a[0], a[1])]
+            if kind == "mom":
+                return [("have_v", g, a[0]) for g in a[3]]
+            if kind == "sub":
+                return [("mom_done", a[0], a[2])]
+            if kind == "mul":
+                return [("sub", a[0], a[2])]
+            if kind == "root":
+                return [("root", i) for i in ROOT_NEEDS[a[0]]]
+            return []
+
+        def gives(item):
+            kind, a = item[0], item[1:]
+            if kind == "turn":
+                return [("turned", r, s) for r, s in a[0]]
+            if kind in ("proj", "sign"):
+                return [(kind, a[0], a[1])]
+            if kind == "qv":
+                return [("have_v", a[0], a[1] + QUARTER * q) for q in range(a[2] // QUARTER)]
+            if kind == "mom":
+                return [("mom_done", a[0], a[2])] if GROUPS - 1 in a[3] else []
+            if kind in ("sub", "mul"):
+                return [(kind, a[0], a[2])]
+            if kind == "spread_c":
+                return [("spread", a[0])]
+            if kind == "gwav":
+                return [("gwa", a[0])]
+            if kind == "sort":
+                return [(kind, a[0], a[1])]
+            return [(kind,) + tuple(a[:1])]
+
+        calls = {
+            "turn": turn,
+            "scale": scale_xb,
+            "sort": lambda r, is_b: sort_words(r, 1, 1, PASSES) if is_b else sort_words(r, SORT_A, 0, 1),
+            "qx": quantize_x,
+            "qwa": quantize_wa,
+            "gwa": group_wa,
+            "gwav": group_wa_vector,
+            "proj": project,
+            "sign": sign_v,
+            "qv": quantize_v,
+            "mom": moment,
+            "sub": subtract_target,
+            "mul": scale_and_store,
+            "root": lambda i: root_step(i, i + 1),
+            "spread": spread_scale,
+            "spread_t": lambda h, w: spread_turn(h, w),
+            "spread_c": lambda h, c: spread_copy(h, c),
+            "warm": warm_up,
+            "ident": lambda: nc.vector.tensor_copy(out=ident_bf16[:], in_=ident[:]),
+        }
+        planned = set(key for item in vector_order for key in gives(item))
+        have = set()
+        queues = [list(tensor_order), list(vector_order)]
+        while queues[0] or queues[1]:
+            ready = [q for q in queues if q and all(key in have for key in needs(q[0]))]
+            assert ready, (queues[0][:1], queues[1][:1])
+            item = ready[0].pop(0)
+            run(item)
+            have.update(gives(item))

@@ -29,14 +29,10 @@ GROUPS = M // K_PASS
 ROWS = GROUPS * PACK
 PASSES = (KA + KB) // K_PASS
 HALF = 512
-QUARTER = 256
+QUARTER = HALF // 2
 C_TILES = C // P
-
-XB_BUFS = 6
-XG_BUFS = 4
-VP_BUFS = 5
-SORT_BUFS = 4
-SORT_A = 2
+TURN_BANKS = (0, 1, 2)
+PRODUCT_BANKS = (3, 4, 5, 6, 7)
 
 FLOPS = 2 * M * N * (KA + KB) + 2 * C * N * M
 
@@ -51,10 +47,10 @@ def tile_projection_moment_gap_s3_kernel(
         work = ctx.enter_context(tc.tile_pool(name="work", bufs=2))
         psum = ctx.enter_context(tc.psum_pool(name="psum", bufs=1))
 
-        def bank(i):
-            return psum.tile([P, HALF], F32, name="bank%d" % i)
+        def bank(i, dtype=F32, width=HALF):
+            return psum.tile([P, width], dtype, name="bank%d" % i)
 
-        def small(name, dtype=F32):
+        def per_row(name, dtype=F32):
             return keep.tile([P, ROWS], dtype, name=name)
 
         scale_col = keep.tile([P, 2, PACK], F32, name="scale_col")
@@ -71,25 +67,24 @@ def tile_projection_moment_gap_s3_kernel(
         target_rows = keep.tile([P, C_TILES, N], BF16, name="target_rows")
         ident = keep.tile([P, P], F32, name="ident")
         ident_bf16 = keep.tile([P, P], BF16, name="ident_bf16")
+        zeros = keep.tile([P, HALF], BF16, name="zeros")
 
-        xa_rows = {}
-        xa_tiles = {}
-        xb_in = {}
+        xa_pairs = {}
+        xb_codes_in = {}
 
-        def load_x(store, src, dtype, width, name, r0, count):
-            g, t0 = divmod(r0, PACK)
-            tile = keep.tile([P, count, width], dtype, name="%s%d" % (name, r0))
-            rows = src[K_PASS * g : K_PASS * (g + 1), :].rearrange("(p t) k -> p t k", t=PACK)
-            nc.sync.dma_start(out=tile[:], in_=rows[:, t0 : t0 + count, :])
+        def sample_rows(src, r, count):
+            g, t = divmod(r, PACK)
+            return src[K_PASS * g : K_PASS * (g + 1), :].rearrange("(p t) k -> p t k", t=PACK)[:, t : t + count, :]
+
+        def load_xa(r):
+            xa_pairs[r] = keep.tile([P, 2, KA], BF16, name="xa_pair%d" % r)
+            nc.sync.dma_start(out=xa_pairs[r][:], in_=sample_rows(xa, r, 2))
+
+        def load_xb(r, count):
+            tile = keep.tile([P, count, KB], U8, name="xb_codes_in%d" % r)
+            nc.sync.dma_start(out=tile[:], in_=sample_rows(xb_bytes, r, count))
             for i in range(count):
-                store[r0 + i] = tile[:, i, :]
-            return tile
-
-        def load_xa(r0, count):
-            xa_tiles[r0] = load_x(xa_rows, xa, BF16, KA, "xa_rows", r0, count)
-
-        def load_xb(r0, count):
-            load_x(xb_in, xb_bytes, U8, KB, "xb_in", r0, count)
+                xb_codes_in[r + i] = tile[:, i, :]
 
         def load_wa(half):
             rows = wa.rearrange("(p j) n -> p j n", j=PACK)
@@ -104,78 +99,59 @@ def tile_projection_moment_gap_s3_kernel(
             for r in range(4):
                 nc.sync.dma_start(out=plane[r:P:32].bitcast(I32), in_=rows[r].bitcast(I32))
 
-        def load_scale_col():
-            nc.sync.dma_start(out=scale_col[:], in_=xb_scale.rearrange("o (h p j) -> p (o h) j", h=2, j=PACK))
+        nc.sync.dma_start(out=scale_col[:], in_=xb_scale.rearrange("o (h p j) -> p (o h) j", h=2, j=PACK))
+        nc.vector.memset(zeros[:].bitcast(I32), 0)
+        make_identity(nc, ident[:])
+        nc.vector.memset(wb_bytes[:].rearrange("p g n -> p (g n)").bitcast(I32), 0)
+        nc.vector.memset(z_bytes[:].rearrange("p g n -> p (g n)").bitcast(I32), 0)
+        nc.sync.dma_start(out=omega_bf16[:], in_=omega.rearrange("(g p t) -> p g t", p=P, t=PACK))
+        load_xb(0, 2)
+        load_wa(0)
+        load_xa(0)
+        load_xb(2, 2)
+        load_xa(2)
+        load_scale_bytes(wb_bytes, wb_scales)
+        load_wb(0)
+        load_wa(1)
+        load_xb(4, 2)
+        load_xa(4)
+        load_xa(6)
+        load_wb(1)
+        load_xb(6, 2)
+        for g in range(2, GROUPS):
+            load_xb(PACK * g, PACK)
+            load_xa(PACK * g)
+            load_xa(PACK * g + 2)
+        load_scale_bytes(z_bytes, z_scales)
+        nc.sync.dma_start(out=z_tile[:], in_=z_words.rearrange("g p n -> p g n"))
+        nc.sync.dma_start(out=target_rows[:], in_=target.rearrange("(ct c) n -> c ct n", c=P))
+        nc.sync.dma_start(out=prec_rows[:], in_=prec.partition_broadcast(P))
 
-        def load_omega():
-            nc.sync.dma_start(out=omega_bf16[:], in_=omega.rearrange("(g p t) -> p g t", p=P, t=PACK))
+        def warm_up(count):
+            tile = bank(PRODUCT_BANKS[-1])
+            for i in range(count):
+                nc.tensor.matmul(out=tile[:], lhsT=zeros[:, :P], rhs=zeros[:], start=True, stop=True)
 
-        def load_rest():
-            load_scale_bytes(z_bytes, z_scales)
-            nc.sync.dma_start(out=z_tile[:], in_=z_words.rearrange("g p n -> p g n"))
-            nc.sync.dma_start(out=target_rows[:], in_=target.rearrange("(ct c) n -> c ct n", c=P))
-            nc.sync.dma_start(out=prec_rows[:], in_=prec.partition_broadcast(P))
-
-        omega_flat = omega_bf16[:].rearrange("p g t -> p (g t)")
-        size, sign, power, inv_power = small("size"), small("sign"), small("power"), small("inv_power")
-        radicand, guess, half_guess, inv_guess = small("radicand"), small("guess"), small("half_guess"), small("inv_guess")
-        quotient, root, factor = small("quotient"), small("root"), small("factor", BF16)
-        root_steps = [
-            lambda: nc.scalar.activation(out=size[:], in_=omega_flat, func=ABS),
-            lambda: nc.scalar.activation(out=sign[:], in_=omega_flat, func=SIGN),
-            lambda: nc.vector.tensor_scalar(
-                out=power[:], in0=size[:], scalar1=2.0**-64, scalar2=2.0**-64, op0=IS_GE, op1=MAX
-            ),
-            lambda: nc.vector.reciprocal(out=inv_power[:], in_=power[:]),
-            lambda: nc.vector.tensor_tensor(out=radicand[:], in0=size[:], in1=inv_power[:], op=MULT),
-            lambda: nc.scalar.activation(out=guess[:], in_=radicand[:], func=SQRT, scale=2.0**-10),
-            lambda: nc.vector.tensor_tensor(out=factor[:], in0=sign[:], in1=power[:], op=MULT),
-            lambda: nc.vector.tensor_scalar(
-                out=half_guess[:], in0=guess[:], scalar1=2.0**-60, scalar2=16.0, op0=MAX, op1=MULT
-            ),
-            lambda: nc.vector.reciprocal(out=inv_guess[:], in_=half_guess[:]),
-            lambda: nc.vector.tensor_tensor(out=quotient[:], in0=radicand[:], in1=inv_guess[:], op=MULT),
-            lambda: nc.vector.scalar_tensor_tensor(
-                out=root[:], in0=quotient[:], scalar=0.25, in1=half_guess[:], op0=MULT, op1=ADD
-            ),
-        ]
-
-        def root_step(first, last):
-            for step in root_steps[first:last]:
-                step()
-
-        def spread_scale(half, where, copy):
+        def spread_scale(half, where):
             tile = bank(where)
             for j in range(PACK):
-                nc.tensor.transpose(
-                    tile[:, P * j : P * (j + 1)], scale_col[:, half, j : j + 1].to_broadcast([P, P]), ident[:]
-                )
+                column = scale_col[:, half, j : j + 1].to_broadcast([P, P])
+                nc.tensor.transpose(tile[:, P * j : P * (j + 1)], column, ident[:])
+            return tile
+
+        def copy_scale(half, tile, copy):
             copy(
                 out=scale_rows[:, HALF * half : HALF * (half + 1)].rearrange("p (n j) -> p n j", j=PACK),
                 in_=tile[:].rearrange("p (j n) -> p n j", j=PACK),
             )
 
-        spread_banks = {}
+        def grouped_tile(width):
+            return work.tile([P, PACK * width], BF16, name="grouped", bufs=3, align_bytes=64)
 
-        def spread_turn(half, where):
-            spread_banks[half] = bank(where)
-            for j in range(PACK):
-                nc.tensor.transpose(
-                    spread_banks[half][:, P * j : P * (j + 1)], scale_col[:, half, j : j + 1].to_broadcast([P, P]), ident[:]
-                )
-
-        def spread_copy(half, copy):
-            copy(
-                out=scale_rows[:, HALF * half : HALF * (half + 1)].rearrange("p (n j) -> p n j", j=PACK),
-                in_=spread_banks[half][:].rearrange("p (j n) -> p n j", j=PACK),
-            )
-
-        wa_grouped = {}
-
-        def group_wa(half, banks, copy):
-            wa_grouped[half] = work.tile([P, PACK * HALF], BF16, name="wa_grouped", align_bytes=64)
+        def group_wa_on_tensor(half, banks):
+            grouped = grouped_tile(HALF)
             for i, where in enumerate(banks):
-                tile = psum.tile([P, 2 * HALF], BF16, name="bank%d" % where)
+                tile = bank(where, BF16, 2 * HALF)
                 for j in range(2):
                     c0 = P * (2 * i + j)
                     nc.tensor.matmul(
@@ -185,365 +161,302 @@ def tile_projection_moment_gap_s3_kernel(
                         start=True,
                         stop=True,
                     )
-                copy(out=wa_grouped[half][:, 2 * HALF * i : 2 * HALF * (i + 1)], in_=tile[:])
+                nc.scalar.copy(out=grouped[:, 2 * HALF * i : 2 * HALF * (i + 1)], in_=tile[:])
+            return grouped
 
-        def group_wa_vector(half):
-            wa_grouped[half] = work.tile([P, PACK * HALF], BF16, name="wa_grouped", align_bytes=64)
+        def group_wa_on_vector(half):
+            grouped = grouped_tile(HALF)
             nc.vector.tensor_copy(
-                out=wa_grouped[half][:].rearrange("p (c i j) -> p c j i", i=4, j=PACK),
+                out=grouped[:].rearrange("p (c i j) -> p c j i", i=4, j=PACK),
                 in_=wa_rows[half][:].rearrange("p j (c i) -> p c j i", i=4),
             )
+            return grouped
 
-        def quantize_wa(half):
+        def quantize_wa(half, grouped):
             cols = slice(HALF * half, HALF * (half + 1))
-            nc.vector.quantize_mx(out=wa_codes[:, cols].bitcast(FP8X4), scales=wa_bytes[:, cols], in_=wa_grouped[half][:])
+            nc.vector.quantize_mx(out=wa_codes[:, cols].bitcast(FP8X4), scales=wa_bytes[:, cols], in_=grouped[:])
+
+        words = {}
+
+        def every_second_word(r, s, values):
+            words[r, s] = [values.bitcast(F32)[:, u::2] for u in range(2)]
+
+        for r in range(ROWS):
+            every_second_word(r, 0, xa_pairs[r - r % 2][:, r % 2, :])
 
         xb_rows = {}
 
-        def scale_xb(r, part=0, parts=1):
-            if part == 0:
-                xb_rows[r] = work.tile([P, KB], BF16, name="xb_scaled", bufs=XB_BUFS)
-            ks = slice(KB // parts * part, KB // parts * (part + 1))
-            nc.vector.tensor_tensor(out=xb_rows[r][:, ks], in0=xb_in[r][:, ks].bitcast(FP8), in1=scale_rows[:, ks], op=MULT)
+        def scale_xb(r):
+            xb_rows[r] = work.tile([P, KB], BF16, name="xb_scaled", bufs=6)
+            nc.vector.tensor_tensor(out=xb_rows[r][:], in0=xb_codes_in[r].bitcast(FP8), in1=scale_rows[:], op=MULT)
+            for s in range(1, PASSES):
+                every_second_word(r, s, xb_rows[r][:, K_PASS * (s - 1) : K_PASS * s])
+
+        def sort_words(values, pieces):
+            tile = work.tile([P, 2, 2, P], F32, name="sorted", bufs=6)
+            nc.vector.tensor_copy(out=tile[:], in_=values.bitcast(F32).rearrange("p (s m u) -> p s u m", m=P, u=2))
+            for i, piece in enumerate(pieces):
+                words[piece] = [tile[:, i, u, :] for u in range(2)]
+
+        def sort_xa(r):
+            sort_words(xa_pairs[r][:].rearrange("p t k -> p (t k)"), [(r, 0), (r + 1, 0)])
+
+        def sort_xb(r):
+            sort_words(xb_rows[r][:], [(r, 1), (r, 2)])
 
         x_grouped = {}
-        x_codes = {}
+        turns = []
 
-        sorted_words = {}
-
-        def sort_words(r, count, first, last):
-            n = count * (last - first)
-            tile = work.tile([P, n, 2, P], F32, name="sorted", bufs=SORT_BUFS)
-            if first == 0:
-                src = xa_tiles[r][:].rearrange("p t k -> p (t k)").bitcast(F32)
-            else:
-                src = xb_rows[r][:].bitcast(F32)
-            nc.vector.tensor_copy(out=tile[:], in_=src.rearrange("p (s m u) -> p s u m", m=P, u=2))
-            for i in range(count):
-                for s in range(first, last):
-                    sorted_words[r + i, s] = tile[:, (last - first) * i + s - first]
-
-        def piece(r, s, u):
-            if (r, s) in sorted_words:
-                return sorted_words[r, s][:, u, :]
-            if s == 0:
-                return xa_rows[r].bitcast(F32)[:, u::2]
-            return xb_rows[r][:, K_PASS * (s - 1) : K_PASS * s].bitcast(F32)[:, u::2]
-
-        def turn(pieces, where, copy=nc.scalar.copy):
-            tile = bank(where)
-            for i, (r, s) in enumerate(pieces):
+        def turn(pieces):
+            tile = bank(TURN_BANKS[len(turns) % len(TURN_BANKS)])
+            turns.append(pieces)
+            for i, piece in enumerate(pieces):
                 for u in range(2):
-                    nc.tensor.transpose(tile[:, P * (2 * i + u) : P * (2 * i + u + 1)], piece(r, s, u), ident[:])
+                    nc.tensor.transpose(tile[:, P * (2 * i + u) : P * (2 * i + u + 1)], words[piece][u], ident[:])
             pair = pieces[0][0] // 2
             if pair not in x_grouped:
-                x_grouped[pair] = work.tile([P, 2 * PASSES, K_PASS], BF16, name="x_grouped", bufs=XG_BUFS, align_bytes=64)
-            slots = [PASSES * (r % 2) + s for r, s in pieces]
-            dst = x_grouped[pair][:, slots[0] : slots[1] + 1 : slots[1] - slots[0], :]
-            copy(
-                out=dst.bitcast(F32).rearrange("p i (m u) -> p i m u", u=2),
+                x_grouped[pair] = work.tile([P, 2 * PASSES, K_PASS], BF16, name="x_grouped", bufs=4, align_bytes=64)
+            first, second = [PASSES * (r % 2) + s for r, s in pieces]
+            nc.scalar.copy(
+                out=x_grouped[pair][:, first : second + 1 : second - first, :]
+                .bitcast(F32)
+                .rearrange("p i (m u) -> p i m u", u=2),
                 in_=tile[:].rearrange("p (i u m) -> p i m u", i=2, u=2),
             )
 
-        def quantize_x(r, first=0, last=PASSES):
-            if r not in x_codes:
-                x_codes[r] = (
-                    keep.tile([P, PASSES * P], U32, name="x_codes%d" % r, align_bytes=64),
-                    keep.tile([P, PASSES * P], U8, name="x_bytes%d" % r, align_bytes=64),
-                )
-            words, scale_bytes = x_codes[r]
-            cols = slice(P * first, P * last)
-            base = PASSES * (r % 2)
-            nc.vector.quantize_mx(
-                out=words[:, cols].bitcast(FP8X4),
-                scales=scale_bytes[:, cols],
-                in_=x_grouped[r // 2][:, base + first : base + last, :].rearrange("p s k -> p (s k)"),
-            )
+        def turn_xa(r):
+            turn([(r, 0), (r + 1, 0)])
 
-        pairs = {}
-        v_codes = {}
+        def turn_xb(r):
+            turn([(r, 1), (r, 2)])
+
+        x_codes = {}
+
+        def quantize_x(r):
+            codes = keep.tile([P, PASSES * P], U32, name="x_codes%d" % r, align_bytes=64)
+            scale_bytes = keep.tile([P, PASSES * P], U8, name="x_bytes%d" % r, align_bytes=64)
+            first = PASSES * (r % 2)
+            nc.vector.quantize_mx(
+                out=codes[:].bitcast(FP8X4),
+                scales=scale_bytes[:],
+                in_=x_grouped[r // 2][:, first : first + PASSES, :].rearrange("p s k -> p (s k)"),
+            )
+            x_codes[r] = (codes, scale_bytes)
+
+        root, factor = per_row("root"), per_row("factor", BF16)
+        squares = {}
 
         def project(r, c0, width, where):
             g, t = divmod(r, PACK)
             tile = bank(where)
             cols = slice(c0, c0 + width)
-            half, off = divmod(c0, HALF)
-            words, scale_bytes = x_codes[r]
+            half, offset = divmod(c0, HALF)
+            codes, scale_bytes = x_codes[r]
             for s in range(PASSES):
                 if s == 0:
                     rhs, rhs_scale = wa_codes[:, cols].bitcast(FP8X4), wa_bytes[:, cols]
                 else:
-                    rhs = wb_tiles[half][:, s - 1, 2 * off : 2 * (off + width)].bitcast(FP4X4)
+                    rhs = wb_tiles[half][:, s - 1, 2 * offset : 2 * (offset + width)].bitcast(FP4X4)
                     rhs_scale = wb_bytes[:, s - 1, cols]
                 nc.tensor.matmul_mx(
                     out=tile[:, :width],
-                    lhsT=words[:, P * s : P * (s + 1)].bitcast(FP8X4),
+                    lhsT=codes[:, P * s : P * (s + 1)].bitcast(FP8X4),
                     lhsT_scale=scale_bytes[:, P * s : P * (s + 1)],
                     rhs=rhs,
                     rhs_scale=rhs_scale,
                     start=(s == 0),
                     stop=(s == PASSES - 1),
                 )
-            if (g, c0) not in pairs:
-                pairs[g, c0] = work.tile([P, PACK * width], BF16, name="v_pairs", bufs=VP_BUFS)
-            slots = pairs[g, c0][:].rearrange("p (a n e) -> p a n e", a=2, e=2)
-            nc.scalar.activation(out=slots[:, t // 2, :, t % 2], in_=tile[:, :width], func=SQUARE, scale=root[:, r : r + 1])
+            if t == 0:
+                squares[g, c0] = work.tile([P, PACK * width], BF16, name="squares", bufs=8)
+            slots = squares[g, c0][:].rearrange("p (a n e) -> p a n e", a=2, e=2)
+            nc.scalar.activation(
+                out=slots[:, t // 2, :, t % 2], in_=tile[:, :width], func=SQUARE, scale=root[:, r : r + 1]
+            )
 
         v_grouped = {}
+        v_codes = {}
 
-        def sign_v(g, c0, width):
-            tile = work.tile([P, PACK * width], BF16, name="v_grouped", bufs=3, align_bytes=64)
+        def finish_v(g, c0, width):
+            v_grouped[g, c0] = grouped_tile(width)
             factors = factor[:, PACK * g : PACK * (g + 1)].rearrange("p (a e) -> p a e", a=2)
             nc.vector.tensor_tensor(
-                out=tile[:].rearrange("p (n a e) -> p n a e", a=2, e=2),
-                in0=pairs[g, c0][:].rearrange("p (a n e) -> p n a e", a=2, e=2),
+                out=v_grouped[g, c0][:].rearrange("p (n a e) -> p n a e", a=2, e=2),
+                in0=squares[g, c0][:].rearrange("p (a n e) -> p n a e", a=2, e=2),
                 in1=factors.unsqueeze(1).to_broadcast([P, width, 2, 2]),
                 op=MULT,
             )
-            v_grouped[g, c0] = tile
 
         def quantize_v(g, c0, width):
-            words = keep.tile([P, width], U32, name="v_codes%d_%d" % (g, c0), align_bytes=64)
+            codes = keep.tile([P, width], U32, name="v_codes%d_%d" % (g, c0), align_bytes=64)
             scale_bytes = keep.tile([P, width], U8, name="v_bytes%d_%d" % (g, c0), align_bytes=64)
-            nc.vector.quantize_mx(out=words[:].bitcast(FP8X4), scales=scale_bytes[:], in_=v_grouped[g, c0][:])
-            for q in range(width // QUARTER):
-                v_codes[g, c0 + QUARTER * q] = (words[:, QUARTER * q :], scale_bytes[:, QUARTER * q :])
+            nc.vector.quantize_mx(out=codes[:].bitcast(FP8X4), scales=scale_bytes[:], in_=v_grouped[g, c0][:])
+            for offset in range(0, width, QUARTER):
+                v_codes[g, c0 + offset] = (codes[:, offset:], scale_bytes[:, offset:])
 
         sums = {}
+        gaps = {}
 
-        def moment(c0, width, cts, groups, where=None):
-            if where is not None:
-                sums[c0, cts] = bank(where)
-            for g in groups:
-                words, scale_bytes = v_codes[g, c0]
+        def moment(tile, where):
+            c0, width, cts = tile
+            sums[tile] = bank(where)
+            for g in range(GROUPS):
+                codes, scale_bytes = v_codes[g, c0]
                 for i, ct in enumerate(cts):
                     nc.tensor.matmul_mx(
-                        out=sums[c0, cts][:, width * i : width * (i + 1)],
+                        out=sums[tile][:, width * i : width * (i + 1)],
                         lhsT=z_tile[:, g, 2 * P * ct : 2 * P * (ct + 1)].bitcast(FP4X4),
                         lhsT_scale=z_bytes[:, g, P * ct : P * (ct + 1)],
-                        rhs=words[:, :width].bitcast(FP8X4),
+                        rhs=codes[:, :width].bitcast(FP8X4),
                         rhs_scale=scale_bytes[:, :width],
                         start=(g == 0 and i == 0),
                         stop=(g == GROUPS - 1 and i == len(cts) - 1),
                     )
 
-        gaps = {}
-
-        def subtract_target(c0, width, cts):
-            tile = work.tile([P, len(cts), width], F32, name="gap", bufs=4)
+        def subtract_target(tile):
+            c0, width, cts = tile
+            gaps[tile] = work.tile([P, len(cts), width], F32, name="gap", bufs=4)
             nc.vector.tensor_tensor(
-                out=tile[:],
-                in0=sums[c0, cts][:].rearrange("p (i n) -> p i n", i=len(cts)),
+                out=gaps[tile][:],
+                in0=sums[tile][:].rearrange("p (i n) -> p i n", i=len(cts)),
                 in1=target_rows[:, cts[0] : cts[-1] + 1, c0 : c0 + width],
                 op=SUBTRACT,
             )
-            gaps[c0, cts] = tile
 
-        def scale_and_store(c0, width, cts, engine=nc.vector):
-            tile = work.tile([P, len(cts), width], F32, name="result", bufs=4)
+        def scale_and_store(tile, engine=nc.vector):
+            c0, width, cts = tile
+            result = work.tile([P, len(cts), width], F32, name="result", bufs=4)
             engine.tensor_tensor(
-                out=tile[:],
-                in0=gaps[c0, cts][:],
+                out=result[:],
+                in0=gaps[tile][:],
                 in1=prec_rows[:, c0 : c0 + width].unsqueeze(1).to_broadcast([P, len(cts), width]),
                 op=MULT,
             )
             rows = out.rearrange("(ct c) n -> c ct n", c=P)
-            nc.sync.dma_start(out=rows[:, cts[0] : cts[-1] + 1, c0 : c0 + width], in_=tile[:])
+            nc.sync.dma_start(out=rows[:, cts[0] : cts[-1] + 1, c0 : c0 + width], in_=result[:])
 
-        load_scale_col()
-        make_identity(nc, ident[:])
-        nc.vector.memset(wb_bytes[:].rearrange("p g n -> p (g n)").bitcast(I32), 0)
-        nc.gpsimd.memset(z_bytes[:].rearrange("p g n -> p (g n)").bitcast(I32), 0)
-        load_omega()
-        load_xb(0, 2)
-        load_wa(0)
-        load_xa(0, 2)
-        load_xb(2, 2)
-        load_xa(2, 2)
-        load_scale_bytes(wb_bytes, wb_scales)
-        load_wb(0)
-        load_wa(1)
-        load_xb(4, 2)
-        load_xa(4, 2)
-        load_xa(6, 2)
-        load_wb(1)
-        load_xb(6, 2)
-        load_xb(8, 4)
-        load_xa(8, 2)
-        load_xa(10, 2)
-        load_xb(12, 4)
-        load_xa(12, 2)
-        load_xa(14, 2)
-        load_rest()
+        order = [(g, 0) for g in range(GROUPS)]
+        order = [order[0], (0, HALF), order[1], (1, HALF), order[2], order[3], (2, HALF)]
+        pending = [(PACK * g + t, c0) for g, c0 in order for t in range(PACK)]
+        projected = []
 
-        zeros = keep.tile([P, HALF], BF16, name="zeros")
-        nc.vector.memset(zeros[:].bitcast(I32), 0)
+        def project_next(count):
+            for r, c0 in pending[len(projected) : len(projected) + count]:
+                project(r, c0, HALF, PRODUCT_BANKS[len(projected) % len(PRODUCT_BANKS)])
+                projected.append((r, c0))
 
-        def warm_up(count, where):
-            tile = bank(where)
-            for i in range(count):
-                nc.tensor.matmul(out=tile[:], lhsT=zeros[:, :P], rhs=zeros[:], start=True, stop=True)
+        omega_flat = omega_bf16[:].rearrange("p g t -> p (g t)")
+        size, sign, power, inv_power = per_row("size"), per_row("sign"), per_row("power"), per_row("inv_power")
+        radicand, guess, guess16 = per_row("radicand"), per_row("guess"), per_row("guess16")
+        inv_guess16, quotient = per_row("inv_guess16"), per_row("quotient")
+        nc.scalar.activation(out=size[:], in_=omega_flat, func=ABS)
+        nc.scalar.activation(out=sign[:], in_=omega_flat, func=SIGN)
+        warm_up(2)
+        copy_scale(0, spread_scale(0, PRODUCT_BANKS[0]), nc.scalar.copy)
+        second_half = spread_scale(1, PRODUCT_BANKS[1])
+        warm_up(2)
+        nc.vector.tensor_copy(out=ident_bf16[:], in_=ident[:])
+        nc.vector.tensor_scalar(out=power[:], in0=size[:], scalar1=2.0**-64, scalar2=2.0**-64, op0=IS_GE, op1=MAX)
+        nc.vector.reciprocal(out=inv_power[:], in_=power[:])
+        copy_scale(1, second_half, nc.vector.tensor_copy)
+        nc.vector.tensor_tensor(out=radicand[:], in0=size[:], in1=inv_power[:], op=MULT)
+        nc.scalar.activation(out=guess[:], in_=radicand[:], func=SQRT, scale=2.0**-10)
+        wa_grouped = group_wa_on_tensor(0, PRODUCT_BANKS[2:4])
+        turn_xa(0)
+        scale_xb(0)
+        turn_xb(0)
+        warm_up(2)
+        nc.vector.tensor_tensor(out=factor[:], in0=sign[:], in1=power[:], op=MULT)
+        scale_xb(1)
+        turn_xb(1)
+        turn_xa(2)
+        warm_up(1)
+        nc.vector.tensor_scalar(out=guess16[:], in0=guess[:], scalar1=2.0**-60, scalar2=16.0, op0=MAX, op1=MULT)
+        quantize_wa(0, wa_grouped)
+        nc.vector.reciprocal(out=inv_guess16[:], in_=guess16[:])
+        scale_xb(2)
+        turn_xb(2)
+        nc.vector.tensor_tensor(out=quotient[:], in0=radicand[:], in1=inv_guess16[:], op=MULT)
+        quantize_x(0)
+        nc.vector.scalar_tensor_tensor(out=root[:], in0=quotient[:], scalar=0.25, in1=guess16[:], op0=MULT, op1=ADD)
+        quantize_x(1)
+        project_next(2)
+        scale_xb(3)
+        turn_xb(3)
+        turn_xa(4)
+        wa_grouped = group_wa_on_vector(1)
+        quantize_x(2)
+        project_next(1)
+        turn_xa(6)
+        scale_xb(4)
+        quantize_x(3)
+        project_next(1)
+        quantize_wa(1, wa_grouped)
+        scale_xb(5)
+        turn_xb(4)
+        turn_xb(5)
+        project_next(2)
 
-        S, V = nc.scalar.copy, nc.vector.tensor_copy
-        flips = [0]
-        count = [0]
+        for g in range(1, GROUPS):
+            r = PACK * g
+            scale_xb(r + 2)
+            scale_xb(r + 3)
+            sort_xb(r + 2)
+            sort_xb(r + 3)
+            turn_xb(r + 2)
+            turn_xb(r + 3)
+            quantize_x(r)
+            quantize_x(r + 1)
+            project_next(2)
+            if g + 1 < GROUPS:
+                sort_xa(r + 4)
+                sort_xa(r + 6)
+                turn_xa(r + 4)
+                turn_xa(r + 6)
+                project_next(2)
+                scale_xb(r + 4)
+                quantize_x(r + 2)
+                scale_xb(r + 5)
+                quantize_x(r + 3)
+                sort_xb(r + 4)
+                sort_xb(r + 5)
+                turn_xb(r + 4)
+                turn_xb(r + 5)
+                project_next(2)
 
-        def ta(r):
-            flips[0] += 1
-            return ("turn", [(r, 0), (r + 1, 0)], (flips[0] - 1) % 3)
+        project_next(2)
+        finish_v(0, 0, HALF)
+        finish_v(1, 0, HALF)
+        quantize_x(ROWS - 2)
+        quantize_v(0, 0, HALF)
+        quantize_x(ROWS - 1)
+        project_next(6)
+        previous = (1, 0)
+        for g, c0 in ((0, HALF), (2, 0), (1, HALF), (3, 0)):
+            finish_v(g, c0, HALF)
+            quantize_v(*previous, HALF)
+            previous = (g, c0)
+        quantize_v(3, 0, HALF)
+        finish_v(2, HALF, HALF)
+        quantize_v(2, HALF, HALF)
 
-        def tb(r):
-            flips[0] += 1
-            return ("turn", [(r, 1), (r, 2)], (flips[0] - 1) % 3)
-
-        def pr(r, c0, width=HALF, banks=(3, 4, 5, 6, 7)):
-            count[0] += 1
-            return ("proj", r, c0, width, banks[(count[0] - 1) % len(banks)])
-
-        def sc(r):
-            return ("scale", r)
-
-        def qx(r):
-            return ("qx", r)
-
-        def sv(g, c0, width=HALF):
-            return ("sign", g, c0, width)
-
-        def qv(g, c0, width=HALF):
-            return ("qv", g, c0, width)
-
-        def mo(c0, width, cts, where, groups=range(GROUPS)):
-            return ("mom", c0, width, cts, groups, where)
-
-        def su(c0, width, cts):
-            return ("sub", c0, width, cts)
-
-        def mu(c0, width, cts, engine=nc.vector):
-            return ("mul", c0, width, cts, engine)
-
-        def so(r, is_b):
-            return ("sort", r, is_b)
-
-        def ro(i):
-            return ("root", i)
-
-        H, Q, Q2, Q3, G = HALF, QUARTER, HALF, HALF + QUARTER, nc.gpsimd
-
-        tensor_order = [ro(0), ro(1), ("warm", 2, 7), ("spread", 0, 3, S), ("spread_t", 1, 4), ("warm", 2, 7), ro(5),
-            ("gwa", 0, (5, 6), S), tb(0), ta(0), ("warm", 2, 7), tb(1), ta(2), tb(2), ("warm", 1, 7), pr(0, 0), pr(1, 0), tb(3), ta(4), pr(2, 0), ta(6), pr(3, 0), pr(0, H), pr(1, H)]
-        tensor_order += [tb(4), tb(5), pr(2, H), pr(3, H), tb(6), tb(7), pr(4, 0), pr(5, 0), pr(4, H)]
-        tensor_order += [ta(8), ta(10), pr(6, 0), pr(7, 0), tb(8), tb(9), pr(5, H), pr(6, H), pr(7, H), tb(10), tb(11), pr(8, 0), pr(9, 0)]
-        tensor_order += [ta(12), ta(14), pr(10, 0), pr(11, 0), tb(12), tb(13), pr(8, H), pr(9, H), tb(14), tb(15), pr(12, 0), pr(13, 0), pr(10, H), pr(14, 0), pr(15, 0), pr(11, H)]
-        count[0] = 0
-        last = (0, 1, 2, 6)
-        tensor_order += [pr(12 + t, Q2, QUARTER, last) for t in range(PACK)]
-        count[0] = 0
-        tensor_order += [pr(12 + t, Q3, QUARTER, (7, 3, 4, 5)) for t in range(PACK)]
-        tensor_order += [mo(0, H, (ct,), ct) for ct in (0, 1, 2)] + [mo(0, H, (3,), 6)]
-        tensor_order += [mo(Q2, Q, (0, 1), 7), mo(Q2, Q, (2, 3), 3), mo(Q3, Q, (0, 1), 4), mo(Q3, Q, (2, 3), 5)]
-
-        vector_order = [("ident",), ro(2), ro(3), ("spread_c", 1, V), ro(4), sc(0), ro(6), sc(1), ro(7), sc(2), ro(8), ("qwa", 0), ro(9), qx(0), ro(10), qx(1),
-            sc(3), qx(2), ("gwav", 1), sc(4), qx(3), ("qwa", 1), sc(5), sc(6), sc(7), qx(4), qx(5), sv(0, 0), sc(8), qv(0, 0), qx(6), qx(7), sc(9),
-            sc(10), sv(0, H), sc(11), qv(0, H), qx(8), qx(9), sc(12), sv(1, 0), sc(13), qx(10), qx(11), qv(1, 0), sc(14), sc(15), sv(1, H), qx(12), qx(13), qv(1, H),
-            sv(2, 0), qx(14), qx(15), qv(2, 0), sv(3, 0), sv(2, H), qv(3, 0), qv(2, H), sv(3, Q2, Q), su(0, H, (0,)), qv(3, Q2, Q),
-            sv(3, Q3, Q), mu(0, H, (0,)), su(0, H, (1,)), qv(3, Q3, Q), mu(0, H, (1,)), su(0, H, (2,)), su(0, H, (3,)), mu(0, H, (2,)),
-            mu(0, H, (3,)), su(Q2, Q, (0, 1)), su(Q2, Q, (2, 3)), mu(Q2, Q, (0, 1)), su(Q3, Q, (0, 1)), mu(Q2, Q, (2, 3)),
-            su(Q3, Q, (2, 3)), mu(Q3, Q, (0, 1)), mu(Q3, Q, (2, 3))]
-
-        def run(item):
-            kind, args = item[0], item[1:]
-            calls[kind](*args)
-
-        ROOT_NEEDS = [(), (), (0,), (2,), (3,), (4,), (1, 2), (5,), (7,), (8,), (9,)]
-
-        def needs(item):
-            kind, a = item[0], item[1:]
-            if kind == "turn":
-                out_ = []
-                for r, s in a[0]:
-                    if s > 0:
-                        out_.append(("scale", r))
-                    key = ("sort", r - r % SORT_A if s == 0 else r, s > 0)
-                    if key in planned:
-                        out_.append(key)
-                    if r // 2 >= XG_BUFS:
-                        out_ += [("qx", 2 * (r // 2 - XG_BUFS)), ("qx", 2 * (r // 2 - XG_BUFS) + 1)]
-                return out_
-            if kind == "scale":
-                return [("spread", 0), ("spread", 1)] + ([("turned", a[0] - XB_BUFS, 1), ("turned", a[0] - XB_BUFS, 2)] if a[0] >= XB_BUFS else [])
-            if kind == "sort":
-                return [("scale", a[0])] if a[1] else []
-            if kind == "spread_c":
-                return [("spread_t", a[0])]
-            if kind == "gwa":
-                return [("ident",)]
-            if kind == "qx":
-                return [("turned", a[0], s) for s in range(PASSES)]
-            if kind == "qwa":
-                return [("gwa", a[0])]
-            if kind == "proj":
-                return [("qx", a[0]), ("qwa", a[1] // HALF), ("root", 10)]
-            if kind == "sign":
-                return [("proj", PACK * a[0] + t, a[1]) for t in range(PACK)]
-            if kind == "qv":
-                return [("sign", a[0], a[1])]
-            if kind == "mom":
-                return [("have_v", g, a[0]) for g in a[3]]
-            if kind == "sub":
-                return [("mom_done", a[0], a[2])]
-            if kind == "mul":
-                return [("sub", a[0], a[2])]
-            if kind == "root":
-                return [("root", i) for i in ROOT_NEEDS[a[0]]]
-            return []
-
-        def gives(item):
-            kind, a = item[0], item[1:]
-            if kind == "turn":
-                return [("turned", r, s) for r, s in a[0]]
-            if kind in ("proj", "sign"):
-                return [(kind, a[0], a[1])]
-            if kind == "qv":
-                return [("have_v", a[0], a[1] + QUARTER * q) for q in range(a[2] // QUARTER)]
-            if kind == "mom":
-                return [("mom_done", a[0], a[2])] if GROUPS - 1 in a[3] else []
-            if kind in ("sub", "mul"):
-                return [(kind, a[0], a[2])]
-            if kind == "spread_c":
-                return [("spread", a[0])]
-            if kind == "gwav":
-                return [("gwa", a[0])]
-            if kind == "sort":
-                return [(kind, a[0], a[1])]
-            return [(kind,) + tuple(a[:1])]
-
-        calls = {
-            "turn": turn,
-            "scale": scale_xb,
-            "sort": lambda r, is_b: sort_words(r, 1, 1, PASSES) if is_b else sort_words(r, SORT_A, 0, 1),
-            "qx": quantize_x,
-            "qwa": quantize_wa,
-            "gwa": group_wa,
-            "gwav": group_wa_vector,
-            "proj": project,
-            "sign": sign_v,
-            "qv": quantize_v,
-            "mom": moment,
-            "sub": subtract_target,
-            "mul": scale_and_store,
-            "root": lambda i: root_step(i, i + 1),
-            "spread": spread_scale,
-            "spread_t": lambda h, w: spread_turn(h, w),
-            "spread_c": lambda h, c: spread_copy(h, c),
-            "warm": warm_up,
-            "ident": lambda: nc.vector.tensor_copy(out=ident_bf16[:], in_=ident[:]),
-        }
-        planned = set(key for item in vector_order for key in gives(item))
-        have = set()
-        queues = [list(tensor_order), list(vector_order)]
-        while queues[0] or queues[1]:
-            ready = [q for q in queues if q and all(key in have for key in needs(q[0]))]
-            assert ready, (queues[0][:1], queues[1][:1])
-            item = ready[0].pop(0)
-            run(item)
-            have.update(gives(item))
+        last = len(projected) % len(PRODUCT_BANKS)
+        banks = TURN_BANKS + PRODUCT_BANKS[last:] + PRODUCT_BANKS[:last]
+        banks = list(banks + banks)
+        tiles = [(0, HALF, (ct,)) for ct in range(C_TILES)]
+        tiles += [(c0, QUARTER, cts) for c0 in (HALF, HALF + QUARTER) for cts in ((0, 1), (2, 3))]
+        for q in range(2):
+            c0 = HALF + QUARTER * q
+            for t in range(PACK):
+                project(PACK * (GROUPS - 1) + t, c0, QUARTER, banks.pop(0))
+            moment(tiles[q], banks.pop(0))
+            finish_v(GROUPS - 1, c0, QUARTER)
+            subtract_target(tiles[q])
+            quantize_v(GROUPS - 1, c0, QUARTER)
+            if q == 0:
+                scale_and_store(tiles[0])
+        for i in range(2, len(tiles)):
+            moment(tiles[i], banks.pop(0))
+            subtract_target(tiles[i])
+            scale_and_store(tiles[i - 1])
+        scale_and_store(tiles[-1])

@@ -194,7 +194,10 @@ def tile_projection_moment_gap_s3_kernel(
 
         def sort_words(values, pieces):
             tile = work.tile([P, 2, 2, P], F32, name="sorted", bufs=6)
-            nc.vector.tensor_copy(out=tile[:], in_=values.bitcast(F32).rearrange("p (s m u) -> p s u m", m=P, u=2))
+            nc.vector.tensor_copy(
+                out=tile[:].rearrange("p s u (c i) -> p s c u i", i=4),
+                in_=values.bitcast(F32).rearrange("p (s c i u) -> p s c u i", s=2, i=4, u=2),
+            )
             for i, piece in enumerate(pieces):
                 words[piece] = [tile[:, i, u, :] for u in range(2)]
 

@@ -193,16 +193,13 @@ def tile_projection_moment_gap_s3_kernel(
                 every_second_word(r, s, xb_rows[r][:, K_PASS * (s - 1) : K_PASS * s])
 
         def sort_words(values, pieces):
-            tile = work.tile([P, 2, 2, P], F32, name="sorted", bufs=6)
+            tile = work.tile([P, 2, 2, P], F32, name="sorted", bufs=4)
             nc.vector.tensor_copy(
                 out=tile[:].rearrange("p s u (c i) -> p s c u i", i=4),
                 in_=values.bitcast(F32).rearrange("p (s c i u) -> p s c u i", s=2, i=4, u=2),
             )
             for i, piece in enumerate(pieces):
                 words[piece] = [tile[:, i, u, :] for u in range(2)]
-
-        def sort_xa(r):
-            sort_words(xa_pairs[r][:].rearrange("p t k -> p (t k)"), [(r, 0), (r + 1, 0)])
 
         def sort_xb(r):
             sort_words(xb_rows[r][:], [(r, 1), (r, 2)])
@@ -280,7 +277,7 @@ def tile_projection_moment_gap_s3_kernel(
         v_grouped = {}
         v_codes = {}
 
-        def finish_v(g, c0, width):
+        def finish_v(g, c0, width, factor=factor):
             v_grouped[g, c0] = grouped_tile(width)
             factors = factor[:, PACK * g : PACK * (g + 1)].rearrange("p (a e) -> p a e", a=2)
             nc.vector.tensor_tensor(
@@ -318,35 +315,37 @@ def tile_projection_moment_gap_s3_kernel(
 
         def subtract_target(tile):
             c0, width, cts = tile
-            gaps[tile] = work.tile([P, len(cts), width], F32, name="gap", bufs=4)
+            gaps[tile] = work.tile([P, len(cts), width], F32, name="gap", bufs=5)
             nc.vector.tensor_tensor(
                 out=gaps[tile][:],
-                in0=sums[tile][:].rearrange("p (i n) -> p i n", i=len(cts)),
+                in0=sums[tile][:, : width * len(cts)].rearrange("p (i n) -> p i n", i=len(cts)),
                 in1=target_rows[:, cts[0] : cts[-1] + 1, c0 : c0 + width],
                 op=SUBTRACT,
             )
 
-        def scale_and_store(tile, engine=nc.vector):
+        def scale_and_store(tile, engine, prec_cols):
             c0, width, cts = tile
-            result = work.tile([P, len(cts), width], F32, name="result", bufs=4)
+            result = work.tile([P, len(cts), width], F32, name="result", bufs=6)
             engine.tensor_tensor(
                 out=result[:],
                 in0=gaps[tile][:],
-                in1=prec_rows[:, c0 : c0 + width].unsqueeze(1).to_broadcast([P, len(cts), width]),
+                in1=prec_cols.unsqueeze(1).to_broadcast([P, len(cts), width]),
                 op=MULT,
             )
             rows = out.rearrange("(ct c) n -> c ct n", c=P)
             nc.sync.dma_start(out=rows[:, cts[0] : cts[-1] + 1, c0 : c0 + width], in_=result[:])
 
-        order = [(g, 0) for g in range(GROUPS)]
-        order = [order[0], (0, HALF), order[1], (1, HALF), order[2], order[3], (2, HALF)]
-        pending = [(PACK * g + t, c0) for g, c0 in order for t in range(PACK)]
-        projected = []
+        order = [(0, 0), (0, HALF), (1, 0), (1, HALF), (2, 0), (3, 0), (2, HALF), (3, HALF)]
+        pending = [(PACK * g + t, c0, HALF) for g, c0 in order for t in range(PACK)]
+        free = list(PRODUCT_BANKS)
+
+        def next_bank():
+            free.append(free.pop(0))
+            return free[-1]
 
         def project_next(count):
-            for r, c0 in pending[len(projected) : len(projected) + count]:
-                project(r, c0, HALF, PRODUCT_BANKS[len(projected) % len(PRODUCT_BANKS)])
-                projected.append((r, c0))
+            for i in range(count):
+                project(*pending.pop(0), next_bank())
 
         omega_flat = omega_bf16[:].rearrange("p g t -> p (g t)")
         size, sign, power, inv_power = per_row("size"), per_row("sign"), per_row("power"), per_row("inv_power")
@@ -396,6 +395,7 @@ def tile_projection_moment_gap_s3_kernel(
         project_next(1)
         quantize_wa(1, wa_grouped)
         scale_xb(5)
+
         turn_xb(4)
         turn_xb(5)
         project_next(2)
@@ -412,8 +412,6 @@ def tile_projection_moment_gap_s3_kernel(
             quantize_x(r + 1)
             project_next(2)
             if g + 1 < GROUPS:
-                sort_xa(r + 4)
-                sort_xa(r + 6)
                 turn_xa(r + 4)
                 turn_xa(r + 6)
                 project_next(2)
@@ -427,39 +425,71 @@ def tile_projection_moment_gap_s3_kernel(
                 turn_xb(r + 5)
                 project_next(2)
 
+        free[2:2] = [0]
+        free[4:4] = [1, 2]
+        tiles = [(0, HALF, (ct,)) for ct in range(C_TILES)] + [(HALF, HALF, (ct,)) for ct in range(C_TILES - 1)]
+        tiles += [(HALF, QUARTER, (3,)), (HALF + QUARTER, QUARTER, (3,))]
+        held = []
+
+        def hold_constants():
+            tile = bank(free.pop(0), BF16, 2 * HALF)
+            nc.tensor.matmul(out=tile[:, :HALF], lhsT=ident_bf16[:], rhs=prec_rows[:, HALF:], start=True, stop=True)
+            nc.tensor.matmul(out=tile[:, HALF : HALF + ROWS], lhsT=ident_bf16[:], rhs=factor[:], start=True, stop=True)
+            held.append(tile)
+
+        def on_gpsimd(i):
+            c0, width, cts = tiles[i]
+            scale_and_store(tiles[i], nc.gpsimd, prec_rows[:, c0 : c0 + width])
+
+        def on_vector(i):
+            c0, width, cts = tiles[i]
+            scale_and_store(tiles[i], nc.vector, held[0][:, c0 - HALF : c0 - HALF + width] if c0 >= HALF and held else prec_rows[:, c0 : c0 + width])
+
         project_next(2)
         finish_v(0, 0, HALF)
+        quantize_x(14)
         finish_v(1, 0, HALF)
-        quantize_x(ROWS - 2)
+        quantize_x(15)
         quantize_v(0, 0, HALF)
-        quantize_x(ROWS - 1)
-        project_next(6)
-        previous = (1, 0)
-        for g, c0 in ((0, HALF), (2, 0), (1, HALF), (3, 0)):
-            finish_v(g, c0, HALF)
-            quantize_v(*previous, HALF)
-            previous = (g, c0)
+        project_next(10)
+        quantize_v(1, 0, HALF)
+        finish_v(2, 0, HALF)
+        finish_v(0, HALF, HALF)
+        quantize_v(2, 0, HALF)
+        finish_v(3, 0, HALF)
+        quantize_v(0, HALF, HALF)
+        finish_v(1, HALF, HALF)
         quantize_v(3, 0, HALF)
+        moment(tiles[0], next_bank())
+        hold_constants()
         finish_v(2, HALF, HALF)
+        quantize_v(1, HALF, HALF)
+        moment(tiles[1], next_bank())
+        moment(tiles[2], next_bank())
+        moment(tiles[3], next_bank())
         quantize_v(2, HALF, HALF)
-
-        last = len(projected) % len(PRODUCT_BANKS)
-        banks = TURN_BANKS + PRODUCT_BANKS[last:] + PRODUCT_BANKS[:last]
-        banks = list(banks + banks)
-        tiles = [(0, HALF, (ct,)) for ct in range(C_TILES)]
-        tiles += [(c0, QUARTER, cts) for c0 in (HALF, HALF + QUARTER) for cts in ((0, 1), (2, 3))]
-        for q in range(2):
-            c0 = HALF + QUARTER * q
-            for t in range(PACK):
-                project(PACK * (GROUPS - 1) + t, c0, QUARTER, banks.pop(0))
-            moment(tiles[q], banks.pop(0))
-            finish_v(GROUPS - 1, c0, QUARTER)
-            subtract_target(tiles[q])
-            quantize_v(GROUPS - 1, c0, QUARTER)
-            if q == 0:
-                scale_and_store(tiles[0])
-        for i in range(2, len(tiles)):
-            moment(tiles[i], banks.pop(0))
-            subtract_target(tiles[i])
-            scale_and_store(tiles[i - 1])
-        scale_and_store(tiles[-1])
+        subtract_target(tiles[0])
+        on_gpsimd(0)
+        finish_v(3, HALF, HALF, held[0][:, HALF:])
+        subtract_target(tiles[1])
+        quantize_v(3, HALF, HALF)
+        on_gpsimd(1)
+        subtract_target(tiles[2])
+        subtract_target(tiles[3])
+        moment(tiles[4], next_bank())
+        subtract_target(tiles[4])
+        on_gpsimd(2)
+        moment(tiles[5], next_bank())
+        on_vector(4)
+        subtract_target(tiles[5])
+        on_gpsimd(3)
+        moment(tiles[6], next_bank())
+        on_vector(5)
+        subtract_target(tiles[6])
+        moment(tiles[7], next_bank())
+        moment(tiles[8], next_bank())
+        subtract_target(tiles[7])
+        on_vector(6)
+        subtract_target(tiles[8])
+        on_vector(7)
+        on_vector(8)

@@ -201,6 +201,9 @@ def tile_projection_moment_gap_s3_kernel(
             for i, piece in enumerate(pieces):
                 words[piece] = [tile[:, i, u, :] for u in range(2)]
 
+        def sort_xa(r):
+            sort_words(xa_pairs[r][:].rearrange("p t k -> p (t k)"), [(r, 0), (r + 1, 0)])
+
         def sort_xb(r):
             sort_words(xb_rows[r][:], [(r, 1), (r, 2)])
 
@@ -217,18 +220,17 @@ def tile_projection_moment_gap_s3_kernel(
             if pair not in x_grouped:
                 x_grouped[pair] = work.tile([P, 2 * PASSES, K_PASS], BF16, name="x_grouped", bufs=4, align_bytes=64)
             first, second = [PASSES * (r % 2) + s for r, s in pieces]
-            nc.scalar.copy(
-                out=x_grouped[pair][:, first : second + 1 : second - first, :]
-                .bitcast(F32)
-                .rearrange("p i (m u) -> p i m u", u=2),
+            grouped = x_grouped[pair][:, first : second + 1 : second - first, :]
+            return dict(
+                out=grouped.bitcast(F32).rearrange("p i (m u) -> p i m u", u=2),
                 in_=tile[:].rearrange("p (i u m) -> p i m u", i=2, u=2),
             )
 
         def turn_xa(r):
-            turn([(r, 0), (r + 1, 0)])
+            nc.scalar.copy(**turn([(r, 0), (r + 1, 0)]))
 
         def turn_xb(r):
-            turn([(r, 1), (r, 2)])
+            nc.scalar.copy(**turn([(r, 1), (r, 2)]))
 
         x_codes = {}
 
@@ -274,12 +276,20 @@ def tile_projection_moment_gap_s3_kernel(
                 out=slots[:, t // 2, :, t % 2], in_=tile[:, :width], func=SQUARE, scale=root[:, r : r + 1]
             )
 
+        held = []
+
+        def hold_constants(where):
+            tile = bank(where, BF16, 2 * HALF)
+            nc.tensor.matmul(out=tile[:, :HALF], lhsT=ident_bf16[:], rhs=prec_rows[:, HALF:], start=True, stop=True)
+            nc.tensor.matmul(out=tile[:, HALF : HALF + ROWS], lhsT=ident_bf16[:], rhs=factor[:], start=True, stop=True)
+            held.append(tile)
+
         v_grouped = {}
         v_codes = {}
 
-        def finish_v(g, c0, width, factor=factor):
+        def finish_v(g, c0, width):
             v_grouped[g, c0] = grouped_tile(width)
-            factors = factor[:, PACK * g : PACK * (g + 1)].rearrange("p (a e) -> p a e", a=2)
+            factors = held[0][:, HALF + PACK * g : HALF + PACK * (g + 1)].rearrange("p (a e) -> p a e", a=2)
             nc.vector.tensor_tensor(
                 out=v_grouped[g, c0][:].rearrange("p (n a e) -> p n a e", a=2, e=2),
                 in0=squares[g, c0][:].rearrange("p (a n e) -> p n a e", a=2, e=2),
@@ -323,8 +333,12 @@ def tile_projection_moment_gap_s3_kernel(
                 op=SUBTRACT,
             )
 
-        def scale_and_store(tile, engine, prec_cols):
+        def scale_and_store(tile):
             c0, width, cts = tile
+            if c0 < HALF:
+                engine, prec_cols = nc.gpsimd, prec_rows[:, c0 : c0 + width]
+            else:
+                engine, prec_cols = nc.vector, held[0][:, c0 - HALF : c0 - HALF + width]
             result = work.tile([P, len(cts), width], F32, name="result", bufs=6)
             engine.tensor_tensor(
                 out=result[:],
@@ -406,12 +420,16 @@ def tile_projection_moment_gap_s3_kernel(
             scale_xb(r + 3)
             sort_xb(r + 2)
             sort_xb(r + 3)
-            turn_xb(r + 2)
-            turn_xb(r + 3)
+            if g + 1 == GROUPS:
+                last_turns = [turn([(row, 1), (row, 2)]) for row in (r + 2, r + 3)]
+            else:
+                turn_xb(r + 2)
+                turn_xb(r + 3)
             quantize_x(r)
             quantize_x(r + 1)
             project_next(2)
             if g + 1 < GROUPS:
+                sort_xa(r + 4)
                 turn_xa(r + 4)
                 turn_xa(r + 6)
                 project_next(2)
@@ -424,72 +442,47 @@ def tile_projection_moment_gap_s3_kernel(
                 turn_xb(r + 4)
                 turn_xb(r + 5)
                 project_next(2)
+        for sides in last_turns:
+            nc.vector.tensor_copy(**sides)
+        quantize_x(ROWS - 2)
+        quantize_x(ROWS - 1)
 
-        free[2:2] = [0]
-        free[4:4] = [1, 2]
+        hold_constants(free.pop(0))
+        free[1:1] = TURN_BANKS[:1]
+        free[3:3] = TURN_BANKS[1:]
+        project_next(len(pending))
         tiles = [(0, HALF, (ct,)) for ct in range(C_TILES)] + [(HALF, HALF, (ct,)) for ct in range(C_TILES - 1)]
-        tiles += [(HALF, QUARTER, (3,)), (HALF + QUARTER, QUARTER, (3,))]
-        held = []
-
-        def hold_constants():
-            tile = bank(free.pop(0), BF16, 2 * HALF)
-            nc.tensor.matmul(out=tile[:, :HALF], lhsT=ident_bf16[:], rhs=prec_rows[:, HALF:], start=True, stop=True)
-            nc.tensor.matmul(out=tile[:, HALF : HALF + ROWS], lhsT=ident_bf16[:], rhs=factor[:], start=True, stop=True)
-            held.append(tile)
-
-        def on_gpsimd(i):
-            c0, width, cts = tiles[i]
-            scale_and_store(tiles[i], nc.gpsimd, prec_rows[:, c0 : c0 + width])
-
-        def on_vector(i):
-            c0, width, cts = tiles[i]
-            scale_and_store(tiles[i], nc.vector, held[0][:, c0 - HALF : c0 - HALF + width] if c0 >= HALF and held else prec_rows[:, c0 : c0 + width])
-
-        project_next(2)
+        tiles += [(HALF, QUARTER, (C_TILES - 1,)), (HALF + QUARTER, QUARTER, (C_TILES - 1,))]
         finish_v(0, 0, HALF)
-        quantize_x(14)
         finish_v(1, 0, HALF)
-        quantize_x(15)
         quantize_v(0, 0, HALF)
-        project_next(10)
-        quantize_v(1, 0, HALF)
-        finish_v(2, 0, HALF)
-        finish_v(0, HALF, HALF)
-        quantize_v(2, 0, HALF)
-        finish_v(3, 0, HALF)
-        quantize_v(0, HALF, HALF)
-        finish_v(1, HALF, HALF)
-        quantize_v(3, 0, HALF)
-        moment(tiles[0], next_bank())
-        hold_constants()
-        finish_v(2, HALF, HALF)
-        quantize_v(1, HALF, HALF)
-        moment(tiles[1], next_bank())
-        moment(tiles[2], next_bank())
-        moment(tiles[3], next_bank())
-        quantize_v(2, HALF, HALF)
+        previous = (1, 0)
+        for g, c0 in ((2, 0), (0, HALF), (3, 0), (1, HALF), (2, HALF)):
+            finish_v(g, c0, HALF)
+            quantize_v(*previous, HALF)
+            previous = (g, c0)
+        quantize_v(*previous, HALF)
+        for tile in tiles[:C_TILES]:
+            moment(tile, next_bank())
         subtract_target(tiles[0])
-        on_gpsimd(0)
-        finish_v(3, HALF, HALF, held[0][:, HALF:])
+        scale_and_store(tiles[0])
+        finish_v(3, HALF, HALF)
         subtract_target(tiles[1])
         quantize_v(3, HALF, HALF)
-        on_gpsimd(1)
+        scale_and_store(tiles[1])
         subtract_target(tiles[2])
         subtract_target(tiles[3])
         moment(tiles[4], next_bank())
         subtract_target(tiles[4])
-        on_gpsimd(2)
+        scale_and_store(tiles[2])
+        scale_and_store(tiles[4])
         moment(tiles[5], next_bank())
-        on_vector(4)
         subtract_target(tiles[5])
-        on_gpsimd(3)
-        moment(tiles[6], next_bank())
-        on_vector(5)
-        subtract_target(tiles[6])
-        moment(tiles[7], next_bank())
-        moment(tiles[8], next_bank())
-        subtract_target(tiles[7])
-        on_vector(6)
-        subtract_target(tiles[8])
-        on_vector(7)
-        on_vector(8)
+        scale_and_store(tiles[3])
+        scale_and_store(tiles[5])
+        for i in range(6, len(tiles)):
+            moment(tiles[i], next_bank())
+            subtract_target(tiles[i])
+            if i > 6:
+                scale_and_store(tiles[i - 1])
+        scale_and_store(tiles[-1])

@@ -32,7 +32,8 @@ HALF = 512
 QUARTER = HALF // 2
 C_TILES = C // P
 TURN_BANKS = (0, 1, 2)
-PRODUCT_BANKS = (3, 4, 5, 6, 7)
+PRODUCT_BANKS = (3, 4, 5, 6)
+HELD_BANK = 7
 
 FLOPS = 2 * M * N * (KA + KB) + 2 * C * N * M
 
@@ -63,7 +64,9 @@ def tile_projection_moment_gap_s3_kernel(
         z_tile = keep.tile([P, GROUPS, 2 * C], U8, name="z_tile", align_bytes=64)
         z_bytes = keep.tile([P, GROUPS, C], U8, name="z_bytes", align_bytes=64)
         omega_bf16 = keep.tile([P, GROUPS, PACK], BF16, name="omega_bf16")
-        prec_rows = keep.tile([P, N], BF16, name="prec_rows")
+        prec_rows = keep.tile([P, HALF], BF16, name="prec_rows")
+        prec_line = keep.tile([P, HALF], BF16, name="prec_line")
+        ones = keep.tile([P, P], BF16, name="ones")
         target_rows = keep.tile([P, C_TILES, N], BF16, name="target_rows")
         ident = keep.tile([P, P], F32, name="ident")
         ident_bf16 = keep.tile([P, P], BF16, name="ident_bf16")
@@ -101,7 +104,9 @@ def tile_projection_moment_gap_s3_kernel(
 
         nc.sync.dma_start(out=scale_col[:], in_=xb_scale.rearrange("o (h p j) -> p (o h) j", h=2, j=PACK))
         nc.vector.memset(zeros[:].bitcast(I32), 0)
+        nc.vector.memset(prec_line[:].bitcast(I32), 0)
         make_identity(nc, ident[:])
+        nc.vector.memset(ones[:], 1.0)
         nc.vector.memset(wb_bytes[:].rearrange("p g n -> p (g n)").bitcast(I32), 0)
         nc.vector.memset(z_bytes[:].rearrange("p g n -> p (g n)").bitcast(I32), 0)
         nc.sync.dma_start(out=omega_bf16[:], in_=omega.rearrange("(g p t) -> p g t", p=P, t=PACK))
@@ -111,6 +116,7 @@ def tile_projection_moment_gap_s3_kernel(
         load_xb(2, 2)
         load_xa(2)
         load_scale_bytes(wb_bytes, wb_scales)
+        nc.sync.dma_start(out=prec_line[0:1, :], in_=prec[HALF:].unsqueeze(0))
         load_wb(0)
         load_wa(1)
         load_xb(4, 2)
@@ -125,10 +131,10 @@ def tile_projection_moment_gap_s3_kernel(
         load_scale_bytes(z_bytes, z_scales)
         nc.sync.dma_start(out=z_tile[:], in_=z_words.rearrange("g p n -> p g n"))
         nc.sync.dma_start(out=target_rows[:], in_=target.rearrange("(ct c) n -> c ct n", c=P))
-        nc.sync.dma_start(out=prec_rows[:], in_=prec.partition_broadcast(P))
+        nc.sync.dma_start(out=prec_rows[:], in_=prec[:HALF].partition_broadcast(P))
 
         def warm_up(count):
-            tile = bank(PRODUCT_BANKS[-1])
+            tile = bank(HELD_BANK)
             for i in range(count):
                 nc.tensor.matmul(out=tile[:], lhsT=zeros[:, :P], rhs=zeros[:], start=True, stop=True)
 
@@ -145,11 +151,11 @@ def tile_projection_moment_gap_s3_kernel(
                 in_=tile[:].rearrange("p (j n) -> p n j", j=PACK),
             )
 
-        def grouped_tile(width):
-            return work.tile([P, PACK * width], BF16, name="grouped", bufs=3, align_bytes=64)
+        def grouped_tile():
+            return work.tile([P, PACK * HALF], BF16, name="grouped", bufs=3, align_bytes=64)
 
         def group_wa_on_tensor(half, banks):
-            grouped = grouped_tile(HALF)
+            grouped = grouped_tile()
             for i, where in enumerate(banks):
                 tile = bank(where, BF16, 2 * HALF)
                 for j in range(2):
@@ -165,7 +171,7 @@ def tile_projection_moment_gap_s3_kernel(
             return grouped
 
         def group_wa_on_vector(half):
-            grouped = grouped_tile(HALF)
+            grouped = grouped_tile()
             nc.vector.tensor_copy(
                 out=grouped[:].rearrange("p (c i j) -> p c j i", i=4, j=PACK),
                 in_=wa_rows[half][:].rearrange("p j (c i) -> p c j i", i=4),
@@ -192,20 +198,14 @@ def tile_projection_moment_gap_s3_kernel(
             for s in range(1, PASSES):
                 every_second_word(r, s, xb_rows[r][:, K_PASS * (s - 1) : K_PASS * s])
 
-        def sort_words(values, pieces):
+        def sort_xb(r):
             tile = work.tile([P, 2, 2, P], F32, name="sorted", bufs=4)
             nc.vector.tensor_copy(
                 out=tile[:].rearrange("p s u (c i) -> p s c u i", i=4),
-                in_=values.bitcast(F32).rearrange("p (s c i u) -> p s c u i", s=2, i=4, u=2),
+                in_=xb_rows[r][:].bitcast(F32).rearrange("p (s c i u) -> p s c u i", s=2, i=4, u=2),
             )
-            for i, piece in enumerate(pieces):
-                words[piece] = [tile[:, i, u, :] for u in range(2)]
-
-        def sort_xa(r):
-            sort_words(xa_pairs[r][:].rearrange("p t k -> p (t k)"), [(r, 0), (r + 1, 0)])
-
-        def sort_xb(r):
-            sort_words(xb_rows[r][:], [(r, 1), (r, 2)])
+            for s in range(1, PASSES):
+                words[r, s] = [tile[:, s - 1, u, :] for u in range(2)]
 
         x_grouped = {}
         turns = []
@@ -221,16 +221,16 @@ def tile_projection_moment_gap_s3_kernel(
                 x_grouped[pair] = work.tile([P, 2 * PASSES, K_PASS], BF16, name="x_grouped", bufs=4, align_bytes=64)
             first, second = [PASSES * (r % 2) + s for r, s in pieces]
             grouped = x_grouped[pair][:, first : second + 1 : second - first, :]
-            return dict(
+            nc.scalar.copy(
                 out=grouped.bitcast(F32).rearrange("p i (m u) -> p i m u", u=2),
                 in_=tile[:].rearrange("p (i u m) -> p i m u", i=2, u=2),
             )
 
         def turn_xa(r):
-            nc.scalar.copy(**turn([(r, 0), (r + 1, 0)]))
+            turn([(r, 0), (r + 1, 0)])
 
         def turn_xb(r):
-            nc.scalar.copy(**turn([(r, 1), (r, 2)]))
+            turn([(r, 1), (r, 2)])
 
         x_codes = {}
 
@@ -248,20 +248,19 @@ def tile_projection_moment_gap_s3_kernel(
         root, factor = per_row("root"), per_row("factor", BF16)
         squares = {}
 
-        def project(r, c0, width, where):
+        def project(r, c0, where):
             g, t = divmod(r, PACK)
             tile = bank(where)
-            cols = slice(c0, c0 + width)
-            half, offset = divmod(c0, HALF)
+            cols = slice(c0, c0 + HALF)
             codes, scale_bytes = x_codes[r]
             for s in range(PASSES):
                 if s == 0:
                     rhs, rhs_scale = wa_codes[:, cols].bitcast(FP8X4), wa_bytes[:, cols]
                 else:
-                    rhs = wb_tiles[half][:, s - 1, 2 * offset : 2 * (offset + width)].bitcast(FP4X4)
+                    rhs = wb_tiles[c0 // HALF][:, s - 1, :].bitcast(FP4X4)
                     rhs_scale = wb_bytes[:, s - 1, cols]
                 nc.tensor.matmul_mx(
-                    out=tile[:, :width],
+                    out=tile[:],
                     lhsT=codes[:, P * s : P * (s + 1)].bitcast(FP8X4),
                     lhsT_scale=scale_bytes[:, P * s : P * (s + 1)],
                     rhs=rhs,
@@ -270,87 +269,75 @@ def tile_projection_moment_gap_s3_kernel(
                     stop=(s == PASSES - 1),
                 )
             if t == 0:
-                squares[g, c0] = work.tile([P, PACK * width], BF16, name="squares", bufs=8)
+                squares[g, c0] = work.tile([P, PACK * HALF], BF16, name="squares", bufs=8)
             slots = squares[g, c0][:].rearrange("p (a n e) -> p a n e", a=2, e=2)
-            nc.scalar.activation(
-                out=slots[:, t // 2, :, t % 2], in_=tile[:, :width], func=SQUARE, scale=root[:, r : r + 1]
-            )
+            nc.scalar.activation(out=slots[:, t // 2, :, t % 2], in_=tile[:], func=SQUARE, scale=root[:, r : r + 1])
 
         held = []
 
         def hold_constants(where):
             tile = bank(where, BF16, 2 * HALF)
-            nc.tensor.matmul(out=tile[:, :HALF], lhsT=ident_bf16[:], rhs=prec_rows[:, HALF:], start=True, stop=True)
+            nc.tensor.matmul(out=tile[:, :HALF], lhsT=ones[:], rhs=prec_line[:], start=True, stop=True)
             nc.tensor.matmul(out=tile[:, HALF : HALF + ROWS], lhsT=ident_bf16[:], rhs=factor[:], start=True, stop=True)
             held.append(tile)
 
         v_grouped = {}
         v_codes = {}
 
-        def finish_v(g, c0, width):
-            v_grouped[g, c0] = grouped_tile(width)
+        def finish_v(g, c0):
+            v_grouped[g, c0] = grouped_tile()
             factors = held[0][:, HALF + PACK * g : HALF + PACK * (g + 1)].rearrange("p (a e) -> p a e", a=2)
             nc.vector.tensor_tensor(
                 out=v_grouped[g, c0][:].rearrange("p (n a e) -> p n a e", a=2, e=2),
                 in0=squares[g, c0][:].rearrange("p (a n e) -> p n a e", a=2, e=2),
-                in1=factors.unsqueeze(1).to_broadcast([P, width, 2, 2]),
+                in1=factors.unsqueeze(1).to_broadcast([P, HALF, 2, 2]),
                 op=MULT,
             )
 
-        def quantize_v(g, c0, width):
-            codes = keep.tile([P, width], U32, name="v_codes%d_%d" % (g, c0), align_bytes=64)
-            scale_bytes = keep.tile([P, width], U8, name="v_bytes%d_%d" % (g, c0), align_bytes=64)
+        def quantize_v(g, c0):
+            codes = keep.tile([P, HALF], U32, name="v_codes%d_%d" % (g, c0), align_bytes=64)
+            scale_bytes = keep.tile([P, HALF], U8, name="v_bytes%d_%d" % (g, c0), align_bytes=64)
             nc.vector.quantize_mx(out=codes[:].bitcast(FP8X4), scales=scale_bytes[:], in_=v_grouped[g, c0][:])
-            for offset in range(0, width, QUARTER):
-                v_codes[g, c0 + offset] = (codes[:, offset:], scale_bytes[:, offset:])
+            v_codes[g, c0] = (codes, scale_bytes)
 
         sums = {}
         gaps = {}
 
         def moment(tile, where):
-            c0, width, cts = tile
+            c0, width, ct = tile
             sums[tile] = bank(where)
+            cols = slice(c0 % HALF, c0 % HALF + width)
             for g in range(GROUPS):
-                codes, scale_bytes = v_codes[g, c0]
-                for i, ct in enumerate(cts):
-                    nc.tensor.matmul_mx(
-                        out=sums[tile][:, width * i : width * (i + 1)],
-                        lhsT=z_tile[:, g, 2 * P * ct : 2 * P * (ct + 1)].bitcast(FP4X4),
-                        lhsT_scale=z_bytes[:, g, P * ct : P * (ct + 1)],
-                        rhs=codes[:, :width].bitcast(FP8X4),
-                        rhs_scale=scale_bytes[:, :width],
-                        start=(g == 0 and i == 0),
-                        stop=(g == GROUPS - 1 and i == len(cts) - 1),
-                    )
+                codes, scale_bytes = v_codes[g, c0 - c0 % HALF]
+                nc.tensor.matmul_mx(
+                    out=sums[tile][:, :width],
+                    lhsT=z_tile[:, g, 2 * P * ct : 2 * P * (ct + 1)].bitcast(FP4X4),
+                    lhsT_scale=z_bytes[:, g, P * ct : P * (ct + 1)],
+                    rhs=codes[:, cols].bitcast(FP8X4),
+                    rhs_scale=scale_bytes[:, cols],
+                    start=(g == 0),
+                    stop=(g == GROUPS - 1),
+                )
 
         def subtract_target(tile):
-            c0, width, cts = tile
-            gaps[tile] = work.tile([P, len(cts), width], F32, name="gap", bufs=5)
+            c0, width, ct = tile
+            gaps[tile] = work.tile([P, width], F32, name="gap", bufs=5)
             nc.vector.tensor_tensor(
-                out=gaps[tile][:],
-                in0=sums[tile][:, : width * len(cts)].rearrange("p (i n) -> p i n", i=len(cts)),
-                in1=target_rows[:, cts[0] : cts[-1] + 1, c0 : c0 + width],
-                op=SUBTRACT,
+                out=gaps[tile][:], in0=sums[tile][:, :width], in1=target_rows[:, ct, c0 : c0 + width], op=SUBTRACT
             )
 
         def scale_and_store(tile):
-            c0, width, cts = tile
+            c0, width, ct = tile
             if c0 < HALF:
                 engine, prec_cols = nc.gpsimd, prec_rows[:, c0 : c0 + width]
             else:
                 engine, prec_cols = nc.vector, held[0][:, c0 - HALF : c0 - HALF + width]
-            result = work.tile([P, len(cts), width], F32, name="result", bufs=6)
-            engine.tensor_tensor(
-                out=result[:],
-                in0=gaps[tile][:],
-                in1=prec_cols.unsqueeze(1).to_broadcast([P, len(cts), width]),
-                op=MULT,
-            )
-            rows = out.rearrange("(ct c) n -> c ct n", c=P)
-            nc.sync.dma_start(out=rows[:, cts[0] : cts[-1] + 1, c0 : c0 + width], in_=result[:])
+            result = work.tile([P, width], F32, name="result", bufs=6)
+            engine.tensor_tensor(out=result[:], in0=gaps[tile][:], in1=prec_cols, op=MULT)
+            nc.sync.dma_start(out=out[P * ct : P * (ct + 1), c0 : c0 + width], in_=result[:])
 
         order = [(0, 0), (0, HALF), (1, 0), (1, HALF), (2, 0), (3, 0), (2, HALF), (3, HALF)]
-        pending = [(PACK * g + t, c0, HALF) for g, c0 in order for t in range(PACK)]
+        pending = [(PACK * g + t, c0) for g, c0 in order for t in range(PACK)]
         free = list(PRODUCT_BANKS)
 
         def next_bank():
@@ -367,10 +354,10 @@ def tile_projection_moment_gap_s3_kernel(
         inv_guess16, quotient = per_row("inv_guess16"), per_row("quotient")
         nc.scalar.activation(out=size[:], in_=omega_flat, func=ABS)
         nc.scalar.activation(out=sign[:], in_=omega_flat, func=SIGN)
-        warm_up(2)
+        warm_up(3)
         copy_scale(0, spread_scale(0, PRODUCT_BANKS[0]), nc.scalar.copy)
         second_half = spread_scale(1, PRODUCT_BANKS[1])
-        warm_up(2)
+        warm_up(3)
         nc.vector.tensor_copy(out=ident_bf16[:], in_=ident[:])
         nc.vector.tensor_scalar(out=power[:], in0=size[:], scalar1=2.0**-64, scalar2=2.0**-64, op0=IS_GE, op1=MAX)
         nc.vector.reciprocal(out=inv_power[:], in_=power[:])
@@ -387,6 +374,7 @@ def tile_projection_moment_gap_s3_kernel(
         turn_xb(1)
         turn_xa(2)
         warm_up(1)
+        hold_constants(HELD_BANK)
         nc.vector.tensor_scalar(out=guess16[:], in0=guess[:], scalar1=2.0**-60, scalar2=16.0, op0=MAX, op1=MULT)
         quantize_wa(0, wa_grouped)
         nc.vector.reciprocal(out=inv_guess16[:], in_=guess16[:])
@@ -416,20 +404,20 @@ def tile_projection_moment_gap_s3_kernel(
 
         for g in range(1, GROUPS):
             r = PACK * g
+            last = g + 1 == GROUPS
             scale_xb(r + 2)
             scale_xb(r + 3)
-            sort_xb(r + 2)
-            sort_xb(r + 3)
-            if g + 1 == GROUPS:
-                last_turns = [turn([(row, 1), (row, 2)]) for row in (r + 2, r + 3)]
+            if last:
+                finish_v(0, 0)
             else:
-                turn_xb(r + 2)
-                turn_xb(r + 3)
+                sort_xb(r + 2)
+                sort_xb(r + 3)
+            turn_xb(r + 2)
+            turn_xb(r + 3)
             quantize_x(r)
             quantize_x(r + 1)
             project_next(2)
-            if g + 1 < GROUPS:
-                sort_xa(r + 4)
+            if not last:
                 turn_xa(r + 4)
                 turn_xa(r + 6)
                 project_next(2)
@@ -442,47 +430,40 @@ def tile_projection_moment_gap_s3_kernel(
                 turn_xb(r + 4)
                 turn_xb(r + 5)
                 project_next(2)
-        for sides in last_turns:
-            nc.vector.tensor_copy(**sides)
-        quantize_x(ROWS - 2)
-        quantize_x(ROWS - 1)
 
-        hold_constants(free.pop(0))
         free[1:1] = TURN_BANKS[:1]
         free[3:3] = TURN_BANKS[1:]
+        quantize_v(0, 0)
+        finish_v(1, 0)
+        quantize_x(ROWS - 2)
+        quantize_x(ROWS - 1)
         project_next(len(pending))
-        tiles = [(0, HALF, (ct,)) for ct in range(C_TILES)] + [(HALF, HALF, (ct,)) for ct in range(C_TILES - 1)]
-        tiles += [(HALF, QUARTER, (C_TILES - 1,)), (HALF + QUARTER, QUARTER, (C_TILES - 1,))]
-        finish_v(0, 0, HALF)
-        finish_v(1, 0, HALF)
-        quantize_v(0, 0, HALF)
-        previous = (1, 0)
-        for g, c0 in ((2, 0), (0, HALF), (3, 0), (1, HALF), (2, HALF)):
-            finish_v(g, c0, HALF)
-            quantize_v(*previous, HALF)
-            previous = (g, c0)
-        quantize_v(*previous, HALF)
+        quantize_v(1, 0)
+        finish_v(2, 0)
+        previous = (2, 0)
+        for piece in ((0, HALF), (3, 0), (1, HALF), (2, HALF)):
+            finish_v(*piece)
+            quantize_v(*previous)
+            previous = piece
+        quantize_v(*previous)
+
+        tiles = [(c0, HALF, ct) for c0 in (0, HALF) for ct in range(C_TILES)][:-1]
+        tiles += [(HALF, QUARTER, C_TILES - 1), (HALF + QUARTER, QUARTER, C_TILES - 1)]
         for tile in tiles[:C_TILES]:
             moment(tile, next_bank())
         subtract_target(tiles[0])
         scale_and_store(tiles[0])
-        finish_v(3, HALF, HALF)
+        finish_v(3, HALF)
         subtract_target(tiles[1])
-        quantize_v(3, HALF, HALF)
+        quantize_v(3, HALF)
         scale_and_store(tiles[1])
         subtract_target(tiles[2])
         subtract_target(tiles[3])
-        moment(tiles[4], next_bank())
-        subtract_target(tiles[4])
-        scale_and_store(tiles[2])
-        scale_and_store(tiles[4])
-        moment(tiles[5], next_bank())
-        subtract_target(tiles[5])
-        scale_and_store(tiles[3])
-        scale_and_store(tiles[5])
-        for i in range(6, len(tiles)):
+        for i in range(C_TILES, len(tiles)):
             moment(tiles[i], next_bank())
             subtract_target(tiles[i])
-            if i > 6:
+            if i > C_TILES:
                 scale_and_store(tiles[i - 1])
+            if i < C_TILES + 2:
+                scale_and_store(tiles[i - 2])
         scale_and_store(tiles[-1])

@@ -35,6 +35,8 @@ TURN_BANKS = (0, 1, 2)
 PRODUCT_BANKS = (3, 4, 5, 6)
 HELD_BANK = 7
 
+MOVING, MOVING_SCALE, STATIONARY, STATIONARY_SCALE = 0, 64, 128, 192
+
 FLOPS = 2 * M * N * (KA + KB) + 2 * C * N * M
 
 
@@ -51,18 +53,22 @@ def tile_projection_moment_gap_s3_kernel(
         def bank(i, dtype=F32, width=HALF):
             return psum.tile([P, width], dtype, name="bank%d" % i)
 
+        def mx_tile(name, dtype, item_bytes, width, start):
+            skip = start // item_bytes
+            return keep.tile([P, skip + width], dtype, name=name, align_bytes=256)[:, skip:]
+
         def per_row(name, dtype=F32):
             return keep.tile([P, ROWS], dtype, name=name)
 
         scale_col = keep.tile([P, 2, PACK], F32, name="scale_col")
         scale_rows = keep.tile([P, KB], F32, name="scale_rows")
-        wa_rows = [keep.tile([P, PACK, HALF], BF16, name="wa_rows%d" % i) for i in range(2)]
-        wa_codes = keep.tile([P, N], U32, name="wa_codes", align_bytes=64)
-        wa_bytes = keep.tile([P, N], U8, name="wa_bytes", align_bytes=64)
-        wb_tiles = [keep.tile([P, 2, 2 * HALF], U8, name="wb_tile%d" % i, align_bytes=64) for i in range(2)]
-        wb_bytes = keep.tile([P, 2, N], U8, name="wb_bytes", align_bytes=64)
-        z_tile = keep.tile([P, GROUPS, 2 * C], U8, name="z_tile", align_bytes=64)
-        z_bytes = keep.tile([P, GROUPS, C], U8, name="z_bytes", align_bytes=64)
+        wa_rows = [work.tile([P, PACK, HALF], BF16, name="four_rows", bufs=8) for i in range(2)]
+        wa_codes = mx_tile("wa_codes", U32, 4, N, MOVING)
+        wa_bytes = mx_tile("wa_bytes", U8, 1, N, MOVING_SCALE)
+        wb_tiles = [mx_tile("wb_tile%d" % i, U8, 1, 4 * HALF, MOVING).rearrange("p (g n) -> p g n", g=2) for i in range(2)]
+        wb_bytes = mx_tile("wb_bytes", U8, 1, 2 * N, MOVING_SCALE).rearrange("p (g n) -> p g n", g=2)
+        z_tile = mx_tile("z_tile", U8, 1, GROUPS * 2 * C, STATIONARY).rearrange("p (g n) -> p g n", g=GROUPS)
+        z_bytes = mx_tile("z_bytes", U8, 1, GROUPS * C, STATIONARY_SCALE).rearrange("p (g n) -> p g n", g=GROUPS)
         omega_bf16 = keep.tile([P, GROUPS, PACK], BF16, name="omega_bf16")
         prec_rows = keep.tile([P, HALF], BF16, name="prec_rows")
         prec_line = keep.tile([P, HALF], BF16, name="prec_line")
@@ -235,8 +241,8 @@ def tile_projection_moment_gap_s3_kernel(
         x_codes = {}
 
         def quantize_x(r):
-            codes = keep.tile([P, PASSES * P], U32, name="x_codes%d" % r, align_bytes=64)
-            scale_bytes = keep.tile([P, PASSES * P], U8, name="x_bytes%d" % r, align_bytes=64)
+            both = mx_tile("x_codes%d" % r, U32, 4, PASSES * P + PASSES * P // PACK, STATIONARY)
+            codes, scale_bytes = both[:, : PASSES * P], both[:, PASSES * P :].bitcast(U8)
             first = PASSES * (r % 2)
             nc.vector.quantize_mx(
                 out=codes[:].bitcast(FP8X4),
@@ -269,7 +275,7 @@ def tile_projection_moment_gap_s3_kernel(
                     stop=(s == PASSES - 1),
                 )
             if t == 0:
-                squares[g, c0] = work.tile([P, PACK * HALF], BF16, name="squares", bufs=8)
+                squares[g, c0] = work.tile([P, PACK * HALF], BF16, name="four_rows", bufs=8)
             slots = squares[g, c0][:].rearrange("p (a n e) -> p a n e", a=2, e=2)
             nc.scalar.activation(out=slots[:, t // 2, :, t % 2], in_=tile[:], func=SQUARE, scale=root[:, r : r + 1])
 
@@ -295,8 +301,8 @@ def tile_projection_moment_gap_s3_kernel(
             )
 
         def quantize_v(g, c0):
-            codes = keep.tile([P, HALF], U32, name="v_codes%d_%d" % (g, c0), align_bytes=64)
-            scale_bytes = keep.tile([P, HALF], U8, name="v_bytes%d_%d" % (g, c0), align_bytes=64)
+            codes = mx_tile("v_codes%d_%d" % (g, c0), U32, 4, HALF, MOVING)
+            scale_bytes = mx_tile("v_bytes%d_%d" % (g, c0), U8, 1, HALF, MOVING_SCALE)
             nc.vector.quantize_mx(out=codes[:].bitcast(FP8X4), scales=scale_bytes[:], in_=v_grouped[g, c0][:])
             v_codes[g, c0] = (codes, scale_bytes)
 

@@ -60,12 +60,18 @@ def tile_projection_moment_gap_s3_kernel(
         def per_row(name, dtype=F32):
             return keep.tile([P, ROWS], dtype, name=name)
 
+        def four_rows():
+            return work.tile([P, PACK * HALF], BF16, name="four_rows", bufs=8)[:]
+
         scale_col = keep.tile([P, 2, PACK], F32, name="scale_col")
         scale_rows = keep.tile([P, KB], F32, name="scale_rows")
-        wa_rows = [work.tile([P, PACK, HALF], BF16, name="four_rows", bufs=8) for i in range(2)]
+        wa_rows = [four_rows().rearrange("p (j n) -> p j n", j=PACK) for half in range(2)]
         wa_codes = mx_tile("wa_codes", U32, 4, N, MOVING)
         wa_bytes = mx_tile("wa_bytes", U8, 1, N, MOVING_SCALE)
-        wb_tiles = [mx_tile("wb_tile%d" % i, U8, 1, 4 * HALF, MOVING).rearrange("p (g n) -> p g n", g=2) for i in range(2)]
+        wb_tiles = [
+            mx_tile("wb_tile%d" % half, U8, 1, 2 * 2 * HALF, MOVING).rearrange("p (g n) -> p g n", g=2)
+            for half in range(2)
+        ]
         wb_bytes = mx_tile("wb_bytes", U8, 1, 2 * N, MOVING_SCALE).rearrange("p (g n) -> p g n", g=2)
         z_tile = mx_tile("z_tile", U8, 1, GROUPS * 2 * C, STATIONARY).rearrange("p (g n) -> p g n", g=GROUPS)
         z_bytes = mx_tile("z_bytes", U8, 1, GROUPS * C, STATIONARY_SCALE).rearrange("p (g n) -> p g n", g=GROUPS)
@@ -97,7 +103,7 @@ def tile_projection_moment_gap_s3_kernel(
 
         def load_wa(half):
             rows = wa.rearrange("(p j) n -> p j n", j=PACK)
-            nc.sync.dma_start(out=wa_rows[half][:], in_=rows[:, :, HALF * half : HALF * (half + 1)])
+            nc.sync.dma_start(out=wa_rows[half], in_=rows[:, :, HALF * half : HALF * (half + 1)])
 
         def load_wb(half):
             words = wb_words.rearrange("g p n -> p g n")
@@ -160,27 +166,11 @@ def tile_projection_moment_gap_s3_kernel(
         def grouped_tile():
             return work.tile([P, PACK * HALF], BF16, name="grouped", bufs=3, align_bytes=64)
 
-        def group_wa_on_tensor(half, banks):
+        def group_wa(half, copy):
             grouped = grouped_tile()
-            for i, where in enumerate(banks):
-                tile = bank(where, BF16, 2 * HALF)
-                for j in range(2):
-                    c0 = P * (2 * i + j)
-                    nc.tensor.matmul(
-                        out=tile[:, HALF * j : HALF * (j + 1)],
-                        lhsT=ident_bf16[:],
-                        rhs=wa_rows[half][:, :, c0 : c0 + P].rearrange("p j n -> p n j"),
-                        start=True,
-                        stop=True,
-                    )
-                nc.scalar.copy(out=grouped[:, 2 * HALF * i : 2 * HALF * (i + 1)], in_=tile[:])
-            return grouped
-
-        def group_wa_on_vector(half):
-            grouped = grouped_tile()
-            nc.vector.tensor_copy(
+            copy(
                 out=grouped[:].rearrange("p (c i j) -> p c j i", i=4, j=PACK),
-                in_=wa_rows[half][:].rearrange("p j (c i) -> p c j i", i=4),
+                in_=wa_rows[half].rearrange("p j (c i) -> p c j i", i=4),
             )
             return grouped
 
@@ -275,8 +265,8 @@ def tile_projection_moment_gap_s3_kernel(
                     stop=(s == PASSES - 1),
                 )
             if t == 0:
-                squares[g, c0] = work.tile([P, PACK * HALF], BF16, name="four_rows", bufs=8)
-            slots = squares[g, c0][:].rearrange("p (a n e) -> p a n e", a=2, e=2)
+                squares[g, c0] = four_rows()
+            slots = squares[g, c0].rearrange("p (a n e) -> p a n e", a=2, e=2)
             nc.scalar.activation(out=slots[:, t // 2, :, t % 2], in_=tile[:], func=SQUARE, scale=root[:, r : r + 1])
 
         held = []
@@ -295,7 +285,7 @@ def tile_projection_moment_gap_s3_kernel(
             factors = held[0][:, HALF + PACK * g : HALF + PACK * (g + 1)].rearrange("p (a e) -> p a e", a=2)
             nc.vector.tensor_tensor(
                 out=v_grouped[g, c0][:].rearrange("p (n a e) -> p n a e", a=2, e=2),
-                in0=squares[g, c0][:].rearrange("p (a n e) -> p n a e", a=2, e=2),
+                in0=squares[g, c0].rearrange("p (a n e) -> p n a e", a=2, e=2),
                 in1=factors.unsqueeze(1).to_broadcast([P, HALF, 2, 2]),
                 op=MULT,
             )
@@ -358,6 +348,7 @@ def tile_projection_moment_gap_s3_kernel(
         size, sign, power, inv_power = per_row("size"), per_row("sign"), per_row("power"), per_row("inv_power")
         radicand, guess, guess16 = per_row("radicand"), per_row("guess"), per_row("guess16")
         inv_guess16, quotient = per_row("inv_guess16"), per_row("quotient")
+        nc.scalar.activation(out=guess[:], in_=zeros[:, :ROWS], func=SQRT)
         nc.scalar.activation(out=size[:], in_=omega_flat, func=ABS)
         nc.scalar.activation(out=sign[:], in_=omega_flat, func=SIGN)
         warm_up(3)
@@ -370,21 +361,22 @@ def tile_projection_moment_gap_s3_kernel(
         copy_scale(1, second_half, nc.vector.tensor_copy)
         nc.vector.tensor_tensor(out=radicand[:], in0=size[:], in1=inv_power[:], op=MULT)
         nc.scalar.activation(out=guess[:], in_=radicand[:], func=SQRT, scale=2.0**-10)
-        wa_grouped = group_wa_on_tensor(0, PRODUCT_BANKS[2:4])
+        wa_first = group_wa(0, nc.scalar.copy)
+        warm_up(1)
         turn_xa(0)
+        warm_up(2)
         scale_xb(0)
         turn_xb(0)
-        warm_up(2)
         nc.vector.tensor_tensor(out=factor[:], in0=sign[:], in1=power[:], op=MULT)
         scale_xb(1)
         turn_xb(1)
-        turn_xa(2)
         warm_up(1)
         hold_constants(HELD_BANK)
+        turn_xa(2)
         nc.vector.tensor_scalar(out=guess16[:], in0=guess[:], scalar1=2.0**-60, scalar2=16.0, op0=MAX, op1=MULT)
-        quantize_wa(0, wa_grouped)
-        nc.vector.reciprocal(out=inv_guess16[:], in_=guess16[:])
         scale_xb(2)
+        nc.vector.reciprocal(out=inv_guess16[:], in_=guess16[:])
+        quantize_wa(0, wa_first)
         turn_xb(2)
         nc.vector.tensor_tensor(out=quotient[:], in0=radicand[:], in1=inv_guess16[:], op=MULT)
         quantize_x(0)
@@ -394,16 +386,15 @@ def tile_projection_moment_gap_s3_kernel(
         scale_xb(3)
         turn_xb(3)
         turn_xa(4)
-        wa_grouped = group_wa_on_vector(1)
+        wa_second = group_wa(1, nc.vector.tensor_copy)
         quantize_x(2)
         project_next(1)
         turn_xa(6)
         scale_xb(4)
         quantize_x(3)
         project_next(1)
-        quantize_wa(1, wa_grouped)
+        quantize_wa(1, wa_second)
         scale_xb(5)
-
         turn_xb(4)
         turn_xb(5)
         project_next(2)
@@ -470,6 +461,6 @@ def tile_projection_moment_gap_s3_kernel(
             subtract_target(tiles[i])
             if i > C_TILES:
                 scale_and_store(tiles[i - 1])
-            if i < C_TILES + 2:
+            if i - 2 < C_TILES:
                 scale_and_store(tiles[i - 2])
         scale_and_store(tiles[-1])

@@ -334,6 +334,13 @@ def tile_projection_moment_gap_s3_kernel(
 
         order = [(0, 0), (0, HALF), (1, 0), (1, HALF), (2, 0), (3, 0), (2, HALF), (3, HALF)]
         pending = [(PACK * g + t, c0) for g, c0 in order for t in range(PACK)]
+
+        def move_ahead(product, ahead_of):
+            pending.remove(product)
+            pending.insert(pending.index(ahead_of), product)
+
+        move_ahead((4, 0), (0, HALF))
+        move_ahead((4, HALF), (6, 0))
         free = list(PRODUCT_BANKS)
 
         def next_bank():
@@ -365,9 +372,9 @@ def tile_projection_moment_gap_s3_kernel(
         warm_up(1)
         turn_xa(0)
         warm_up(2)
+        nc.vector.tensor_tensor(out=factor[:], in0=sign[:], in1=power[:], op=MULT)
         scale_xb(0)
         turn_xb(0)
-        nc.vector.tensor_tensor(out=factor[:], in0=sign[:], in1=power[:], op=MULT)
         scale_xb(1)
         turn_xb(1)
         warm_up(1)
@@ -386,17 +393,20 @@ def tile_projection_moment_gap_s3_kernel(
         scale_xb(3)
         turn_xb(3)
         turn_xa(4)
-        wa_second = group_wa(1, nc.vector.tensor_copy)
         quantize_x(2)
         project_next(1)
-        turn_xa(6)
         scale_xb(4)
+        turn_xb(4)
+        turn_xa(6)
+        scale_xb(5)
         quantize_x(3)
         project_next(1)
-        quantize_wa(1, wa_second)
-        scale_xb(5)
-        turn_xb(4)
+        wa_second = group_wa(1, nc.vector.tensor_copy)
         turn_xb(5)
+        turn_xa(8)
+        quantize_x(4)
+        project_next(1)
+        quantize_wa(1, wa_second)
         project_next(2)
 
         for g in range(1, GROUPS):
@@ -411,11 +421,13 @@ def tile_projection_moment_gap_s3_kernel(
                 sort_xb(r + 3)
             turn_xb(r + 2)
             turn_xb(r + 3)
-            quantize_x(r)
+            if g > 1:
+                quantize_x(r)
             quantize_x(r + 1)
             project_next(2)
             if not last:
-                turn_xa(r + 4)
+                if g > 1:
+                    turn_xa(r + 4)
                 turn_xa(r + 6)
                 project_next(2)
                 scale_xb(r + 4)

@@ -37,6 +37,9 @@ HELD_BANK = 7
 
 MOVING, MOVING_SCALE, STATIONARY, STATIONARY_SCALE = 0, 64, 128, 192
 
+BUFS = {"wide": 4, "sorted": 5, "grouped": 3, "four_rows": 8}
+SLOTS = 4
+
 FLOPS = 2 * M * N * (KA + KB) + 2 * C * N * M
 
 
@@ -64,7 +67,7 @@ def tile_projection_moment_gap_s3_kernel(
             return work.tile([P, PACK * HALF], BF16, name="four_rows", bufs=8)[:]
 
         scale_col = keep.tile([P, 2, PACK], F32, name="scale_col")
-        scale_rows = keep.tile([P, KB], F32, name="scale_rows")
+        one = keep.tile([P, 1], F32, name="one")
         wa_rows = [four_rows().rearrange("p (j n) -> p j n", j=PACK) for half in range(2)]
         wa_codes = mx_tile("wa_codes", U32, 4, N, MOVING)
         wa_bytes = mx_tile("wa_bytes", U8, 1, N, MOVING_SCALE)
@@ -76,7 +79,7 @@ def tile_projection_moment_gap_s3_kernel(
         z_tile = mx_tile("z_tile", U8, 1, GROUPS * 2 * C, STATIONARY).rearrange("p (g n) -> p g n", g=GROUPS)
         z_bytes = mx_tile("z_bytes", U8, 1, GROUPS * C, STATIONARY_SCALE).rearrange("p (g n) -> p g n", g=GROUPS)
         omega_bf16 = keep.tile([P, GROUPS, PACK], BF16, name="omega_bf16")
-        prec_rows = keep.tile([P, HALF], BF16, name="prec_rows")
+        prec_rows = keep.tile([P, N], BF16, name="prec_rows")
         prec_line = keep.tile([P, HALF], BF16, name="prec_line")
         ones = keep.tile([P, P], BF16, name="ones")
         target_rows = keep.tile([P, C_TILES, N], BF16, name="target_rows")
@@ -99,7 +102,7 @@ def tile_projection_moment_gap_s3_kernel(
             tile = keep.tile([P, count, KB], U8, name="xb_codes_in%d" % r)
             nc.sync.dma_start(out=tile[:], in_=sample_rows(xb_bytes, r, count))
             for i in range(count):
-                xb_codes_in[r + i] = tile[:, i, :]
+                xb_codes_in[r + i] = tile[:].rearrange("p i k -> p (i k)")[:, KB * i :]
 
         def load_wa(half):
             rows = wa.rearrange("(p j) n -> p j n", j=PACK)
@@ -114,65 +117,58 @@ def tile_projection_moment_gap_s3_kernel(
             for r in range(4):
                 nc.sync.dma_start(out=plane[r:P:32].bitcast(I32), in_=rows[r].bitcast(I32))
 
-        nc.sync.dma_start(out=scale_col[:], in_=xb_scale.rearrange("o (h p j) -> p (o h) j", h=2, j=PACK))
         nc.vector.memset(zeros[:].bitcast(I32), 0)
-        nc.vector.memset(prec_line[:].bitcast(I32), 0)
-        make_identity(nc, ident[:])
-        nc.vector.memset(ones[:], 1.0)
+        nc.vector.memset(ident[:], 0.0)
+        make_identity(nc, ident[:], nomemset=True)
+        nc.vector.memset(one[:], 1.0)
         nc.vector.memset(wb_bytes[:].rearrange("p g n -> p (g n)").bitcast(I32), 0)
+        nc.vector.memset(prec_line[:].bitcast(I32), 0)
+        nc.vector.memset(ones[:], 1.0)
         nc.vector.memset(z_bytes[:].rearrange("p g n -> p (g n)").bitcast(I32), 0)
-        nc.sync.dma_start(out=omega_bf16[:], in_=omega.rearrange("(g p t) -> p g t", p=P, t=PACK))
         load_xb(0, 2)
+        nc.sync.dma_start(out=scale_col[:], in_=xb_scale.rearrange("o (h p j) -> p (o h) j", h=2, j=PACK))
+        nc.sync.dma_start(out=omega_bf16[:], in_=omega.rearrange("(g p t) -> p g t", p=P, t=PACK))
         load_wa(0)
         load_xa(0)
         load_xb(2, 2)
-        load_xa(2)
         load_scale_bytes(wb_bytes, wb_scales)
-        nc.sync.dma_start(out=prec_line[0:1, :], in_=prec[HALF:].unsqueeze(0))
         load_wb(0)
-        load_wa(1)
+        load_xa(2)
         load_xb(4, 2)
+        load_wa(1)
         load_xa(4)
-        load_xa(6)
         load_wb(1)
         load_xb(6, 2)
-        for g in range(2, GROUPS):
-            load_xb(PACK * g, PACK)
-            load_xa(PACK * g)
-            load_xa(PACK * g + 2)
+        nc.sync.dma_start(out=prec_line[0:1, :], in_=prec[HALF:].unsqueeze(0))
+        load_xa(6)
+        load_xb(8, 4)
+        load_xa(8)
+        load_xa(10)
+        load_xb(12, 4)
+        load_xa(12)
+        load_xa(14)
         load_scale_bytes(z_bytes, z_scales)
         nc.sync.dma_start(out=z_tile[:], in_=z_words.rearrange("g p n -> p g n"))
         nc.sync.dma_start(out=target_rows[:], in_=target.rearrange("(ct c) n -> c ct n", c=P))
-        nc.sync.dma_start(out=prec_rows[:], in_=prec[:HALF].partition_broadcast(P))
+        nc.sync.dma_start(out=prec_rows[:], in_=prec.partition_broadcast(P))
 
-        def warm_up(count):
-            tile = bank(HELD_BANK)
+        def warm_up(count, where):
+            tile = bank(where)
             for i in range(count):
                 nc.tensor.matmul(out=tile[:], lhsT=zeros[:, :P], rhs=zeros[:], start=True, stop=True)
 
-        def spread_scale(half, where):
-            tile = bank(where)
-            for j in range(PACK):
-                column = scale_col[:, half, j : j + 1].to_broadcast([P, P])
-                nc.tensor.transpose(tile[:, P * j : P * (j + 1)], column, ident[:])
-            return tile
-
-        def copy_scale(half, tile, copy):
-            copy(
-                out=scale_rows[:, HALF * half : HALF * (half + 1)].rearrange("p (n j) -> p n j", j=PACK),
-                in_=tile[:].rearrange("p (j n) -> p n j", j=PACK),
-            )
-
         def grouped_tile():
-            return work.tile([P, PACK * HALF], BF16, name="grouped", bufs=3, align_bytes=64)
+            return work.tile([P, PACK * HALF], BF16, name="grouped", bufs=BUFS["grouped"], align_bytes=64)
 
-        def group_wa(half, copy):
-            grouped = grouped_tile()
+        wa_grouped = {}
+
+        def group_wa(half, c0, c1, copy):
+            if half not in wa_grouped:
+                wa_grouped[half] = grouped_tile()
             copy(
-                out=grouped[:].rearrange("p (c i j) -> p c j i", i=4, j=PACK),
-                in_=wa_rows[half].rearrange("p j (c i) -> p c j i", i=4),
+                out=wa_grouped[half][:, PACK * c0 : PACK * c1].rearrange("p (c i j) -> p c j i", i=4, j=PACK),
+                in_=wa_rows[half][:, :, c0:c1].rearrange("p j (c i) -> p c j i", i=4),
             )
-            return grouped
 
         def quantize_wa(half, grouped):
             cols = slice(HALF * half, HALF * (half + 1))
@@ -188,45 +184,88 @@ def tile_projection_moment_gap_s3_kernel(
 
         xb_rows = {}
 
-        def scale_xb(r):
-            xb_rows[r] = work.tile([P, KB], BF16, name="xb_scaled", bufs=6)
-            nc.vector.tensor_tensor(out=xb_rows[r][:], in0=xb_codes_in[r].bitcast(FP8), in1=scale_rows[:], op=MULT)
-            for s in range(1, PASSES):
-                every_second_word(r, s, xb_rows[r][:, K_PASS * (s - 1) : K_PASS * s])
+        def slot(i):
+            return work.tile([P, 2 * PASSES * K_PASS], BF16, name="slot%d" % i, bufs=1, align_bytes=64)
 
-        def sort_xb(r):
-            tile = work.tile([P, 2, 2, P], F32, name="sorted", bufs=4)
-            nc.vector.tensor_copy(
-                out=tile[:].rearrange("p s u (c i) -> p s c u i", i=4),
-                in_=xb_rows[r][:].bitcast(F32).rearrange("p (s c i u) -> p s c u i", s=2, i=4, u=2),
-            )
+        def widen(r, count, copy, gate):
+            tile = slot(gate) if gate >= 0 else work.tile([P, count * KB], BF16, name="wide", bufs=BUFS["wide"])
+            copy(out=tile[:, : count * KB], in_=xb_codes_in[r][:, : count * KB].bitcast(FP8))
+            for i in range(count):
+                xb_rows[r + i] = tile[:, KB * i :]
+                for s in range(1, PASSES):
+                    every_second_word(r + i, s, xb_rows[r + i][:, K_PASS * (s - 1) : K_PASS * s])
+
+        def sorted_words(r, count):
+            tile = work.tile([P, 2 * count, 2, P], F32, name="sorted", bufs=BUFS["sorted"])
+            for i in range(count):
+                for s in range(1, PASSES):
+                    words[r + i, s] = [tile[:, 2 * i + s - 1, u, :] for u in range(2)]
+            return tile
+
+        def widen_sorted(r):
+            tile = work.tile([P, 2, 2, P], F32, name="sorted", bufs=BUFS["sorted"])
             for s in range(1, PASSES):
-                words[r, s] = [tile[:, s - 1, u, :] for u in range(2)]
+                words[r, s] = [tile[:, u, s - 1, :] for u in range(2)]
+            nc.vector.tensor_scalar(
+                out=tile[:].rearrange("p u s m -> p (u s m)").bitcast(BF16).rearrange("p (u m e) -> p m u e", u=2, e=2),
+                in0=xb_codes_in[r][:, :KB].bitcast(FP8).rearrange("p (m u e) -> p m u e", u=2, e=2),
+                scalar1=one[:],
+                scalar2=None,
+                op0=MULT,
+            )
+
+        def sort_xb(r, count):
+            tile = sorted_words(r, count)
+            copy_of[engine_of["sort", r, count]](
+                out=tile[:].rearrange("p s u (c i) -> p s c u i", i=4),
+                in_=xb_rows[r][:, : count * KB].bitcast(F32).rearrange("p (s c i u) -> p s c u i", s=2 * count, i=4, u=2),
+            )
+
+        def sort_xa(r):
+            tile = work.tile([P, 2, 2, P], F32, name="sorted", bufs=BUFS["sorted"])
+            copy_of[engine_of["sort_xa", r]](
+                out=tile[:].rearrange("p s u (c i) -> p s c u i", i=4),
+                in_=xa_pairs[r][:].rearrange("p s k -> p (s k)").bitcast(F32).rearrange("p (s c i u) -> p s c u i", s=2, i=4, u=2),
+            )
+            for i in range(2):
+                words[r + i, 0] = [tile[:, i, u, :] for u in range(2)]
 
         x_grouped = {}
-        turns = []
+        turned = {}
 
-        def turn(pieces):
-            tile = bank(TURN_BANKS[len(turns) % len(TURN_BANKS)])
-            turns.append(pieces)
-            for i, piece in enumerate(pieces):
+        def pieces_of(step):
+            kind, r = step
+            return [(r, 0), (r + 1, 0)] if kind == "a" else [(r, 1), (r, 2)]
+
+        def turn(step, where):
+            turned[step] = bank(where)
+            for i, piece in enumerate(pieces_of(step)):
                 for u in range(2):
-                    nc.tensor.transpose(tile[:, P * (2 * i + u) : P * (2 * i + u + 1)], words[piece][u], ident[:])
-            pair = pieces[0][0] // 2
+                    nc.tensor.transpose(turned[step][:, P * (2 * u + i) : P * (2 * u + i + 1)], words[piece][u], ident[:])
+
+        def open_pair(pair):
             if pair not in x_grouped:
-                x_grouped[pair] = work.tile([P, 2 * PASSES, K_PASS], BF16, name="x_grouped", bufs=4, align_bytes=64)
-            first, second = [PASSES * (r % 2) + s for r, s in pieces]
-            grouped = x_grouped[pair][:, first : second + 1 : second - first, :]
-            nc.scalar.copy(
-                out=grouped.bitcast(F32).rearrange("p i (m u) -> p i m u", u=2),
-                in_=tile[:].rearrange("p (i u m) -> p i m u", i=2, u=2),
+                x_grouped[pair] = slot(pair % SLOTS)[:].rearrange("p (s k) -> p s k", k=K_PASS)
+
+        def scale_xb(r):
+            open_pair(r // 2)
+            first = PASSES * (r % 2) + 1
+            nc.vector.tensor_tensor(
+                out=x_grouped[r // 2][:, first : first + 2, :].rearrange("p i (m u e) -> p i m u e", u=2, e=2),
+                in0=turned["b", r][:].bitcast(BF16).rearrange("p (u i m e) -> p i m u e", u=2, i=2, e=2),
+                in1=scale_col[:].rearrange("p i (u e) -> p i u e", u=2).unsqueeze(2).to_broadcast([P, 2, P, 2, 2]),
+                op=MULT,
             )
 
-        def turn_xa(r):
-            turn([(r, 0), (r + 1, 0)])
-
-        def turn_xb(r):
-            turn([(r, 1), (r, 2)])
+        def empty(step, copy):
+            pair = step[1] // 2
+            open_pair(pair)
+            first, second = [PASSES * (r % 2) + s for r, s in pieces_of(step)]
+            grouped = x_grouped[pair][:, first : second + 1 : second - first, :]
+            copy(
+                out=grouped.bitcast(F32).rearrange("p i (m u) -> p i m u", u=2),
+                in_=turned[step][:].rearrange("p (u i m) -> p i m u", i=2, u=2),
+            )
 
         x_codes = {}
 
@@ -244,9 +283,11 @@ def tile_projection_moment_gap_s3_kernel(
         root, factor = per_row("root"), per_row("factor", BF16)
         squares = {}
 
+        products = {}
+
         def project(r, c0, where):
-            g, t = divmod(r, PACK)
             tile = bank(where)
+            products[r, c0] = tile
             cols = slice(c0, c0 + HALF)
             codes, scale_bytes = x_codes[r]
             for s in range(PASSES):
@@ -264,7 +305,11 @@ def tile_projection_moment_gap_s3_kernel(
                     start=(s == 0),
                     stop=(s == PASSES - 1),
                 )
-            if t == 0:
+
+        def square(r, c0):
+            g, t = divmod(r, PACK)
+            tile = products[r, c0]
+            if (g, c0) not in squares:
                 squares[g, c0] = four_rows()
             slots = squares[g, c0].rearrange("p (a n e) -> p a n e", a=2, e=2)
             nc.scalar.activation(out=slots[:, t // 2, :, t % 2], in_=tile[:], func=SQUARE, scale=root[:, r : r + 1])
@@ -299,11 +344,12 @@ def tile_projection_moment_gap_s3_kernel(
         sums = {}
         gaps = {}
 
-        def moment(tile, where):
+        def moment(tile, where, groups=range(GROUPS)):
             c0, width, ct = tile
-            sums[tile] = bank(where)
+            if tile not in sums:
+                sums[tile] = bank(where)
             cols = slice(c0 % HALF, c0 % HALF + width)
-            for g in range(GROUPS):
+            for g in groups:
                 codes, scale_bytes = v_codes[g, c0 - c0 % HALF]
                 nc.tensor.matmul_mx(
                     out=sums[tile][:, :width],
@@ -317,162 +363,267 @@ def tile_projection_moment_gap_s3_kernel(
 
         def subtract_target(tile):
             c0, width, ct = tile
-            gaps[tile] = work.tile([P, width], F32, name="gap", bufs=5)
+            gaps[tile] = work.tile([P, width], F32, name="wide", bufs=BUFS["wide"])
             nc.vector.tensor_tensor(
                 out=gaps[tile][:], in0=sums[tile][:, :width], in1=target_rows[:, ct, c0 : c0 + width], op=SUBTRACT
             )
 
-        def scale_and_store(tile):
+        results = {}
+
+        def scale_gap(tile, on_gpsimd):
             c0, width, ct = tile
-            if c0 < HALF:
+            if on_gpsimd:
                 engine, prec_cols = nc.gpsimd, prec_rows[:, c0 : c0 + width]
             else:
                 engine, prec_cols = nc.vector, held[0][:, c0 - HALF : c0 - HALF + width]
-            result = work.tile([P, width], F32, name="result", bufs=6)
-            engine.tensor_tensor(out=result[:], in0=gaps[tile][:], in1=prec_cols, op=MULT)
-            nc.sync.dma_start(out=out[P * ct : P * (ct + 1), c0 : c0 + width], in_=result[:])
+            name = "four_rows" if on_gpsimd else "sorted"
+            results[tile] = work.tile([P, width], F32, name=name, bufs=BUFS[name])
+            engine.tensor_tensor(out=results[tile][:], in0=gaps[tile][:], in1=prec_cols, op=MULT)
 
-        order = [(0, 0), (0, HALF), (1, 0), (1, HALF), (2, 0), (3, 0), (2, HALF), (3, HALF)]
-        pending = [(PACK * g + t, c0) for g, c0 in order for t in range(PACK)]
+        def store(tile):
+            c0, width, ct = tile
+            nc.sync.dma_start(out=out[P * ct : P * (ct + 1), c0 : c0 + width], in_=results[tile][:])
 
-        def move_ahead(product, ahead_of):
-            pending.remove(product)
-            pending.insert(pending.index(ahead_of), product)
-
-        move_ahead((4, 0), (0, HALF))
-        move_ahead((4, HALF), (6, 0))
-        free = list(PRODUCT_BANKS)
-
-        def next_bank():
-            free.append(free.pop(0))
-            return free[-1]
-
-        def project_next(count):
-            for i in range(count):
-                project(*pending.pop(0), next_bank())
 
         omega_flat = omega_bf16[:].rearrange("p g t -> p (g t)")
         size, sign, power, inv_power = per_row("size"), per_row("sign"), per_row("power"), per_row("inv_power")
         radicand, guess, guess16 = per_row("radicand"), per_row("guess"), per_row("guess16")
         inv_guess16, quotient = per_row("inv_guess16"), per_row("quotient")
-        nc.scalar.activation(out=guess[:], in_=zeros[:, :ROWS], func=SQRT)
-        nc.scalar.activation(out=size[:], in_=omega_flat, func=ABS)
-        nc.scalar.activation(out=sign[:], in_=omega_flat, func=SIGN)
-        warm_up(3)
-        copy_scale(0, spread_scale(0, PRODUCT_BANKS[0]), nc.scalar.copy)
-        second_half = spread_scale(1, PRODUCT_BANKS[1])
-        warm_up(3)
-        nc.vector.tensor_copy(out=ident_bf16[:], in_=ident[:])
-        nc.vector.tensor_scalar(out=power[:], in0=size[:], scalar1=2.0**-64, scalar2=2.0**-64, op0=IS_GE, op1=MAX)
-        nc.vector.reciprocal(out=inv_power[:], in_=power[:])
-        copy_scale(1, second_half, nc.vector.tensor_copy)
-        nc.vector.tensor_tensor(out=radicand[:], in0=size[:], in1=inv_power[:], op=MULT)
-        nc.scalar.activation(out=guess[:], in_=radicand[:], func=SQRT, scale=2.0**-10)
-        wa_first = group_wa(0, nc.scalar.copy)
-        warm_up(1)
-        turn_xa(0)
-        warm_up(2)
-        nc.vector.tensor_tensor(out=factor[:], in0=sign[:], in1=power[:], op=MULT)
-        scale_xb(0)
-        turn_xb(0)
-        scale_xb(1)
-        turn_xb(1)
-        warm_up(1)
-        hold_constants(HELD_BANK)
-        turn_xa(2)
-        nc.vector.tensor_scalar(out=guess16[:], in0=guess[:], scalar1=2.0**-60, scalar2=16.0, op0=MAX, op1=MULT)
-        scale_xb(2)
-        nc.vector.reciprocal(out=inv_guess16[:], in_=guess16[:])
-        quantize_wa(0, wa_first)
-        turn_xb(2)
-        nc.vector.tensor_tensor(out=quotient[:], in0=radicand[:], in1=inv_guess16[:], op=MULT)
-        quantize_x(0)
-        nc.vector.scalar_tensor_tensor(out=root[:], in0=quotient[:], scalar=0.25, in1=guess16[:], op0=MULT, op1=ADD)
-        quantize_x(1)
-        project_next(2)
-        scale_xb(3)
-        turn_xb(3)
-        turn_xa(4)
-        quantize_x(2)
-        project_next(1)
-        scale_xb(4)
-        turn_xb(4)
-        turn_xa(6)
-        scale_xb(5)
-        quantize_x(3)
-        project_next(1)
-        wa_second = group_wa(1, nc.vector.tensor_copy)
-        turn_xb(5)
-        turn_xa(8)
-        quantize_x(4)
-        project_next(1)
-        quantize_wa(1, wa_second)
-        project_next(2)
-
-        for g in range(1, GROUPS):
-            r = PACK * g
-            last = g + 1 == GROUPS
-            scale_xb(r + 2)
-            scale_xb(r + 3)
-            if last:
-                finish_v(0, 0)
-            else:
-                sort_xb(r + 2)
-                sort_xb(r + 3)
-            turn_xb(r + 2)
-            turn_xb(r + 3)
-            if g > 1:
-                quantize_x(r)
-            quantize_x(r + 1)
-            project_next(2)
-            if not last:
-                if g > 1:
-                    turn_xa(r + 4)
-                turn_xa(r + 6)
-                project_next(2)
-                scale_xb(r + 4)
-                quantize_x(r + 2)
-                scale_xb(r + 5)
-                quantize_x(r + 3)
-                sort_xb(r + 4)
-                sort_xb(r + 5)
-                turn_xb(r + 4)
-                turn_xb(r + 5)
-                project_next(2)
-
-        free[1:1] = TURN_BANKS[:1]
-        free[3:3] = TURN_BANKS[1:]
-        quantize_v(0, 0)
-        finish_v(1, 0)
-        quantize_x(ROWS - 2)
-        quantize_x(ROWS - 1)
-        project_next(len(pending))
-        quantize_v(1, 0)
-        finish_v(2, 0)
-        previous = (2, 0)
-        for piece in ((0, HALF), (3, 0), (1, HALF), (2, HALF)):
-            finish_v(*piece)
-            quantize_v(*previous)
-            previous = piece
-        quantize_v(*previous)
-
+        spread = {}
+        small = {
+            "table": ([], lambda: nc.scalar.activation(out=guess[:], in_=zeros[:, :ROWS], func=SQRT)),
+            "size": ([], lambda: nc.scalar.activation(out=size[:], in_=omega_flat, func=ABS)),
+            "sign": ([], lambda: nc.scalar.activation(out=sign[:], in_=omega_flat, func=SIGN)),
+            "ident16": ([], lambda: nc.vector.tensor_copy(out=ident_bf16[:], in_=ident[:])),
+            "power": (["size"], lambda: nc.vector.tensor_scalar(out=power[:], in0=size[:], scalar1=2.0**-64, scalar2=2.0**-64, op0=IS_GE, op1=MAX)),
+            "inv_power": (["power"], lambda: nc.vector.reciprocal(out=inv_power[:], in_=power[:])),
+            "radicand": (["inv_power"], lambda: nc.vector.tensor_tensor(out=radicand[:], in0=size[:], in1=inv_power[:], op=MULT)),
+            "factor": (["power", "sign"], lambda: nc.vector.tensor_tensor(out=factor[:], in0=sign[:], in1=power[:], op=MULT)),
+            "guess": (["radicand", "table"], lambda: nc.scalar.activation(out=guess[:], in_=radicand[:], func=SQRT, scale=2.0**-10)),
+            "guess16": (["guess"], lambda: nc.vector.tensor_scalar(out=guess16[:], in0=guess[:], scalar1=2.0**-60, scalar2=16.0, op0=MAX, op1=MULT)),
+            "inv_guess16": (["guess16"], lambda: nc.vector.reciprocal(out=inv_guess16[:], in_=guess16[:])),
+            "quotient": (["inv_guess16"], lambda: nc.vector.tensor_tensor(out=quotient[:], in0=radicand[:], in1=inv_guess16[:], op=MULT)),
+            "root": (["quotient"], lambda: nc.vector.scalar_tensor_tensor(out=root[:], in0=quotient[:], scalar=0.25, in1=guess16[:], op0=MULT, op1=ADD)),
+        }
+        H = HALF
         tiles = [(c0, HALF, ct) for c0 in (0, HALF) for ct in range(C_TILES)][:-1]
         tiles += [(HALF, QUARTER, C_TILES - 1), (HALF + QUARTER, QUARTER, C_TILES - 1)]
-        for tile in tiles[:C_TILES]:
-            moment(tile, next_bank())
-        subtract_target(tiles[0])
-        scale_and_store(tiles[0])
-        finish_v(3, HALF)
-        subtract_target(tiles[1])
-        quantize_v(3, HALF)
-        scale_and_store(tiles[1])
-        subtract_target(tiles[2])
-        subtract_target(tiles[3])
-        for i in range(C_TILES, len(tiles)):
-            moment(tiles[i], next_bank())
-            subtract_target(tiles[i])
-            if i > C_TILES:
-                scale_and_store(tiles[i - 1])
-            if i - 2 < C_TILES:
-                scale_and_store(tiles[i - 2])
-        scale_and_store(tiles[-1])
+        ALL = (0, 1, 2, 3)
+
+        def parse(text):
+            steps = []
+            for word in text.split():
+                letters = "".join(ch for ch in word if ch not in "0123456789")
+                digits = [int(x) for x in "".join(ch if ch in "0123456789" else " " for ch in word).split()]
+                if word in small:
+                    steps.append(word)
+                elif letters in ("a", "b"):
+                    steps.append((letters, digits[0]))
+                elif letters == "w":
+                    steps.append(("warm", len(steps), digits[0]))
+                elif letters in ("p", "P"):
+                    steps.append(("project", digits[0], 0 if letters == "p" else H))
+                elif letters in ("s", "S"):
+                    steps.append(("square", digits[0], 0 if letters == "s" else H))
+                elif letters in ("ea", "eb"):
+                    steps.append(("empty", (letters[1], digits[0])))
+                elif letters == "m":
+                    steps.append(("moment", tiles[digits[0]], ALL))
+                elif letters == "m:":
+                    steps.append(("moment", tiles[digits[0]], tuple(int(ch) for ch in word.split(":")[1])))
+                elif letters in ("f", "F", "v", "V"):
+                    steps.append(("finish_v" if letters in "fF" else "quantize_v", digits[0], 0 if letters in "fv" else H))
+                elif letters == "wd:":
+                    steps.append(("widen", digits[0], digits[1], -1, -1))
+                elif letters == "wd::":
+                    steps.append(("widen", digits[0], digits[1], digits[2] % SLOTS, digits[2]))
+                elif letters == "so:":
+                    steps.append(("sort", digits[0], digits[1]))
+                elif letters == "ws":
+                    steps.append(("widen_sorted", digits[0]))
+                elif letters == "il::":
+                    steps.append(("group_wa", digits[0], digits[1], digits[2]))
+                elif letters in ("sub", "mul", "st"):
+                    steps.append(({"sub": "subtract", "mul": "scale_gap", "st": "store"}[letters], tiles[digits[0]]))
+                else:
+                    steps.append(({"sp": "spread", "cs": "copy_scale", "sc": "scale", "so": "sort", "sa": "sort_xa", "q": "quantize_x", "qw": "quantize_wa", "hold": "hold"}[letters], digits[0]))
+            return steps
+
+        tensor = parse("""w5 b0 b1 w2 a0 w2 a2 p0 b2 b3 p1 a4 b4 b5 p2 a6 P0 p3 hold0 P1 P2 a8 b6 b7 p4 p5 P3 P4 b8 b9 a10 P5 p6 p7 P6 b10 b11 a12 P7 p8 p9 b12 b13 a14 P8 p10 p11 b14 b15 P9 p12 p13 P10 P11 p14 p15 P12 P13 P14 P15 m0 m1 m2 m3 m4 m5 m6 m7 m8""")
+        vector = parse("""ident16 ws0 ws1 power inv_power sc0 radicand il0:256:512 factor sc1 guess16 qw0 inv_guess16 q0 quotient q1 root ws4 sc2 ws5 il1:256:512 q2 sc3 qw1 q3 ws6 ws7 sc4 sc5 q4 q5 sc6 sc7 f0 q6 v0 q7 sc8 sc9 F0 q8 V0 q9 sc10 sc11 f1 q10 v1 q11 sc12 sc13 q12 q13 sc14 F1 sc15 q14 V1 q15 f2 F2 v2 f3 V2 v3 sub0 F3 sub1 V3 sub2 sub3 sub4 mul4 sub5 mul5 sub6 sub7 mul6 sub8 mul7 mul8""")
+        scalar = parse("""table size sign il0:0:256 guess ea0 wd2:1 wd3:1 ea2 s0 il1:0:256 s1 ea4 s2 ea6 S0 s3 S1 S2 ea8 so8:2 s4 s5 S3 S4 so10:2 ea10 S5 s6 s7 S6 so12:2 ea12 S7 s8 s9 so14:2 ea14 S8 s10 s11 S9 s12 s13 S10 S11 s14 s15 S12 S13 S14 S15""")
+        gpsimd = parse("""wd8:2:1 wd10:2:2 wd12:2:3 wd14:2:4 mul0 mul1 mul2 mul3""")
+        sync = parse("""st0 st1 st2 st4 st3 st5 st6 st7 st8""")
+        free = [0, 1, 2, 3, 4, 5, 6]
+        banks = []
+        first_bank = {}
+        for step in tensor:
+            if step[0] in ("warm", "hold"):
+                banks.append(HELD_BANK)
+            elif step[0] == "moment" and step[1] in first_bank:
+                banks.append(first_bank[step[1]])
+            else:
+                free.append(free.pop(0))
+                banks.append(free[-1])
+                first_bank[step[1]] = free[-1]
+        queues = {"tensor": tensor, "vector": vector, "scalar": scalar, "gpsimd": gpsimd, "sync": sync}
+        prepared = {}
+        widened = {}
+        for steps in queues.values():
+            for step in steps:
+                if step[0] == "widen":
+                    for r in range(step[1], step[1] + step[2]):
+                        widened[r] = step
+                        prepared.setdefault(r, step)
+                if step[0] == "widen_sorted":
+                    prepared[step[1]] = step
+        for steps in queues.values():
+            for step in steps:
+                if step[0] == "sort":
+                    for r in range(step[1], step[1] + step[2]):
+                        prepared[r] = step
+        copy_of = {"vector": nc.vector.tensor_copy, "scalar": nc.scalar.copy, "gpsimd": nc.gpsimd.tensor_copy}
+        engine_of = {step: name for name, steps in queues.items() for step in steps}
+        where = {}
+        bank_reader = {}
+        after = {}
+        for step, at in zip(tensor, banks):
+            where[step] = at
+            kind = step[0]
+            reader = {"a": ("empty", step), "b": ("scale", step[1]), "project": ("square",) + step[1:], "moment": ("subtract", step[1]), "warm": step, "hold": step}[kind]
+            if at in bank_reader and bank_reader[at] != reader:
+                after[step] = [bank_reader[at]]
+            bank_reader[at] = reader
+
+        def group_rows(g):
+            return range(PACK * g, PACK * (g + 1))
+
+        def gated(pair):
+            return [s for s in engine_of if s[0] == "widen" and s[3] >= 0 and s[4] + SLOTS == pair]
+
+        def needs(step):
+            kind = step[0]
+            if step in small:
+                return small[step][0]
+            first = after.get(step, [])
+            if kind == "b":
+                return first + [prepared[step[1]]]
+            if kind == "project":
+                return first + [("quantize_x", step[1]), ("quantize_wa", step[2] // HALF)]
+            if kind == "moment":
+                return first + [("quantize_v", g, step[1][0] - step[1][0] % HALF) for g in step[2]]
+            if kind == "hold":
+                return first + ["ident16", "factor"]
+            if kind == "a" and ("sort_xa", step[1]) in engine_of:
+                return first + [("sort_xa", step[1])]
+            if kind == "sort_xa":
+                return []
+            if kind in ("a", "spread", "warm"):
+                return first
+            if kind == "widen" and step[3] >= 0:
+                return [("quantize_x", 2 * step[4] + 1)]
+            if kind in ("widen", "widen_sorted"):
+                return []
+            if kind == "scale":
+                return [("b", step[1])] + gated(step[1] // 2)
+            if kind == "sort":
+                return [widened[r] for r in range(step[1], step[1] + step[2])]
+            if kind == "empty":
+                return [step[1]] + gated(step[1][1] // 2)
+            if kind == "quantize_x":
+                return [("empty", ("a", step[1] - step[1] % 2)), ("scale", step[1])]
+            if kind == "group_wa":
+                return []
+            if kind == "quantize_wa":
+                return [s for s in engine_of if s[0] == "group_wa" and s[1] == step[1]]
+            if kind == "square":
+                return [("project",) + step[1:], "root"]
+            if kind == "finish_v":
+                return [("hold", 0)] + [("square", r, step[2]) for r in group_rows(step[1])]
+            if kind == "quantize_v":
+                return [("finish_v",) + step[1:]]
+            if kind == "subtract":
+                return [s for s in tensor if s[0] == "moment" and s[1] == step[1]]
+            if kind == "scale_gap":
+                return [("subtract", step[1])]
+            return [("scale_gap", step[1])]
+
+        def takes(step):
+            kind = step[0]
+            if kind == "widen":
+                users = [prepared[r] if prepared[r] != step else ("b", r) for r in range(step[1], step[1] + step[2])]
+                return ("wide" if step[3] < 0 else "slot%d" % step[3], step, users)
+            if kind == "widen_sorted":
+                return ("sorted", step, [("b", step[1])])
+            if kind == "subtract":
+                return ("wide", step, [("scale_gap", step[1])])
+            if kind == "sort":
+                return ("sorted", step, [("b", r) for r in range(step[1], step[1] + step[2])])
+            if kind == "sort_xa":
+                return ("sorted", step, [("a", step[1])])
+            if kind == "scale_gap":
+                return ("four_rows" if engine_of[step] == "gpsimd" else "sorted", step, [("store", step[1])])
+            if kind in ("empty", "scale"):
+                r = step[1][1] if kind == "empty" else step[1] - step[1] % 2
+                return ("slot%d" % (r // 2 % SLOTS), r, [("quantize_x", r), ("quantize_x", r + 1)])
+            if kind == "group_wa":
+                return ("grouped", step[1], [("quantize_wa", step[1])])
+            if kind == "finish_v":
+                return ("grouped", step, [("quantize_v",) + step[1:]])
+            if kind == "square":
+                return ("four_rows", (step[1] // PACK, step[2]), [("finish_v", step[1] // PACK, step[2])])
+            return None
+
+        def issue(step):
+            kind = step[0]
+            if step in small:
+                small[step][1]()
+            elif kind in ("a", "b"):
+                turn(step, where[step])
+            elif kind == "empty":
+                empty(step[1], copy_of[engine_of[step]])
+            elif kind == "project":
+                project(step[1], step[2], where[step])
+            elif kind == "moment":
+                moment(step[1], where[step], step[2])
+            elif kind == "hold":
+                hold_constants(where[step])
+            elif kind == "warm":
+                warm_up(step[2], where[step])
+            elif kind == "widen":
+                widen(step[1], step[2], copy_of[engine_of[step]], step[3])
+            elif kind == "group_wa":
+                group_wa(*step[1:], copy_of[engine_of[step]])
+            elif kind == "quantize_wa":
+                quantize_wa(step[1], wa_grouped[step[1]])
+            elif kind == "scale_gap":
+                scale_gap(step[1], engine_of[step] == "gpsimd")
+            else:
+                plain = {"scale": scale_xb, "sort": sort_xb, "widen_sorted": widen_sorted, "sort_xa": sort_xa, "quantize_x": quantize_x, "square": square, "finish_v": finish_v,
+                         "quantize_v": quantize_v, "subtract": subtract_target, "store": store}
+                plain[kind](*step[1:])
+
+        done = set()
+        bufs = dict(BUFS)
+        for i in range(SLOTS):
+            bufs["slot%d" % i] = 1
+        taken = {name: [] for name in bufs}
+        taken["four_rows"] = [(half, [s for s in engine_of if s[0] == "group_wa" and s[1] == half]) for half in range(2)]
+        left = {name: list(steps) for name, steps in queues.items()}
+        for turn_number in range(sum(len(steps) for steps in queues.values())):
+            ready = []
+            for name, steps in left.items():
+                if steps and all(need in done for need in needs(steps[0])):
+                    wanted = takes(steps[0])
+                    if wanted and wanted[1] not in [key for key, users in taken[wanted[0]]]:
+                        earlier = taken[wanted[0]]
+                        if len(earlier) >= bufs[wanted[0]] and not all(user in done for user in earlier[-bufs[wanted[0]]][1]):
+                            continue
+                    ready.append(name)
+            assert ready, [steps[:1] for steps in left.values()]
+            step = left[ready[0]].pop(0)
+            wanted = takes(step)
+            if wanted and wanted[1] not in [key for key, users in taken[wanted[0]]]:
+                taken[wanted[0]].append(wanted[1:])
+            issue(step)
+            done.add(step)

@@ -15,6 +15,7 @@ MULT = mybir.AluOpType.mult
 ADD = mybir.AluOpType.add
 MAX = mybir.AluOpType.max
 IS_GE = mybir.AluOpType.is_ge
+POW = mybir.AluOpType.pow
 SUBTRACT = mybir.AluOpType.subtract
 SQUARE = mybir.ActivationFunctionType.Square
 SQRT = mybir.ActivationFunctionType.Sqrt
@@ -37,7 +38,7 @@ HELD_BANK = 7
 
 MOVING, MOVING_SCALE, STATIONARY, STATIONARY_SCALE = 0, 64, 128, 192
 
-BUFS = {"wide": 4, "sorted": 5, "grouped": 3, "four_rows": 8}
+BUFS = {"wide": 6, "sorted": 5, "grouped": 3, "four_rows": 8}
 SLOTS = 4
 
 FLOPS = 2 * M * N * (KA + KB) + 2 * C * N * M
@@ -68,6 +69,7 @@ def tile_projection_moment_gap_s3_kernel(
 
         scale_col = keep.tile([P, 2, PACK], F32, name="scale_col")
         one = keep.tile([P, 1], F32, name="one")
+        half_exponent = keep.tile([P, ROWS], F32, name="half_exponent")
         wa_rows = [four_rows().rearrange("p (j n) -> p j n", j=PACK) for half in range(2)]
         wa_codes = mx_tile("wa_codes", U32, 4, N, MOVING)
         wa_bytes = mx_tile("wa_bytes", U8, 1, N, MOVING_SCALE)
@@ -98,11 +100,13 @@ def tile_projection_moment_gap_s3_kernel(
             xa_pairs[r] = keep.tile([P, 2, KA], BF16, name="xa_pair%d" % r)
             nc.sync.dma_start(out=xa_pairs[r][:], in_=sample_rows(xa, r, 2))
 
+        xb_codes = keep.tile([P, ROWS * KB], U8, name="xb_codes")
+
         def load_xb(r, count):
-            tile = keep.tile([P, count, KB], U8, name="xb_codes_in%d" % r)
-            nc.sync.dma_start(out=tile[:], in_=sample_rows(xb_bytes, r, count))
+            rows = xb_codes[:, KB * r : KB * (r + count)].rearrange("p (t k) -> p t k", t=count)
+            nc.sync.dma_start(out=rows, in_=sample_rows(xb_bytes, r, count))
             for i in range(count):
-                xb_codes_in[r + i] = tile[:].rearrange("p i k -> p (i k)")[:, KB * i :]
+                xb_codes_in[r + i] = xb_codes[:, KB * (r + i) :]
 
         def load_wa(half):
             rows = wa.rearrange("(p j) n -> p j n", j=PACK)
@@ -121,30 +125,31 @@ def tile_projection_moment_gap_s3_kernel(
         nc.vector.memset(ident[:], 0.0)
         make_identity(nc, ident[:], nomemset=True)
         nc.vector.memset(one[:], 1.0)
+        nc.vector.memset(half_exponent[:], 0.5)
         nc.vector.memset(wb_bytes[:].rearrange("p g n -> p (g n)").bitcast(I32), 0)
         nc.vector.memset(prec_line[:].bitcast(I32), 0)
         nc.vector.memset(ones[:], 1.0)
         nc.vector.memset(z_bytes[:].rearrange("p g n -> p (g n)").bitcast(I32), 0)
         load_xb(0, 2)
-        nc.sync.dma_start(out=scale_col[:], in_=xb_scale.rearrange("o (h p j) -> p (o h) j", h=2, j=PACK))
         nc.sync.dma_start(out=omega_bf16[:], in_=omega.rearrange("(g p t) -> p g t", p=P, t=PACK))
+        load_xb(2, 2)
+        nc.sync.dma_start(out=scale_col[:], in_=xb_scale.rearrange("o (h p j) -> p (o h) j", h=2, j=PACK))
         load_wa(0)
         load_xa(0)
-        load_xb(2, 2)
+        nc.sync.dma_start(out=prec_line[0:1, :], in_=prec[HALF:].unsqueeze(0))
         load_scale_bytes(wb_bytes, wb_scales)
         load_wb(0)
-        load_xa(2)
         load_xb(4, 2)
+        load_xa(2)
         load_wa(1)
         load_xa(4)
-        load_wb(1)
         load_xb(6, 2)
-        nc.sync.dma_start(out=prec_line[0:1, :], in_=prec[HALF:].unsqueeze(0))
-        load_xa(6)
+        load_wb(1)
         load_xb(8, 4)
+        load_xa(6)
         load_xa(8)
-        load_xa(10)
         load_xb(12, 4)
+        load_xa(10)
         load_xa(12)
         load_xa(14)
         load_scale_bytes(z_bytes, z_scales)
@@ -387,8 +392,7 @@ def tile_projection_moment_gap_s3_kernel(
 
         omega_flat = omega_bf16[:].rearrange("p g t -> p (g t)")
         size, sign, power, inv_power = per_row("size"), per_row("sign"), per_row("power"), per_row("inv_power")
-        radicand, guess, guess16 = per_row("radicand"), per_row("guess"), per_row("guess16")
-        inv_guess16, quotient = per_row("inv_guess16"), per_row("quotient")
+        radicand, guess = per_row("radicand"), per_row("guess")
         spread = {}
         small = {
             "table": ([], lambda: nc.scalar.activation(out=guess[:], in_=zeros[:, :ROWS], func=SQRT)),
@@ -397,13 +401,9 @@ def tile_projection_moment_gap_s3_kernel(
             "ident16": ([], lambda: nc.vector.tensor_copy(out=ident_bf16[:], in_=ident[:])),
             "power": (["size"], lambda: nc.vector.tensor_scalar(out=power[:], in0=size[:], scalar1=2.0**-64, scalar2=2.0**-64, op0=IS_GE, op1=MAX)),
             "inv_power": (["power"], lambda: nc.vector.reciprocal(out=inv_power[:], in_=power[:])),
-            "radicand": (["inv_power"], lambda: nc.vector.tensor_tensor(out=radicand[:], in0=size[:], in1=inv_power[:], op=MULT)),
-            "factor": (["power", "sign"], lambda: nc.vector.tensor_tensor(out=factor[:], in0=sign[:], in1=power[:], op=MULT)),
-            "guess": (["radicand", "table"], lambda: nc.scalar.activation(out=guess[:], in_=radicand[:], func=SQRT, scale=2.0**-10)),
-            "guess16": (["guess"], lambda: nc.vector.tensor_scalar(out=guess16[:], in0=guess[:], scalar1=2.0**-60, scalar2=16.0, op0=MAX, op1=MULT)),
-            "inv_guess16": (["guess16"], lambda: nc.vector.reciprocal(out=inv_guess16[:], in_=guess16[:])),
-            "quotient": (["inv_guess16"], lambda: nc.vector.tensor_tensor(out=quotient[:], in0=radicand[:], in1=inv_guess16[:], op=MULT)),
-            "root": (["quotient"], lambda: nc.vector.scalar_tensor_tensor(out=root[:], in0=quotient[:], scalar=0.25, in1=guess16[:], op0=MULT, op1=ADD)),
+            "radicand": (["inv_power"], lambda: nc.gpsimd.tensor_tensor(out=radicand[:], in0=size[:], in1=inv_power[:], op=MULT)),
+            "factor": (["power", "sign"], lambda: nc.gpsimd.tensor_tensor(out=factor[:], in0=sign[:], in1=power[:], op=MULT)),
+            "root": (["radicand"], lambda: nc.gpsimd.tensor_tensor(out=root[:], in0=radicand[:], in1=half_exponent[:], op=POW)),
         }
         H = HALF
         tiles = [(c0, HALF, ct) for c0 in (0, HALF) for ct in range(C_TILES)][:-1]
@@ -449,16 +449,16 @@ def tile_projection_moment_gap_s3_kernel(
                     steps.append(({"sp": "spread", "cs": "copy_scale", "sc": "scale", "so": "sort", "sa": "sort_xa", "q": "quantize_x", "qw": "quantize_wa", "hold": "hold"}[letters], digits[0]))
             return steps
 
-        tensor = parse("""w5 b0 b1 w2 a0 w2 a2 p0 b2 b3 p1 a4 b4 b5 p2 a6 P0 p3 hold0 P1 P2 a8 b6 b7 p4 p5 P3 P4 b8 b9 a10 P5 p6 p7 P6 b10 b11 a12 P7 p8 p9 b12 b13 a14 P8 p10 p11 b14 b15 P9 p12 p13 P10 P11 p14 p15 P12 P13 P14 P15 m0 m1 m2 m3 m4 m5 m6 m7 m8""")
-        vector = parse("""ident16 ws0 ws1 power inv_power sc0 radicand il0:256:512 factor sc1 guess16 qw0 inv_guess16 q0 quotient q1 root ws4 sc2 ws5 il1:256:512 q2 sc3 qw1 q3 ws6 ws7 sc4 sc5 q4 q5 sc6 sc7 f0 q6 v0 q7 sc8 sc9 F0 q8 V0 q9 sc10 sc11 f1 q10 v1 q11 sc12 sc13 q12 q13 sc14 F1 sc15 q14 V1 q15 f2 F2 v2 f3 V2 v3 sub0 F3 sub1 V3 sub2 sub3 sub4 mul4 sub5 mul5 sub6 sub7 mul6 sub8 mul7 mul8""")
-        scalar = parse("""table size sign il0:0:256 guess ea0 wd2:1 wd3:1 ea2 s0 il1:0:256 s1 ea4 s2 ea6 S0 s3 S1 S2 ea8 so8:2 s4 s5 S3 S4 so10:2 ea10 S5 s6 s7 S6 so12:2 ea12 S7 s8 s9 so14:2 ea14 S8 s10 s11 S9 s12 s13 S10 S11 s14 s15 S12 S13 S14 S15""")
-        gpsimd = parse("""wd8:2:1 wd10:2:2 wd12:2:3 wd14:2:4 mul0 mul1 mul2 mul3""")
-        sync = parse("""st0 st1 st2 st4 st3 st5 st6 st7 st8""")
+        tensor = parse("""w5 b0 b1 w2 b2 a0 b3 w2 hold0 a2 p0 b4 p1 a4 b5 p2 a6 p3 b6 b7 P0 P1 p4 p5 P2 b8 b9 P3 a8 a10 p6 P4 p7 b10 b11 P5 p8 P6 p9 b12 b13 P7 a12 a14 p10 p11 b14 b15 p12 p13 P8 P9 P10 p14 p15 P11 P12 P13 P14 P15 m0 m1 m2 m3 m4 m5 m6 m7 m8""")
+        vector = parse("""ident16 ws0 power ws1 inv_power sc0 sc1 il0:256:512 qw0 q0 q1 sc2 sc3 q2 q3 sc4 sc5 ws7 qw1 q4 q5 sc6 sc7 f0 q6 v0 q7 sc8 sc9 F0 q8 V0 q9 sc10 sc11 f1 q10 v1 q11 ws15 sc12 sc13 q12 q13 sc14 sc15 q14 q15 f2 F1 v2 V1 f3 F2 v3 V2 sub0 F3 sub1 V3 sub2 sub3 sub4 mul4 sub5 sub6 sub7 mul6 sub8 mul7 mul8""")
+        scalar = parse("""table size sign wd2:1 wd3:1 il0:0:256 ea0 wd4:1 ea2 il1:0:256 s0 il1:256:512 s1 ea4 s2 ea6 s3 S0 sa8 S1 s4 sa10 s5 S2 S3 ea8 ea10 s6 S4 s7 S5 sa12 s8 sa14 S6 s9 S7 ea12 ea14 s10 s11 s12 s13 S8 S9 S10 s14 s15 S11 S12 S13 S14 S15""")
+        gpsimd = parse("""radicand root factor wd5:1:0 wd6:1:1 wd8:2:2 wd10:2:3 wd12:2:4 wd14:1:5 mul0 mul1 mul2 mul3 mul5""")
+        sync = parse("""st0 st1 st2 st4 st3 st6 st7 st5 st8""")
         free = [0, 1, 2, 3, 4, 5, 6]
         banks = []
         first_bank = {}
         for step in tensor:
-            if step[0] in ("warm", "hold"):
+            if step[0] == "hold" or (step[0] == "warm" and tensor.index(step) < tensor.index(("hold", 0))):
                 banks.append(HELD_BANK)
             elif step[0] == "moment" and step[1] in first_bank:
                 banks.append(first_bank[step[1]])

@@ -15,7 +15,6 @@ MULT = mybir.AluOpType.mult
 ADD = mybir.AluOpType.add
 MAX = mybir.AluOpType.max
 IS_GE = mybir.AluOpType.is_ge
-POW = mybir.AluOpType.pow
 SUBTRACT = mybir.AluOpType.subtract
 SQUARE = mybir.ActivationFunctionType.Square
 SQRT = mybir.ActivationFunctionType.Sqrt
@@ -69,7 +68,6 @@ def tile_projection_moment_gap_s3_kernel(
 
         scale_col = keep.tile([P, 2, PACK], F32, name="scale_col")
         one = keep.tile([P, 1], F32, name="one")
-        half_exponent = keep.tile([P, ROWS], F32, name="half_exponent")
         wa_rows = [four_rows().rearrange("p (j n) -> p j n", j=PACK) for half in range(2)]
         wa_codes = mx_tile("wa_codes", U32, 4, N, MOVING)
         wa_bytes = mx_tile("wa_bytes", U8, 1, N, MOVING_SCALE)
@@ -125,7 +123,6 @@ def tile_projection_moment_gap_s3_kernel(
         nc.vector.memset(ident[:], 0.0)
         make_identity(nc, ident[:], nomemset=True)
         nc.vector.memset(one[:], 1.0)
-        nc.vector.memset(half_exponent[:], 0.5)
         nc.vector.memset(wb_bytes[:].rearrange("p g n -> p (g n)").bitcast(I32), 0)
         nc.vector.memset(prec_line[:].bitcast(I32), 0)
         nc.vector.memset(ones[:], 1.0)
@@ -392,7 +389,8 @@ def tile_projection_moment_gap_s3_kernel(
 
         omega_flat = omega_bf16[:].rearrange("p g t -> p (g t)")
         size, sign, power, inv_power = per_row("size"), per_row("sign"), per_row("power"), per_row("inv_power")
-        radicand, guess = per_row("radicand"), per_row("guess")
+        radicand, guess, guess16 = per_row("radicand"), per_row("guess"), per_row("guess16")
+        inv_guess16, quotient = per_row("inv_guess16"), per_row("quotient")
         spread = {}
         small = {
             "table": ([], lambda: nc.scalar.activation(out=guess[:], in_=zeros[:, :ROWS], func=SQRT)),
@@ -403,7 +401,11 @@ def tile_projection_moment_gap_s3_kernel(
             "inv_power": (["power"], lambda: nc.vector.reciprocal(out=inv_power[:], in_=power[:])),
             "radicand": (["inv_power"], lambda: nc.gpsimd.tensor_tensor(out=radicand[:], in0=size[:], in1=inv_power[:], op=MULT)),
             "factor": (["power", "sign"], lambda: nc.gpsimd.tensor_tensor(out=factor[:], in0=sign[:], in1=power[:], op=MULT)),
-            "root": (["radicand"], lambda: nc.gpsimd.tensor_tensor(out=root[:], in0=radicand[:], in1=half_exponent[:], op=POW)),
+            "guess": (["radicand", "table"], lambda: nc.scalar.activation(out=guess[:], in_=radicand[:], func=SQRT, scale=2.0**-10)),
+            "guess16": (["guess"], lambda: nc.vector.tensor_scalar(out=guess16[:], in0=guess[:], scalar1=2.0**-60, scalar2=16.0, op0=MAX, op1=MULT)),
+            "inv_guess16": (["guess16"], lambda: nc.vector.reciprocal(out=inv_guess16[:], in_=guess16[:])),
+            "quotient": (["inv_guess16"], lambda: nc.vector.tensor_tensor(out=quotient[:], in0=radicand[:], in1=inv_guess16[:], op=MULT)),
+            "root": (["quotient"], lambda: nc.vector.scalar_tensor_tensor(out=root[:], in0=quotient[:], scalar=0.25, in1=guess16[:], op0=MULT, op1=ADD)),
         }
         H = HALF
         tiles = [(c0, HALF, ct) for c0 in (0, HALF) for ct in range(C_TILES)][:-1]
@@ -450,9 +452,9 @@ def tile_projection_moment_gap_s3_kernel(
             return steps
 
         tensor = parse("""w5 b0 b1 w2 b2 a0 b3 w2 hold0 a2 p0 b4 p1 a4 b5 p2 a6 p3 b6 b7 P0 P1 p4 p5 P2 b8 b9 P3 a8 a10 p6 P4 p7 b10 b11 P5 p8 P6 p9 b12 b13 P7 a12 a14 p10 p11 b14 b15 p12 p13 P8 P9 P10 p14 p15 P11 P12 P13 P14 P15 m0 m1 m2 m3 m4 m5 m6 m7 m8""")
-        vector = parse("""ident16 ws0 power ws1 inv_power sc0 sc1 il0:256:512 qw0 q0 q1 sc2 sc3 q2 q3 sc4 sc5 ws7 qw1 q4 q5 sc6 sc7 f0 q6 v0 q7 sc8 sc9 F0 q8 V0 q9 sc10 sc11 f1 q10 v1 q11 ws15 sc12 sc13 q12 q13 sc14 sc15 q14 q15 f2 F1 v2 V1 f3 F2 v3 V2 sub0 F3 sub1 V3 sub2 sub3 sub4 mul4 sub5 sub6 sub7 mul6 sub8 mul7 mul8""")
-        scalar = parse("""table size sign wd2:1 wd3:1 il0:0:256 ea0 wd4:1 ea2 il1:0:256 s0 il1:256:512 s1 ea4 s2 ea6 s3 S0 sa8 S1 s4 sa10 s5 S2 S3 ea8 ea10 s6 S4 s7 S5 sa12 s8 sa14 S6 s9 S7 ea12 ea14 s10 s11 s12 s13 S8 S9 S10 s14 s15 S11 S12 S13 S14 S15""")
-        gpsimd = parse("""radicand root factor wd5:1:0 wd6:1:1 wd8:2:2 wd10:2:3 wd12:2:4 wd14:1:5 mul0 mul1 mul2 mul3 mul5""")
+        vector = parse("""ident16 ws0 power ws1 inv_power sc0 sc1 guess16 il0:256:512 inv_guess16 qw0 quotient q0 root q1 sc2 sc3 q2 q3 sc4 sc5 ws7 qw1 q4 q5 sc6 sc7 f0 q6 v0 q7 sc8 sc9 F0 q8 V0 q9 sc10 sc11 f1 q10 v1 q11 sc12 sc13 ws15 q12 q13 sc14 sc15 q14 q15 f2 F1 v2 V1 f3 F2 v3 V2 sub0 F3 sub1 V3 sub2 sub3 sub4 mul4 sub5 sub6 sub7 mul6 sub8 mul7 mul8""")
+        scalar = parse("""table size sign wd2:1 wd3:1 guess il0:0:256 ea0 wd4:1 ea2 il1:0:256 s0 il1:256:512 s1 ea4 s2 ea6 s3 S0 sa8 S1 s4 sa10 s5 S2 S3 ea8 ea10 s6 S4 s7 S5 sa12 s8 sa14 S6 s9 S7 ea12 ea14 s10 s11 s12 s13 S8 S9 S10 s14 s15 S11 S12 S13 S14 S15""")
+        gpsimd = parse("""radicand factor wd5:1:0 wd6:1:1 wd8:2:2 wd10:2:3 wd12:2:4 wd14:1:5 mul0 mul1 mul2 mul3 mul5""")
         sync = parse("""st0 st1 st2 st4 st3 st6 st7 st5 st8""")
         free = [0, 1, 2, 3, 4, 5, 6]
         banks = []

@@ -15,6 +15,7 @@ MULT = mybir.AluOpType.mult
 ADD = mybir.AluOpType.add
 MAX = mybir.AluOpType.max
 IS_GE = mybir.AluOpType.is_ge
+IS_LT = mybir.AluOpType.is_lt
 SUBTRACT = mybir.AluOpType.subtract
 SQUARE = mybir.ActivationFunctionType.Square
 SQRT = mybir.ActivationFunctionType.Sqrt
@@ -39,6 +40,7 @@ MOVING, MOVING_SCALE, STATIONARY, STATIONARY_SCALE = 0, 64, 128, 192
 
 BUFS = {"wide": 6, "sorted": 5, "grouped": 3, "four_rows": 8}
 SLOTS = 4
+SPLIT = 2
 
 FLOPS = 2 * M * N * (KA + KB) + 2 * C * N * M
 
@@ -133,17 +135,17 @@ def tile_projection_moment_gap_s3_kernel(
         nc.sync.dma_start(out=scale_col[:], in_=xb_scale.rearrange("o (h p j) -> p (o h) j", h=2, j=PACK))
         load_wa(0)
         load_xa(0)
+        load_xb(4, 2)
         nc.sync.dma_start(out=prec_line[0:1, :], in_=prec[HALF:].unsqueeze(0))
         load_scale_bytes(wb_bytes, wb_scales)
         load_wb(0)
-        load_xb(4, 2)
         load_xa(2)
         load_wa(1)
         load_xa(4)
         load_xb(6, 2)
         load_wb(1)
-        load_xb(8, 4)
         load_xa(6)
+        load_xb(8, 4)
         load_xa(8)
         load_xb(12, 4)
         load_xa(10)
@@ -166,7 +168,7 @@ def tile_projection_moment_gap_s3_kernel(
 
         def group_wa(half, c0, c1, copy):
             if half not in wa_grouped:
-                wa_grouped[half] = grouped_tile()
+                wa_grouped[half] = grouped_tile() if half == 0 else slot(0)[:, : PACK * HALF]
             copy(
                 out=wa_grouped[half][:, PACK * c0 : PACK * c1].rearrange("p (c i j) -> p c j i", i=4, j=PACK),
                 in_=wa_rows[half][:, :, c0:c1].rearrange("p j (c i) -> p c j i", i=4),
@@ -190,7 +192,10 @@ def tile_projection_moment_gap_s3_kernel(
             return work.tile([P, 2 * PASSES * K_PASS], BF16, name="slot%d" % i, bufs=1, align_bytes=64)
 
         def widen(r, count, copy, gate):
-            tile = slot(gate) if gate >= 0 else work.tile([P, count * KB], BF16, name="wide", bufs=BUFS["wide"])
+            if gate == -2:
+                tile = work.tile([P, count * KB], BF16, name="first", bufs=1)
+            else:
+                tile = slot(gate) if gate >= 0 else work.tile([P, count * KB], BF16, name="wide", bufs=BUFS["wide"])
             copy(out=tile[:, : count * KB], in_=xb_codes_in[r][:, : count * KB].bitcast(FP8))
             for i in range(count):
                 xb_rows[r + i] = tile[:, KB * i :]
@@ -388,7 +393,7 @@ def tile_projection_moment_gap_s3_kernel(
 
 
         omega_flat = omega_bf16[:].rearrange("p g t -> p (g t)")
-        size, sign, power, inv_power = per_row("size"), per_row("sign"), per_row("power"), per_row("inv_power")
+        size, sign, power, inv_power = per_row("size"), per_row("sign"), per_row("power"), work.tile([P, ROWS], F32, name="first", bufs=1)
         radicand, guess, guess16 = per_row("radicand"), per_row("guess"), per_row("guess16")
         inv_guess16, quotient = per_row("inv_guess16"), per_row("quotient")
         spread = {}
@@ -397,9 +402,9 @@ def tile_projection_moment_gap_s3_kernel(
             "size": ([], lambda: nc.scalar.activation(out=size[:], in_=omega_flat, func=ABS)),
             "sign": ([], lambda: nc.scalar.activation(out=sign[:], in_=omega_flat, func=SIGN)),
             "ident16": ([], lambda: nc.vector.tensor_copy(out=ident_bf16[:], in_=ident[:])),
-            "power": (["size"], lambda: nc.vector.tensor_scalar(out=power[:], in0=size[:], scalar1=2.0**-64, scalar2=2.0**-64, op0=IS_GE, op1=MAX)),
-            "inv_power": (["power"], lambda: nc.vector.reciprocal(out=inv_power[:], in_=power[:])),
-            "radicand": (["inv_power"], lambda: nc.gpsimd.tensor_tensor(out=radicand[:], in0=size[:], in1=inv_power[:], op=MULT)),
+            "power": (["size"], lambda: nc.gpsimd.tensor_scalar(out=power[:], in0=size[:], scalar1=2.0**-64, scalar2=2.0**-64, op0=IS_GE, op1=MAX)),
+            "inv_power": (["size"], lambda: nc.vector.tensor_scalar(out=inv_power[:], in0=size[:], scalar1=2.0**-64, scalar2=2.0**64, op0=IS_LT, op1=MULT)),
+            "radicand": (["inv_power"], lambda: nc.vector.scalar_tensor_tensor(out=radicand[:], in0=inv_power[:], scalar=1.0, in1=size[:], op0=MAX, op1=MULT)),
             "factor": (["power", "sign"], lambda: nc.gpsimd.tensor_tensor(out=factor[:], in0=sign[:], in1=power[:], op=MULT)),
             "guess": (["radicand", "table"], lambda: nc.scalar.activation(out=guess[:], in_=radicand[:], func=SQRT, scale=2.0**-10)),
             "guess16": (["guess"], lambda: nc.vector.tensor_scalar(out=guess16[:], in0=guess[:], scalar1=2.0**-60, scalar2=16.0, op0=MAX, op1=MULT)),
@@ -408,8 +413,8 @@ def tile_projection_moment_gap_s3_kernel(
             "root": (["quotient"], lambda: nc.vector.scalar_tensor_tensor(out=root[:], in0=quotient[:], scalar=0.25, in1=guess16[:], op0=MULT, op1=ADD)),
         }
         H = HALF
-        tiles = [(c0, HALF, ct) for c0 in (0, HALF) for ct in range(C_TILES)][:-1]
-        tiles += [(HALF, QUARTER, C_TILES - 1), (HALF + QUARTER, QUARTER, C_TILES - 1)]
+        tiles = [(c0, HALF, ct) for c0 in (0, HALF) for ct in range(C_TILES)][:-SPLIT]
+        tiles += [(c0, QUARTER, ct) for ct in range(C_TILES - SPLIT, C_TILES) for c0 in (HALF, HALF + QUARTER)]
         ALL = (0, 1, 2, 3)
 
         def parse(text):
@@ -437,6 +442,8 @@ def tile_projection_moment_gap_s3_kernel(
                     steps.append(("finish_v" if letters in "fF" else "quantize_v", digits[0], 0 if letters in "fv" else H))
                 elif letters == "wd:":
                     steps.append(("widen", digits[0], digits[1], -1, -1))
+                elif letters == "wg:":
+                    steps.append(("widen", digits[0], digits[1], -2, -1))
                 elif letters == "wd::":
                     steps.append(("widen", digits[0], digits[1], digits[2] % SLOTS, digits[2]))
                 elif letters == "so:":
@@ -451,19 +458,28 @@ def tile_projection_moment_gap_s3_kernel(
                     steps.append(({"sp": "spread", "cs": "copy_scale", "sc": "scale", "so": "sort", "sa": "sort_xa", "q": "quantize_x", "qw": "quantize_wa", "hold": "hold"}[letters], digits[0]))
             return steps
 
-        tensor = parse("""w5 b0 b1 w2 b2 a0 b3 w2 hold0 a2 p0 b4 p1 a4 b5 p2 a6 p3 b6 b7 P0 P1 p4 p5 P2 b8 b9 P3 a8 a10 p6 P4 p7 b10 b11 P5 p8 P6 p9 b12 b13 P7 a12 a14 p10 p11 b14 b15 p12 p13 P8 P9 P10 p14 p15 P11 P12 P13 P14 P15 m0 m1 m2 m3 m4 m5 m6 m7 m8""")
-        vector = parse("""ident16 ws0 power ws1 inv_power sc0 sc1 guess16 il0:256:512 inv_guess16 qw0 quotient q0 root q1 sc2 sc3 q2 q3 sc4 sc5 ws7 qw1 q4 q5 sc6 sc7 f0 q6 v0 q7 sc8 sc9 F0 q8 V0 q9 sc10 sc11 f1 q10 v1 q11 sc12 sc13 ws15 q12 q13 sc14 sc15 q14 q15 f2 F1 v2 V1 f3 F2 v3 V2 sub0 F3 sub1 V3 sub2 sub3 sub4 mul4 sub5 sub6 sub7 mul6 sub8 mul7 mul8""")
-        scalar = parse("""table size sign wd2:1 wd3:1 guess il0:0:256 ea0 wd4:1 ea2 il1:0:256 s0 il1:256:512 s1 ea4 s2 ea6 s3 S0 sa8 S1 s4 sa10 s5 S2 S3 ea8 ea10 s6 S4 s7 S5 sa12 s8 sa14 S6 s9 S7 ea12 ea14 s10 s11 s12 s13 S8 S9 S10 s14 s15 S11 S12 S13 S14 S15""")
-        gpsimd = parse("""radicand factor wd5:1:0 wd6:1:1 wd8:2:2 wd10:2:3 wd12:2:4 wd14:1:5 mul0 mul1 mul2 mul3 mul5""")
-        sync = parse("""st0 st1 st2 st4 st3 st6 st7 st5 st8""")
+        tensor = parse("""w5 b0 w1 b1 w2 b2 a0 b3 w2 hold0 a2 p0 p1 a4 b4 b5 p2 p3 P0 P1 a6 b6 b7 P2 P3 p4 p5 a8 b8 b9 p6 p7 P4 P5 a10 b10 b11 P6 P7 p8 p9 a12 b12 b13 p10 p11 P8 P9 a14 b14 b15 p12 p13 P10 P11 p14 p15 P12 P13 P14 P15 m0 m1 m2 m3 m4 m5 m6 m7 m8 m9""")
+        vector = parse("""ident16 ws0 inv_power ws1 radicand sc0 sc1 guess16 il0:352:512 inv_guess16 qw0 quotient q0 root q1 sc2 sc3 q2 qw1 q3 sc4 sc5 q4 q5 f0 sc6 sc7 q6 v0 q7 F0 sc8 sc9 q8 V0 q9 f1 sc10 sc11 q10 v1 q11 F1 sc12 sc13 q12 V1 q13 f2 sc14 sc15 q14 q15 v2 F2 f3 V2 v3 sub0 F3 sub1 V3 sub2 sub3 sub4 mul4 sub5 sub6 mul5 sub7 sub8 mul7 sub9 mul8 mul9""")
+        scalar = parse("""table size sign wd2:1 guess il0:0:352 ea0 wd4:1 wd5:1 ea2 il1:0:256 ea4 s0 s1 s2 s3 wd7:1 ea6 S0 S1 sa8 S2 S3 s4 ea8 s5 sa10 s6 s7 S4 ea10 S5 sa12 S6 S7 s8 ea12 s9 sa14 s10 s11 S8 ea14 S9 s12 s13 S10 S11 s14 s15 S12 S13 S14 S15""")
+        gpsimd = parse("""wg3:1 power factor il1:256:512 wd6:1:1 wd8:2:2 wd10:2:3 wd12:2:4 wd14:2:5 mul0 mul1 mul2 mul3 mul6""")
+        sync = parse("""st0 st1 st2 st4 st3 st5 st6 st7 st8 st9""")
         free = [0, 1, 2, 3, 4, 5, 6]
         banks = []
         first_bank = {}
-        for step in tensor:
+        turn_ring, product_ring = [0, 1, 2], [6, 3, 4, 5]
+        first_product = tensor.index(("project", 0, 0))
+        last_turn = max(i for i, step in enumerate(tensor) if step[0] in ("a", "b"))
+        for place, step in enumerate(tensor):
             if step[0] == "hold" or (step[0] == "warm" and tensor.index(step) < tensor.index(("hold", 0))):
                 banks.append(HELD_BANK)
             elif step[0] == "moment" and step[1] in first_bank:
                 banks.append(first_bank[step[1]])
+            elif first_product <= place <= last_turn:
+                ring = turn_ring if step[0] in ("a", "b") else product_ring
+                ring.append(ring.pop(0))
+                banks.append(ring[-1])
+                free.remove(ring[-1])
+                free.append(ring[-1])
             else:
                 free.append(free.pop(0))
                 banks.append(free[-1])
@@ -524,6 +540,8 @@ def tile_projection_moment_gap_s3_kernel(
                 return first
             if kind == "widen" and step[3] >= 0:
                 return [("quantize_x", 2 * step[4] + 1)]
+            if kind == "widen" and step[3] == -2:
+                return ["radicand"]
             if kind in ("widen", "widen_sorted"):
                 return []
             if kind == "scale":
@@ -535,7 +553,7 @@ def tile_projection_moment_gap_s3_kernel(
             if kind == "quantize_x":
                 return [("empty", ("a", step[1] - step[1] % 2)), ("scale", step[1])]
             if kind == "group_wa":
-                return []
+                return [("quantize_x", 1)] if step[1] == 1 else []
             if kind == "quantize_wa":
                 return [s for s in engine_of if s[0] == "group_wa" and s[1] == step[1]]
             if kind == "square":
@@ -554,6 +572,8 @@ def tile_projection_moment_gap_s3_kernel(
             kind = step[0]
             if kind == "widen":
                 users = [prepared[r] if prepared[r] != step else ("b", r) for r in range(step[1], step[1] + step[2])]
+                if step[3] == -2:
+                    return None
                 return ("wide" if step[3] < 0 else "slot%d" % step[3], step, users)
             if kind == "widen_sorted":
                 return ("sorted", step, [("b", step[1])])
@@ -569,7 +589,7 @@ def tile_projection_moment_gap_s3_kernel(
                 r = step[1][1] if kind == "empty" else step[1] - step[1] % 2
                 return ("slot%d" % (r // 2 % SLOTS), r, [("quantize_x", r), ("quantize_x", r + 1)])
             if kind == "group_wa":
-                return ("grouped", step[1], [("quantize_wa", step[1])])
+                return ("grouped" if step[1] == 0 else "slot0", ("wa", step[1]), [("quantize_wa", step[1])])
             if kind == "finish_v":
                 return ("grouped", step, [("quantize_v",) + step[1:]])
             if kind == "square":

@@ -19,6 +19,7 @@ IS_LT = mybir.AluOpType.is_lt
 SUBTRACT = mybir.AluOpType.subtract
 SQUARE = mybir.ActivationFunctionType.Square
 SQRT = mybir.ActivationFunctionType.Sqrt
+COPY = mybir.ActivationFunctionType.Copy
 ABS = mybir.ActivationFunctionType.Abs
 SIGN = mybir.ActivationFunctionType.Sign
 
@@ -40,6 +41,8 @@ MOVING, MOVING_SCALE, STATIONARY, STATIONARY_SCALE = 0, 64, 128, 192
 
 BUFS = {"wide": 6, "sorted": 5, "grouped": 3, "four_rows": 8}
 SLOTS = 4
+TURN_RING = (0, 1, 2)
+PRODUCT_RING = (4, 5, 6, 3)
 SPLIT = 2
 
 FLOPS = 2 * M * N * (KA + KB) + 2 * C * N * M
@@ -123,11 +126,11 @@ def tile_projection_moment_gap_s3_kernel(
 
         nc.vector.memset(zeros[:].bitcast(I32), 0)
         nc.vector.memset(ident[:], 0.0)
-        make_identity(nc, ident[:], nomemset=True)
         nc.vector.memset(one[:], 1.0)
         nc.vector.memset(wb_bytes[:].rearrange("p g n -> p (g n)").bitcast(I32), 0)
         nc.vector.memset(prec_line[:].bitcast(I32), 0)
         nc.vector.memset(ones[:], 1.0)
+        make_identity(nc, ident[:], nomemset=True)
         nc.vector.memset(z_bytes[:].rearrange("p g n -> p (g n)").bitcast(I32), 0)
         load_xb(0, 2)
         nc.sync.dma_start(out=omega_bf16[:], in_=omega.rearrange("(g p t) -> p g t", p=P, t=PACK))
@@ -191,11 +194,18 @@ def tile_projection_moment_gap_s3_kernel(
         def slot(i):
             return work.tile([P, 2 * PASSES * K_PASS], BF16, name="slot%d" % i, bufs=1, align_bytes=64)
 
+        gate_tiles = {}
+
+        def gate_tile(gate):
+            if gate not in gate_tiles:
+                gate_tiles[gate] = slot(gate % SLOTS)
+            return gate_tiles[gate]
+
         def widen(r, count, copy, gate):
             if gate == -2:
                 tile = work.tile([P, count * KB], BF16, name="first", bufs=1)
             else:
-                tile = slot(gate) if gate >= 0 else work.tile([P, count * KB], BF16, name="wide", bufs=BUFS["wide"])
+                tile = gate_tile(gate) if gate >= 0 else work.tile([P, count * KB], BF16, name="wide", bufs=BUFS["wide"])
             copy(out=tile[:, : count * KB], in_=xb_codes_in[r][:, : count * KB].bitcast(FP8))
             for i in range(count):
                 xb_rows[r + i] = tile[:, KB * i :]
@@ -237,6 +247,19 @@ def tile_projection_moment_gap_s3_kernel(
             for i in range(2):
                 words[r + i, 0] = [tile[:, i, u, :] for u in range(2)]
 
+        def gate_sort(kind, r, gate):
+            count = 4 if kind == "b" else 2
+            first = 0 if kind == "b" else 4 * 2 * P
+            tile = gate_tile(gate)[:].bitcast(F32)[:, first : first + count * 2 * P].rearrange("p (s u m) -> p s u m", s=count, u=2)
+            source = xb_rows[r][:, : 2 * KB] if kind == "b" else xa_pairs[r][:].rearrange("p s k -> p (s k)")
+            nc.gpsimd.tensor_copy(
+                out=tile.rearrange("p s u (c i) -> p s c u i", i=4),
+                in_=source.bitcast(F32).rearrange("p (s c i u) -> p s c u i", s=count, i=4, u=2),
+            )
+            for i in range(2):
+                for s in ((1, 2) if kind == "b" else (0,)):
+                    words[r + i, s] = [tile[:, 2 * i + s - 1 if kind == "b" else i, u, :] for u in range(2)]
+
         x_grouped = {}
         turned = {}
 
@@ -276,28 +299,30 @@ def tile_projection_moment_gap_s3_kernel(
 
         x_codes = {}
 
-        def quantize_x(r):
-            both = mx_tile("x_codes%d" % r, U32, 4, PASSES * P + PASSES * P // PACK, STATIONARY)
-            codes, scale_bytes = both[:, : PASSES * P], both[:, PASSES * P :].bitcast(U8)
+        def quantize_x(r, s0, s1):
+            if r not in x_codes:
+                both = mx_tile("x_codes%d" % r, U32, 4, PASSES * P + PASSES * P // PACK, STATIONARY)
+                x_codes[r] = (both[:, : PASSES * P], both[:, PASSES * P :].bitcast(U8))
+            codes, scale_bytes = x_codes[r]
             first = PASSES * (r % 2)
             nc.vector.quantize_mx(
-                out=codes[:].bitcast(FP8X4),
-                scales=scale_bytes[:],
-                in_=x_grouped[r // 2][:, first : first + PASSES, :].rearrange("p s k -> p (s k)"),
+                out=codes[:, P * s0 : P * s1].bitcast(FP8X4),
+                scales=scale_bytes[:, P * s0 : P * s1],
+                in_=x_grouped[r // 2][:, first + s0 : first + s1, :].rearrange("p s k -> p (s k)"),
             )
-            x_codes[r] = (codes, scale_bytes)
 
         root, factor = per_row("root"), per_row("factor", BF16)
         squares = {}
 
         products = {}
 
-        def project(r, c0, where):
-            tile = bank(where)
-            products[r, c0] = tile
+        def project(r, c0, passes, where):
+            if (r, c0) not in products:
+                products[r, c0] = bank(where)
+            tile = products[r, c0]
             cols = slice(c0, c0 + HALF)
             codes, scale_bytes = x_codes[r]
-            for s in range(PASSES):
+            for s in passes:
                 if s == 0:
                     rhs, rhs_scale = wa_codes[:, cols].bitcast(FP8X4), wa_bytes[:, cols]
                 else:
@@ -309,8 +334,8 @@ def tile_projection_moment_gap_s3_kernel(
                     lhsT_scale=scale_bytes[:, P * s : P * (s + 1)],
                     rhs=rhs,
                     rhs_scale=rhs_scale,
-                    start=(s == 0),
-                    stop=(s == PASSES - 1),
+                    start=(s == (0 if len(passes) == PASSES else 1)),
+                    stop=(s == (PASSES - 1 if len(passes) == PASSES else 0)),
                 )
 
         def square(r, c0):
@@ -394,8 +419,7 @@ def tile_projection_moment_gap_s3_kernel(
 
         omega_flat = omega_bf16[:].rearrange("p g t -> p (g t)")
         size, sign, power, inv_power = per_row("size"), per_row("sign"), per_row("power"), work.tile([P, ROWS], F32, name="first", bufs=1)
-        radicand, guess, guess16 = per_row("radicand"), per_row("guess"), per_row("guess16")
-        inv_guess16, quotient = per_row("inv_guess16"), per_row("quotient")
+        radicand, guess = per_row("radicand"), per_row("guess")
         spread = {}
         small = {
             "table": ([], lambda: nc.scalar.activation(out=guess[:], in_=zeros[:, :ROWS], func=SQRT)),
@@ -407,19 +431,21 @@ def tile_projection_moment_gap_s3_kernel(
             "radicand": (["inv_power"], lambda: nc.vector.scalar_tensor_tensor(out=radicand[:], in0=inv_power[:], scalar=1.0, in1=size[:], op0=MAX, op1=MULT)),
             "factor": (["power", "sign"], lambda: nc.gpsimd.tensor_tensor(out=factor[:], in0=sign[:], in1=power[:], op=MULT)),
             "guess": (["radicand", "table"], lambda: nc.scalar.activation(out=guess[:], in_=radicand[:], func=SQRT, scale=2.0**-10)),
-            "guess16": (["guess"], lambda: nc.vector.tensor_scalar(out=guess16[:], in0=guess[:], scalar1=2.0**-60, scalar2=16.0, op0=MAX, op1=MULT)),
-            "inv_guess16": (["guess16"], lambda: nc.vector.reciprocal(out=inv_guess16[:], in_=guess16[:])),
-            "quotient": (["inv_guess16"], lambda: nc.vector.tensor_tensor(out=quotient[:], in0=radicand[:], in1=inv_guess16[:], op=MULT)),
-            "root": (["quotient"], lambda: nc.vector.scalar_tensor_tensor(out=root[:], in0=quotient[:], scalar=0.25, in1=guess16[:], op0=MULT, op1=ADD)),
+            "root": (["guess"], lambda: nc.scalar.activation(out=root[:], in_=guess[:], func=COPY, scale=32.0)),
         }
         H = HALF
         tiles = [(c0, HALF, ct) for c0 in (0, HALF) for ct in range(C_TILES)][:-SPLIT]
         tiles += [(c0, QUARTER, ct) for ct in range(C_TILES - SPLIT, C_TILES) for c0 in (HALF, HALF + QUARTER)]
         ALL = (0, 1, 2, 3)
 
+        forced = {}
+
         def parse(text):
             steps = []
             for word in text.split():
+                if "@" in word:
+                    forced[len(steps)] = int(word.split("@")[1])
+                    word = word.split("@")[0]
                 letters = "".join(ch for ch in word if ch not in "0123456789")
                 digits = [int(x) for x in "".join(ch if ch in "0123456789" else " " for ch in word).split()]
                 if word in small:
@@ -429,7 +455,11 @@ def tile_projection_moment_gap_s3_kernel(
                 elif letters == "w":
                     steps.append(("warm", len(steps), digits[0]))
                 elif letters in ("p", "P"):
-                    steps.append(("project", digits[0], 0 if letters == "p" else H))
+                    steps.append(("project", digits[0], 0 if letters == "p" else H, (0, 1, 2)))
+                elif letters in ("p:", "P:"):
+                    steps.append(("project", digits[0], 0 if letters == "p:" else H, (0,) if digits[1] == 0 else (1, 2)))
+                elif letters in ("q", "qa", "qb"):
+                    steps.append(("quantize_x", digits[0]) + {"q": (0, 3), "qa": (0, 1), "qb": (1, 3)}[letters])
                 elif letters in ("s", "S"):
                     steps.append(("square", digits[0], 0 if letters == "s" else H))
                 elif letters in ("ea", "eb"):
@@ -448,6 +478,8 @@ def tile_projection_moment_gap_s3_kernel(
                     steps.append(("widen", digits[0], digits[1], digits[2] % SLOTS, digits[2]))
                 elif letters == "so:":
                     steps.append(("sort", digits[0], digits[1]))
+                elif letters in ("gs:", "ga:"):
+                    steps.append(("gate_sort", "b" if letters == "gs:" else "a", digits[0], digits[1]))
                 elif letters == "ws":
                     steps.append(("widen_sorted", digits[0]))
                 elif letters == "il::":
@@ -455,29 +487,35 @@ def tile_projection_moment_gap_s3_kernel(
                 elif letters in ("sub", "mul", "st"):
                     steps.append(({"sub": "subtract", "mul": "scale_gap", "st": "store"}[letters], tiles[digits[0]]))
                 else:
-                    steps.append(({"sp": "spread", "cs": "copy_scale", "sc": "scale", "so": "sort", "sa": "sort_xa", "q": "quantize_x", "qw": "quantize_wa", "hold": "hold"}[letters], digits[0]))
+                    steps.append(({"sp": "spread", "cs": "copy_scale", "sc": "scale", "so": "sort", "sa": "sort_xa", "qw": "quantize_wa", "hold": "hold"}[letters], digits[0]))
             return steps
 
-        tensor = parse("""w5 b0 w1 b1 w2 b2 a0 b3 w2 hold0 a2 p0 p1 a4 b4 b5 p2 p3 P0 P1 a6 b6 b7 P2 P3 p4 p5 a8 b8 b9 p6 p7 P4 P5 a10 b10 b11 P6 P7 p8 p9 a12 b12 b13 p10 p11 P8 P9 a14 b14 b15 p12 p13 P10 P11 p14 p15 P12 P13 P14 P15 m0 m1 m2 m3 m4 m5 m6 m7 m8 m9""")
-        vector = parse("""ident16 ws0 inv_power ws1 radicand sc0 sc1 guess16 il0:352:512 inv_guess16 qw0 quotient q0 root q1 sc2 sc3 q2 qw1 q3 sc4 sc5 q4 q5 f0 sc6 sc7 q6 v0 q7 F0 sc8 sc9 q8 V0 q9 f1 sc10 sc11 q10 v1 q11 F1 sc12 sc13 q12 V1 q13 f2 sc14 sc15 q14 q15 v2 F2 f3 V2 v3 sub0 F3 sub1 V3 sub2 sub3 sub4 mul4 sub5 sub6 mul5 sub7 sub8 mul7 sub9 mul8 mul9""")
-        scalar = parse("""table size sign wd2:1 guess il0:0:352 ea0 wd4:1 wd5:1 ea2 il1:0:256 ea4 s0 s1 s2 s3 wd7:1 ea6 S0 S1 sa8 S2 S3 s4 ea8 s5 sa10 s6 s7 S4 ea10 S5 sa12 S6 S7 s8 ea12 s9 sa14 s10 s11 S8 ea14 S9 s12 s13 S10 S11 s14 s15 S12 S13 S14 S15""")
-        gpsimd = parse("""wg3:1 power factor il1:256:512 wd6:1:1 wd8:2:2 wd10:2:3 wd12:2:4 wd14:2:5 mul0 mul1 mul2 mul3 mul6""")
+        tensor = parse("""w5 b0@0 w1 b1@1 w2 b2@2 a0@3 b3@4 w2 hold0 a2@5 p0@6 p1@3 a4 b4 b5 p2 p3 P0 P1 a6 b6 b7 P2 P3 p4 p5 a8 b8 b9 p6 p7 P4 P5 a10 b10 b11 P6 P7 p8 p9 a12 b12 b13 p10 p11 P8 P9 a14 b14 b15 p12 p13 P10 P11 p14 p15 P12 P13 P14 P15 m0 m1 m2 m3 m4 m5 m6 m7 m8 m9""")
+        vector = parse("""ws0 inv_power ws1 radicand sc0 sc1 il0:352:512 ident16 qw0 q0 q1 sc2 sc3 q2 qw1 q3 sc4 sc5 q4 q5 f0 sc6 sc7 ws9 q6 v0 q7 F0 sc8 sc9 q8 V0 q9 f1 sc10 sc11 q10 v1 q11 F1 sc12 sc13 q12 V1 q13 sc14 sc15 q14 q15 f2 v2 F2 f3 v3 V2 sub0 F3 sub1 V3 sub2 sub3 sub4 mul4 sub5 sub6 mul5 sub7 sub8 mul7 sub9 mul8 mul9""")
+        scalar = parse("""table size sign wd2:1 guess il0:0:352 root ea0 wd4:1 wd5:1 ea2 il1:0:256 ea4 s0 s1 s2 s3 wd7:1 ea6 S0 S1 so8:1 S2 S3 s4 ea8 s5 sa10 s6 s7 S4 ea10 S5 sa12 S6 S7 s8 ea12 s9 sa14 s10 so14:1 s11 S8 ea14 S9 s12 s13 S10 S11 s14 s15 S12 S13 S14 S15""")
+        gpsimd = parse("""wg3:1 power factor il1:256:512 wd6:1:1 wd8:1:2 ga8:2 wd10:2:3 wd12:2:4 wd14:2:5 mul0 mul1 mul2 mul3 mul6""")
         sync = parse("""st0 st1 st2 st4 st3 st5 st6 st7 st8 st9""")
         free = [0, 1, 2, 3, 4, 5, 6]
         banks = []
         first_bank = {}
-        turn_ring, product_ring = [0, 1, 2], [6, 3, 4, 5]
-        first_product = tensor.index(("project", 0, 0))
+        turn_ring, product_ring = list(TURN_RING), list(PRODUCT_RING)
+        first_product = max(forced) + 1
         last_turn = max(i for i, step in enumerate(tensor) if step[0] in ("a", "b"))
         for place, step in enumerate(tensor):
             if step[0] == "hold" or (step[0] == "warm" and tensor.index(step) < tensor.index(("hold", 0))):
                 banks.append(HELD_BANK)
             elif step[0] == "moment" and step[1] in first_bank:
                 banks.append(first_bank[step[1]])
+            elif step[0] == "project" and step[1:3] in first_bank:
+                banks.append(first_bank[step[1:3]])
+            elif place in forced:
+                banks.append(forced[place])
+                first_bank[step[1:3]] = forced[place]
             elif first_product <= place <= last_turn:
                 ring = turn_ring if step[0] in ("a", "b") else product_ring
                 ring.append(ring.pop(0))
                 banks.append(ring[-1])
+                first_bank[step[1:3]] = ring[-1]
                 free.remove(ring[-1])
                 free.append(ring[-1])
             else:
@@ -497,6 +535,9 @@ def tile_projection_moment_gap_s3_kernel(
                     prepared[step[1]] = step
         for steps in queues.values():
             for step in steps:
+                if step[:2] == ("gate_sort", "b"):
+                    prepared[step[2]] = step
+                    prepared[step[2] + 1] = step
                 if step[0] == "sort":
                     for r in range(step[1], step[1] + step[2]):
                         prepared[r] = step
@@ -508,16 +549,19 @@ def tile_projection_moment_gap_s3_kernel(
         for step, at in zip(tensor, banks):
             where[step] = at
             kind = step[0]
-            reader = {"a": ("empty", step), "b": ("scale", step[1]), "project": ("square",) + step[1:], "moment": ("subtract", step[1]), "warm": step, "hold": step}[kind]
+            reader = {"a": ("empty", step), "b": ("scale", step[1]), "project": ("square",) + step[1:3], "moment": ("subtract", step[1]), "warm": step, "hold": step}[kind]
             if at in bank_reader and bank_reader[at] != reader:
                 after[step] = [bank_reader[at]]
             bank_reader[at] = reader
+
+        def quantisers(r):
+            return [s for s in vector if s[:2] == ("quantize_x", r)]
 
         def group_rows(g):
             return range(PACK * g, PACK * (g + 1))
 
         def gated(pair):
-            return [s for s in engine_of if s[0] == "widen" and s[3] >= 0 and s[4] + SLOTS == pair]
+            return [s for s in engine_of if s[0] == "widen" and s[3] >= 0 and s[4] + SLOTS == pair] + [s for s in engine_of if s[0] == "gate_sort" and s[3] + SLOTS == pair]
 
         def needs(step):
             kind = step[0]
@@ -527,19 +571,24 @@ def tile_projection_moment_gap_s3_kernel(
             if kind == "b":
                 return first + [prepared[step[1]]]
             if kind == "project":
-                return first + [("quantize_x", step[1]), ("quantize_wa", step[2] // HALF)]
+                wanted_codes = [s for s in vector if s[:2] == ("quantize_x", step[1]) and any(s[2] <= i < s[3] for i in step[3])]
+                return first + wanted_codes + ([("quantize_wa", step[2] // HALF)] if 0 in step[3] else [])
             if kind == "moment":
                 return first + [("quantize_v", g, step[1][0] - step[1][0] % HALF) for g in step[2]]
             if kind == "hold":
                 return first + ["ident16", "factor"]
             if kind == "a" and ("sort_xa", step[1]) in engine_of:
                 return first + [("sort_xa", step[1])]
+            if kind == "a" and any(s[:3] == ("gate_sort", "a", step[1]) for s in engine_of):
+                return first + [s for s in engine_of if s[:3] == ("gate_sort", "a", step[1])]
+            if kind == "gate_sort":
+                return quantisers(2 * step[3]) + quantisers(2 * step[3] + 1) + ([widened[step[2]], widened[step[2] + 1]] if step[1] == "b" else [])
             if kind == "sort_xa":
                 return []
             if kind in ("a", "spread", "warm"):
                 return first
             if kind == "widen" and step[3] >= 0:
-                return [("quantize_x", 2 * step[4] + 1)]
+                return quantisers(2 * step[4]) + quantisers(2 * step[4] + 1)
             if kind == "widen" and step[3] == -2:
                 return ["radicand"]
             if kind in ("widen", "widen_sorted"):
@@ -551,13 +600,13 @@ def tile_projection_moment_gap_s3_kernel(
             if kind == "empty":
                 return [step[1]] + gated(step[1][1] // 2)
             if kind == "quantize_x":
-                return [("empty", ("a", step[1] - step[1] % 2)), ("scale", step[1])]
+                return ([("empty", ("a", step[1] - step[1] % 2))] if step[2] == 0 else []) + ([("scale", step[1])] if step[3] == 3 else [])
             if kind == "group_wa":
-                return [("quantize_x", 1)] if step[1] == 1 else []
+                return quantisers(0) + quantisers(1) if step[1] == 1 else []
             if kind == "quantize_wa":
                 return [s for s in engine_of if s[0] == "group_wa" and s[1] == step[1]]
             if kind == "square":
-                return [("project",) + step[1:], "root"]
+                return [s for s in tensor if s[:3] == ("project",) + step[1:]] + ["root"]
             if kind == "finish_v":
                 return [("hold", 0)] + [("square", r, step[2]) for r in group_rows(step[1])]
             if kind == "quantize_v":
@@ -568,13 +617,25 @@ def tile_projection_moment_gap_s3_kernel(
                 return [("subtract", step[1])]
             return [("scale_gap", step[1])]
 
+        def gate_takes(gate):
+            mates = [s for s in engine_of if s[0] == "gate_sort" and s[3] == gate]
+            users = [("a", s[2]) for s in mates if s[1] == "a"] + [("b", s[2] + i) for s in mates if s[1] == "b" for i in range(2)]
+            for s in engine_of:
+                if s[0] == "widen" and s[3] >= 0 and s[4] == gate:
+                    users = users + [prepared[r] if prepared[r] != s else ("b", r) for r in range(s[1], s[1] + s[2])]
+            return ("slot%d" % (gate % SLOTS), ("gate", gate), users)
+
         def takes(step):
             kind = step[0]
             if kind == "widen":
                 users = [prepared[r] if prepared[r] != step else ("b", r) for r in range(step[1], step[1] + step[2])]
                 if step[3] == -2:
                     return None
-                return ("wide" if step[3] < 0 else "slot%d" % step[3], step, users)
+                if step[3] >= 0:
+                    return gate_takes(step[4])
+                return ("wide", step, users)
+            if kind == "gate_sort":
+                return gate_takes(step[3])
             if kind == "widen_sorted":
                 return ("sorted", step, [("b", step[1])])
             if kind == "subtract":
@@ -587,7 +648,7 @@ def tile_projection_moment_gap_s3_kernel(
                 return ("four_rows" if engine_of[step] == "gpsimd" else "sorted", step, [("store", step[1])])
             if kind in ("empty", "scale"):
                 r = step[1][1] if kind == "empty" else step[1] - step[1] % 2
-                return ("slot%d" % (r // 2 % SLOTS), r, [("quantize_x", r), ("quantize_x", r + 1)])
+                return ("slot%d" % (r // 2 % SLOTS), r, quantisers(r) + quantisers(r + 1))
             if kind == "group_wa":
                 return ("grouped" if step[1] == 0 else "slot0", ("wa", step[1]), [("quantize_wa", step[1])])
             if kind == "finish_v":
@@ -605,7 +666,7 @@ def tile_projection_moment_gap_s3_kernel(
             elif kind == "empty":
                 empty(step[1], copy_of[engine_of[step]])
             elif kind == "project":
-                project(step[1], step[2], where[step])
+                project(step[1], step[2], step[3], where[step])
             elif kind == "moment":
                 moment(step[1], where[step], step[2])
             elif kind == "hold":
@@ -613,7 +674,7 @@ def tile_projection_moment_gap_s3_kernel(
             elif kind == "warm":
                 warm_up(step[2], where[step])
             elif kind == "widen":
-                widen(step[1], step[2], copy_of[engine_of[step]], step[3])
+                widen(step[1], step[2], copy_of[engine_of[step]], step[4] if step[3] >= 0 else step[3])
             elif kind == "group_wa":
                 group_wa(*step[1:], copy_of[engine_of[step]])
             elif kind == "quantize_wa":
@@ -621,7 +682,7 @@ def tile_projection_moment_gap_s3_kernel(
             elif kind == "scale_gap":
                 scale_gap(step[1], engine_of[step] == "gpsimd")
             else:
-                plain = {"scale": scale_xb, "sort": sort_xb, "widen_sorted": widen_sorted, "sort_xa": sort_xa, "quantize_x": quantize_x, "square": square, "finish_v": finish_v,
+                plain = {"scale": scale_xb, "sort": sort_xb, "widen_sorted": widen_sorted, "gate_sort": gate_sort, "sort_xa": sort_xa, "quantize_x": quantize_x, "square": square, "finish_v": finish_v,
                          "quantize_v": quantize_v, "subtract": subtract_target, "store": store}
                 plain[kind](*step[1:])
 

@@ -73,6 +73,8 @@ def tile_projection_moment_gap_s3_kernel(
 
         scale_col = keep.tile([P, 2, PACK], F32, name="scale_col")
         one = keep.tile([P, 1], F32, name="one")
+        first_one = work.tile([P, 1], F32, name="first", bufs=1)
+        threshold = keep.tile([P, 1], F32, name="threshold")
         wa_rows = [four_rows().rearrange("p (j n) -> p j n", j=PACK) for half in range(2)]
         wa_codes = mx_tile("wa_codes", U32, 4, N, MOVING)
         wa_bytes = mx_tile("wa_bytes", U8, 1, N, MOVING_SCALE)
@@ -89,7 +91,7 @@ def tile_projection_moment_gap_s3_kernel(
         ones = keep.tile([P, P], BF16, name="ones")
         target_rows = keep.tile([P, C_TILES, N], BF16, name="target_rows")
         ident = keep.tile([P, P], F32, name="ident")
-        ident_bf16 = keep.tile([P, P], BF16, name="ident_bf16")
+        ident_bf16 = ident[:].bitcast(BF16)[:, 1::2]
         zeros = keep.tile([P, HALF], BF16, name="zeros")
 
         xa_pairs = {}
@@ -126,23 +128,25 @@ def tile_projection_moment_gap_s3_kernel(
 
         nc.vector.memset(zeros[:].bitcast(I32), 0)
         nc.vector.memset(ident[:], 0.0)
-        nc.vector.memset(one[:], 1.0)
-        nc.vector.memset(wb_bytes[:].rearrange("p g n -> p (g n)").bitcast(I32), 0)
         nc.vector.memset(prec_line[:].bitcast(I32), 0)
+        nc.vector.memset(one[:], 1.0)
         nc.vector.memset(ones[:], 1.0)
+        nc.vector.memset(first_one[:], 1.0)
+        nc.vector.memset(threshold[:], -(2.0**-40) * (1 + 2.0**-12))
+        nc.vector.memset(wb_bytes[:].rearrange("p g n -> p (g n)").bitcast(I32), 0)
         make_identity(nc, ident[:], nomemset=True)
         nc.vector.memset(z_bytes[:].rearrange("p g n -> p (g n)").bitcast(I32), 0)
         load_xb(0, 2)
         nc.sync.dma_start(out=omega_bf16[:], in_=omega.rearrange("(g p t) -> p g t", p=P, t=PACK))
         load_xb(2, 2)
         nc.sync.dma_start(out=scale_col[:], in_=xb_scale.rearrange("o (h p j) -> p (o h) j", h=2, j=PACK))
+        nc.sync.dma_start(out=prec_line[0:1, :], in_=prec[HALF:].unsqueeze(0))
         load_wa(0)
         load_xa(0)
         load_xb(4, 2)
-        nc.sync.dma_start(out=prec_line[0:1, :], in_=prec[HALF:].unsqueeze(0))
-        load_scale_bytes(wb_bytes, wb_scales)
-        load_wb(0)
         load_xa(2)
+        load_wb(0)
+        load_scale_bytes(wb_bytes, wb_scales)
         load_wa(1)
         load_xa(4)
         load_xb(6, 2)
@@ -205,7 +209,7 @@ def tile_projection_moment_gap_s3_kernel(
             if gate == -2:
                 tile = work.tile([P, count * KB], BF16, name="first", bufs=1)
             else:
-                tile = gate_tile(gate) if gate >= 0 else work.tile([P, count * KB], BF16, name="wide", bufs=BUFS["wide"])
+                tile = gate_tile(gate) if gate >= 0 or gate == -4 else work.tile([P, count * KB], BF16, name="wide", bufs=BUFS["wide"])
             copy(out=tile[:, : count * KB], in_=xb_codes_in[r][:, : count * KB].bitcast(FP8))
             for i in range(count):
                 xb_rows[r + i] = tile[:, KB * i :]
@@ -226,7 +230,7 @@ def tile_projection_moment_gap_s3_kernel(
             nc.vector.tensor_scalar(
                 out=tile[:].rearrange("p u s m -> p (u s m)").bitcast(BF16).rearrange("p (u m e) -> p m u e", u=2, e=2),
                 in0=xb_codes_in[r][:, :KB].bitcast(FP8).rearrange("p (m u e) -> p m u e", u=2, e=2),
-                scalar1=one[:],
+                scalar1=first_one[:] if r < 2 else one[:],
                 scalar2=None,
                 op0=MULT,
             )
@@ -348,10 +352,13 @@ def tile_projection_moment_gap_s3_kernel(
 
         held = []
 
-        def hold_constants(where):
+        def hold_constants(which, where):
             tile = bank(where, BF16, 2 * HALF)
-            nc.tensor.matmul(out=tile[:, :HALF], lhsT=ones[:], rhs=prec_line[:], start=True, stop=True)
-            nc.tensor.matmul(out=tile[:, HALF : HALF + ROWS], lhsT=ident_bf16[:], rhs=factor[:], start=True, stop=True)
+            if which == 0:
+                nc.tensor.matmul(out=tile[:, :HALF], lhsT=ones[:], rhs=prec_line[:], start=True, stop=True)
+                nc.tensor.matmul(out=tile[:, HALF : HALF + ROWS], lhsT=ident_bf16, rhs=factor[:], start=True, stop=True)
+            else:
+                nc.tensor.matmul(out=tile[:, :HALF], lhsT=ident_bf16, rhs=prec_rows[:, HALF:], start=True, stop=True)
             held.append(tile)
 
         v_grouped = {}
@@ -418,20 +425,17 @@ def tile_projection_moment_gap_s3_kernel(
 
 
         omega_flat = omega_bf16[:].rearrange("p g t -> p (g t)")
-        size, sign, power, inv_power = per_row("size"), per_row("sign"), per_row("power"), work.tile([P, ROWS], F32, name="first", bufs=1)
-        radicand, guess = per_row("radicand"), per_row("guess")
-        spread = {}
+        size, sign, side, boost, power, radicand = [per_row(name) for name in ("size", "sign", "side", "boost", "power", "radicand")]
         small = {
-            "table": ([], lambda: nc.scalar.activation(out=guess[:], in_=zeros[:, :ROWS], func=SQRT)),
+            "table": ([], lambda: nc.scalar.activation(out=root[:], in_=zeros[:, :ROWS], func=SQRT)),
             "size": ([], lambda: nc.scalar.activation(out=size[:], in_=omega_flat, func=ABS)),
             "sign": ([], lambda: nc.scalar.activation(out=sign[:], in_=omega_flat, func=SIGN)),
-            "ident16": ([], lambda: nc.vector.tensor_copy(out=ident_bf16[:], in_=ident[:])),
-            "power": (["size"], lambda: nc.gpsimd.tensor_scalar(out=power[:], in0=size[:], scalar1=2.0**-64, scalar2=2.0**-64, op0=IS_GE, op1=MAX)),
-            "inv_power": (["size"], lambda: nc.vector.tensor_scalar(out=inv_power[:], in0=size[:], scalar1=2.0**-64, scalar2=2.0**64, op0=IS_LT, op1=MULT)),
-            "radicand": (["inv_power"], lambda: nc.vector.scalar_tensor_tensor(out=radicand[:], in0=inv_power[:], scalar=1.0, in1=size[:], op0=MAX, op1=MULT)),
+            "side": (["size"], lambda: nc.scalar.activation(out=side[:], in_=size[:], func=SIGN, bias=threshold[:])),
+            "boost": (["side"], lambda: nc.scalar.activation(out=boost[:], in_=side[:], func=COPY, scale=(1.0 - 2.0**22) / 2, bias=(1.0 + 2.0**22) / 2)),
+            "power": (["side"], lambda: nc.scalar.activation(out=power[:], in_=side[:], func=COPY, scale=(2.0**10 - 2.0**-12) / 2, bias=(2.0**10 + 2.0**-12) / 2)),
+            "radicand": (["boost", "size"], lambda: nc.gpsimd.tensor_tensor(out=radicand[:], in0=size[:], in1=boost[:], op=MULT)),
             "factor": (["power", "sign"], lambda: nc.gpsimd.tensor_tensor(out=factor[:], in0=sign[:], in1=power[:], op=MULT)),
-            "guess": (["radicand", "table"], lambda: nc.scalar.activation(out=guess[:], in_=radicand[:], func=SQRT, scale=2.0**-10)),
-            "root": (["guess"], lambda: nc.scalar.activation(out=root[:], in_=guess[:], func=COPY, scale=32.0)),
+            "root": (["radicand", "table"], lambda: nc.scalar.activation(out=root[:], in_=radicand[:], func=SQRT, scale=2.0**-10)),
         }
         H = HALF
         tiles = [(c0, HALF, ct) for c0 in (0, HALF) for ct in range(C_TILES)][:-SPLIT]
@@ -472,6 +476,8 @@ def tile_projection_moment_gap_s3_kernel(
                     steps.append(("finish_v" if letters in "fF" else "quantize_v", digits[0], 0 if letters in "fv" else H))
                 elif letters == "wd:":
                     steps.append(("widen", digits[0], digits[1], -1, -1))
+                elif letters == "wq:":
+                    steps.append(("widen", digits[0], digits[1], 0, -4))
                 elif letters == "wg:":
                     steps.append(("widen", digits[0], digits[1], -2, -1))
                 elif letters == "wd::":
@@ -490,10 +496,10 @@ def tile_projection_moment_gap_s3_kernel(
                     steps.append(({"sp": "spread", "cs": "copy_scale", "sc": "scale", "so": "sort", "sa": "sort_xa", "qw": "quantize_wa", "hold": "hold"}[letters], digits[0]))
             return steps
 
-        tensor = parse("""w5 b0@0 w1 b1@1 w2 b2@2 a0@3 b3@4 w2 hold0 a2@5 p0@6 p1@3 a4 b4 b5 p2 p3 P0 P1 a6 b6 b7 P2 P3 p4 p5 a8 b8 b9 p6 p7 P4 P5 a10 b10 b11 P6 P7 p8 p9 a12 b12 b13 p10 p11 P8 P9 a14 b14 b15 p12 p13 P10 P11 p14 p15 P12 P13 P14 P15 m0 m1 m2 m3 m4 m5 m6 m7 m8 m9""")
-        vector = parse("""ws0 inv_power ws1 radicand sc0 sc1 il0:352:512 ident16 qw0 q0 q1 sc2 sc3 q2 qw1 q3 sc4 sc5 q4 q5 f0 sc6 sc7 ws9 q6 v0 q7 F0 sc8 sc9 q8 V0 q9 f1 sc10 sc11 q10 v1 q11 F1 sc12 sc13 q12 V1 q13 sc14 sc15 q14 q15 f2 v2 F2 f3 v3 V2 sub0 F3 sub1 V3 sub2 sub3 sub4 mul4 sub5 sub6 mul5 sub7 sub8 mul7 sub9 mul8 mul9""")
-        scalar = parse("""table size sign wd2:1 guess il0:0:352 root ea0 wd4:1 wd5:1 ea2 il1:0:256 ea4 s0 s1 s2 s3 wd7:1 ea6 S0 S1 so8:1 S2 S3 s4 ea8 s5 sa10 s6 s7 S4 ea10 S5 sa12 S6 S7 s8 ea12 s9 sa14 s10 so14:1 s11 S8 ea14 S9 s12 s13 S10 S11 s14 s15 S12 S13 S14 S15""")
-        gpsimd = parse("""wg3:1 power factor il1:256:512 wd6:1:1 wd8:1:2 ga8:2 wd10:2:3 wd12:2:4 wd14:2:5 mul0 mul1 mul2 mul3 mul6""")
+        tensor = parse("""w5 b0@0 w1 b1@1 w2 b2@2 a0@3 w1 b3@4 a2@5 hold0 p0@6 p1@3 a4 b4 b5 p2 p3 P0 P1 a6 b6 b7 P2 P3 p4 p5 a8 b8 b9 p6 p7 P4 P5 a10 b10 b11 P6 P7 p8 p9 a12 b12 b13 p10 p11 P8 P9 a14 b14 b15 p12 p13 P10 P11 p14 p15 P12 P13 P14 P15 m0 m1 m2 m3 m4 m5 m6 m7 m8 m9""")
+        vector = parse("""ws0 ws1 sc0 sc1 il0:336:512 qw0 q0 q1 sc2 sc3 q2 q3 qw1 sc4 sc5 ws7 q4 q5 f0 sc6 sc7 ws9 q6 v0 q7 F0 sc8 sc9 q8 V0 q9 f1 sc10 sc11 q10 v1 q11 F1 sc12 sc13 q12 q13 sc14 sc15 q14 q15 f2 V1 v2 F2 f3 v3 V2 sub0 F3 sub1 V3 sub2 sub3 sub4 mul4 sub5 sub6 mul5 sub7 sub8 mul7 sub9 mul8 mul9""")
+        scalar = parse("""table size sign side wd2:1 boost power il0:0:336 root ea0 wd4:1 ea2 wd5:1 il1:0:256 ea4 s0 s1 sa6 s2 s3 ea6 S0 S1 so8:1 S2 S3 s4 ea8 s5 sa10 s6 s7 S4 ea10 S5 sa12 S6 S7 s8 ea12 s9 sa14 s10 s11 S8 ea14 S9 s12 s13 S10 S11 s14 s15 S12 S13 S14 S15""")
+        gpsimd = parse("""wg3:1 radicand factor il1:256:512 wq6:1 wd8:1:2 ga8:2 wd10:2:3 wd12:2:4 wd14:2:5 mul0 mul1 mul2 mul3 mul6""")
         sync = parse("""st0 st1 st2 st4 st3 st5 st6 st7 st8 st9""")
         free = [0, 1, 2, 3, 4, 5, 6]
         banks = []
@@ -502,7 +508,9 @@ def tile_projection_moment_gap_s3_kernel(
         first_product = max(forced) + 1
         last_turn = max(i for i, step in enumerate(tensor) if step[0] in ("a", "b"))
         for place, step in enumerate(tensor):
-            if step[0] == "hold" or (step[0] == "warm" and tensor.index(step) < tensor.index(("hold", 0))):
+            if step == ("hold", 1):
+                banks.append(free.pop(0))
+            elif step[0] == "hold" or (step[0] == "warm" and tensor.index(step) < tensor.index(("hold", 0))):
                 banks.append(HELD_BANK)
             elif step[0] == "moment" and step[1] in first_bank:
                 banks.append(first_bank[step[1]])
@@ -561,7 +569,7 @@ def tile_projection_moment_gap_s3_kernel(
             return range(PACK * g, PACK * (g + 1))
 
         def gated(pair):
-            return [s for s in engine_of if s[0] == "widen" and s[3] >= 0 and s[4] + SLOTS == pair] + [s for s in engine_of if s[0] == "gate_sort" and s[3] + SLOTS == pair]
+            return [s for s in engine_of if s[0] == "widen" and s[3] >= 0 and (SLOTS if s[4] == -4 else s[4] + SLOTS) == pair] + [s for s in engine_of if s[0] == "gate_sort" and s[3] + SLOTS == pair]
 
         def needs(step):
             kind = step[0]
@@ -576,7 +584,7 @@ def tile_projection_moment_gap_s3_kernel(
             if kind == "moment":
                 return first + [("quantize_v", g, step[1][0] - step[1][0] % HALF) for g in step[2]]
             if kind == "hold":
-                return first + ["ident16", "factor"]
+                return first + ["factor"]
             if kind == "a" and ("sort_xa", step[1]) in engine_of:
                 return first + [("sort_xa", step[1])]
             if kind == "a" and any(s[:3] == ("gate_sort", "a", step[1]) for s in engine_of):
@@ -587,10 +595,12 @@ def tile_projection_moment_gap_s3_kernel(
                 return []
             if kind in ("a", "spread", "warm"):
                 return first
+            if kind == "widen" and step[4] == -4:
+                return [("quantize_wa", 1)]
             if kind == "widen" and step[3] >= 0:
                 return quantisers(2 * step[4]) + quantisers(2 * step[4] + 1)
             if kind == "widen" and step[3] == -2:
-                return ["radicand"]
+                return [("widen_sorted", 0), ("widen_sorted", 1)]
             if kind in ("widen", "widen_sorted"):
                 return []
             if kind == "scale":
@@ -614,7 +624,7 @@ def tile_projection_moment_gap_s3_kernel(
             if kind == "subtract":
                 return [s for s in tensor if s[0] == "moment" and s[1] == step[1]]
             if kind == "scale_gap":
-                return [("subtract", step[1])]
+                return [("subtract", step[1])] + ([("hold", 0)] if engine_of[step] == "vector" else [])
             return [("scale_gap", step[1])]
 
         def gate_takes(gate):
@@ -670,7 +680,7 @@ def tile_projection_moment_gap_s3_kernel(
             elif kind == "moment":
                 moment(step[1], where[step], step[2])
             elif kind == "hold":
-                hold_constants(where[step])
+                hold_constants(step[1], where[step])
             elif kind == "warm":
                 warm_up(step[2], where[step])
             elif kind == "widen":

@@ -12,10 +12,6 @@ FP8 = mybir.dt.float8_e4m3fn
 FP8X4 = mybir.dt.float8_e4m3fn_x4
 FP4X4 = mybir.dt.float4_e2m1fn_x4
 MULT = mybir.AluOpType.mult
-ADD = mybir.AluOpType.add
-MAX = mybir.AluOpType.max
-IS_GE = mybir.AluOpType.is_ge
-IS_LT = mybir.AluOpType.is_lt
 SUBTRACT = mybir.AluOpType.subtract
 SQUARE = mybir.ActivationFunctionType.Square
 SQRT = mybir.ActivationFunctionType.Sqrt
@@ -33,17 +29,14 @@ PASSES = (KA + KB) // K_PASS
 HALF = 512
 QUARTER = HALF // 2
 C_TILES = C // P
-TURN_BANKS = (0, 1, 2)
-PRODUCT_BANKS = (3, 4, 5, 6)
 HELD_BANK = 7
+STAGES = 4
+
+SCALAR_WA_COLUMNS = (320, 256)
+
+DOWN, BOOST, SMALL = 2.0**-10, 2.0**22, 2.0**-40 * (1 + 2.0**-12)
 
 MOVING, MOVING_SCALE, STATIONARY, STATIONARY_SCALE = 0, 64, 128, 192
-
-BUFS = {"wide": 6, "sorted": 5, "grouped": 3, "four_rows": 8}
-SLOTS = 4
-TURN_RING = (0, 1, 2)
-PRODUCT_RING = (4, 5, 6, 3)
-SPLIT = 2
 
 FLOPS = 2 * M * N * (KA + KB) + 2 * C * N * M
 
@@ -68,14 +61,29 @@ def tile_projection_moment_gap_s3_kernel(
         def per_row(name, dtype=F32):
             return keep.tile([P, ROWS], dtype, name=name)
 
-        def four_rows():
-            return work.tile([P, PACK * HALF], BF16, name="four_rows", bufs=8)[:]
+        def large_tile(dtype, width):
+            return work.tile([P, width], dtype, name="large", bufs=8)[:]
+
+        def plain_tile(dtype, width):
+            return work.tile([P, width], dtype, name="plain", bufs=6)[:]
+
+        def sorted_tile(width=HALF):
+            return work.tile([P, width], F32, name="sorted", bufs=5)[:]
+
+        def grouped_tile():
+            return work.tile([P, PACK * HALF], BF16, name="grouped", bufs=3, align_bytes=64)[:]
+
+        def stage_tile(i):
+            return work.tile([P, 2 * PASSES * K_PASS], BF16, name="stage%d" % i, bufs=1, align_bytes=64)[:]
+
+        def opening_tile(dtype, width):
+            return work.tile([P, width], dtype, name="opening", bufs=1)[:]
 
         scale_col = keep.tile([P, 2, PACK], F32, name="scale_col")
         one = keep.tile([P, 1], F32, name="one")
-        first_one = work.tile([P, 1], F32, name="first", bufs=1)
-        threshold = keep.tile([P, 1], F32, name="threshold")
-        wa_rows = [four_rows().rearrange("p (j n) -> p j n", j=PACK) for half in range(2)]
+        opening_one = opening_tile(F32, 1)
+        minus_small = keep.tile([P, 1], F32, name="minus_small")
+        wa_rows = [large_tile(BF16, PACK * HALF).rearrange("p (t n) -> p t n", t=PACK) for half in range(2)]
         wa_codes = mx_tile("wa_codes", U32, 4, N, MOVING)
         wa_bytes = mx_tile("wa_bytes", U8, 1, N, MOVING_SCALE)
         wb_tiles = [
@@ -85,17 +93,16 @@ def tile_projection_moment_gap_s3_kernel(
         wb_bytes = mx_tile("wb_bytes", U8, 1, 2 * N, MOVING_SCALE).rearrange("p (g n) -> p g n", g=2)
         z_tile = mx_tile("z_tile", U8, 1, GROUPS * 2 * C, STATIONARY).rearrange("p (g n) -> p g n", g=GROUPS)
         z_bytes = mx_tile("z_bytes", U8, 1, GROUPS * C, STATIONARY_SCALE).rearrange("p (g n) -> p g n", g=GROUPS)
-        omega_bf16 = keep.tile([P, GROUPS, PACK], BF16, name="omega_bf16")
-        prec_rows = keep.tile([P, N], BF16, name="prec_rows")
+        omega_rows = keep.tile([P, GROUPS, PACK], BF16, name="omega_rows")
+        prec_rows = keep.tile([P, HALF + QUARTER], BF16, name="prec_rows")
         prec_line = keep.tile([P, HALF], BF16, name="prec_line")
         ones = keep.tile([P, P], BF16, name="ones")
         target_rows = keep.tile([P, C_TILES, N], BF16, name="target_rows")
         ident = keep.tile([P, P], F32, name="ident")
         ident_bf16 = ident[:].bitcast(BF16)[:, 1::2]
         zeros = keep.tile([P, HALF], BF16, name="zeros")
-
+        xb_codes = keep.tile([P, ROWS * KB], U8, name="xb_codes")
         xa_pairs = {}
-        xb_codes_in = {}
 
         def sample_rows(src, r, count):
             g, t = divmod(r, PACK)
@@ -105,41 +112,39 @@ def tile_projection_moment_gap_s3_kernel(
             xa_pairs[r] = keep.tile([P, 2, KA], BF16, name="xa_pair%d" % r)
             nc.sync.dma_start(out=xa_pairs[r][:], in_=sample_rows(xa, r, 2))
 
-        xb_codes = keep.tile([P, ROWS * KB], U8, name="xb_codes")
-
         def load_xb(r, count):
             rows = xb_codes[:, KB * r : KB * (r + count)].rearrange("p (t k) -> p t k", t=count)
             nc.sync.dma_start(out=rows, in_=sample_rows(xb_bytes, r, count))
-            for i in range(count):
-                xb_codes_in[r + i] = xb_codes[:, KB * (r + i) :]
 
         def load_wa(half):
-            rows = wa.rearrange("(p j) n -> p j n", j=PACK)
+            rows = wa.rearrange("(p t) n -> p t n", t=PACK)
             nc.sync.dma_start(out=wa_rows[half], in_=rows[:, :, HALF * half : HALF * (half + 1)])
 
         def load_wb(half):
-            words = wb_words.rearrange("g p n -> p g n")
-            nc.sync.dma_start(out=wb_tiles[half][:], in_=words[:, :, 2 * HALF * half : 2 * HALF * (half + 1)])
+            wb_view = wb_words.rearrange("g p n -> p g n")
+            nc.sync.dma_start(out=wb_tiles[half][:], in_=wb_view[:, :, 2 * HALF * half : 2 * HALF * (half + 1)])
 
-        def load_scale_bytes(plane, scale_bytes):
-            rows = scale_bytes.rearrange("g (q r) n -> r q g n", r=4)
-            for r in range(4):
-                nc.sync.dma_start(out=plane[r:P:32].bitcast(I32), in_=rows[r].bitcast(I32))
+        def load_scale_bytes(tile, scale_bytes):
+            rows = scale_bytes.rearrange("g (q i) n -> i q g n", i=4)
+            for i in range(4):
+                nc.sync.dma_start(out=tile[i:P:32].bitcast(I32), in_=rows[i].bitcast(I32))
 
         nc.vector.memset(zeros[:].bitcast(I32), 0)
         nc.vector.memset(ident[:], 0.0)
         nc.vector.memset(prec_line[:].bitcast(I32), 0)
         nc.vector.memset(one[:], 1.0)
         nc.vector.memset(ones[:], 1.0)
-        nc.vector.memset(first_one[:], 1.0)
-        nc.vector.memset(threshold[:], -(2.0**-40) * (1 + 2.0**-12))
+        nc.vector.memset(opening_one, 1.0)
+        nc.vector.memset(minus_small[:], -SMALL)
         nc.vector.memset(wb_bytes[:].rearrange("p g n -> p (g n)").bitcast(I32), 0)
         make_identity(nc, ident[:], nomemset=True)
         nc.vector.memset(z_bytes[:].rearrange("p g n -> p (g n)").bitcast(I32), 0)
-        load_xb(0, 2)
-        nc.sync.dma_start(out=omega_bf16[:], in_=omega.rearrange("(g p t) -> p g t", p=P, t=PACK))
+
+        load_xb(0, 1)
+        load_xb(1, 1)
+        nc.sync.dma_start(out=omega_rows[:], in_=omega.rearrange("(g p t) -> p g t", p=P, t=PACK))
         load_xb(2, 2)
-        nc.sync.dma_start(out=scale_col[:], in_=xb_scale.rearrange("o (h p j) -> p (o h) j", h=2, j=PACK))
+        nc.sync.dma_start(out=scale_col[:], in_=xb_scale.rearrange("o (i p t) -> p (o i) t", i=2, t=PACK))
         nc.sync.dma_start(out=prec_line[0:1, :], in_=prec[HALF:].unsqueeze(0))
         load_wa(0)
         load_xa(0)
@@ -155,243 +160,180 @@ def tile_projection_moment_gap_s3_kernel(
         load_xb(8, 4)
         load_xa(8)
         load_xb(12, 4)
-        load_xa(10)
-        load_xa(12)
-        load_xa(14)
+        for r in (10, 12, 14):
+            load_xa(r)
         load_scale_bytes(z_bytes, z_scales)
         nc.sync.dma_start(out=z_tile[:], in_=z_words.rearrange("g p n -> p g n"))
         nc.sync.dma_start(out=target_rows[:], in_=target.rearrange("(ct c) n -> c ct n", c=P))
-        nc.sync.dma_start(out=prec_rows[:], in_=prec.partition_broadcast(P))
+        nc.sync.dma_start(out=prec_rows[:], in_=prec[: HALF + QUARTER].partition_broadcast(P))
 
-        def warm_up(count, where):
-            tile = bank(where)
+        def warm_up(count):
+            tile = bank(HELD_BANK)
             for i in range(count):
                 nc.tensor.matmul(out=tile[:], lhsT=zeros[:, :P], rhs=zeros[:], start=True, stop=True)
 
-        def grouped_tile():
-            return work.tile([P, PACK * HALF], BF16, name="grouped", bufs=BUFS["grouped"], align_bytes=64)
-
-        wa_grouped = {}
-
-        def group_wa(half, c0, c1, copy):
-            if half not in wa_grouped:
-                wa_grouped[half] = grouped_tile() if half == 0 else slot(0)[:, : PACK * HALF]
+        def group_wa(half, grouped, c0, c1, copy):
             copy(
-                out=wa_grouped[half][:, PACK * c0 : PACK * c1].rearrange("p (c i j) -> p c j i", i=4, j=PACK),
-                in_=wa_rows[half][:, :, c0:c1].rearrange("p j (c i) -> p c j i", i=4),
+                out=grouped[:, PACK * c0 : PACK * c1].rearrange("p (c i t) -> p c t i", i=4, t=PACK),
+                in_=wa_rows[half][:, :, c0:c1].rearrange("p t (c i) -> p c t i", i=4),
             )
 
         def quantize_wa(half, grouped):
             cols = slice(HALF * half, HALF * (half + 1))
-            nc.vector.quantize_mx(out=wa_codes[:, cols].bitcast(FP8X4), scales=wa_bytes[:, cols], in_=grouped[:])
+            nc.vector.quantize_mx(out=wa_codes[:, cols].bitcast(FP8X4), scales=wa_bytes[:, cols], in_=grouped)
 
         words = {}
 
-        def every_second_word(r, s, values):
+        def words_as_they_lie(r, s, values):
             words[r, s] = [values.bitcast(F32)[:, u::2] for u in range(2)]
 
         for r in range(ROWS):
-            every_second_word(r, 0, xa_pairs[r - r % 2][:, r % 2, :])
+            words_as_they_lie(r, 0, xa_pairs[r - r % 2][:, r % 2, :])
 
         xb_rows = {}
 
-        def slot(i):
-            return work.tile([P, 2 * PASSES * K_PASS], BF16, name="slot%d" % i, bufs=1, align_bytes=64)
+        def xb_values(r, count):
+            return xb_codes[:, KB * r : KB * (r + count)].bitcast(FP8)
 
-        gate_tiles = {}
-
-        def gate_tile(gate):
-            if gate not in gate_tiles:
-                gate_tiles[gate] = slot(gate % SLOTS)
-            return gate_tiles[gate]
-
-        def widen(r, count, copy, gate):
-            if gate == -2:
-                tile = work.tile([P, count * KB], BF16, name="first", bufs=1)
-            else:
-                tile = gate_tile(gate) if gate >= 0 or gate == -4 else work.tile([P, count * KB], BF16, name="wide", bufs=BUFS["wide"])
-            copy(out=tile[:, : count * KB], in_=xb_codes_in[r][:, : count * KB].bitcast(FP8))
+        def widen(r, count, tile, copy):
+            copy(out=tile[:, : count * KB], in_=xb_values(r, count))
             for i in range(count):
-                xb_rows[r + i] = tile[:, KB * i :]
+                xb_rows[r + i] = tile[:, KB * i : KB * (i + 1)]
                 for s in range(1, PASSES):
-                    every_second_word(r + i, s, xb_rows[r + i][:, K_PASS * (s - 1) : K_PASS * s])
+                    words_as_they_lie(r + i, s, xb_rows[r + i][:, K_PASS * (s - 1) : K_PASS * s])
 
-        def sorted_words(r, count):
-            tile = work.tile([P, 2 * count, 2, P], F32, name="sorted", bufs=BUFS["sorted"])
-            for i in range(count):
-                for s in range(1, PASSES):
-                    words[r + i, s] = [tile[:, 2 * i + s - 1, u, :] for u in range(2)]
-            return tile
-
-        def widen_sorted(r):
-            tile = work.tile([P, 2, 2, P], F32, name="sorted", bufs=BUFS["sorted"])
-            for s in range(1, PASSES):
-                words[r, s] = [tile[:, u, s - 1, :] for u in range(2)]
+        def widen_sorted(r, unit):
+            tile = sorted_tile()
             nc.vector.tensor_scalar(
-                out=tile[:].rearrange("p u s m -> p (u s m)").bitcast(BF16).rearrange("p (u m e) -> p m u e", u=2, e=2),
-                in0=xb_codes_in[r][:, :KB].bitcast(FP8).rearrange("p (m u e) -> p m u e", u=2, e=2),
-                scalar1=first_one[:] if r < 2 else one[:],
+                out=tile.bitcast(BF16).rearrange("p (u m e) -> p m u e", u=2, e=2),
+                in0=xb_values(r, 1).rearrange("p (m u e) -> p m u e", u=2, e=2),
+                scalar1=unit,
                 scalar2=None,
                 op0=MULT,
             )
+            for s in range(1, PASSES):
+                words[r, s] = [tile[:, P * (2 * u + s - 1) : P * (2 * u + s)] for u in range(2)]
 
-        def sort_xb(r, count):
-            tile = sorted_words(r, count)
-            copy_of[engine_of["sort", r, count]](
-                out=tile[:].rearrange("p s u (c i) -> p s c u i", i=4),
-                in_=xb_rows[r][:, : count * KB].bitcast(F32).rearrange("p (s c i u) -> p s c u i", s=2 * count, i=4, u=2),
+        def parts_of(operand, r):
+            return [(r, 0), (r + 1, 0)] if operand == "xa" else [(r, 1), (r, 2)]
+
+        def sort_words(operand, r, tile, copy):
+            values = xa_pairs[r][:].rearrange("p i k -> p (i k)") if operand == "xa" else xb_rows[r]
+            copy(
+                out=tile.rearrange("p (i u c j) -> p i c u j", i=2, u=2, j=4),
+                in_=values.bitcast(F32).rearrange("p (i c j u) -> p i c u j", i=2, j=4, u=2),
             )
+            for i, part in enumerate(parts_of(operand, r)):
+                words[part] = [tile[:, P * (2 * i + u) : P * (2 * i + u + 1)] for u in range(2)]
 
-        def sort_xa(r):
-            tile = work.tile([P, 2, 2, P], F32, name="sorted", bufs=BUFS["sorted"])
-            copy_of[engine_of["sort_xa", r]](
-                out=tile[:].rearrange("p s u (c i) -> p s c u i", i=4),
-                in_=xa_pairs[r][:].rearrange("p s k -> p (s k)").bitcast(F32).rearrange("p (s c i u) -> p s c u i", s=2, i=4, u=2),
-            )
-            for i in range(2):
-                words[r + i, 0] = [tile[:, i, u, :] for u in range(2)]
-
-        def gate_sort(kind, r, gate):
-            count = 4 if kind == "b" else 2
-            first = 0 if kind == "b" else 4 * 2 * P
-            tile = gate_tile(gate)[:].bitcast(F32)[:, first : first + count * 2 * P].rearrange("p (s u m) -> p s u m", s=count, u=2)
-            source = xb_rows[r][:, : 2 * KB] if kind == "b" else xa_pairs[r][:].rearrange("p s k -> p (s k)")
-            nc.gpsimd.tensor_copy(
-                out=tile.rearrange("p s u (c i) -> p s c u i", i=4),
-                in_=source.bitcast(F32).rearrange("p (s c i u) -> p s c u i", s=count, i=4, u=2),
-            )
-            for i in range(2):
-                for s in ((1, 2) if kind == "b" else (0,)):
-                    words[r + i, s] = [tile[:, 2 * i + s - 1 if kind == "b" else i, u, :] for u in range(2)]
-
-        x_grouped = {}
         turned = {}
 
-        def pieces_of(step):
-            kind, r = step
-            return [(r, 0), (r + 1, 0)] if kind == "a" else [(r, 1), (r, 2)]
-
-        def turn(step, where):
-            turned[step] = bank(where)
-            for i, piece in enumerate(pieces_of(step)):
+        def turn(operand, r, where):
+            tile = bank(where)
+            turned[operand, r] = tile
+            for i, part in enumerate(parts_of(operand, r)):
                 for u in range(2):
-                    nc.tensor.transpose(turned[step][:, P * (2 * u + i) : P * (2 * u + i + 1)], words[piece][u], ident[:])
+                    nc.tensor.transpose(tile[:, P * (2 * u + i) : P * (2 * u + i + 1)], words[part][u], ident[:])
 
-        def open_pair(pair):
-            if pair not in x_grouped:
-                x_grouped[pair] = slot(pair % SLOTS)[:].rearrange("p (s k) -> p s k", k=K_PASS)
+        x_grouped = {}
+
+        def grouped_pair(r):
+            if r // 2 not in x_grouped:
+                x_grouped[r // 2] = stage_tile(r // 2 % STAGES).rearrange("p (s k) -> p s k", k=K_PASS)
+            return x_grouped[r // 2]
+
+        def empty_xa(r):
+            nc.scalar.copy(
+                out=grouped_pair(r)[:, 0 : PASSES + 1 : PASSES, :].bitcast(F32).rearrange("p i (m u) -> p i m u", u=2),
+                in_=turned["xa", r][:].rearrange("p (u i m) -> p i m u", i=2, u=2),
+            )
 
         def scale_xb(r):
-            open_pair(r // 2)
             first = PASSES * (r % 2) + 1
             nc.vector.tensor_tensor(
-                out=x_grouped[r // 2][:, first : first + 2, :].rearrange("p i (m u e) -> p i m u e", u=2, e=2),
-                in0=turned["b", r][:].bitcast(BF16).rearrange("p (u i m e) -> p i m u e", u=2, i=2, e=2),
+                out=grouped_pair(r)[:, first : first + 2, :].rearrange("p i (m u e) -> p i m u e", u=2, e=2),
+                in0=turned["xb", r][:].bitcast(BF16).rearrange("p (u i m e) -> p i m u e", u=2, i=2, e=2),
                 in1=scale_col[:].rearrange("p i (u e) -> p i u e", u=2).unsqueeze(2).to_broadcast([P, 2, P, 2, 2]),
                 op=MULT,
             )
 
-        def empty(step, copy):
-            pair = step[1] // 2
-            open_pair(pair)
-            first, second = [PASSES * (r % 2) + s for r, s in pieces_of(step)]
-            grouped = x_grouped[pair][:, first : second + 1 : second - first, :]
-            copy(
-                out=grouped.bitcast(F32).rearrange("p i (m u) -> p i m u", u=2),
-                in_=turned[step][:].rearrange("p (u i m) -> p i m u", i=2, u=2),
-            )
-
         x_codes = {}
 
-        def quantize_x(r, s0, s1):
-            if r not in x_codes:
-                both = mx_tile("x_codes%d" % r, U32, 4, PASSES * P + PASSES * P // PACK, STATIONARY)
-                x_codes[r] = (both[:, : PASSES * P], both[:, PASSES * P :].bitcast(U8))
-            codes, scale_bytes = x_codes[r]
+        def quantize_x(r):
+            both = mx_tile("x_codes%d" % r, U32, 4, PASSES * P + PASSES * P // PACK, STATIONARY)
+            codes, scale_bytes = both[:, : PASSES * P], both[:, PASSES * P :].bitcast(U8)
             first = PASSES * (r % 2)
             nc.vector.quantize_mx(
-                out=codes[:, P * s0 : P * s1].bitcast(FP8X4),
-                scales=scale_bytes[:, P * s0 : P * s1],
-                in_=x_grouped[r // 2][:, first + s0 : first + s1, :].rearrange("p s k -> p (s k)"),
+                out=codes.bitcast(FP8X4),
+                scales=scale_bytes,
+                in_=x_grouped[r // 2][:, first : first + PASSES, :].rearrange("p s k -> p (s k)"),
             )
-
-        root, factor = per_row("root"), per_row("factor", BF16)
-        squares = {}
+            x_codes[r] = (codes, scale_bytes)
 
         products = {}
 
-        def project(r, c0, passes, where):
-            if (r, c0) not in products:
-                products[r, c0] = bank(where)
-            tile = products[r, c0]
-            cols = slice(c0, c0 + HALF)
+        def project(r, half, where):
+            tile = bank(where)
+            products[r, half] = tile
+            cols = slice(HALF * half, HALF * (half + 1))
             codes, scale_bytes = x_codes[r]
-            for s in passes:
+            for s in range(PASSES):
                 if s == 0:
                     rhs, rhs_scale = wa_codes[:, cols].bitcast(FP8X4), wa_bytes[:, cols]
                 else:
-                    rhs = wb_tiles[c0 // HALF][:, s - 1, :].bitcast(FP4X4)
-                    rhs_scale = wb_bytes[:, s - 1, cols]
+                    rhs, rhs_scale = wb_tiles[half][:, s - 1, :].bitcast(FP4X4), wb_bytes[:, s - 1, cols]
                 nc.tensor.matmul_mx(
                     out=tile[:],
                     lhsT=codes[:, P * s : P * (s + 1)].bitcast(FP8X4),
                     lhsT_scale=scale_bytes[:, P * s : P * (s + 1)],
                     rhs=rhs,
                     rhs_scale=rhs_scale,
-                    start=(s == (0 if len(passes) == PASSES else 1)),
-                    stop=(s == (PASSES - 1 if len(passes) == PASSES else 0)),
+                    start=(s == 0),
+                    stop=(s == PASSES - 1),
                 )
 
-        def square(r, c0):
+        root, factor = per_row("root"), per_row("factor", BF16)
+        squares = {}
+
+        def square(r, half):
             g, t = divmod(r, PACK)
-            tile = products[r, c0]
-            if (g, c0) not in squares:
-                squares[g, c0] = four_rows()
-            slots = squares[g, c0].rearrange("p (a n e) -> p a n e", a=2, e=2)
-            nc.scalar.activation(out=slots[:, t // 2, :, t % 2], in_=tile[:], func=SQUARE, scale=root[:, r : r + 1])
-
-        held = []
-
-        def hold_constants(which, where):
-            tile = bank(where, BF16, 2 * HALF)
-            if which == 0:
-                nc.tensor.matmul(out=tile[:, :HALF], lhsT=ones[:], rhs=prec_line[:], start=True, stop=True)
-                nc.tensor.matmul(out=tile[:, HALF : HALF + ROWS], lhsT=ident_bf16, rhs=factor[:], start=True, stop=True)
-            else:
-                nc.tensor.matmul(out=tile[:, :HALF], lhsT=ident_bf16, rhs=prec_rows[:, HALF:], start=True, stop=True)
-            held.append(tile)
+            if (g, half) not in squares:
+                squares[g, half] = large_tile(BF16, PACK * HALF).rearrange("p (a n e) -> p a n e", a=2, e=2)
+            nc.scalar.activation(
+                out=squares[g, half][:, t // 2, :, t % 2], in_=products[r, half][:], func=SQUARE, scale=root[:, r : r + 1]
+            )
 
         v_grouped = {}
         v_codes = {}
 
-        def finish_v(g, c0):
-            v_grouped[g, c0] = grouped_tile()
-            factors = held[0][:, HALF + PACK * g : HALF + PACK * (g + 1)].rearrange("p (a e) -> p a e", a=2)
+        def finish_v(g, half):
+            v_grouped[g, half] = grouped_tile()
+            factors = held[:, HALF + PACK * g : HALF + PACK * (g + 1)].rearrange("p (a e) -> p a e", a=2)
             nc.vector.tensor_tensor(
-                out=v_grouped[g, c0][:].rearrange("p (n a e) -> p n a e", a=2, e=2),
-                in0=squares[g, c0].rearrange("p (a n e) -> p n a e", a=2, e=2),
+                out=v_grouped[g, half].rearrange("p (n a e) -> p n a e", a=2, e=2),
+                in0=squares[g, half].rearrange("p a n e -> p n a e"),
                 in1=factors.unsqueeze(1).to_broadcast([P, HALF, 2, 2]),
                 op=MULT,
             )
 
-        def quantize_v(g, c0):
-            codes = mx_tile("v_codes%d_%d" % (g, c0), U32, 4, HALF, MOVING)
-            scale_bytes = mx_tile("v_bytes%d_%d" % (g, c0), U8, 1, HALF, MOVING_SCALE)
-            nc.vector.quantize_mx(out=codes[:].bitcast(FP8X4), scales=scale_bytes[:], in_=v_grouped[g, c0][:])
-            v_codes[g, c0] = (codes, scale_bytes)
+        def quantize_v(g, half):
+            codes = mx_tile("v_codes%d_%d" % (g, half), U32, 4, HALF, MOVING)
+            scale_bytes = mx_tile("v_bytes%d_%d" % (g, half), U8, 1, HALF, MOVING_SCALE)
+            nc.vector.quantize_mx(out=codes.bitcast(FP8X4), scales=scale_bytes, in_=v_grouped[g, half])
+            v_codes[g, half] = (codes, scale_bytes)
 
-        sums = {}
-        gaps = {}
+        tiles = [(c0, HALF, ct) for c0 in (0, HALF) for ct in range(C_TILES)][:-2]
+        tiles = tiles + [(c0, QUARTER, ct) for ct in (C_TILES - 2, C_TILES - 1) for c0 in (HALF, HALF + QUARTER)]
+        sums, gaps, results = {}, {}, {}
 
-        def moment(tile, where, groups=range(GROUPS)):
-            c0, width, ct = tile
-            if tile not in sums:
-                sums[tile] = bank(where)
+        def moment(i, where):
+            c0, width, ct = tiles[i]
+            sums[i] = bank(where)
             cols = slice(c0 % HALF, c0 % HALF + width)
-            for g in groups:
-                codes, scale_bytes = v_codes[g, c0 - c0 % HALF]
+            for g in range(GROUPS):
+                codes, scale_bytes = v_codes[g, c0 // HALF]
                 nc.tensor.matmul_mx(
-                    out=sums[tile][:, :width],
+                    out=sums[i][:, :width],
                     lhsT=z_tile[:, g, 2 * P * ct : 2 * P * (ct + 1)].bitcast(FP4X4),
                     lhsT_scale=z_bytes[:, g, P * ct : P * (ct + 1)],
                     rhs=codes[:, cols].bitcast(FP8X4),
@@ -400,323 +342,214 @@ def tile_projection_moment_gap_s3_kernel(
                     stop=(g == GROUPS - 1),
                 )
 
-        def subtract_target(tile):
-            c0, width, ct = tile
-            gaps[tile] = work.tile([P, width], F32, name="wide", bufs=BUFS["wide"])
+        def subtract_target(i):
+            c0, width, ct = tiles[i]
+            gaps[i] = plain_tile(F32, width)
             nc.vector.tensor_tensor(
-                out=gaps[tile][:], in0=sums[tile][:, :width], in1=target_rows[:, ct, c0 : c0 + width], op=SUBTRACT
+                out=gaps[i], in0=sums[i][:, :width], in1=target_rows[:, ct, c0 : c0 + width], op=SUBTRACT
             )
 
-        results = {}
+        def scale_on_gpsimd(i):
+            c0, width, ct = tiles[i]
+            results[i] = large_tile(F32, width)
+            nc.gpsimd.tensor_tensor(out=results[i], in0=gaps[i], in1=prec_rows[:, c0 : c0 + width], op=MULT)
 
-        def scale_gap(tile, on_gpsimd):
-            c0, width, ct = tile
-            if on_gpsimd:
-                engine, prec_cols = nc.gpsimd, prec_rows[:, c0 : c0 + width]
-            else:
-                engine, prec_cols = nc.vector, held[0][:, c0 - HALF : c0 - HALF + width]
-            name = "four_rows" if on_gpsimd else "sorted"
-            results[tile] = work.tile([P, width], F32, name=name, bufs=BUFS[name])
-            engine.tensor_tensor(out=results[tile][:], in0=gaps[tile][:], in1=prec_cols, op=MULT)
+        def scale_on_vector(i):
+            c0, width, ct = tiles[i]
+            results[i] = sorted_tile(width)
+            nc.vector.tensor_tensor(out=results[i], in0=gaps[i], in1=held[:, c0 - HALF : c0 - HALF + width], op=MULT)
 
-        def store(tile):
-            c0, width, ct = tile
-            nc.sync.dma_start(out=out[P * ct : P * (ct + 1), c0 : c0 + width], in_=results[tile][:])
+        def store(i):
+            c0, width, ct = tiles[i]
+            nc.sync.dma_start(out=out[P * ct : P * (ct + 1), c0 : c0 + width], in_=results[i])
 
+        def take(ring):
+            ring.append(ring.pop(0))
+            return ring[-1]
 
-        omega_flat = omega_bf16[:].rearrange("p g t -> p (g t)")
-        size, sign, side, boost, power, radicand = [per_row(name) for name in ("size", "sign", "side", "boost", "power", "radicand")]
-        small = {
-            "table": ([], lambda: nc.scalar.activation(out=root[:], in_=zeros[:, :ROWS], func=SQRT)),
-            "size": ([], lambda: nc.scalar.activation(out=size[:], in_=omega_flat, func=ABS)),
-            "sign": ([], lambda: nc.scalar.activation(out=sign[:], in_=omega_flat, func=SIGN)),
-            "side": (["size"], lambda: nc.scalar.activation(out=side[:], in_=size[:], func=SIGN, bias=threshold[:])),
-            "boost": (["side"], lambda: nc.scalar.activation(out=boost[:], in_=side[:], func=COPY, scale=(1.0 - 2.0**22) / 2, bias=(1.0 + 2.0**22) / 2)),
-            "power": (["side"], lambda: nc.scalar.activation(out=power[:], in_=side[:], func=COPY, scale=(2.0**10 - 2.0**-12) / 2, bias=(2.0**10 + 2.0**-12) / 2)),
-            "radicand": (["boost", "size"], lambda: nc.gpsimd.tensor_tensor(out=radicand[:], in0=size[:], in1=boost[:], op=MULT)),
-            "factor": (["power", "sign"], lambda: nc.gpsimd.tensor_tensor(out=factor[:], in0=sign[:], in1=power[:], op=MULT)),
-            "root": (["radicand", "table"], lambda: nc.scalar.activation(out=root[:], in_=radicand[:], func=SQRT, scale=2.0**-10)),
-        }
-        H = HALF
-        tiles = [(c0, HALF, ct) for c0 in (0, HALF) for ct in range(C_TILES)][:-SPLIT]
-        tiles += [(c0, QUARTER, ct) for ct in range(C_TILES - SPLIT, C_TILES) for c0 in (HALF, HALF + QUARTER)]
-        ALL = (0, 1, 2, 3)
+        omega_flat = omega_rows[:].rearrange("p g t -> p (g t)")
+        size, sign, side = per_row("size"), per_row("sign"), per_row("side")
+        boost, power, radicand = per_row("boost"), per_row("power"), per_row("radicand")
+        warm_up(5)
+        nc.scalar.activation(out=root[:], in_=zeros[:, :ROWS], func=SQRT)
+        nc.scalar.activation(out=size[:], in_=omega_flat, func=ABS)
+        nc.scalar.activation(out=sign[:], in_=omega_flat, func=SIGN)
+        nc.scalar.activation(out=side[:], in_=size[:], func=SIGN, bias=minus_small[:])
+        for r in range(2):
+            widen_sorted(r, opening_one)
+            turn("xb", r, r)
+            warm_up(r + 1)
+        widen(2, 1, plain_tile(BF16, KB), nc.scalar.copy)
+        widen(3, 1, opening_tile(BF16, KB), nc.gpsimd.tensor_copy)
+        nc.scalar.activation(out=boost[:], in_=side[:], func=COPY, scale=(1 - BOOST) / 2, bias=(1 + BOOST) / 2)
+        nc.scalar.activation(
+            out=power[:], in_=side[:], func=COPY, scale=(1 - 1 / BOOST) / DOWN / 2, bias=(1 + 1 / BOOST) / DOWN / 2
+        )
+        nc.gpsimd.tensor_tensor(out=radicand[:], in0=size[:], in1=boost[:], op=MULT)
+        nc.gpsimd.tensor_tensor(out=factor[:], in0=sign[:], in1=power[:], op=MULT)
+        scale_xb(0)
+        scale_xb(1)
+        wa_first = grouped_tile()
+        group_wa(0, wa_first, 0, SCALAR_WA_COLUMNS[0], nc.scalar.copy)
+        group_wa(0, wa_first, SCALAR_WA_COLUMNS[0], HALF, nc.vector.tensor_copy)
+        nc.scalar.activation(out=root[:], in_=radicand[:], func=SQRT, scale=DOWN)
+        turn("xb", 2, 2)
+        turn("xa", 0, 3)
+        held = bank(HELD_BANK, BF16, 2 * HALF)
+        nc.tensor.matmul(out=held[:, :HALF], lhsT=ones[:], rhs=prec_line[:], start=True, stop=True)
+        nc.tensor.matmul(out=held[:, HALF : HALF + ROWS], lhsT=ident_bf16, rhs=factor[:], start=True, stop=True)
+        turn("xb", 3, 4)
+        turn("xa", 2, 5)
+        empty_xa(0)
+        quantize_wa(0, wa_first)
+        quantize_x(0)
+        quantize_x(1)
 
-        forced = {}
+        turn_banks, product_banks = [0, 1, 2], [6, 3, 4, 5]
 
-        def parse(text):
-            steps = []
-            for word in text.split():
-                if "@" in word:
-                    forced[len(steps)] = int(word.split("@")[1])
-                    word = word.split("@")[0]
-                letters = "".join(ch for ch in word if ch not in "0123456789")
-                digits = [int(x) for x in "".join(ch if ch in "0123456789" else " " for ch in word).split()]
-                if word in small:
-                    steps.append(word)
-                elif letters in ("a", "b"):
-                    steps.append((letters, digits[0]))
-                elif letters == "w":
-                    steps.append(("warm", len(steps), digits[0]))
-                elif letters in ("p", "P"):
-                    steps.append(("project", digits[0], 0 if letters == "p" else H, (0, 1, 2)))
-                elif letters in ("p:", "P:"):
-                    steps.append(("project", digits[0], 0 if letters == "p:" else H, (0,) if digits[1] == 0 else (1, 2)))
-                elif letters in ("q", "qa", "qb"):
-                    steps.append(("quantize_x", digits[0]) + {"q": (0, 3), "qa": (0, 1), "qb": (1, 3)}[letters])
-                elif letters in ("s", "S"):
-                    steps.append(("square", digits[0], 0 if letters == "s" else H))
-                elif letters in ("ea", "eb"):
-                    steps.append(("empty", (letters[1], digits[0])))
-                elif letters == "m":
-                    steps.append(("moment", tiles[digits[0]], ALL))
-                elif letters == "m:":
-                    steps.append(("moment", tiles[digits[0]], tuple(int(ch) for ch in word.split(":")[1])))
-                elif letters in ("f", "F", "v", "V"):
-                    steps.append(("finish_v" if letters in "fF" else "quantize_v", digits[0], 0 if letters in "fv" else H))
-                elif letters == "wd:":
-                    steps.append(("widen", digits[0], digits[1], -1, -1))
-                elif letters == "wq:":
-                    steps.append(("widen", digits[0], digits[1], 0, -4))
-                elif letters == "wg:":
-                    steps.append(("widen", digits[0], digits[1], -2, -1))
-                elif letters == "wd::":
-                    steps.append(("widen", digits[0], digits[1], digits[2] % SLOTS, digits[2]))
-                elif letters == "so:":
-                    steps.append(("sort", digits[0], digits[1]))
-                elif letters in ("gs:", "ga:"):
-                    steps.append(("gate_sort", "b" if letters == "gs:" else "a", digits[0], digits[1]))
-                elif letters == "ws":
-                    steps.append(("widen_sorted", digits[0]))
-                elif letters == "il::":
-                    steps.append(("group_wa", digits[0], digits[1], digits[2]))
-                elif letters in ("sub", "mul", "st"):
-                    steps.append(({"sub": "subtract", "mul": "scale_gap", "st": "store"}[letters], tiles[digits[0]]))
-                else:
-                    steps.append(({"sp": "spread", "cs": "copy_scale", "sc": "scale", "so": "sort", "sa": "sort_xa", "qw": "quantize_wa", "hold": "hold"}[letters], digits[0]))
-            return steps
+        def turn_pair(r, xb_order=(0, 1)):
+            turn("xa", r, take(turn_banks))
+            for i in xb_order:
+                turn("xb", r + i, take(turn_banks))
 
-        tensor = parse("""w5 b0@0 w1 b1@1 w2 b2@2 a0@3 w1 b3@4 a2@5 hold0 p0@6 p1@3 a4 b4 b5 p2 p3 P0 P1 a6 b6 b7 P2 P3 p4 p5 a8 b8 b9 p6 p7 P4 P5 a10 b10 b11 P6 P7 p8 p9 a12 b12 b13 p10 p11 P8 P9 a14 b14 b15 p12 p13 P10 P11 p14 p15 P12 P13 P14 P15 m0 m1 m2 m3 m4 m5 m6 m7 m8 m9""")
-        vector = parse("""ws0 ws1 sc0 sc1 il0:336:512 qw0 q0 q1 sc2 sc3 q2 q3 qw1 sc4 sc5 ws7 q4 q5 f0 sc6 sc7 ws9 q6 v0 q7 F0 sc8 sc9 q8 V0 q9 f1 sc10 sc11 q10 v1 q11 F1 sc12 sc13 q12 q13 sc14 sc15 q14 q15 f2 V1 v2 F2 f3 v3 V2 sub0 F3 sub1 V3 sub2 sub3 sub4 mul4 sub5 sub6 mul5 sub7 sub8 mul7 sub9 mul8 mul9""")
-        scalar = parse("""table size sign side wd2:1 boost power il0:0:336 root ea0 wd4:1 ea2 wd5:1 il1:0:256 ea4 s0 s1 sa6 s2 s3 ea6 S0 S1 so8:1 S2 S3 s4 ea8 s5 sa10 s6 s7 S4 ea10 S5 sa12 S6 S7 s8 ea12 s9 sa14 s10 s11 S8 ea14 S9 s12 s13 S10 S11 s14 s15 S12 S13 S14 S15""")
-        gpsimd = parse("""wg3:1 radicand factor il1:256:512 wq6:1 wd8:1:2 ga8:2 wd10:2:3 wd12:2:4 wd14:2:5 mul0 mul1 mul2 mul3 mul6""")
-        sync = parse("""st0 st1 st2 st4 st3 st5 st6 st7 st8 st9""")
-        free = [0, 1, 2, 3, 4, 5, 6]
-        banks = []
-        first_bank = {}
-        turn_ring, product_ring = list(TURN_RING), list(PRODUCT_RING)
-        first_product = max(forced) + 1
-        last_turn = max(i for i, step in enumerate(tensor) if step[0] in ("a", "b"))
-        for place, step in enumerate(tensor):
-            if step == ("hold", 1):
-                banks.append(free.pop(0))
-            elif step[0] == "hold" or (step[0] == "warm" and tensor.index(step) < tensor.index(("hold", 0))):
-                banks.append(HELD_BANK)
-            elif step[0] == "moment" and step[1] in first_bank:
-                banks.append(first_bank[step[1]])
-            elif step[0] == "project" and step[1:3] in first_bank:
-                banks.append(first_bank[step[1:3]])
-            elif place in forced:
-                banks.append(forced[place])
-                first_bank[step[1:3]] = forced[place]
-            elif first_product <= place <= last_turn:
-                ring = turn_ring if step[0] in ("a", "b") else product_ring
-                ring.append(ring.pop(0))
-                banks.append(ring[-1])
-                first_bank[step[1:3]] = ring[-1]
-                free.remove(ring[-1])
-                free.append(ring[-1])
-            else:
-                free.append(free.pop(0))
-                banks.append(free[-1])
-                first_bank[step[1]] = free[-1]
-        queues = {"tensor": tensor, "vector": vector, "scalar": scalar, "gpsimd": gpsimd, "sync": sync}
-        prepared = {}
-        widened = {}
-        for steps in queues.values():
-            for step in steps:
-                if step[0] == "widen":
-                    for r in range(step[1], step[1] + step[2]):
-                        widened[r] = step
-                        prepared.setdefault(r, step)
-                if step[0] == "widen_sorted":
-                    prepared[step[1]] = step
-        for steps in queues.values():
-            for step in steps:
-                if step[:2] == ("gate_sort", "b"):
-                    prepared[step[2]] = step
-                    prepared[step[2] + 1] = step
-                if step[0] == "sort":
-                    for r in range(step[1], step[1] + step[2]):
-                        prepared[r] = step
-        copy_of = {"vector": nc.vector.tensor_copy, "scalar": nc.scalar.copy, "gpsimd": nc.gpsimd.tensor_copy}
-        engine_of = {step: name for name, steps in queues.items() for step in steps}
-        where = {}
-        bank_reader = {}
-        after = {}
-        for step, at in zip(tensor, banks):
-            where[step] = at
-            kind = step[0]
-            reader = {"a": ("empty", step), "b": ("scale", step[1]), "project": ("square",) + step[1:3], "moment": ("subtract", step[1]), "warm": step, "hold": step}[kind]
-            if at in bank_reader and bank_reader[at] != reader:
-                after[step] = [bank_reader[at]]
-            bank_reader[at] = reader
+        def project_each(*parts):
+            for r, half in parts:
+                project(r, half, take(product_banks))
 
-        def quantisers(r):
-            return [s for s in vector if s[:2] == ("quantize_x", r)]
+        def square_each(*parts):
+            for r, half in parts:
+                square(r, half)
 
-        def group_rows(g):
-            return range(PACK * g, PACK * (g + 1))
+        def scale_pair(r):
+            scale_xb(r)
+            scale_xb(r + 1)
 
-        def gated(pair):
-            return [s for s in engine_of if s[0] == "widen" and s[3] >= 0 and (SLOTS if s[4] == -4 else s[4] + SLOTS) == pair] + [s for s in engine_of if s[0] == "gate_sort" and s[3] + SLOTS == pair]
+        def quantize_pair_around(r, piece):
+            quantize_x(r)
+            quantize_v(*piece)
+            quantize_x(r + 1)
 
-        def needs(step):
-            kind = step[0]
-            if step in small:
-                return small[step][0]
-            first = after.get(step, [])
-            if kind == "b":
-                return first + [prepared[step[1]]]
-            if kind == "project":
-                wanted_codes = [s for s in vector if s[:2] == ("quantize_x", step[1]) and any(s[2] <= i < s[3] for i in step[3])]
-                return first + wanted_codes + ([("quantize_wa", step[2] // HALF)] if 0 in step[3] else [])
-            if kind == "moment":
-                return first + [("quantize_v", g, step[1][0] - step[1][0] % HALF) for g in step[2]]
-            if kind == "hold":
-                return first + ["factor"]
-            if kind == "a" and ("sort_xa", step[1]) in engine_of:
-                return first + [("sort_xa", step[1])]
-            if kind == "a" and any(s[:3] == ("gate_sort", "a", step[1]) for s in engine_of):
-                return first + [s for s in engine_of if s[:3] == ("gate_sort", "a", step[1])]
-            if kind == "gate_sort":
-                return quantisers(2 * step[3]) + quantisers(2 * step[3] + 1) + ([widened[step[2]], widened[step[2] + 1]] if step[1] == "b" else [])
-            if kind == "sort_xa":
-                return []
-            if kind in ("a", "spread", "warm"):
-                return first
-            if kind == "widen" and step[4] == -4:
-                return [("quantize_wa", 1)]
-            if kind == "widen" and step[3] >= 0:
-                return quantisers(2 * step[4]) + quantisers(2 * step[4] + 1)
-            if kind == "widen" and step[3] == -2:
-                return [("widen_sorted", 0), ("widen_sorted", 1)]
-            if kind in ("widen", "widen_sorted"):
-                return []
-            if kind == "scale":
-                return [("b", step[1])] + gated(step[1] // 2)
-            if kind == "sort":
-                return [widened[r] for r in range(step[1], step[1] + step[2])]
-            if kind == "empty":
-                return [step[1]] + gated(step[1][1] // 2)
-            if kind == "quantize_x":
-                return ([("empty", ("a", step[1] - step[1] % 2))] if step[2] == 0 else []) + ([("scale", step[1])] if step[3] == 3 else [])
-            if kind == "group_wa":
-                return quantisers(0) + quantisers(1) if step[1] == 1 else []
-            if kind == "quantize_wa":
-                return [s for s in engine_of if s[0] == "group_wa" and s[1] == step[1]]
-            if kind == "square":
-                return [s for s in tensor if s[:3] == ("project",) + step[1:]] + ["root"]
-            if kind == "finish_v":
-                return [("hold", 0)] + [("square", r, step[2]) for r in group_rows(step[1])]
-            if kind == "quantize_v":
-                return [("finish_v",) + step[1:]]
-            if kind == "subtract":
-                return [s for s in tensor if s[0] == "moment" and s[1] == step[1]]
-            if kind == "scale_gap":
-                return [("subtract", step[1])] + ([("hold", 0)] if engine_of[step] == "vector" else [])
-            return [("scale_gap", step[1])]
+        project_each((0, 0), (1, 0))
+        widen(4, 1, plain_tile(BF16, KB), nc.scalar.copy)
+        empty_xa(2)
+        widen(5, 1, plain_tile(BF16, KB), nc.scalar.copy)
+        wa_second = stage_tile(0)[:, : PACK * HALF]
+        group_wa(1, wa_second, 0, SCALAR_WA_COLUMNS[1], nc.scalar.copy)
+        group_wa(1, wa_second, SCALAR_WA_COLUMNS[1], HALF, nc.gpsimd.tensor_copy)
+        scale_pair(2)
+        quantize_x(2)
+        quantize_x(3)
+        quantize_wa(1, wa_second)
+        turn_pair(4)
 
-        def gate_takes(gate):
-            mates = [s for s in engine_of if s[0] == "gate_sort" and s[3] == gate]
-            users = [("a", s[2]) for s in mates if s[1] == "a"] + [("b", s[2] + i) for s in mates if s[1] == "b" for i in range(2)]
-            for s in engine_of:
-                if s[0] == "widen" and s[3] >= 0 and s[4] == gate:
-                    users = users + [prepared[r] if prepared[r] != s else ("b", r) for r in range(s[1], s[1] + s[2])]
-            return ("slot%d" % (gate % SLOTS), ("gate", gate), users)
+        widen(6, 1, stage_tile(0), nc.gpsimd.tensor_copy)
+        empty_xa(4)
+        project_each((2, 0), (3, 0))
+        square_each((0, 0), (1, 0))
+        project_each((0, 1), (1, 1))
+        sort_words("xa", 6, sorted_tile(), nc.scalar.copy)
+        square_each((2, 0), (3, 0))
+        scale_pair(4)
+        widen_sorted(7, one[:])
+        quantize_x(4)
+        quantize_x(5)
+        turn_pair(6)
 
-        def takes(step):
-            kind = step[0]
-            if kind == "widen":
-                users = [prepared[r] if prepared[r] != step else ("b", r) for r in range(step[1], step[1] + step[2])]
-                if step[3] == -2:
-                    return None
-                if step[3] >= 0:
-                    return gate_takes(step[4])
-                return ("wide", step, users)
-            if kind == "gate_sort":
-                return gate_takes(step[3])
-            if kind == "widen_sorted":
-                return ("sorted", step, [("b", step[1])])
-            if kind == "subtract":
-                return ("wide", step, [("scale_gap", step[1])])
-            if kind == "sort":
-                return ("sorted", step, [("b", r) for r in range(step[1], step[1] + step[2])])
-            if kind == "sort_xa":
-                return ("sorted", step, [("a", step[1])])
-            if kind == "scale_gap":
-                return ("four_rows" if engine_of[step] == "gpsimd" else "sorted", step, [("store", step[1])])
-            if kind in ("empty", "scale"):
-                r = step[1][1] if kind == "empty" else step[1] - step[1] % 2
-                return ("slot%d" % (r // 2 % SLOTS), r, quantisers(r) + quantisers(r + 1))
-            if kind == "group_wa":
-                return ("grouped" if step[1] == 0 else "slot0", ("wa", step[1]), [("quantize_wa", step[1])])
-            if kind == "finish_v":
-                return ("grouped", step, [("quantize_v",) + step[1:]])
-            if kind == "square":
-                return ("four_rows", (step[1] // PACK, step[2]), [("finish_v", step[1] // PACK, step[2])])
-            return None
+        stage = stage_tile(2)
+        widen(8, 1, stage, nc.gpsimd.tensor_copy)
+        sort_words("xa", 8, stage.bitcast(F32)[:, KB : KB + HALF], nc.gpsimd.tensor_copy)
+        finish_v(0, 0)
+        empty_xa(6)
+        project_each((2, 1), (3, 1))
+        square_each((0, 1), (1, 1))
+        project_each((4, 0), (5, 0))
+        sort_words("xb", 8, sorted_tile(), nc.scalar.copy)
+        square_each((2, 1), (3, 1), (4, 0))
+        scale_pair(6)
+        widen_sorted(9, one[:])
+        quantize_pair_around(6, (0, 0))
+        turn_pair(8)
 
-        def issue(step):
-            kind = step[0]
-            if step in small:
-                small[step][1]()
-            elif kind in ("a", "b"):
-                turn(step, where[step])
-            elif kind == "empty":
-                empty(step[1], copy_of[engine_of[step]])
-            elif kind == "project":
-                project(step[1], step[2], step[3], where[step])
-            elif kind == "moment":
-                moment(step[1], where[step], step[2])
-            elif kind == "hold":
-                hold_constants(step[1], where[step])
-            elif kind == "warm":
-                warm_up(step[2], where[step])
-            elif kind == "widen":
-                widen(step[1], step[2], copy_of[engine_of[step]], step[4] if step[3] >= 0 else step[3])
-            elif kind == "group_wa":
-                group_wa(*step[1:], copy_of[engine_of[step]])
-            elif kind == "quantize_wa":
-                quantize_wa(step[1], wa_grouped[step[1]])
-            elif kind == "scale_gap":
-                scale_gap(step[1], engine_of[step] == "gpsimd")
-            else:
-                plain = {"scale": scale_xb, "sort": sort_xb, "widen_sorted": widen_sorted, "gate_sort": gate_sort, "sort_xa": sort_xa, "quantize_x": quantize_x, "square": square, "finish_v": finish_v,
-                         "quantize_v": quantize_v, "subtract": subtract_target, "store": store}
-                plain[kind](*step[1:])
+        widen(10, 2, stage_tile(3), nc.gpsimd.tensor_copy)
+        finish_v(0, 1)
+        empty_xa(8)
+        square(5, 0)
+        sort_words("xa", 10, sorted_tile(), nc.scalar.copy)
+        project_each((4, 1), (6, 0), (7, 0), (5, 1))
+        square_each((4, 1), (6, 0), (7, 0))
+        scale_pair(8)
+        quantize_pair_around(8, (0, 1))
+        turn_pair(10)
 
-        done = set()
-        bufs = dict(BUFS)
-        for i in range(SLOTS):
-            bufs["slot%d" % i] = 1
-        taken = {name: [] for name in bufs}
-        taken["four_rows"] = [(half, [s for s in engine_of if s[0] == "group_wa" and s[1] == half]) for half in range(2)]
-        left = {name: list(steps) for name, steps in queues.items()}
-        for turn_number in range(sum(len(steps) for steps in queues.values())):
-            ready = []
-            for name, steps in left.items():
-                if steps and all(need in done for need in needs(steps[0])):
-                    wanted = takes(steps[0])
-                    if wanted and wanted[1] not in [key for key, users in taken[wanted[0]]]:
-                        earlier = taken[wanted[0]]
-                        if len(earlier) >= bufs[wanted[0]] and not all(user in done for user in earlier[-bufs[wanted[0]]][1]):
-                            continue
-                    ready.append(name)
-            assert ready, [steps[:1] for steps in left.values()]
-            step = left[ready[0]].pop(0)
-            wanted = takes(step)
-            if wanted and wanted[1] not in [key for key, users in taken[wanted[0]]]:
-                taken[wanted[0]].append(wanted[1:])
-            issue(step)
-            done.add(step)
+        widen(12, 2, stage_tile(0), nc.gpsimd.tensor_copy)
+        finish_v(1, 0)
+        empty_xa(10)
+        square(5, 1)
+        sort_words("xa", 12, sorted_tile(), nc.scalar.copy)
+        project_each((6, 1), (7, 1), (8, 0), (9, 0))
+        square(6, 1)
+        project_each((8, 1))
+        square_each((7, 1), (8, 0))
+        sort_words("xb", 12, sorted_tile(), nc.scalar.copy)
+        scale_pair(10)
+        quantize_pair_around(10, (1, 0))
+        turn_pair(12, xb_order=(1, 0))
+
+        widen(14, 2, stage_tile(1), nc.gpsimd.tensor_copy)
+        finish_v(1, 1)
+        square_each((9, 0), (8, 1))
+        empty_xa(12)
+        sort_words("xa", 14, sorted_tile(), nc.scalar.copy)
+        project_each((10, 0), (11, 0), (9, 1))
+        square_each((10, 0), (11, 0))
+        for r in (13, 12):
+            scale_xb(r)
+        for r in (13, 12):
+            quantize_x(r)
+        turn_pair(14)
+
+        product_banks.extend(turn_banks)
+        empty_xa(14)
+        square(9, 1)
+        late = [(13, 0), (12, 0), (10, 1), (11, 1), (14, 0), (15, 0)] + [(r, 1) for r in range(12, ROWS)]
+        project_each(*late[:4])
+        scale_pair(14)
+        quantize_x(14)
+        quantize_x(15)
+        for part in late[4:]:
+            square(*late[late.index(part) - 4])
+            project_each(part)
+        square_each(*late[-4:])
+        finish_v(2, 0)
+        quantize_v(1, 1)
+        quantize_v(2, 0)
+        finish_v(2, 1)
+        finish_v(3, 0)
+        quantize_v(3, 0)
+        quantize_v(2, 1)
+
+        def moment_gap(i):
+            moment(i, take(product_banks))
+            subtract_target(i)
+
+        moment_gap(0)
+        scale_on_gpsimd(0)
+        finish_v(3, 1)
+        moment_gap(1)
+        quantize_v(3, 1)
+        for i in (1, 2, 3):
+            moment_gap(i + 1)
+            scale_on_gpsimd(i)
+        scale_on_vector(4)
+        moment_gap(5)
+        moment_gap(6)
+        scale_on_gpsimd(6)
+        scale_on_vector(5)
+        moment_gap(7)
+        moment_gap(8)
+        scale_on_vector(7)
+        moment_gap(9)
+        scale_on_vector(8)
+        scale_on_vector(9)
+        for i in (0, 1, 2, 4, 3, 5, 6, 7, 8, 9):
+            store(i)

@@ -58,9 +58,6 @@ def tile_projection_moment_gap_s3_kernel(
             skip = start // item_bytes
             return keep.tile([P, skip + width], dtype, name=name, align_bytes=256)[:, skip:]
 
-        def per_row(name, dtype=F32):
-            return keep.tile([P, ROWS], dtype, name=name)
-
         def large_tile(dtype, width):
             return work.tile([P, width], dtype, name="large", bufs=8)[:]
 
@@ -292,7 +289,9 @@ def tile_projection_moment_gap_s3_kernel(
                     stop=(s == PASSES - 1),
                 )
 
-        root, factor = per_row("root"), per_row("factor", BF16)
+        root = keep.tile([P, ROWS], F32, name="root")
+        radicand_factor = keep.tile([P, 2 * ROWS], BF16, name="radicand_factor")
+        radicand, factor = radicand_factor[:, :ROWS], radicand_factor[:, ROWS:]
         squares = {}
 
         def square(r, half):
@@ -368,39 +367,40 @@ def tile_projection_moment_gap_s3_kernel(
             return ring[-1]
 
         omega_flat = omega_rows[:].rearrange("p g t -> p (g t)")
-        size, sign, side = per_row("size"), per_row("sign"), per_row("side")
-        boost, power, radicand = per_row("boost"), per_row("power"), per_row("radicand")
+        size_sign = keep.tile([P, 2 * ROWS], F32, name="size_sign")
+        boost_power = keep.tile([P, 2 * ROWS], F32, name="boost_power")
+        size, sign, boost, power = size_sign[:, :ROWS], size_sign[:, ROWS:], boost_power[:, :ROWS], boost_power[:, ROWS:]
+        side = keep.tile([P, ROWS], F32, name="side")
         warm_up(5)
         nc.scalar.activation(out=root[:], in_=zeros[:, :ROWS], func=SQRT)
-        nc.scalar.activation(out=size[:], in_=omega_flat, func=ABS)
-        nc.scalar.activation(out=sign[:], in_=omega_flat, func=SIGN)
-        nc.scalar.activation(out=side[:], in_=size[:], func=SIGN, bias=minus_small[:])
+        nc.scalar.activation(out=size, in_=omega_flat, func=ABS)
+        nc.scalar.activation(out=sign, in_=omega_flat, func=SIGN)
+        nc.scalar.activation(out=side[:], in_=size, func=SIGN, bias=minus_small[:])
         for r in range(2):
             widen_sorted(r, opening_one)
             turn("xb", r, r)
             warm_up(r + 1)
         widen(2, 1, plain_tile(BF16, KB), nc.scalar.copy)
         widen(3, 1, opening_tile(BF16, KB), nc.gpsimd.tensor_copy)
-        nc.scalar.activation(out=boost[:], in_=side[:], func=COPY, scale=(1 - BOOST) / 2, bias=(1 + BOOST) / 2)
+        nc.scalar.activation(out=boost, in_=side[:], func=COPY, scale=(1 - BOOST) / 2, bias=(1 + BOOST) / 2)
         nc.scalar.activation(
-            out=power[:], in_=side[:], func=COPY, scale=(1 - 1 / BOOST) / DOWN / 2, bias=(1 + 1 / BOOST) / DOWN / 2
+            out=power, in_=side[:], func=COPY, scale=(1 - 1 / BOOST) / DOWN / 2, bias=(1 + 1 / BOOST) / DOWN / 2
         )
-        nc.gpsimd.tensor_tensor(out=radicand[:], in0=size[:], in1=boost[:], op=MULT)
-        nc.gpsimd.tensor_tensor(out=factor[:], in0=sign[:], in1=power[:], op=MULT)
         scale_xb(0)
         scale_xb(1)
         wa_first = grouped_tile()
         group_wa(0, wa_first, 0, SCALAR_WA_COLUMNS[0], nc.scalar.copy)
         group_wa(0, wa_first, SCALAR_WA_COLUMNS[0], HALF, nc.vector.tensor_copy)
-        nc.scalar.activation(out=root[:], in_=radicand[:], func=SQRT, scale=DOWN)
+        nc.vector.tensor_tensor(out=radicand_factor[:], in0=size_sign[:], in1=boost_power[:], op=MULT)
         turn("xb", 2, 2)
         turn("xa", 0, 3)
         held = bank(HELD_BANK, BF16, 2 * HALF)
         nc.tensor.matmul(out=held[:, :HALF], lhsT=ones[:], rhs=prec_line[:], start=True, stop=True)
-        nc.tensor.matmul(out=held[:, HALF : HALF + ROWS], lhsT=ident_bf16, rhs=factor[:], start=True, stop=True)
         turn("xb", 3, 4)
         turn("xa", 2, 5)
+        nc.tensor.matmul(out=held[:, HALF : HALF + ROWS], lhsT=ident_bf16, rhs=factor, start=True, stop=True)
         empty_xa(0)
+        nc.scalar.activation(out=root[:], in_=radicand, func=SQRT, scale=DOWN)
         quantize_wa(0, wa_first)
         quantize_x(0)
         quantize_x(1)
@@ -442,7 +442,7 @@ def tile_projection_moment_gap_s3_kernel(
         quantize_wa(1, wa_second)
         turn_pair(4)
 
-        widen(6, 1, stage_tile(0), nc.gpsimd.tensor_copy)
+        widen(6, 2, stage_tile(0), nc.gpsimd.tensor_copy)
         empty_xa(4)
         project_each((2, 0), (3, 0))
         square_each((0, 0), (1, 0))
@@ -450,7 +450,6 @@ def tile_projection_moment_gap_s3_kernel(
         sort_words("xa", 6, sorted_tile(), nc.scalar.copy)
         square_each((2, 0), (3, 0))
         scale_pair(4)
-        widen_sorted(7, one[:])
         quantize_x(4)
         quantize_x(5)
         turn_pair(6)

@@ -394,10 +394,11 @@ def tile_projection_moment_gap_s3_kernel(
         nc.vector.tensor_tensor(out=radicand_factor[:], in0=size_sign[:], in1=boost_power[:], op=MULT)
         turn("xb", 2, 2)
         turn("xa", 0, 3)
-        held = bank(HELD_BANK, BF16, 2 * HALF)
-        nc.tensor.matmul(out=held[:, :HALF], lhsT=ones[:], rhs=prec_line[:], start=True, stop=True)
+        warm_up(1)
         turn("xb", 3, 4)
         turn("xa", 2, 5)
+        held = bank(HELD_BANK, BF16, 2 * HALF)
+        nc.tensor.matmul(out=held[:, :HALF], lhsT=ones[:], rhs=prec_line[:], start=True, stop=True)
         nc.tensor.matmul(out=held[:, HALF : HALF + ROWS], lhsT=ident_bf16, rhs=factor, start=True, stop=True)
         empty_xa(0)
         nc.scalar.activation(out=root[:], in_=radicand, func=SQRT, scale=DOWN)
@@ -442,7 +443,7 @@ def tile_projection_moment_gap_s3_kernel(
         quantize_wa(1, wa_second)
         turn_pair(4)
 
-        widen(6, 2, stage_tile(0), nc.gpsimd.tensor_copy)
+        widen(6, 1, stage_tile(0), nc.gpsimd.tensor_copy)
         empty_xa(4)
         project_each((2, 0), (3, 0))
         square_each((0, 0), (1, 0))
@@ -450,6 +451,7 @@ def tile_projection_moment_gap_s3_kernel(
         sort_words("xa", 6, sorted_tile(), nc.scalar.copy)
         square_each((2, 0), (3, 0))
         scale_pair(4)
+        widen_sorted(7, one[:])
         quantize_x(4)
         quantize_x(5)
         turn_pair(6)

@@ -395,10 +395,10 @@ def tile_projection_moment_gap_s3_kernel(
         turn("xb", 2, 2)
         turn("xa", 0, 3)
         warm_up(1)
-        turn("xb", 3, 4)
-        turn("xa", 2, 5)
         held = bank(HELD_BANK, BF16, 2 * HALF)
         nc.tensor.matmul(out=held[:, :HALF], lhsT=ones[:], rhs=prec_line[:], start=True, stop=True)
+        turn("xb", 3, 4)
+        turn("xa", 2, 5)
         nc.tensor.matmul(out=held[:, HALF : HALF + ROWS], lhsT=ident_bf16, rhs=factor, start=True, stop=True)
         empty_xa(0)
         nc.scalar.activation(out=root[:], in_=radicand, func=SQRT, scale=DOWN)

@@ -34,6 +34,8 @@ STAGES = 4
 
 SCALAR_WA_COLUMNS = (320, 256)
 
+GPSIMD_V_COLUMNS = 128
+
 DOWN, BOOST, SMALL = 2.0**-10, 2.0**22, 2.0**-40 * (1 + 2.0**-12)
 
 MOVING, MOVING_SCALE, STATIONARY, STATIONARY_SCALE = 0, 64, 128, 192
@@ -305,15 +307,27 @@ def tile_projection_moment_gap_s3_kernel(
         v_grouped = {}
         v_codes = {}
 
-        def finish_v(g, half):
-            v_grouped[g, half] = grouped_tile()
-            factors = held[:, HALF + PACK * g : HALF + PACK * (g + 1)].rearrange("p (a e) -> p a e", a=2)
-            nc.vector.tensor_tensor(
-                out=v_grouped[g, half].rearrange("p (n a e) -> p n a e", a=2, e=2),
-                in0=squares[g, half].rearrange("p a n e -> p n a e"),
-                in1=factors.unsqueeze(1).to_broadcast([P, HALF, 2, 2]),
+        def finish_columns(g, half, c0, c1, engine, factors):
+            engine.tensor_tensor(
+                out=v_grouped[g, half].rearrange("p (n a e) -> p n a e", a=2, e=2)[:, c0:c1],
+                in0=squares[g, half].rearrange("p a n e -> p n a e")[:, c0:c1],
+                in1=factors[:, PACK * g : PACK * (g + 1)]
+                .rearrange("p (a e) -> p a e", a=2)
+                .unsqueeze(1)
+                .to_broadcast([P, c1 - c0, 2, 2]),
                 op=MULT,
             )
+
+        def finish_v(g, half):
+            v_grouped[g, half] = grouped_tile()
+            finish_columns(g, half, 0, HALF, nc.vector, held[:, HALF:])
+
+        def begin_on_gpsimd(g, half, stage):
+            v_grouped[g, half] = stage_tile(stage)[:, : PACK * HALF]
+            finish_columns(g, half, 0, GPSIMD_V_COLUMNS, nc.gpsimd, factor)
+
+        def finish_rest(g, half):
+            finish_columns(g, half, GPSIMD_V_COLUMNS, HALF, nc.vector, held[:, HALF:])
 
         def quantize_v(g, half):
             codes = mx_tile("v_codes%d_%d" % (g, half), U32, 4, HALF, MOVING)
@@ -467,7 +481,7 @@ def tile_projection_moment_gap_s3_kernel(
         sort_words("xb", 8, sorted_tile(), nc.scalar.copy)
         square_each((2, 1), (3, 1), (4, 0))
         scale_pair(6)
-        widen_sorted(9, one[:])
+        widen(9, 1, plain_tile(BF16, KB), nc.vector.tensor_copy)
         quantize_pair_around(6, (0, 0))
         turn_pair(8)
 
@@ -508,6 +522,7 @@ def tile_projection_moment_gap_s3_kernel(
         for r in (13, 12):
             quantize_x(r)
         turn_pair(14)
+        begin_on_gpsimd(2, 0, 2)
 
         product_banks.extend(turn_banks)
         empty_xa(14)
@@ -521,7 +536,7 @@ def tile_projection_moment_gap_s3_kernel(
             square(*late[late.index(part) - 4])
             project_each(part)
         square_each(*late[-4:])
-        finish_v(2, 0)
+        finish_rest(2, 0)
         quantize_v(1, 1)
         quantize_v(2, 0)
         finish_v(2, 1)

@@ -32,9 +32,8 @@ C_TILES = C // P
 HELD_BANK = 7
 STAGES = 4
 
-SCALAR_WA_COLUMNS = (320, 256)
-
-GPSIMD_V_COLUMNS = 128
+SCALAR_WA_COLUMNS = (256, 256)
+GAP = 16
 
 DOWN, BOOST, SMALL = 2.0**-10, 2.0**22, 2.0**-40 * (1 + 2.0**-12)
 
@@ -66,7 +65,7 @@ def tile_projection_moment_gap_s3_kernel(
         def plain_tile(dtype, width):
             return work.tile([P, width], dtype, name="plain", bufs=6)[:]
 
-        def sorted_tile(width=HALF):
+        def sorted_tile(width=HALF + GAP):
             return work.tile([P, width], F32, name="sorted", bufs=5)[:]
 
         def grouped_tile():
@@ -92,8 +91,8 @@ def tile_projection_moment_gap_s3_kernel(
         wb_bytes = mx_tile("wb_bytes", U8, 1, 2 * N, MOVING_SCALE).rearrange("p (g n) -> p g n", g=2)
         z_tile = mx_tile("z_tile", U8, 1, GROUPS * 2 * C, STATIONARY).rearrange("p (g n) -> p g n", g=GROUPS)
         z_bytes = mx_tile("z_bytes", U8, 1, GROUPS * C, STATIONARY_SCALE).rearrange("p (g n) -> p g n", g=GROUPS)
-        omega_rows = keep.tile([P, GROUPS, PACK], BF16, name="omega_rows")
-        prec_rows = keep.tile([P, HALF + QUARTER], BF16, name="prec_rows")
+        omega_lines = keep.tile([P, K_PASS], BF16, name="omega_lines")
+        prec_rows = keep.tile([P, N], BF16, name="prec_rows")
         prec_line = keep.tile([P, HALF], BF16, name="prec_line")
         ones = keep.tile([P, P], BF16, name="ones")
         target_rows = keep.tile([P, C_TILES, N], BF16, name="target_rows")
@@ -129,6 +128,7 @@ def tile_projection_moment_gap_s3_kernel(
                 nc.sync.dma_start(out=tile[i:P:32].bitcast(I32), in_=rows[i].bitcast(I32))
 
         nc.vector.memset(zeros[:].bitcast(I32), 0)
+        nc.vector.memset(omega_lines[:].bitcast(I32), 0)
         nc.vector.memset(ident[:], 0.0)
         nc.vector.memset(prec_line[:].bitcast(I32), 0)
         nc.vector.memset(one[:], 1.0)
@@ -141,30 +141,31 @@ def tile_projection_moment_gap_s3_kernel(
 
         load_xb(0, 1)
         load_xb(1, 1)
-        nc.sync.dma_start(out=omega_rows[:], in_=omega.rearrange("(g p t) -> p g t", p=P, t=PACK))
-        load_xb(2, 2)
         nc.sync.dma_start(out=scale_col[:], in_=xb_scale.rearrange("o (i p t) -> p (o i) t", i=2, t=PACK))
-        nc.sync.dma_start(out=prec_line[0:1, :], in_=prec[HALF:].unsqueeze(0))
-        load_wa(0)
+        load_xb(2, 2)
         load_xa(0)
-        load_xb(4, 2)
+        load_wa(0)
+        nc.sync.dma_start(out=omega_lines[0:GROUPS, :], in_=omega.rearrange("(g k) -> g k", g=GROUPS))
+        nc.sync.dma_start(out=prec_line[0:1, :], in_=prec[HALF:].unsqueeze(0))
         load_xa(2)
         load_wb(0)
         load_scale_bytes(wb_bytes, wb_scales)
-        load_wa(1)
+        load_xb(4, 2)
         load_xa(4)
-        load_xb(6, 2)
+        load_wa(1)
         load_wb(1)
+        load_xb(6, 2)
         load_xa(6)
         load_xb(8, 4)
         load_xa(8)
+        load_xa(10)
         load_xb(12, 4)
-        for r in (10, 12, 14):
+        for r in (12, 14):
             load_xa(r)
         load_scale_bytes(z_bytes, z_scales)
         nc.sync.dma_start(out=z_tile[:], in_=z_words.rearrange("g p n -> p g n"))
         nc.sync.dma_start(out=target_rows[:], in_=target.rearrange("(ct c) n -> c ct n", c=P))
-        nc.sync.dma_start(out=prec_rows[:], in_=prec[: HALF + QUARTER].partition_broadcast(P))
+        nc.sync.dma_start(out=prec_rows[:], in_=prec.partition_broadcast(P))
 
         def warm_up(count):
             tile = bank(HELD_BANK)
@@ -189,40 +190,52 @@ def tile_projection_moment_gap_s3_kernel(
         for r in range(ROWS):
             words_as_they_lie(r, 0, xa_pairs[r - r % 2][:, r % 2, :])
 
-        xb_rows = {}
-
         def xb_values(r, count):
             return xb_codes[:, KB * r : KB * (r + count)].bitcast(FP8)
 
-        def widen(r, count, tile, copy):
-            copy(out=tile[:, : count * KB], in_=xb_values(r, count))
+        def note_sorted(r, count, halves):
             for i in range(count):
-                xb_rows[r + i] = tile[:, KB * i : KB * (i + 1)]
                 for s in range(1, PASSES):
-                    words_as_they_lie(r + i, s, xb_rows[r + i][:, K_PASS * (s - 1) : K_PASS * s])
+                    first = P * (2 * i + s - 1)
+                    words[r + i, s] = [halves[:, u, :].bitcast(F32)[:, first : first + P] for u in range(2)]
 
-        def widen_sorted(r, unit):
-            tile = sorted_tile()
+        def widen_on_vector(r, unit):
+            halves = sorted_tile().bitcast(BF16).rearrange("p (u k) -> p u k", u=2)[:, :, :HALF]
             nc.vector.tensor_scalar(
-                out=tile.bitcast(BF16).rearrange("p (u m e) -> p m u e", u=2, e=2),
-                in0=xb_values(r, 1).rearrange("p (m u e) -> p m u e", u=2, e=2),
+                out=halves.rearrange("p u (m e) -> p u m e", e=2),
+                in0=xb_values(r, 1).rearrange("p (m u e) -> p u m e", u=2, e=2),
                 scalar1=unit,
                 scalar2=None,
                 op0=MULT,
             )
-            for s in range(1, PASSES):
-                words[r, s] = [tile[:, P * (2 * u + s - 1) : P * (2 * u + s)] for u in range(2)]
+            note_sorted(r, 1, halves)
+
+        def widen_on_scalar(r):
+            halves = plain_tile(BF16, KB).rearrange("p (u k) -> p u k", u=2)
+            nc.scalar.copy(
+                out=halves.rearrange("p u (m e) -> p u m e", e=2),
+                in_=xb_values(r, 1).rearrange("p (m u e) -> p u m e", u=2, e=2),
+            )
+            note_sorted(r, 1, halves)
+
+        def widen_on_gpsimd(r, count, tile):
+            halves = tile[:, : count * KB].rearrange("p (u k) -> p u k", u=2)
+            nc.gpsimd.tensor_copy(
+                out=halves.rearrange("p u (m e) -> p m u e", e=2),
+                in_=xb_values(r, count).rearrange("p (m u e) -> p m u e", u=2, e=2),
+            )
+            note_sorted(r, count, halves)
 
         def parts_of(operand, r):
             return [(r, 0), (r + 1, 0)] if operand == "xa" else [(r, 1), (r, 2)]
 
-        def sort_words(operand, r, tile, copy):
-            values = xa_pairs[r][:].rearrange("p i k -> p (i k)") if operand == "xa" else xb_rows[r]
+        def sort_xa(r, tile, copy):
+            values = xa_pairs[r][:].rearrange("p i k -> p (i k)")
             copy(
-                out=tile.rearrange("p (i u c j) -> p i c u j", i=2, u=2, j=4),
+                out=tile[:, :HALF].rearrange("p (i u c j) -> p i c u j", i=2, u=2, j=4),
                 in_=values.bitcast(F32).rearrange("p (i c j u) -> p i c u j", i=2, j=4, u=2),
             )
-            for i, part in enumerate(parts_of(operand, r)):
+            for i, part in enumerate(parts_of("xa", r)):
                 words[part] = [tile[:, P * (2 * i + u) : P * (2 * i + u + 1)] for u in range(2)]
 
         turned = {}
@@ -322,13 +335,6 @@ def tile_projection_moment_gap_s3_kernel(
             v_grouped[g, half] = grouped_tile()
             finish_columns(g, half, 0, HALF, nc.vector, held[:, HALF:])
 
-        def begin_on_gpsimd(g, half, stage):
-            v_grouped[g, half] = stage_tile(stage)[:, : PACK * HALF]
-            finish_columns(g, half, 0, GPSIMD_V_COLUMNS, nc.gpsimd, factor)
-
-        def finish_rest(g, half):
-            finish_columns(g, half, GPSIMD_V_COLUMNS, HALF, nc.vector, held[:, HALF:])
-
         def quantize_v(g, half):
             codes = mx_tile("v_codes%d_%d" % (g, half), U32, 4, HALF, MOVING)
             scale_bytes = mx_tile("v_bytes%d_%d" % (g, half), U8, 1, HALF, MOVING_SCALE)
@@ -339,11 +345,12 @@ def tile_projection_moment_gap_s3_kernel(
         tiles = tiles + [(c0, QUARTER, ct) for ct in (C_TILES - 2, C_TILES - 1) for c0 in (HALF, HALF + QUARTER)]
         sums, gaps, results = {}, {}, {}
 
-        def moment(i, where):
+        def moment(i, where, groups=range(GROUPS)):
             c0, width, ct = tiles[i]
-            sums[i] = bank(where)
+            if i not in sums:
+                sums[i] = bank(where)
             cols = slice(c0 % HALF, c0 % HALF + width)
-            for g in range(GROUPS):
+            for g in groups:
                 codes, scale_bytes = v_codes[g, c0 // HALF]
                 nc.tensor.matmul_mx(
                     out=sums[i][:, :width],
@@ -380,52 +387,56 @@ def tile_projection_moment_gap_s3_kernel(
             ring.append(ring.pop(0))
             return ring[-1]
 
-        omega_flat = omega_rows[:].rearrange("p g t -> p (g t)")
         size_sign = keep.tile([P, 2 * ROWS], F32, name="size_sign")
         boost_power = keep.tile([P, 2 * ROWS], F32, name="boost_power")
         size, sign, boost, power = size_sign[:, :ROWS], size_sign[:, ROWS:], boost_power[:, :ROWS], boost_power[:, ROWS:]
         side = keep.tile([P, ROWS], F32, name="side")
         warm_up(5)
         nc.scalar.activation(out=root[:], in_=zeros[:, :ROWS], func=SQRT)
-        nc.scalar.activation(out=size, in_=omega_flat, func=ABS)
-        nc.scalar.activation(out=sign, in_=omega_flat, func=SIGN)
-        nc.scalar.activation(out=side[:], in_=size, func=SIGN, bias=minus_small[:])
         for r in range(2):
-            widen_sorted(r, opening_one)
+            widen_on_vector(r, opening_one)
             turn("xb", r, r)
-            warm_up(r + 1)
-        widen(2, 1, plain_tile(BF16, KB), nc.scalar.copy)
-        widen(3, 1, opening_tile(BF16, KB), nc.gpsimd.tensor_copy)
+            warm_up(1 - r)
+        widen_on_scalar(2)
+        widen_on_gpsimd(3, 1, opening_tile(BF16, KB))
+        scale_xb(0)
+        scale_xb(1)
+        turn("xa", 0, 3)
+        turn("xb", 2, 2)
+        warm_up(1)
+        turn("xb", 3, 4)
+        omega_bank = bank(6)
+        for t in range(PACK):
+            nc.tensor.matmul(
+                out=omega_bank[:, t:ROWS:PACK], lhsT=omega_lines[:, t::PACK], rhs=ident_bf16[:, :GROUPS], start=True, stop=True
+            )
+        warm_up(1)
+        turn("xa", 2, 5)
+        warm_up(2)
+        held = bank(HELD_BANK, BF16, 2 * HALF)
+        nc.tensor.matmul(out=held[:, :HALF], lhsT=ones[:], rhs=prec_line[:], start=True, stop=True)
+        empty_xa(0)
+        wa_first = grouped_tile()
+        group_wa(0, wa_first, 0, SCALAR_WA_COLUMNS[0], nc.scalar.copy)
+        group_wa(0, wa_first, SCALAR_WA_COLUMNS[0], HALF, nc.vector.tensor_copy)
+        nc.scalar.activation(out=size, in_=omega_bank[:, :ROWS], func=ABS)
+        nc.scalar.activation(out=sign, in_=omega_bank[:, :ROWS], func=SIGN)
+        nc.scalar.activation(out=side[:], in_=size, func=SIGN, bias=minus_small[:])
         nc.scalar.activation(out=boost, in_=side[:], func=COPY, scale=(1 - BOOST) / 2, bias=(1 + BOOST) / 2)
         nc.scalar.activation(
             out=power, in_=side[:], func=COPY, scale=(1 - 1 / BOOST) / DOWN / 2, bias=(1 + 1 / BOOST) / DOWN / 2
         )
-        scale_xb(0)
-        scale_xb(1)
-        wa_first = grouped_tile()
-        group_wa(0, wa_first, 0, SCALAR_WA_COLUMNS[0], nc.scalar.copy)
-        group_wa(0, wa_first, SCALAR_WA_COLUMNS[0], HALF, nc.vector.tensor_copy)
-        nc.vector.tensor_tensor(out=radicand_factor[:], in0=size_sign[:], in1=boost_power[:], op=MULT)
-        turn("xb", 2, 2)
-        turn("xa", 0, 3)
-        warm_up(1)
-        held = bank(HELD_BANK, BF16, 2 * HALF)
-        nc.tensor.matmul(out=held[:, :HALF], lhsT=ones[:], rhs=prec_line[:], start=True, stop=True)
-        turn("xb", 3, 4)
-        turn("xa", 2, 5)
-        nc.tensor.matmul(out=held[:, HALF : HALF + ROWS], lhsT=ident_bf16, rhs=factor, start=True, stop=True)
-        empty_xa(0)
-        nc.scalar.activation(out=root[:], in_=radicand, func=SQRT, scale=DOWN)
-        quantize_wa(0, wa_first)
         quantize_x(0)
+        quantize_wa(0, wa_first)
         quantize_x(1)
+        nc.vector.tensor_tensor(out=radicand_factor[:], in0=size_sign[:], in1=boost_power[:], op=MULT)
 
-        turn_banks, product_banks = [0, 1, 2], [6, 3, 4, 5]
+        turn_banks, product_banks = [0, 1, 2], [6, 3, 5, 4]
 
-        def turn_pair(r, xb_order=(0, 1)):
-            turn("xa", r, take(turn_banks))
-            for i in xb_order:
+        def turn_pair(r):
+            for i in range(2):
                 turn("xb", r + i, take(turn_banks))
+            turn("xa", r, take(turn_banks))
 
         def project_each(*parts):
             for r, half in parts:
@@ -444,105 +455,91 @@ def tile_projection_moment_gap_s3_kernel(
             quantize_v(*piece)
             quantize_x(r + 1)
 
-        project_each((0, 0), (1, 0))
-        widen(4, 1, plain_tile(BF16, KB), nc.scalar.copy)
+        def project_block(r, sort=None):
+            project_each((r - 2, 1), (r - 1, 1))
+            square(r - 2, 1)
+            project_each((r, 0))
+            if sort:
+                sort_xa(sort, sorted_tile(), nc.scalar.copy)
+            square(r - 1, 1)
+            project_each((r + 1, 0))
+
+        widen_on_gpsimd(5, 1, stage_tile(0))
         empty_xa(2)
-        widen(5, 1, plain_tile(BF16, KB), nc.scalar.copy)
-        wa_second = stage_tile(0)[:, : PACK * HALF]
-        group_wa(1, wa_second, 0, SCALAR_WA_COLUMNS[1], nc.scalar.copy)
-        group_wa(1, wa_second, SCALAR_WA_COLUMNS[1], HALF, nc.gpsimd.tensor_copy)
+        widen_on_scalar(4)
+        nc.scalar.activation(out=root[:], in_=radicand, func=SQRT, scale=DOWN)
+        project_each((0, 0), (1, 0))
         scale_pair(2)
+        turn_pair(4)
+        nc.tensor.matmul(out=held[:, HALF : HALF + ROWS], lhsT=ident_bf16, rhs=factor, start=True, stop=True)
+        wa_second = stage_tile(STAGES)[:, : PACK * HALF]
+        square(0, 0)
+        group_wa(1, wa_second, 0, SCALAR_WA_COLUMNS[1], nc.scalar.copy)
         quantize_x(2)
+        group_wa(1, wa_second, SCALAR_WA_COLUMNS[1], HALF, nc.vector.tensor_copy)
         quantize_x(3)
         quantize_wa(1, wa_second)
-        turn_pair(4)
+        square(1, 0)
 
-        widen(6, 1, stage_tile(0), nc.gpsimd.tensor_copy)
-        empty_xa(4)
-        project_each((2, 0), (3, 0))
-        square_each((0, 0), (1, 0))
-        project_each((0, 1), (1, 1))
-        sort_words("xa", 6, sorted_tile(), nc.scalar.copy)
+        stage = stage_tile(STAGES)
+        widen_on_gpsimd(6, 1, stage)
+        widen_on_gpsimd(7, 1, stage[:, KB:])
+        project_each((2, 0), (3, 0), (0, 1), (1, 1))
         square_each((2, 0), (3, 0))
+        empty_xa(4)
         scale_pair(4)
-        widen_sorted(7, one[:])
+        finish_v(0, 0)
         quantize_x(4)
         quantize_x(5)
-        turn_pair(6)
+        for operand, r, where in (("xb", 6, 0), ("xa", 6, 2), ("xb", 7, 1)):
+            turn(operand, r, where)
 
         stage = stage_tile(2)
-        widen(8, 1, stage, nc.gpsimd.tensor_copy)
-        sort_words("xa", 8, stage.bitcast(F32)[:, KB : KB + HALF], nc.gpsimd.tensor_copy)
-        finish_v(0, 0)
-        empty_xa(6)
+        widen_on_gpsimd(8, 2, stage)
         project_each((2, 1), (3, 1))
-        square_each((0, 1), (1, 1))
-        project_each((4, 0), (5, 0))
-        sort_words("xb", 8, sorted_tile(), nc.scalar.copy)
-        square_each((2, 1), (3, 1), (4, 0))
+        square(0, 1)
+        empty_xa(6)
+        project_each((4, 0))
+        square(1, 1)
+        project_each((5, 0))
+        square_each((2, 1), (3, 1))
         scale_pair(6)
-        widen(9, 1, plain_tile(BF16, KB), nc.vector.tensor_copy)
         quantize_pair_around(6, (0, 0))
         turn_pair(8)
 
-        widen(10, 2, stage_tile(3), nc.gpsimd.tensor_copy)
-        finish_v(0, 1)
-        empty_xa(8)
-        square(5, 0)
-        sort_words("xa", 10, sorted_tile(), nc.scalar.copy)
-        project_each((4, 1), (6, 0), (7, 0), (5, 1))
-        square_each((4, 1), (6, 0), (7, 0))
-        scale_pair(8)
-        quantize_pair_around(8, (0, 1))
-        turn_pair(10)
+        for r in (8, 10, 12):
+            piece = divmod(r // 2 - 3, 2)
+            widen_on_gpsimd(r + 2, 2, stage_tile((r // 2 + 3) % STAGES))
+            square_each((r - 4, 0), (r - 3, 0))
+            empty_xa(r)
+            if r != 10:
+                finish_v(*piece)
+            project_block(r - 2, r + 2)
+            scale_pair(r)
+            if r == 10:
+                finish_v(*piece)
+            quantize_pair_around(r, piece)
+            turn_pair(r + 2)
 
-        widen(12, 2, stage_tile(0), nc.gpsimd.tensor_copy)
-        finish_v(1, 0)
-        empty_xa(10)
-        square(5, 1)
-        sort_words("xa", 12, sorted_tile(), nc.scalar.copy)
-        project_each((6, 1), (7, 1), (8, 0), (9, 0))
-        square(6, 1)
-        project_each((8, 1))
-        square_each((7, 1), (8, 0))
-        sort_words("xb", 12, sorted_tile(), nc.scalar.copy)
-        scale_pair(10)
-        quantize_pair_around(10, (1, 0))
-        turn_pair(12, xb_order=(1, 0))
-
-        widen(14, 2, stage_tile(1), nc.gpsimd.tensor_copy)
-        finish_v(1, 1)
-        square_each((9, 0), (8, 1))
-        empty_xa(12)
-        sort_words("xa", 14, sorted_tile(), nc.scalar.copy)
-        project_each((10, 0), (11, 0), (9, 1))
+        late = [(10, 1), (11, 1), (12, 0), (13, 0), (14, 0), (15, 0), (12, 1), (13, 1), (14, 1), (15, 1)]
+        project_each(*late[:2])
         square_each((10, 0), (11, 0))
-        for r in (13, 12):
-            scale_xb(r)
-        for r in (13, 12):
-            quantize_x(r)
-        turn_pair(14)
-        begin_on_gpsimd(2, 0, 2)
-
-        product_banks.extend(turn_banks)
         empty_xa(14)
-        square(9, 1)
-        late = [(13, 0), (12, 0), (10, 1), (11, 1), (14, 0), (15, 0)] + [(r, 1) for r in range(12, ROWS)]
-        project_each(*late[:4])
         scale_pair(14)
         quantize_x(14)
         quantize_x(15)
-        for part in late[4:]:
-            square(*late[late.index(part) - 4])
-            project_each(part)
+        project_each(*late[2:4])
+        product_banks.extend(turn_banks)
+        for i in range(4, len(late)):
+            square(*late[i - 4])
+            project_each(late[i])
         square_each(*late[-4:])
-        finish_rest(2, 0)
-        quantize_v(1, 1)
-        quantize_v(2, 0)
+        finish_v(2, 0)
         finish_v(2, 1)
+        quantize_v(2, 0)
+        quantize_v(2, 1)
         finish_v(3, 0)
         quantize_v(3, 0)
-        quantize_v(2, 1)
 
         def moment_gap(i):
             moment(i, take(product_banks))
@@ -553,17 +550,24 @@ def tile_projection_moment_gap_s3_kernel(
         finish_v(3, 1)
         moment_gap(1)
         quantize_v(3, 1)
-        for i in (1, 2, 3):
-            moment_gap(i + 1)
-            scale_on_gpsimd(i)
+        scale_on_gpsimd(1)
+        moment_gap(2)
+        scale_on_gpsimd(2)
+        moment(4, take(product_banks), range(3))
+        moment(3, take(product_banks), range(2))
+        moment(4, None, [3])
+        moment(3, None, [2, 3])
+        subtract_target(4)
+        subtract_target(3)
+        scale_on_gpsimd(3)
         scale_on_vector(4)
         moment_gap(5)
         moment_gap(6)
         scale_on_gpsimd(6)
         scale_on_vector(5)
         moment_gap(7)
+        scale_on_gpsimd(7)
         moment_gap(8)
-        scale_on_vector(7)
         moment_gap(9)
         scale_on_vector(8)
         scale_on_vector(9)

@@ -28,11 +28,12 @@ ROWS = GROUPS * PACK
 PASSES = (KA + KB) // K_PASS
 HALF = 512
 QUARTER = HALF // 2
+PAIR = 2 * PASSES * K_PASS
 C_TILES = C // P
 HELD_BANK = 7
 STAGES = 4
 
-SCALAR_WA_COLUMNS = (256, 256)
+SCALAR_WA_COLUMNS = (336, 352)
 GAP = 16
 
 DOWN, BOOST, SMALL = 2.0**-10, 2.0**22, 2.0**-40 * (1 + 2.0**-12)
@@ -71,16 +72,14 @@ def tile_projection_moment_gap_s3_kernel(
         def grouped_tile():
             return work.tile([P, PACK * HALF], BF16, name="grouped", bufs=3, align_bytes=64)[:]
 
-        def stage_tile(i):
-            return work.tile([P, 2 * PASSES * K_PASS], BF16, name="stage%d" % i, bufs=1, align_bytes=64)[:]
+        def stage_tile(i, extra=0):
+            return work.tile([P, PAIR + extra], BF16, name="stage%d" % i, bufs=1, align_bytes=64)[:]
 
         def opening_tile(dtype, width):
             return work.tile([P, width], dtype, name="opening", bufs=1)[:]
 
         scale_col = keep.tile([P, 2, PACK], F32, name="scale_col")
-        one = keep.tile([P, 1], F32, name="one")
         opening_one = opening_tile(F32, 1)
-        minus_small = keep.tile([P, 1], F32, name="minus_small")
         wa_rows = [large_tile(BF16, PACK * HALF).rearrange("p (t n) -> p t n", t=PACK) for half in range(2)]
         wa_codes = mx_tile("wa_codes", U32, 4, N, MOVING)
         wa_bytes = mx_tile("wa_bytes", U8, 1, N, MOVING_SCALE)
@@ -91,9 +90,10 @@ def tile_projection_moment_gap_s3_kernel(
         wb_bytes = mx_tile("wb_bytes", U8, 1, 2 * N, MOVING_SCALE).rearrange("p (g n) -> p g n", g=2)
         z_tile = mx_tile("z_tile", U8, 1, GROUPS * 2 * C, STATIONARY).rearrange("p (g n) -> p g n", g=GROUPS)
         z_bytes = mx_tile("z_bytes", U8, 1, GROUPS * C, STATIONARY_SCALE).rearrange("p (g n) -> p g n", g=GROUPS)
-        omega_lines = keep.tile([P, K_PASS], BF16, name="omega_lines")
+        lines = keep.tile([P, 2 * HALF], BF16, name="lines")
+        omega_lines = lines[:, :K_PASS]
         prec_rows = keep.tile([P, N], BF16, name="prec_rows")
-        prec_line = keep.tile([P, HALF], BF16, name="prec_line")
+        prec_line = lines[:, HALF:]
         ones = keep.tile([P, P], BF16, name="ones")
         target_rows = keep.tile([P, C_TILES, N], BF16, name="target_rows")
         ident = keep.tile([P, P], F32, name="ident")
@@ -128,31 +128,27 @@ def tile_projection_moment_gap_s3_kernel(
                 nc.sync.dma_start(out=tile[i:P:32].bitcast(I32), in_=rows[i].bitcast(I32))
 
         nc.vector.memset(zeros[:].bitcast(I32), 0)
-        nc.vector.memset(omega_lines[:].bitcast(I32), 0)
         nc.vector.memset(ident[:], 0.0)
-        nc.vector.memset(prec_line[:].bitcast(I32), 0)
-        nc.vector.memset(one[:], 1.0)
+        make_identity(nc, ident[:], nomemset=True)
+        nc.vector.memset(lines[:].bitcast(I32), 0)
+        nc.vector.memset(wb_bytes[:].rearrange("p g n -> p (g n)").bitcast(I32), 0)
         nc.vector.memset(ones[:], 1.0)
         nc.vector.memset(opening_one, 1.0)
-        nc.vector.memset(minus_small[:], -SMALL)
-        nc.vector.memset(wb_bytes[:].rearrange("p g n -> p (g n)").bitcast(I32), 0)
-        make_identity(nc, ident[:], nomemset=True)
-        nc.vector.memset(z_bytes[:].rearrange("p g n -> p (g n)").bitcast(I32), 0)
 
         load_xb(0, 1)
         load_xb(1, 1)
         nc.sync.dma_start(out=scale_col[:], in_=xb_scale.rearrange("o (i p t) -> p (o i) t", i=2, t=PACK))
+        nc.sync.dma_start(out=omega_lines[0:GROUPS, :], in_=omega.rearrange("(g k) -> g k", g=GROUPS))
         load_xb(2, 2)
         load_xa(0)
         load_wa(0)
-        nc.sync.dma_start(out=omega_lines[0:GROUPS, :], in_=omega.rearrange("(g k) -> g k", g=GROUPS))
         nc.sync.dma_start(out=prec_line[0:1, :], in_=prec[HALF:].unsqueeze(0))
         load_xa(2)
         load_wb(0)
         load_scale_bytes(wb_bytes, wb_scales)
         load_xb(4, 2)
-        load_xa(4)
         load_wa(1)
+        load_xa(4)
         load_wb(1)
         load_xb(6, 2)
         load_xa(6)
@@ -162,10 +158,6 @@ def tile_projection_moment_gap_s3_kernel(
         load_xb(12, 4)
         for r in (12, 14):
             load_xa(r)
-        load_scale_bytes(z_bytes, z_scales)
-        nc.sync.dma_start(out=z_tile[:], in_=z_words.rearrange("g p n -> p g n"))
-        nc.sync.dma_start(out=target_rows[:], in_=target.rearrange("(ct c) n -> c ct n", c=P))
-        nc.sync.dma_start(out=prec_rows[:], in_=prec.partition_broadcast(P))
 
         def warm_up(count):
             tile = bank(HELD_BANK)
@@ -247,11 +239,13 @@ def tile_projection_moment_gap_s3_kernel(
                 for u in range(2):
                     nc.tensor.transpose(tile[:, P * (2 * u + i) : P * (2 * u + i + 1)], words[part][u], ident[:])
 
+        x_stage = {}
         x_grouped = {}
 
         def grouped_pair(r):
             if r // 2 not in x_grouped:
-                x_grouped[r // 2] = stage_tile(r // 2 % STAGES).rearrange("p (s k) -> p s k", k=K_PASS)
+                x_stage[r // 2] = stage_tile(r // 2 % STAGES, PACK * HALF if r // 2 == 6 else 0)
+                x_grouped[r // 2] = x_stage[r // 2][:, :PAIR].rearrange("p (s k) -> p s k", k=K_PASS)
             return x_grouped[r // 2]
 
         def empty_xa(r):
@@ -331,9 +325,13 @@ def tile_projection_moment_gap_s3_kernel(
                 op=MULT,
             )
 
-        def finish_v(g, half):
-            v_grouped[g, half] = grouped_tile()
-            finish_columns(g, half, 0, HALF, nc.vector, held[:, HALF:])
+        def finish_v(g, half, c0=0, c1=HALF):
+            if (g, half) not in v_grouped:
+                v_grouped[g, half] = grouped_tile()
+            finish_columns(g, half, c0, c1, nc.vector, held[:, HALF:])
+
+        def finish_on_gpsimd(g, half, c0, c1):
+            finish_columns(g, half, c0, c1, nc.gpsimd, factor)
 
         def quantize_v(g, half):
             codes = mx_tile("v_codes%d_%d" % (g, half), U32, 4, HALF, MOVING)
@@ -391,12 +389,17 @@ def tile_projection_moment_gap_s3_kernel(
         boost_power = keep.tile([P, 2 * ROWS], F32, name="boost_power")
         size, sign, boost, power = size_sign[:, :ROWS], size_sign[:, ROWS:], boost_power[:, :ROWS], boost_power[:, ROWS:]
         side = keep.tile([P, ROWS], F32, name="side")
-        warm_up(5)
+        warm_up(4)
         nc.scalar.activation(out=root[:], in_=zeros[:, :ROWS], func=SQRT)
         for r in range(2):
             widen_on_vector(r, opening_one)
             turn("xb", r, r)
             warm_up(1 - r)
+        omega_bank = bank(6)
+        for t in range(PACK):
+            nc.tensor.matmul(
+                out=omega_bank[:, t:ROWS:PACK], lhsT=omega_lines[:, t::PACK], rhs=ident_bf16[:, :GROUPS], start=True, stop=True
+            )
         widen_on_scalar(2)
         widen_on_gpsimd(3, 1, opening_tile(BF16, KB))
         scale_xb(0)
@@ -405,31 +408,26 @@ def tile_projection_moment_gap_s3_kernel(
         turn("xb", 2, 2)
         warm_up(1)
         turn("xb", 3, 4)
-        omega_bank = bank(6)
-        for t in range(PACK):
-            nc.tensor.matmul(
-                out=omega_bank[:, t:ROWS:PACK], lhsT=omega_lines[:, t::PACK], rhs=ident_bf16[:, :GROUPS], start=True, stop=True
-            )
         warm_up(1)
         turn("xa", 2, 5)
         warm_up(2)
         held = bank(HELD_BANK, BF16, 2 * HALF)
-        nc.tensor.matmul(out=held[:, :HALF], lhsT=ones[:], rhs=prec_line[:], start=True, stop=True)
-        empty_xa(0)
-        wa_first = grouped_tile()
-        group_wa(0, wa_first, 0, SCALAR_WA_COLUMNS[0], nc.scalar.copy)
-        group_wa(0, wa_first, SCALAR_WA_COLUMNS[0], HALF, nc.vector.tensor_copy)
+        nc.tensor.matmul(out=held[:, :HALF], lhsT=ones[:], rhs=prec_line, start=True, stop=True)
         nc.scalar.activation(out=size, in_=omega_bank[:, :ROWS], func=ABS)
         nc.scalar.activation(out=sign, in_=omega_bank[:, :ROWS], func=SIGN)
-        nc.scalar.activation(out=side[:], in_=size, func=SIGN, bias=minus_small[:])
+        nc.scalar.activation(out=side[:], in_=size, func=SIGN, bias=-SMALL)
+        empty_xa(0)
         nc.scalar.activation(out=boost, in_=side[:], func=COPY, scale=(1 - BOOST) / 2, bias=(1 + BOOST) / 2)
         nc.scalar.activation(
             out=power, in_=side[:], func=COPY, scale=(1 - 1 / BOOST) / DOWN / 2, bias=(1 + 1 / BOOST) / DOWN / 2
         )
+        wa_first = stage_tile(STAGES)[:, : PACK * HALF]
+        group_wa(0, wa_first, 0, SCALAR_WA_COLUMNS[0], nc.scalar.copy)
+        group_wa(0, wa_first, SCALAR_WA_COLUMNS[0], HALF, nc.gpsimd.tensor_copy)
         quantize_x(0)
-        quantize_wa(0, wa_first)
-        quantize_x(1)
         nc.vector.tensor_tensor(out=radicand_factor[:], in0=size_sign[:], in1=boost_power[:], op=MULT)
+        quantize_x(1)
+        quantize_wa(0, wa_first)
 
         turn_banks, product_banks = [0, 1, 2], [6, 3, 5, 4]
 
@@ -464,7 +462,7 @@ def tile_projection_moment_gap_s3_kernel(
             square(r - 1, 1)
             project_each((r + 1, 0))
 
-        widen_on_gpsimd(5, 1, stage_tile(0))
+        widen_on_gpsimd(5, 1, stage_tile(STAGES))
         empty_xa(2)
         widen_on_scalar(4)
         nc.scalar.activation(out=root[:], in_=radicand, func=SQRT, scale=DOWN)
@@ -472,23 +470,23 @@ def tile_projection_moment_gap_s3_kernel(
         scale_pair(2)
         turn_pair(4)
         nc.tensor.matmul(out=held[:, HALF : HALF + ROWS], lhsT=ident_bf16, rhs=factor, start=True, stop=True)
-        wa_second = stage_tile(STAGES)[:, : PACK * HALF]
-        square(0, 0)
+        wa_second = stage_tile(STAGES + 1)[:, : PACK * HALF]
         group_wa(1, wa_second, 0, SCALAR_WA_COLUMNS[1], nc.scalar.copy)
+        square(0, 0)
+        group_wa(1, wa_second, SCALAR_WA_COLUMNS[1], HALF, nc.gpsimd.tensor_copy)
         quantize_x(2)
-        group_wa(1, wa_second, SCALAR_WA_COLUMNS[1], HALF, nc.vector.tensor_copy)
         quantize_x(3)
         quantize_wa(1, wa_second)
         square(1, 0)
 
-        stage = stage_tile(STAGES)
+        stage = stage_tile(STAGES + 1)
         widen_on_gpsimd(6, 1, stage)
         widen_on_gpsimd(7, 1, stage[:, KB:])
         project_each((2, 0), (3, 0), (0, 1), (1, 1))
         square_each((2, 0), (3, 0))
         empty_xa(4)
         scale_pair(4)
-        finish_v(0, 0)
+        finish_v(0, 0, 0, QUARTER)
         quantize_x(4)
         quantize_x(5)
         for operand, r, where in (("xb", 6, 0), ("xa", 6, 2), ("xb", 7, 1)):
@@ -504,15 +502,22 @@ def tile_projection_moment_gap_s3_kernel(
         project_each((5, 0))
         square_each((2, 1), (3, 1))
         scale_pair(6)
+        finish_v(0, 0, QUARTER, HALF)
         quantize_pair_around(6, (0, 0))
         turn_pair(8)
 
-        for r in (8, 10, 12):
+        for r in (8, 10):
             piece = divmod(r // 2 - 3, 2)
             widen_on_gpsimd(r + 2, 2, stage_tile((r // 2 + 3) % STAGES))
+            if r == 8:
+                nc.gpsimd.memset(z_bytes[:].rearrange("p g n -> p (g n)").bitcast(I32), 0)
+                load_scale_bytes(z_bytes, z_scales)
+                nc.sync.dma_start(out=z_tile[:], in_=z_words.rearrange("g p n -> p g n"))
+                nc.sync.dma_start(out=target_rows[:], in_=target.rearrange("(ct c) n -> c ct n", c=P))
+                nc.sync.dma_start(out=prec_rows[:], in_=prec.partition_broadcast(P))
             square_each((r - 4, 0), (r - 3, 0))
             empty_xa(r)
-            if r != 10:
+            if r == 8:
                 finish_v(*piece)
             project_block(r - 2, r + 2)
             scale_pair(r)
@@ -521,9 +526,21 @@ def tile_projection_moment_gap_s3_kernel(
             quantize_pair_around(r, piece)
             turn_pair(r + 2)
 
+        widen_on_gpsimd(14, 2, stage_tile(1))
+        square_each((8, 0), (9, 0))
+        empty_xa(12)
+        project_block(10, 14)
+        scale_pair(12)
+        v_grouped[1, 1] = x_stage[6][:, PAIR - PACK * 224 : PAIR + PACK * (HALF - 224)]
+        finish_v(1, 1, 224, HALF)
+        quantize_x(12)
+        quantize_x(13)
+        turn_pair(14)
+
         late = [(10, 1), (11, 1), (12, 0), (13, 0), (14, 0), (15, 0), (12, 1), (13, 1), (14, 1), (15, 1)]
         project_each(*late[:2])
         square_each((10, 0), (11, 0))
+        finish_on_gpsimd(1, 1, 0, 224)
         empty_xa(14)
         scale_pair(14)
         quantize_x(14)
@@ -534,11 +551,14 @@ def tile_projection_moment_gap_s3_kernel(
             square(*late[i - 4])
             project_each(late[i])
         square_each(*late[-4:])
+        v_grouped[2, 1] = stage_tile(3)[:, : PACK * HALF]
+        finish_on_gpsimd(2, 1, 0, 144)
         finish_v(2, 0)
-        finish_v(2, 1)
+        finish_v(2, 1, 144, HALF)
         quantize_v(2, 0)
-        quantize_v(2, 1)
+        quantize_v(1, 1)
         finish_v(3, 0)
+        quantize_v(2, 1)
         quantize_v(3, 0)
 
         def moment_gap(i):

@@ -137,11 +137,11 @@ def tile_projection_moment_gap_s3_kernel(
 
         load_xb(0, 1)
         load_xb(1, 1)
+        load_xb(2, 2)
         nc.sync.dma_start(out=scale_col[:], in_=xb_scale.rearrange("o (i p t) -> p (o i) t", i=2, t=PACK))
         nc.sync.dma_start(out=omega_lines[0:GROUPS, :], in_=omega.rearrange("(g k) -> g k", g=GROUPS))
-        load_xb(2, 2)
-        load_xa(0)
         load_wa(0)
+        load_xa(0)
         nc.sync.dma_start(out=prec_line[0:1, :], in_=prec[HALF:].unsqueeze(0))
         load_xa(2)
         load_wb(0)
@@ -379,7 +379,8 @@ def tile_projection_moment_gap_s3_kernel(
 
         def store(i):
             c0, width, ct = tiles[i]
-            nc.sync.dma_start(out=out[P * ct : P * (ct + 1), c0 : c0 + width], in_=results[i])
+            queue = nc.scalar if i in (0, 1, 2, 3, 6, 7) else nc.sync
+            queue.dma_start(out=out[P * ct : P * (ct + 1), c0 : c0 + width], in_=results[i])
 
         def take(ring):
             ring.append(ring.pop(0))
@@ -391,50 +392,61 @@ def tile_projection_moment_gap_s3_kernel(
         side = keep.tile([P, ROWS], F32, name="side")
         warm_up(4)
         nc.scalar.activation(out=root[:], in_=zeros[:, :ROWS], func=SQRT)
-        for r in range(2):
-            widen_on_vector(r, opening_one)
-            turn("xb", r, r)
-            warm_up(1 - r)
+        widen_on_vector(0, opening_one)
+        widen_on_vector(1, opening_one)
+        turn("xb", 0, 0)
+        warm_up(1)
         omega_bank = bank(6)
         for t in range(PACK):
             nc.tensor.matmul(
                 out=omega_bank[:, t:ROWS:PACK], lhsT=omega_lines[:, t::PACK], rhs=ident_bf16[:, :GROUPS], start=True, stop=True
             )
+        turn("xb", 1, 1)
         widen_on_scalar(2)
         widen_on_gpsimd(3, 1, opening_tile(BF16, KB))
-        scale_xb(0)
-        scale_xb(1)
-        turn("xa", 0, 3)
-        turn("xb", 2, 2)
-        warm_up(1)
-        turn("xb", 3, 4)
-        warm_up(1)
-        turn("xa", 2, 5)
-        warm_up(2)
-        held = bank(HELD_BANK, BF16, 2 * HALF)
-        nc.tensor.matmul(out=held[:, :HALF], lhsT=ones[:], rhs=prec_line, start=True, stop=True)
         nc.scalar.activation(out=size, in_=omega_bank[:, :ROWS], func=ABS)
         nc.scalar.activation(out=sign, in_=omega_bank[:, :ROWS], func=SIGN)
         nc.scalar.activation(out=side[:], in_=size, func=SIGN, bias=-SMALL)
-        empty_xa(0)
+        scale_xb(0)
+        scale_xb(1)
+        warm_up(1)
+        turn("xb", 2, 2)
+        warm_up(1)
+        turn("xa", 0, 3)
+        turn("xb", 3, 4)
+        warm_up(1)
+        turn("xa", 2, 5)
+        warm_up(1)
+        held = bank(HELD_BANK, BF16, 2 * HALF)
+        nc.tensor.matmul(out=held[:, :HALF], lhsT=ones[:], rhs=prec_line, start=True, stop=True)
+        wa_first = grouped_tile()
+        group_wa(0, wa_first, 0, 336, nc.scalar.copy)
+        group_wa(0, wa_first, 336, 336 + 176, nc.gpsimd.tensor_copy)
         nc.scalar.activation(out=boost, in_=side[:], func=COPY, scale=(1 - BOOST) / 2, bias=(1 + BOOST) / 2)
         nc.scalar.activation(
             out=power, in_=side[:], func=COPY, scale=(1 - 1 / BOOST) / DOWN / 2, bias=(1 + 1 / BOOST) / DOWN / 2
         )
-        wa_first = stage_tile(STAGES)[:, : PACK * HALF]
-        group_wa(0, wa_first, 0, SCALAR_WA_COLUMNS[0], nc.scalar.copy)
-        group_wa(0, wa_first, SCALAR_WA_COLUMNS[0], HALF, nc.gpsimd.tensor_copy)
-        quantize_x(0)
-        nc.vector.tensor_tensor(out=radicand_factor[:], in0=size_sign[:], in1=boost_power[:], op=MULT)
-        quantize_x(1)
+        empty_xa(0)
+        nc.vector.memset(z_bytes[:].rearrange("p g n -> p (g n)").bitcast(I32), 0)
+        load_scale_bytes(z_bytes, z_scales)
+        nc.sync.dma_start(out=z_tile[:], in_=z_words.rearrange("g p n -> p g n"))
+        nc.sync.dma_start(out=target_rows[:], in_=target.rearrange("(ct c) n -> c ct n", c=P))
+        nc.sync.dma_start(out=prec_rows[:], in_=prec.partition_broadcast(P))
         quantize_wa(0, wa_first)
+        nc.vector.tensor_tensor(out=radicand_factor[:], in0=size_sign[:], in1=boost_power[:], op=MULT)
+        quantize_x(0)
+        quantize_x(1)
 
         turn_banks, product_banks = [0, 1, 2], [6, 3, 5, 4]
 
         def turn_pair(r):
+            turn("xb", r, 0)
+            turn("xa", r, 2)
+            turn("xb", r + 1, 1)
+
+        def widen_pair_on_gpsimd(r, stage):
             for i in range(2):
-                turn("xb", r + i, take(turn_banks))
-            turn("xa", r, take(turn_banks))
+                widen_on_gpsimd(r + i, 1, stage[:, KB * i :])
 
         def project_each(*parts):
             for r, half in parts:
@@ -462,7 +474,7 @@ def tile_projection_moment_gap_s3_kernel(
             square(r - 1, 1)
             project_each((r + 1, 0))
 
-        widen_on_gpsimd(5, 1, stage_tile(STAGES))
+        widen_on_gpsimd(5, 1, stage_tile(0))
         empty_xa(2)
         widen_on_scalar(4)
         nc.scalar.activation(out=root[:], in_=radicand, func=SQRT, scale=DOWN)
@@ -470,18 +482,16 @@ def tile_projection_moment_gap_s3_kernel(
         scale_pair(2)
         turn_pair(4)
         nc.tensor.matmul(out=held[:, HALF : HALF + ROWS], lhsT=ident_bf16, rhs=factor, start=True, stop=True)
-        wa_second = stage_tile(STAGES + 1)[:, : PACK * HALF]
+        wa_second = stage_tile(STAGES)[:, : PACK * HALF]
         group_wa(1, wa_second, 0, SCALAR_WA_COLUMNS[1], nc.scalar.copy)
         square(0, 0)
-        group_wa(1, wa_second, SCALAR_WA_COLUMNS[1], HALF, nc.gpsimd.tensor_copy)
         quantize_x(2)
+        group_wa(1, wa_second, SCALAR_WA_COLUMNS[1], HALF, nc.vector.tensor_copy)
         quantize_x(3)
         quantize_wa(1, wa_second)
         square(1, 0)
 
-        stage = stage_tile(STAGES + 1)
-        widen_on_gpsimd(6, 1, stage)
-        widen_on_gpsimd(7, 1, stage[:, KB:])
+        widen_pair_on_gpsimd(6, stage_tile(STAGES))
         project_each((2, 0), (3, 0), (0, 1), (1, 1))
         square_each((2, 0), (3, 0))
         empty_xa(4)
@@ -489,11 +499,9 @@ def tile_projection_moment_gap_s3_kernel(
         finish_v(0, 0, 0, QUARTER)
         quantize_x(4)
         quantize_x(5)
-        for operand, r, where in (("xb", 6, 0), ("xa", 6, 2), ("xb", 7, 1)):
-            turn(operand, r, where)
+        turn_pair(6)
 
-        stage = stage_tile(2)
-        widen_on_gpsimd(8, 2, stage)
+        widen_on_gpsimd(8, 2, stage_tile(2))
         project_each((2, 1), (3, 1))
         square(0, 1)
         empty_xa(6)
@@ -508,13 +516,7 @@ def tile_projection_moment_gap_s3_kernel(
 
         for r in (8, 10):
             piece = divmod(r // 2 - 3, 2)
-            widen_on_gpsimd(r + 2, 2, stage_tile((r // 2 + 3) % STAGES))
-            if r == 8:
-                nc.gpsimd.memset(z_bytes[:].rearrange("p g n -> p (g n)").bitcast(I32), 0)
-                load_scale_bytes(z_bytes, z_scales)
-                nc.sync.dma_start(out=z_tile[:], in_=z_words.rearrange("g p n -> p g n"))
-                nc.sync.dma_start(out=target_rows[:], in_=target.rearrange("(ct c) n -> c ct n", c=P))
-                nc.sync.dma_start(out=prec_rows[:], in_=prec.partition_broadcast(P))
+            widen_pair_on_gpsimd(r + 2, stage_tile((r // 2 + 3) % STAGES))
             square_each((r - 4, 0), (r - 3, 0))
             empty_xa(r)
             if r == 8:
@@ -526,13 +528,13 @@ def tile_projection_moment_gap_s3_kernel(
             quantize_pair_around(r, piece)
             turn_pair(r + 2)
 
-        widen_on_gpsimd(14, 2, stage_tile(1))
+        widen_pair_on_gpsimd(14, stage_tile(1))
         square_each((8, 0), (9, 0))
         empty_xa(12)
         project_block(10, 14)
         scale_pair(12)
-        v_grouped[1, 1] = x_stage[6][:, PAIR - PACK * 224 : PAIR + PACK * (HALF - 224)]
-        finish_v(1, 1, 224, HALF)
+        v_grouped[1, 1] = x_stage[6][:, PAIR - PACK * 192 : PAIR + PACK * (HALF - 192)]
+        finish_v(1, 1, 192, HALF)
         quantize_x(12)
         quantize_x(13)
         turn_pair(14)
@@ -540,7 +542,7 @@ def tile_projection_moment_gap_s3_kernel(
         late = [(10, 1), (11, 1), (12, 0), (13, 0), (14, 0), (15, 0), (12, 1), (13, 1), (14, 1), (15, 1)]
         project_each(*late[:2])
         square_each((10, 0), (11, 0))
-        finish_on_gpsimd(1, 1, 0, 224)
+        finish_on_gpsimd(1, 1, 0, 192)
         empty_xa(14)
         scale_pair(14)
         quantize_x(14)
@@ -552,9 +554,9 @@ def tile_projection_moment_gap_s3_kernel(
             project_each(late[i])
         square_each(*late[-4:])
         v_grouped[2, 1] = stage_tile(3)[:, : PACK * HALF]
-        finish_on_gpsimd(2, 1, 0, 144)
+        finish_on_gpsimd(2, 1, 0, 112)
         finish_v(2, 0)
-        finish_v(2, 1, 144, HALF)
+        finish_v(2, 1, 112, HALF)
         quantize_v(2, 0)
         quantize_v(1, 1)
         finish_v(3, 0)
@@ -591,5 +593,5 @@ def tile_projection_moment_gap_s3_kernel(
         moment_gap(9)
         scale_on_vector(8)
         scale_on_vector(9)
-        for i in (0, 1, 2, 4, 3, 5, 6, 7, 8, 9):
+        for i in (0, 1, 4, 2, 5, 3, 6, 7, 8, 9):
             store(i)

@@ -278,18 +278,20 @@ def tile_projection_moment_gap_s3_kernel(
 
         products = {}
 
-        def project(r, half, where):
+        def project(r, half, where, c0=0, width=HALF):
             tile = bank(where)
-            products[r, half] = tile
-            cols = slice(HALF * half, HALF * (half + 1))
+            products[r, half, c0] = tile[:, :width]
+            first = HALF * half + c0
+            cols = slice(first, first + width)
             codes, scale_bytes = x_codes[r]
             for s in range(PASSES):
                 if s == 0:
                     rhs, rhs_scale = wa_codes[:, cols].bitcast(FP8X4), wa_bytes[:, cols]
                 else:
-                    rhs, rhs_scale = wb_tiles[half][:, s - 1, :].bitcast(FP4X4), wb_bytes[:, s - 1, cols]
+                    rhs = wb_tiles[half][:, s - 1, 2 * c0 : 2 * (c0 + width)].bitcast(FP4X4)
+                    rhs_scale = wb_bytes[:, s - 1, cols]
                 nc.tensor.matmul_mx(
-                    out=tile[:],
+                    out=tile[:, :width],
                     lhsT=codes[:, P * s : P * (s + 1)].bitcast(FP8X4),
                     lhsT_scale=scale_bytes[:, P * s : P * (s + 1)],
                     rhs=rhs,
@@ -303,12 +305,15 @@ def tile_projection_moment_gap_s3_kernel(
         radicand, factor = radicand_factor[:, :ROWS], radicand_factor[:, ROWS:]
         squares = {}
 
-        def square(r, half):
+        def square(r, half, c0=0, width=HALF):
             g, t = divmod(r, PACK)
             if (g, half) not in squares:
                 squares[g, half] = large_tile(BF16, PACK * HALF).rearrange("p (a n e) -> p a n e", a=2, e=2)
             nc.scalar.activation(
-                out=squares[g, half][:, t // 2, :, t % 2], in_=products[r, half][:], func=SQUARE, scale=root[:, r : r + 1]
+                out=squares[g, half][:, t // 2, c0 : c0 + width, t % 2],
+                in_=products[r, half, c0],
+                func=SQUARE,
+                scale=root[:, r : r + 1],
             )
 
         v_grouped = {}
@@ -333,11 +338,18 @@ def tile_projection_moment_gap_s3_kernel(
         def finish_on_gpsimd(g, half, c0, c1):
             finish_columns(g, half, c0, c1, nc.gpsimd, factor)
 
-        def quantize_v(g, half):
-            codes = mx_tile("v_codes%d_%d" % (g, half), U32, 4, HALF, MOVING)
-            scale_bytes = mx_tile("v_bytes%d_%d" % (g, half), U8, 1, HALF, MOVING_SCALE)
-            nc.vector.quantize_mx(out=codes.bitcast(FP8X4), scales=scale_bytes, in_=v_grouped[g, half])
-            v_codes[g, half] = (codes, scale_bytes)
+        def quantize_v(g, half, c0=0, c1=HALF):
+            if (g, half) not in v_codes:
+                v_codes[g, half] = (
+                    mx_tile("v_codes%d_%d" % (g, half), U32, 4, HALF, MOVING),
+                    mx_tile("v_bytes%d_%d" % (g, half), U8, 1, HALF, MOVING_SCALE),
+                )
+            codes, scale_bytes = v_codes[g, half]
+            nc.vector.quantize_mx(
+                out=codes[:, c0:c1].bitcast(FP8X4),
+                scales=scale_bytes[:, c0:c1],
+                in_=v_grouped[g, half][:, PACK * c0 : PACK * c1],
+            )
 
         tiles = [(c0, HALF, ct) for c0 in (0, HALF) for ct in range(C_TILES)][:-2]
         tiles = tiles + [(c0, QUARTER, ct) for ct in (C_TILES - 2, C_TILES - 1) for c0 in (HALF, HALF + QUARTER)]
@@ -367,9 +379,9 @@ def tile_projection_moment_gap_s3_kernel(
                 out=gaps[i], in0=sums[i][:, :width], in1=target_rows[:, ct, c0 : c0 + width], op=SUBTRACT
             )
 
-        def scale_on_gpsimd(i):
+        def scale_on_gpsimd(i, tile=None):
             c0, width, ct = tiles[i]
-            results[i] = large_tile(F32, width)
+            results[i] = large_tile(F32, width) if tile is None else tile
             nc.gpsimd.tensor_tensor(out=results[i], in0=gaps[i], in1=prec_rows[:, c0 : c0 + width], op=MULT)
 
         def scale_on_vector(i):
@@ -521,7 +533,7 @@ def tile_projection_moment_gap_s3_kernel(
             empty_xa(r)
             if r == 8:
                 finish_v(*piece)
-            project_block(r - 2, r + 2)
+            project_block(r - 2, r + 2 if r + 2 in (10, 12) else None)
             scale_pair(r)
             if r == 10:
                 finish_v(*piece)
@@ -531,7 +543,7 @@ def tile_projection_moment_gap_s3_kernel(
         widen_pair_on_gpsimd(14, stage_tile(1))
         square_each((8, 0), (9, 0))
         empty_xa(12)
-        project_block(10, 14)
+        project_block(10)
         scale_pair(12)
         v_grouped[1, 1] = x_stage[6][:, PAIR - PACK * 192 : PAIR + PACK * (HALF - 192)]
         finish_v(1, 1, 192, HALF)
@@ -560,8 +572,8 @@ def tile_projection_moment_gap_s3_kernel(
         quantize_v(2, 0)
         quantize_v(1, 1)
         finish_v(3, 0)
-        quantize_v(2, 1)
         quantize_v(3, 0)
+        quantize_v(2, 1)
 
         def moment_gap(i):
             moment(i, take(product_banks))
@@ -572,7 +584,7 @@ def tile_projection_moment_gap_s3_kernel(
         finish_v(3, 1)
         moment_gap(1)
         quantize_v(3, 1)
-        scale_on_gpsimd(1)
+        scale_on_gpsimd(1, v_grouped[3, 1].bitcast(F32)[:, HALF:])
         moment_gap(2)
         scale_on_gpsimd(2)
         moment(4, take(product_banks), range(3))

@@ -159,10 +159,9 @@ def tile_projection_moment_gap_s3_kernel(
         for r in (12, 14):
             load_xa(r)
 
-        def warm_up(count):
-            tile = bank(HELD_BANK)
+        def warm_up(count, tile, moving=zeros[:]):
             for i in range(count):
-                nc.tensor.matmul(out=tile[:], lhsT=zeros[:, :P], rhs=zeros[:], start=True, stop=True)
+                nc.tensor.matmul(out=tile[:], lhsT=zeros[:, :P], rhs=moving, start=True, stop=True)
 
         def group_wa(half, grouped, c0, c1, copy):
             copy(
@@ -278,8 +277,7 @@ def tile_projection_moment_gap_s3_kernel(
 
         products = {}
 
-        def project(r, half, where, c0=0, width=HALF):
-            tile = bank(where)
+        def project(r, half, tile, c0=0, width=HALF):
             products[r, half, c0] = tile[:, :width]
             first = HALF * half + c0
             cols = slice(first, first + width)
@@ -402,12 +400,13 @@ def tile_projection_moment_gap_s3_kernel(
         boost_power = keep.tile([P, 2 * ROWS], F32, name="boost_power")
         size, sign, boost, power = size_sign[:, :ROWS], size_sign[:, ROWS:], boost_power[:, :ROWS], boost_power[:, ROWS:]
         side = keep.tile([P, ROWS], F32, name="side")
-        warm_up(4)
+        idle_bank = bank(HELD_BANK)
+        warm_up(4, idle_bank)
         nc.scalar.activation(out=root[:], in_=zeros[:, :ROWS], func=SQRT)
         widen_on_vector(0, opening_one)
         widen_on_vector(1, opening_one)
         turn("xb", 0, 0)
-        warm_up(1)
+        warm_up(1, idle_bank)
         omega_bank = bank(6)
         for t in range(PACK):
             nc.tensor.matmul(
@@ -421,24 +420,24 @@ def tile_projection_moment_gap_s3_kernel(
         nc.scalar.activation(out=side[:], in_=size, func=SIGN, bias=-SMALL)
         scale_xb(0)
         scale_xb(1)
-        warm_up(1)
+        warm_up(1, idle_bank)
         turn("xb", 2, 2)
-        warm_up(1)
+        warm_up(1, idle_bank)
         turn("xa", 0, 3)
         turn("xb", 3, 4)
-        warm_up(1)
-        turn("xa", 2, 5)
-        warm_up(1)
         held = bank(HELD_BANK, BF16, 2 * HALF)
         nc.tensor.matmul(out=held[:, :HALF], lhsT=ones[:], rhs=prec_line, start=True, stop=True)
+        turn("xa", 2, 5)
         wa_first = grouped_tile()
-        group_wa(0, wa_first, 0, 336, nc.scalar.copy)
-        group_wa(0, wa_first, 336, 336 + 176, nc.gpsimd.tensor_copy)
+        group_wa(0, wa_first, 0, 320, nc.scalar.copy)
+        group_wa(0, wa_first, 320, 320 + 192, nc.gpsimd.tensor_copy)
         nc.scalar.activation(out=boost, in_=side[:], func=COPY, scale=(1 - BOOST) / 2, bias=(1 + BOOST) / 2)
         nc.scalar.activation(
             out=power, in_=side[:], func=COPY, scale=(1 - 1 / BOOST) / DOWN / 2, bias=(1 + 1 / BOOST) / DOWN / 2
         )
         empty_xa(0)
+        first_bank = bank(6)
+        warm_up(2, first_bank, x_stage[0][:, :HALF])
         nc.vector.memset(z_bytes[:].rearrange("p g n -> p (g n)").bitcast(I32), 0)
         load_scale_bytes(z_bytes, z_scales)
         nc.sync.dma_start(out=z_tile[:], in_=z_words.rearrange("g p n -> p g n"))
@@ -449,7 +448,7 @@ def tile_projection_moment_gap_s3_kernel(
         quantize_x(0)
         quantize_x(1)
 
-        turn_banks, product_banks = [0, 1, 2], [6, 3, 5, 4]
+        turn_banks, product_banks = [0, 1, 2], [3, 5, 4, 6]
 
         def turn_pair(r):
             turn("xb", r, 0)
@@ -462,7 +461,7 @@ def tile_projection_moment_gap_s3_kernel(
 
         def project_each(*parts):
             for r, half in parts:
-                project(r, half, take(product_banks))
+                project(r, half, bank(take(product_banks)))
 
         def square_each(*parts):
             for r, half in parts:
@@ -490,15 +489,17 @@ def tile_projection_moment_gap_s3_kernel(
         empty_xa(2)
         widen_on_scalar(4)
         nc.scalar.activation(out=root[:], in_=radicand, func=SQRT, scale=DOWN)
-        project_each((0, 0), (1, 0))
+        project(0, 0, first_bank)
+        project_each((1, 0))
         scale_pair(2)
         turn_pair(4)
         nc.tensor.matmul(out=held[:, HALF : HALF + ROWS], lhsT=ident_bf16, rhs=factor, start=True, stop=True)
         wa_second = stage_tile(STAGES)[:, : PACK * HALF]
         group_wa(1, wa_second, 0, SCALAR_WA_COLUMNS[1], nc.scalar.copy)
         square(0, 0)
+        group_wa(1, wa_second, SCALAR_WA_COLUMNS[1], SCALAR_WA_COLUMNS[1] + 80, nc.gpsimd.tensor_copy)
         quantize_x(2)
-        group_wa(1, wa_second, SCALAR_WA_COLUMNS[1], HALF, nc.vector.tensor_copy)
+        group_wa(1, wa_second, SCALAR_WA_COLUMNS[1] + 80, HALF, nc.vector.tensor_copy)
         quantize_x(3)
         quantize_wa(1, wa_second)
         square(1, 0)
@@ -507,6 +508,7 @@ def tile_projection_moment_gap_s3_kernel(
         project_each((2, 0), (3, 0), (0, 1), (1, 1))
         square_each((2, 0), (3, 0))
         empty_xa(4)
+        project_each((2, 1))
         scale_pair(4)
         finish_v(0, 0, 0, QUARTER)
         quantize_x(4)
@@ -514,13 +516,15 @@ def tile_projection_moment_gap_s3_kernel(
         turn_pair(6)
 
         widen_on_gpsimd(8, 2, stage_tile(2))
-        project_each((2, 1), (3, 1))
         square(0, 1)
+        project_each((3, 1))
+        square(1, 1)
         empty_xa(6)
         project_each((4, 0))
-        square(1, 1)
         project_each((5, 0))
-        square_each((2, 1), (3, 1))
+        square(2, 1)
+        sort_xa(8, sorted_tile(), nc.scalar.copy)
+        square(3, 1)
         scale_pair(6)
         finish_v(0, 0, QUARTER, HALF)
         quantize_pair_around(6, (0, 0))
@@ -568,10 +572,11 @@ def tile_projection_moment_gap_s3_kernel(
         v_grouped[2, 1] = stage_tile(3)[:, : PACK * HALF]
         finish_on_gpsimd(2, 1, 0, 112)
         finish_v(2, 0)
-        finish_v(2, 1, 112, HALF)
+        finish_v(2, 1, 112, 384)
         quantize_v(2, 0)
         quantize_v(1, 1)
         finish_v(3, 0)
+        finish_v(2, 1, 384, HALF)
         quantize_v(3, 0)
         quantize_v(2, 1)
 

@@ -418,6 +418,11 @@ def tile_projection_moment_gap_s3_kernel(
         nc.scalar.activation(out=size, in_=omega_bank[:, :ROWS], func=ABS)
         nc.scalar.activation(out=sign, in_=omega_bank[:, :ROWS], func=SIGN)
         nc.scalar.activation(out=side[:], in_=size, func=SIGN, bias=-SMALL)
+        nc.vector.memset(z_bytes[:].rearrange("p g n -> p (g n)").bitcast(I32), 0)
+        load_scale_bytes(z_bytes, z_scales)
+        nc.sync.dma_start(out=z_tile[:], in_=z_words.rearrange("g p n -> p g n"))
+        nc.sync.dma_start(out=target_rows[:], in_=target.rearrange("(ct c) n -> c ct n", c=P))
+        nc.sync.dma_start(out=prec_rows[:], in_=prec.partition_broadcast(P))
         scale_xb(0)
         scale_xb(1)
         warm_up(1, idle_bank)
@@ -438,11 +443,6 @@ def tile_projection_moment_gap_s3_kernel(
         empty_xa(0)
         first_bank = bank(6)
         warm_up(2, first_bank, x_stage[0][:, :HALF])
-        nc.vector.memset(z_bytes[:].rearrange("p g n -> p (g n)").bitcast(I32), 0)
-        load_scale_bytes(z_bytes, z_scales)
-        nc.sync.dma_start(out=z_tile[:], in_=z_words.rearrange("g p n -> p g n"))
-        nc.sync.dma_start(out=target_rows[:], in_=target.rearrange("(ct c) n -> c ct n", c=P))
-        nc.sync.dma_start(out=prec_rows[:], in_=prec.partition_broadcast(P))
         quantize_wa(0, wa_first)
         nc.vector.tensor_tensor(out=radicand_factor[:], in0=size_sign[:], in1=boost_power[:], op=MULT)
         quantize_x(0)
@@ -497,14 +497,13 @@ def tile_projection_moment_gap_s3_kernel(
         wa_second = stage_tile(STAGES)[:, : PACK * HALF]
         group_wa(1, wa_second, 0, SCALAR_WA_COLUMNS[1], nc.scalar.copy)
         square(0, 0)
-        group_wa(1, wa_second, SCALAR_WA_COLUMNS[1], SCALAR_WA_COLUMNS[1] + 80, nc.gpsimd.tensor_copy)
         quantize_x(2)
-        group_wa(1, wa_second, SCALAR_WA_COLUMNS[1] + 80, HALF, nc.vector.tensor_copy)
+        group_wa(1, wa_second, SCALAR_WA_COLUMNS[1], HALF, nc.vector.tensor_copy)
         quantize_x(3)
         quantize_wa(1, wa_second)
         square(1, 0)
 
-        widen_pair_on_gpsimd(6, stage_tile(STAGES))
+        widen_on_gpsimd(6, 2, stage_tile(STAGES))
         project_each((2, 0), (3, 0), (0, 1), (1, 1))
         square_each((2, 0), (3, 0))
         empty_xa(4)

@@ -434,8 +434,8 @@ def tile_projection_moment_gap_s3_kernel(
         nc.tensor.matmul(out=held[:, :HALF], lhsT=ones[:], rhs=prec_line, start=True, stop=True)
         turn("xa", 2, 5)
         wa_first = grouped_tile()
-        group_wa(0, wa_first, 0, 320, nc.scalar.copy)
-        group_wa(0, wa_first, 320, 320 + 192, nc.gpsimd.tensor_copy)
+        group_wa(0, wa_first, 0, 336, nc.scalar.copy)
+        group_wa(0, wa_first, 336, 336 + 176, nc.gpsimd.tensor_copy)
         nc.scalar.activation(out=boost, in_=side[:], func=COPY, scale=(1 - BOOST) / 2, bias=(1 + BOOST) / 2)
         nc.scalar.activation(
             out=power, in_=side[:], func=COPY, scale=(1 - 1 / BOOST) / DOWN / 2, bias=(1 + 1 / BOOST) / DOWN / 2
@@ -521,9 +521,7 @@ def tile_projection_moment_gap_s3_kernel(
         empty_xa(6)
         project_each((4, 0))
         project_each((5, 0))
-        square(2, 1)
-        sort_xa(8, sorted_tile(), nc.scalar.copy)
-        square(3, 1)
+        square_each((2, 1), (3, 1))
         scale_pair(6)
         finish_v(0, 0, QUARTER, HALF)
         quantize_pair_around(6, (0, 0))
@@ -531,15 +529,23 @@ def tile_projection_moment_gap_s3_kernel(
 
         for r in (8, 10):
             piece = divmod(r // 2 - 3, 2)
-            widen_pair_on_gpsimd(r + 2, stage_tile((r // 2 + 3) % STAGES))
+            shared = 112 if r in (8,) else 0
+            if shared:
+                widen_on_gpsimd(r + 2, 1, stage_tile((r // 2 + 3) % STAGES))
+            else:
+                widen_pair_on_gpsimd(r + 2, stage_tile((r // 2 + 3) % STAGES))
             square_each((r - 4, 0), (r - 3, 0))
             empty_xa(r)
+            if shared:
+                widen_on_scalar(r + 3)
+                v_grouped[piece] = grouped_tile()
+                finish_on_gpsimd(*piece, 0, shared)
             if r == 8:
-                finish_v(*piece)
-            project_block(r - 2, r + 2 if r + 2 in (10, 12) else None)
+                finish_v(*piece, shared)
+            project_block(r - 2, r + 2 if r + 2 in (12,) else None)
             scale_pair(r)
             if r == 10:
-                finish_v(*piece)
+                finish_v(*piece, shared)
             quantize_pair_around(r, piece)
             turn_pair(r + 2)
 
@@ -571,11 +577,10 @@ def tile_projection_moment_gap_s3_kernel(
         v_grouped[2, 1] = stage_tile(3)[:, : PACK * HALF]
         finish_on_gpsimd(2, 1, 0, 112)
         finish_v(2, 0)
-        finish_v(2, 1, 112, 384)
+        finish_v(2, 1, 112, HALF)
         quantize_v(2, 0)
         quantize_v(1, 1)
         finish_v(3, 0)
-        finish_v(2, 1, 384, HALF)
         quantize_v(3, 0)
         quantize_v(2, 1)
 

from contextlib import ExitStack

import concourse.mybir as mybir
from concourse.masks import make_identity

F32 = mybir.dt.float32
BF16 = mybir.dt.bfloat16
U32 = mybir.dt.uint32
I32 = mybir.dt.int32
U8 = mybir.dt.uint8
FP8 = mybir.dt.float8_e4m3fn
FP8X4 = mybir.dt.float8_e4m3fn_x4
FP4X4 = mybir.dt.float4_e2m1fn_x4
MULT = mybir.AluOpType.mult
SUBTRACT = mybir.AluOpType.subtract
SQUARE = mybir.ActivationFunctionType.Square
SQRT = mybir.ActivationFunctionType.Sqrt
COPY = mybir.ActivationFunctionType.Copy
ABS = mybir.ActivationFunctionType.Abs
SIGN = mybir.ActivationFunctionType.Sign

M, KA, KB, N, C = 2048, 512, 1024, 1024, 512
P = 128
PACK = 4
K_PASS = P * PACK
GROUPS = M // K_PASS
ROWS = GROUPS * PACK
PASSES = (KA + KB) // K_PASS
HALF = 512
QUARTER = HALF // 2
PAIR = 2 * PASSES * K_PASS
C_TILES = C // P
HELD_BANK = 7
STAGES = 4

SCALAR_WA_COLUMNS = (336, 352)
GAP = 16

DOWN, BOOST, SMALL = 2.0**-10, 2.0**22, 2.0**-40 * (1 + 2.0**-12)

MOVING, MOVING_SCALE, STATIONARY, STATIONARY_SCALE = 0, 64, 128, 192

FLOPS = 2 * M * N * (KA + KB) + 2 * C * N * M


def tile_projection_moment_gap_s3_kernel(
    tc, xa, wa, xb_bytes, xb_scale, wb_words, wb_scales, omega, z_words, z_scales, target, prec, out
):
    nc = tc.nc
    with ExitStack() as ctx:
        ctx.enter_context(tc.manual_schedule())
        keep = ctx.enter_context(tc.tile_pool(name="keep", bufs=1))
        work = ctx.enter_context(tc.tile_pool(name="work", bufs=2))
        psum = ctx.enter_context(tc.psum_pool(name="psum", bufs=1))

        def bank(i, dtype=F32, width=HALF):
            return psum.tile([P, width], dtype, name="bank%d" % i)

        def mx_tile(name, dtype, item_bytes, width, start):
            skip = start // item_bytes
            return keep.tile([P, skip + width], dtype, name=name, align_bytes=256)[:, skip:]

        def large_tile(dtype, width):
            return work.tile([P, width], dtype, name="large", bufs=8)[:]

        def plain_tile(dtype, width):
            return work.tile([P, width], dtype, name="plain", bufs=6)[:]

        def sorted_tile(width=HALF + GAP):
            return work.tile([P, width], F32, name="sorted", bufs=5)[:]

        def grouped_tile():
            return work.tile([P, PACK * HALF], BF16, name="grouped", bufs=3, align_bytes=64)[:]

        def stage_tile(i, extra=0):
            return work.tile([P, PAIR + extra], BF16, name="stage%d" % i, bufs=1, align_bytes=64)[:]

        def opening_tile(dtype, width):
            return work.tile([P, width], dtype, name="opening", bufs=1)[:]

        scale_col = keep.tile([P, 2, PACK], F32, name="scale_col")
        opening_one = opening_tile(F32, 1)
        wa_rows = [large_tile(BF16, PACK * HALF).rearrange("p (t n) -> p t n", t=PACK) for half in range(2)]
        wa_codes = mx_tile("wa_codes", U32, 4, N, MOVING)
        wa_bytes = mx_tile("wa_bytes", U8, 1, N, MOVING_SCALE)
        wb_tiles = [
            mx_tile("wb_tile%d" % half, U8, 1, 2 * 2 * HALF, MOVING).rearrange("p (g n) -> p g n", g=2)
            for half in range(2)
        ]
        wb_bytes = mx_tile("wb_bytes", U8, 1, 2 * N, MOVING_SCALE).rearrange("p (g n) -> p g n", g=2)
        z_tile = mx_tile("z_tile", U8, 1, GROUPS * 2 * C, STATIONARY).rearrange("p (g n) -> p g n", g=GROUPS)
        z_bytes = mx_tile("z_bytes", U8, 1, GROUPS * C, STATIONARY_SCALE).rearrange("p (g n) -> p g n", g=GROUPS)
        lines = keep.tile([P, 2 * HALF], BF16, name="lines")
        omega_lines = lines[:, :K_PASS]
        prec_rows = keep.tile([P, N], BF16, name="prec_rows")
        prec_line = lines[:, HALF:]
        ones = keep.tile([P, P], BF16, name="ones")
        target_rows = keep.tile([P, C_TILES, N], BF16, name="target_rows")
        ident = keep.tile([P, P], F32, name="ident")
        ident_bf16 = ident[:].bitcast(BF16)[:, 1::2]
        zeros = keep.tile([P, HALF], BF16, name="zeros")
        xb_codes = keep.tile([P, ROWS * KB], U8, name="xb_codes")
        xa_pairs = {}

        def sample_rows(src, r, count):
            g, t = divmod(r, PACK)
            return src[K_PASS * g : K_PASS * (g + 1), :].rearrange("(p t) k -> p t k", t=PACK)[:, t : t + count, :]

        def load_xa(r):
            xa_pairs[r] = keep.tile([P, 2, KA], BF16, name="xa_pair%d" % r)
            nc.sync.dma_start(out=xa_pairs[r][:], in_=sample_rows(xa, r, 2))

        def load_xb(r, count):
            rows = xb_codes[:, KB * r : KB * (r + count)].rearrange("p (t k) -> p t k", t=count)
            nc.sync.dma_start(out=rows, in_=sample_rows(xb_bytes, r, count))

        def load_wa(half):
            rows = wa.rearrange("(p t) n -> p t n", t=PACK)
            nc.sync.dma_start(out=wa_rows[half], in_=rows[:, :, HALF * half : HALF * (half + 1)])

        def load_wb(half):
            wb_view = wb_words.rearrange("g p n -> p g n")
            nc.sync.dma_start(out=wb_tiles[half][:], in_=wb_view[:, :, 2 * HALF * half : 2 * HALF * (half + 1)])

        def load_scale_bytes(tile, scale_bytes):
            rows = scale_bytes.rearrange("g (q i) n -> i q g n", i=4)
            for i in range(4):
                nc.sync.dma_start(out=tile[i:P:32].bitcast(I32), in_=rows[i].bitcast(I32))

        nc.vector.memset(zeros[:].bitcast(I32), 0)
        nc.vector.memset(ident[:], 0.0)
        make_identity(nc, ident[:], nomemset=True)
        nc.vector.memset(lines[:].bitcast(I32), 0)
        nc.vector.memset(wb_bytes[:].rearrange("p g n -> p (g n)").bitcast(I32), 0)
        nc.vector.memset(ones[:], 1.0)
        nc.vector.memset(opening_one, 1.0)

        load_xb(0, 1)
        load_xb(1, 1)
        load_xb(2, 2)
        nc.sync.dma_start(out=scale_col[:], in_=xb_scale.rearrange("o (i p t) -> p (o i) t", i=2, t=PACK))
        nc.sync.dma_start(out=omega_lines[0:GROUPS, :], in_=omega.rearrange("(g k) -> g k", g=GROUPS))
        load_wa(0)
        load_xa(0)
        nc.sync.dma_start(out=prec_line[0:1, :], in_=prec[HALF:].unsqueeze(0))
        load_xa(2)
        load_wb(0)
        load_scale_bytes(wb_bytes, wb_scales)
        load_xb(4, 2)
        load_wa(1)
        load_xa(4)
        load_wb(1)
        load_xb(6, 2)
        load_xa(6)
        load_xb(8, 4)
        load_xa(8)
        load_xa(10)
        load_xb(12, 4)
        for r in (12, 14):
            load_xa(r)

        def warm_up(count, tile, moving=zeros[:]):
            for i in range(count):
                nc.tensor.matmul(out=tile[:], lhsT=zeros[:, :P], rhs=moving, start=True, stop=True)

        def group_wa(half, grouped, c0, c1, copy):
            copy(
                out=grouped[:, PACK * c0 : PACK * c1].rearrange("p (c i t) -> p c t i", i=4, t=PACK),
                in_=wa_rows[half][:, :, c0:c1].rearrange("p t (c i) -> p c t i", i=4),
            )

        def quantize_wa(half, grouped):
            cols = slice(HALF * half, HALF * (half + 1))
            nc.vector.quantize_mx(out=wa_codes[:, cols].bitcast(FP8X4), scales=wa_bytes[:, cols], in_=grouped)

        words = {}

        def words_as_they_lie(r, s, values):
            words[r, s] = [values.bitcast(F32)[:, u::2] for u in range(2)]

        for r in range(ROWS):
            words_as_they_lie(r, 0, xa_pairs[r - r % 2][:, r % 2, :])

        def xb_values(r, count):
            return xb_codes[:, KB * r : KB * (r + count)].bitcast(FP8)

        def note_sorted(r, count, halves):
            for i in range(count):
                for s in range(1, PASSES):
                    first = P * (2 * i + s - 1)
                    words[r + i, s] = [halves[:, u, :].bitcast(F32)[:, first : first + P] for u in range(2)]

        def widen_on_vector(r, unit):
            halves = sorted_tile().bitcast(BF16).rearrange("p (u k) -> p u k", u=2)[:, :, :HALF]
            nc.vector.tensor_scalar(
                out=halves.rearrange("p u (m e) -> p u m e", e=2),
                in0=xb_values(r, 1).rearrange("p (m u e) -> p u m e", u=2, e=2),
                scalar1=unit,
                scalar2=None,
                op0=MULT,
            )
            note_sorted(r, 1, halves)

        def widen_on_scalar(r):
            halves = plain_tile(BF16, KB).rearrange("p (u k) -> p u k", u=2)
            nc.scalar.copy(
                out=halves.rearrange("p u (m e) -> p u m e", e=2),
                in_=xb_values(r, 1).rearrange("p (m u e) -> p u m e", u=2, e=2),
            )
            note_sorted(r, 1, halves)

        def widen_on_gpsimd(r, count, tile):
            halves = tile[:, : count * KB].rearrange("p (u k) -> p u k", u=2)
            nc.gpsimd.tensor_copy(
                out=halves.rearrange("p u (m e) -> p m u e", e=2),
                in_=xb_values(r, count).rearrange("p (m u e) -> p m u e", u=2, e=2),
            )
            note_sorted(r, count, halves)

        def parts_of(operand, r):
            return [(r, 0), (r + 1, 0)] if operand == "xa" else [(r, 1), (r, 2)]

        def sort_xa(r, tile, copy):
            values = xa_pairs[r][:].rearrange("p i k -> p (i k)")
            copy(
                out=tile[:, :HALF].rearrange("p (i u c j) -> p i c u j", i=2, u=2, j=4),
                in_=values.bitcast(F32).rearrange("p (i c j u) -> p i c u j", i=2, j=4, u=2),
            )
            for i, part in enumerate(parts_of("xa", r)):
                words[part] = [tile[:, P * (2 * i + u) : P * (2 * i + u + 1)] for u in range(2)]

        turned = {}

        def turn(operand, r, where):
            tile = bank(where)
            turned[operand, r] = tile
            for i, part in enumerate(parts_of(operand, r)):
                for u in range(2):
                    nc.tensor.transpose(tile[:, P * (2 * u + i) : P * (2 * u + i + 1)], words[part][u], ident[:])

        x_stage = {}
        x_grouped = {}

        def grouped_pair(r):
            if r // 2 not in x_grouped:
                x_stage[r // 2] = stage_tile(r // 2 % STAGES, PACK * HALF if r // 2 == 6 else 0)
                x_grouped[r // 2] = x_stage[r // 2][:, :PAIR].rearrange("p (s k) -> p s k", k=K_PASS)
            return x_grouped[r // 2]

        def empty_xa(r):
            nc.scalar.copy(
                out=grouped_pair(r)[:, 0 : PASSES + 1 : PASSES, :].bitcast(F32).rearrange("p i (m u) -> p i m u", u=2),
                in_=turned["xa", r][:].rearrange("p (u i m) -> p i m u", i=2, u=2),
            )

        def scale_xb(r):
            first = PASSES * (r % 2) + 1
            nc.vector.tensor_tensor(
                out=grouped_pair(r)[:, first : first + 2, :].rearrange("p i (m u e) -> p i m u e", u=2, e=2),
                in0=turned["xb", r][:].bitcast(BF16).rearrange("p (u i m e) -> p i m u e", u=2, i=2, e=2),
                in1=scale_col[:].rearrange("p i (u e) -> p i u e", u=2).unsqueeze(2).to_broadcast([P, 2, P, 2, 2]),
                op=MULT,
            )

        x_codes = {}

        def quantize_x(r):
            both = mx_tile("x_codes%d" % r, U32, 4, PASSES * P + PASSES * P // PACK, STATIONARY)
            codes, scale_bytes = both[:, : PASSES * P], both[:, PASSES * P :].bitcast(U8)
            first = PASSES * (r % 2)
            nc.vector.quantize_mx(
                out=codes.bitcast(FP8X4),
                scales=scale_bytes,
                in_=x_grouped[r // 2][:, first : first + PASSES, :].rearrange("p s k -> p (s k)"),
            )
            x_codes[r] = (codes, scale_bytes)

        products = {}

        def project(r, half, tile, c0=0, width=HALF):
            products[r, half, c0] = tile[:, :width]
            first = HALF * half + c0
            cols = slice(first, first + width)
            codes, scale_bytes = x_codes[r]
            for s in range(PASSES):
                if s == 0:
                    rhs, rhs_scale = wa_codes[:, cols].bitcast(FP8X4), wa_bytes[:, cols]
                else:
                    rhs = wb_tiles[half][:, s - 1, 2 * c0 : 2 * (c0 + width)].bitcast(FP4X4)
                    rhs_scale = wb_bytes[:, s - 1, cols]
                nc.tensor.matmul_mx(
                    out=tile[:, :width],
                    lhsT=codes[:, P * s : P * (s + 1)].bitcast(FP8X4),
                    lhsT_scale=scale_bytes[:, P * s : P * (s + 1)],
                    rhs=rhs,
                    rhs_scale=rhs_scale,
                    start=(s == 0),
                    stop=(s == PASSES - 1),
                )

        root = keep.tile([P, ROWS], F32, name="root")
        radicand_factor = keep.tile([P, 2 * ROWS], BF16, name="radicand_factor")
        radicand, factor = radicand_factor[:, :ROWS], radicand_factor[:, ROWS:]
        squares = {}

        def square(r, half, c0=0, width=HALF):
            g, t = divmod(r, PACK)
            if (g, half) not in squares:
                squares[g, half] = large_tile(BF16, PACK * HALF).rearrange("p (a n e) -> p a n e", a=2, e=2)
            nc.scalar.activation(
                out=squares[g, half][:, t // 2, c0 : c0 + width, t % 2],
                in_=products[r, half, c0],
                func=SQUARE,
                scale=root[:, r : r + 1],
            )

        v_grouped = {}
        v_codes = {}

        def finish_columns(g, half, c0, c1, engine, factors):
            engine.tensor_tensor(
                out=v_grouped[g, half].rearrange("p (n a e) -> p n a e", a=2, e=2)[:, c0:c1],
                in0=squares[g, half].rearrange("p a n e -> p n a e")[:, c0:c1],
                in1=factors[:, PACK * g : PACK * (g + 1)]
                .rearrange("p (a e) -> p a e", a=2)
                .unsqueeze(1)
                .to_broadcast([P, c1 - c0, 2, 2]),
                op=MULT,
            )

        def finish_v(g, half, c0=0, c1=HALF):
            if (g, half) not in v_grouped:
                v_grouped[g, half] = grouped_tile()
            finish_columns(g, half, c0, c1, nc.vector, held[:, HALF:])

        def finish_on_gpsimd(g, half, c0, c1):
            finish_columns(g, half, c0, c1, nc.gpsimd, factor)

        def quantize_v(g, half, c0=0, c1=HALF):
            if (g, half) not in v_codes:
                v_codes[g, half] = (
                    mx_tile("v_codes%d_%d" % (g, half), U32, 4, HALF, MOVING),
                    mx_tile("v_bytes%d_%d" % (g, half), U8, 1, HALF, MOVING_SCALE),
                )
            codes, scale_bytes = v_codes[g, half]
            nc.vector.quantize_mx(
                out=codes[:, c0:c1].bitcast(FP8X4),
                scales=scale_bytes[:, c0:c1],
                in_=v_grouped[g, half][:, PACK * c0 : PACK * c1],
            )

        tiles = [(c0, HALF, ct) for c0 in (0, HALF) for ct in range(C_TILES)][:-2]
        tiles = tiles + [(c0, QUARTER, ct) for ct in (C_TILES - 2, C_TILES - 1) for c0 in (HALF, HALF + QUARTER)]
        sums, gaps, results = {}, {}, {}

        def moment(i, where, groups=range(GROUPS)):
            c0, width, ct = tiles[i]
            if i not in sums:
                sums[i] = bank(where)
            cols = slice(c0 % HALF, c0 % HALF + width)
            for g in groups:
                codes, scale_bytes = v_codes[g, c0 // HALF]
                nc.tensor.matmul_mx(
                    out=sums[i][:, :width],
                    lhsT=z_tile[:, g, 2 * P * ct : 2 * P * (ct + 1)].bitcast(FP4X4),
                    lhsT_scale=z_bytes[:, g, P * ct : P * (ct + 1)],
                    rhs=codes[:, cols].bitcast(FP8X4),
                    rhs_scale=scale_bytes[:, cols],
                    start=(g == 0),
                    stop=(g == GROUPS - 1),
                )

        def subtract_target(i):
            c0, width, ct = tiles[i]
            gaps[i] = plain_tile(F32, width)
            nc.vector.tensor_tensor(
                out=gaps[i], in0=sums[i][:, :width], in1=target_rows[:, ct, c0 : c0 + width], op=SUBTRACT
            )

        def scale_on_gpsimd(i, tile=None):
            c0, width, ct = tiles[i]
            results[i] = large_tile(F32, width) if tile is None else tile
            nc.gpsimd.tensor_tensor(out=results[i], in0=gaps[i], in1=prec_rows[:, c0 : c0 + width], op=MULT)

        def scale_on_vector(i):
            c0, width, ct = tiles[i]
            results[i] = sorted_tile(width)
            nc.vector.tensor_tensor(out=results[i], in0=gaps[i], in1=held[:, c0 - HALF : c0 - HALF + width], op=MULT)

        def store(i):
            c0, width, ct = tiles[i]
            queue = nc.scalar if i in (0, 1, 2, 3, 6, 7) else nc.sync
            queue.dma_start(out=out[P * ct : P * (ct + 1), c0 : c0 + width], in_=results[i])

        def take(ring):
            ring.append(ring.pop(0))
            return ring[-1]

        size_sign = keep.tile([P, 2 * ROWS], F32, name="size_sign")
        boost_power = keep.tile([P, 2 * ROWS], F32, name="boost_power")
        size, sign, boost, power = size_sign[:, :ROWS], size_sign[:, ROWS:], boost_power[:, :ROWS], boost_power[:, ROWS:]
        side = keep.tile([P, ROWS], F32, name="side")
        idle_bank = bank(HELD_BANK)
        warm_up(4, idle_bank)
        nc.scalar.activation(out=root[:], in_=zeros[:, :ROWS], func=SQRT)
        widen_on_vector(0, opening_one)
        widen_on_vector(1, opening_one)
        turn("xb", 0, 0)
        warm_up(1, idle_bank)
        omega_bank = bank(6)
        for t in range(PACK):
            nc.tensor.matmul(
                out=omega_bank[:, t:ROWS:PACK], lhsT=omega_lines[:, t::PACK], rhs=ident_bf16[:, :GROUPS], start=True, stop=True
            )
        turn("xb", 1, 1)
        widen_on_scalar(2)
        widen_on_gpsimd(3, 1, opening_tile(BF16, KB))
        nc.scalar.activation(out=size, in_=omega_bank[:, :ROWS], func=ABS)
        nc.scalar.activation(out=sign, in_=omega_bank[:, :ROWS], func=SIGN)
        nc.scalar.activation(out=side[:], in_=size, func=SIGN, bias=-SMALL)
        nc.vector.memset(z_bytes[:].rearrange("p g n -> p (g n)").bitcast(I32), 0)
        load_scale_bytes(z_bytes, z_scales)
        nc.sync.dma_start(out=z_tile[:], in_=z_words.rearrange("g p n -> p g n"))
        nc.sync.dma_start(out=target_rows[:], in_=target.rearrange("(ct c) n -> c ct n", c=P))
        nc.sync.dma_start(out=prec_rows[:], in_=prec.partition_broadcast(P))
        scale_xb(0)
        scale_xb(1)
        warm_up(1, idle_bank)
        turn("xb", 2, 2)
        warm_up(1, idle_bank)
        turn("xa", 0, 3)
        turn("xb", 3, 4)
        held = bank(HELD_BANK, BF16, 2 * HALF)
        nc.tensor.matmul(out=held[:, :HALF], lhsT=ones[:], rhs=prec_line, start=True, stop=True)
        turn("xa", 2, 5)
        wa_first = grouped_tile()
        group_wa(0, wa_first, 0, 336, nc.scalar.copy)
        group_wa(0, wa_first, 336, 336 + 176, nc.gpsimd.tensor_copy)
        nc.scalar.activation(out=boost, in_=side[:], func=COPY, scale=(1 - BOOST) / 2, bias=(1 + BOOST) / 2)
        nc.scalar.activation(
            out=power, in_=side[:], func=COPY, scale=(1 - 1 / BOOST) / DOWN / 2, bias=(1 + 1 / BOOST) / DOWN / 2
        )
        empty_xa(0)
        first_bank = bank(6)
        warm_up(2, first_bank, x_stage[0][:, :HALF])
        quantize_wa(0, wa_first)
        nc.vector.tensor_tensor(out=radicand_factor[:], in0=size_sign[:], in1=boost_power[:], op=MULT)
        quantize_x(0)
        quantize_x(1)

        turn_banks, product_banks = [0, 1, 2], [3, 5, 4, 6]

        def turn_pair(r):
            turn("xb", r, 0)
            turn("xa", r, 2)
            turn("xb", r + 1, 1)

        def widen_pair_on_gpsimd(r, stage):
            for i in range(2):
                widen_on_gpsimd(r + i, 1, stage[:, KB * i :])

        def project_each(*parts):
            for r, half in parts:
                project(r, half, bank(take(product_banks)))

        def square_each(*parts):
            for r, half in parts:
                square(r, half)

        def scale_pair(r):
            scale_xb(r)
            scale_xb(r + 1)

        def quantize_pair_around(r, piece):
            quantize_x(r)
            quantize_v(*piece)
            quantize_x(r + 1)

        def project_block(r, sort=None):
            project_each((r - 2, 1), (r - 1, 1))
            square(r - 2, 1)
            project_each((r, 0))
            if sort:
                sort_xa(sort, sorted_tile(), nc.scalar.copy)
            square(r - 1, 1)
            project_each((r + 1, 0))

        widen_on_gpsimd(5, 1, stage_tile(0))
        empty_xa(2)
        widen_on_scalar(4)
        nc.scalar.activation(out=root[:], in_=radicand, func=SQRT, scale=DOWN)
        project(0, 0, first_bank)
        project_each((1, 0))
        scale_pair(2)
        turn_pair(4)
        nc.tensor.matmul(out=held[:, HALF : HALF + ROWS], lhsT=ident_bf16, rhs=factor, start=True, stop=True)
        wa_second = stage_tile(STAGES)[:, : PACK * HALF]
        group_wa(1, wa_second, 0, SCALAR_WA_COLUMNS[1], nc.scalar.copy)
        square(0, 0)
        quantize_x(2)
        group_wa(1, wa_second, SCALAR_WA_COLUMNS[1], HALF, nc.vector.tensor_copy)
        quantize_x(3)
        quantize_wa(1, wa_second)
        square(1, 0)

        widen_on_gpsimd(6, 2, stage_tile(STAGES))
        project_each((2, 0), (3, 0), (0, 1), (1, 1))
        square_each((2, 0), (3, 0))
        empty_xa(4)
        project_each((2, 1))
        scale_pair(4)
        finish_v(0, 0, 0, QUARTER)
        quantize_x(4)
        quantize_x(5)
        turn_pair(6)

        widen_on_gpsimd(8, 2, stage_tile(2))
        square(0, 1)
        project_each((3, 1))
        square(1, 1)
        empty_xa(6)
        project_each((4, 0))
        project_each((5, 0))
        square_each((2, 1), (3, 1))
        scale_pair(6)
        finish_v(0, 0, QUARTER, HALF)
        quantize_pair_around(6, (0, 0))
        turn_pair(8)

        for r in (8, 10):
            piece = divmod(r // 2 - 3, 2)
            shared = 112 if r in (8,) else 0
            if shared:
                widen_on_gpsimd(r + 2, 1, stage_tile((r // 2 + 3) % STAGES))
            else:
                widen_pair_on_gpsimd(r + 2, stage_tile((r // 2 + 3) % STAGES))
            square_each((r - 4, 0), (r - 3, 0))
            empty_xa(r)
            if shared:
                widen_on_scalar(r + 3)
                v_grouped[piece] = grouped_tile()
                finish_on_gpsimd(*piece, 0, shared)
            if r == 8:
                finish_v(*piece, shared)
            project_block(r - 2, r + 2 if r + 2 in (12,) else None)
            scale_pair(r)
            if r == 10:
                finish_v(*piece, shared)
            quantize_pair_around(r, piece)
            turn_pair(r + 2)

        widen_pair_on_gpsimd(14, stage_tile(1))
        square_each((8, 0), (9, 0))
        empty_xa(12)
        project_block(10)
        scale_pair(12)
        v_grouped[1, 1] = x_stage[6][:, PAIR - PACK * 192 : PAIR + PACK * (HALF - 192)]
        finish_v(1, 1, 192, HALF)
        quantize_x(12)
        quantize_x(13)
        turn_pair(14)

        late = [(10, 1), (11, 1), (12, 0), (13, 0), (14, 0), (15, 0), (12, 1), (13, 1), (14, 1), (15, 1)]
        project_each(*late[:2])
        square_each((10, 0), (11, 0))
        finish_on_gpsimd(1, 1, 0, 192)
        empty_xa(14)
        scale_pair(14)
        quantize_x(14)
        quantize_x(15)
        project_each(*late[2:4])
        product_banks.extend(turn_banks)
        for i in range(4, len(late)):
            square(*late[i - 4])
            project_each(late[i])
        square_each(*late[-4:])
        v_grouped[2, 1] = stage_tile(3)[:, : PACK * HALF]
        finish_on_gpsimd(2, 1, 0, 112)
        finish_v(2, 0)
        finish_v(2, 1, 112, HALF)
        quantize_v(2, 0)
        quantize_v(1, 1)
        finish_v(3, 0)
        quantize_v(3, 0)
        quantize_v(2, 1)

        def moment_gap(i):
            moment(i, take(product_banks))
            subtract_target(i)

        moment_gap(0)
        scale_on_gpsimd(0)
        finish_v(3, 1)
        moment_gap(1)
        quantize_v(3, 1)
        scale_on_gpsimd(1, v_grouped[3, 1].bitcast(F32)[:, HALF:])
        moment_gap(2)
        scale_on_gpsimd(2)
        moment(4, take(product_banks), range(3))
        moment(3, take(product_banks), range(2))
        moment(4, None, [3])
        moment(3, None, [2, 3])
        subtract_target(4)
        subtract_target(3)
        scale_on_gpsimd(3)
        scale_on_vector(4)
        moment_gap(5)
        moment_gap(6)
        scale_on_gpsimd(6)
        scale_on_vector(5)
        moment_gap(7)
        scale_on_gpsimd(7)
        moment_gap(8)
        moment_gap(9)
        scale_on_vector(8)
        scale_on_vector(9)
        for i in (0, 1, 4, 2, 5, 3, 6, 7, 8, 9):
            store(i)
